import numpy as np, ml_dtypes
CORES = [2,6,10,14,18,22,26,30]
N = 8
BF = ml_dtypes.bfloat16
def gentries(a):
    return np.ascontiguousarray(a.reshape(8, 16, -1).transpose(0, 2, 1)).reshape(8, -1)
def gtable(e):
    e = np.asarray(e); return np.ascontiguousarray(e.reshape(8, -1, 16).transpose(0, 2, 1)).reshape(128, -1).astype(np.int32)
M, MB, Q, BASE, L, LA, T, C = 4096, 12, 2048, 1920, 256, 64, 3, 11
def boxes(rng):
    c = rng.integers(-255, 256, (2, N, 8, 8, M))
    return np.concatenate([np.minimum(c[0], c[1]), -np.maximum(c[0], c[1])], axis=2)
def tags(rng):
    u = rng.integers(0, 20, (N, 8, 16, BASE))
    return (u >= 8).astype(np.int64) + (u >= 15)
def grow(rng, fill):
    tag = tags(rng); name = np.where(tag == 0, rng.integers(1, M, tag.shape), rng.integers(1, BASE, tag.shape))
    return np.where(rng.random(tag.shape) < fill, name + M * tag, 0)
def starts(rng):
    v = rng.integers(1, BASE, (N, 8, T, L)); few = rng.integers(1, BASE, (N, 8, T, 12))
    return np.where(rng.random(v.shape) < 0.3, np.take_along_axis(few, rng.integers(0, 12, v.shape), 3), v)
def pack(R, e, x, v):
    return {"rg": R.reshape(N, 128, M).astype(np.float32).astype(BF), "nd": np.ascontiguousarray(e.reshape(N, 128, BASE)).astype(np.int32),
            "z": np.concatenate([x, -x], axis=2).reshape(N, 128, L).astype(np.float32).astype(BF), "vs": np.stack([gtable(a.reshape(8, -1)) for a in v])}
def setup_inputs(rng):
    fill = rng.choice(np.array([0.0, 0.3, 0.5, 0.7, 0.85, 0.85, 0.95, 1.0]), (N, 8, 1, BASE))
    return pack(boxes(rng), grow(rng, fill), rng.integers(-255, 256, (N, 8, 8, L)), starts(rng))
def setup_inputs_spread(rng):
    R = np.floor(511 * rng.random((N, 8, 16, M)) ** rng.choice(np.array([0.5, 1.0, 2.0, 4.0, 4.0]), (N, 8, 1, M))).astype(np.int64) - 255
    x = np.floor(511 * rng.random((N, 8, 8, L)) ** rng.choice(np.array([0.5, 1.0, 2.0]), (N, 8, 1, L))).astype(np.int64) - 255
    tag = tags(rng); u = rng.random(tag.shape)
    name = 1 + np.where(tag == 0, np.floor((M - 1) * u ** 3), np.floor((BASE - 1) * u ** 2)).astype(np.int64)
    e = np.where(rng.random(tag.shape) < rng.choice(np.array([0.2, 0.5, 0.8, 0.95, 1.0]), (N, 8, 1, BASE)), name + M * tag, 0)
    return pack(R, e, x, 1 + np.floor((BASE - 1) * rng.random((N, 8, T, L)) ** 2).astype(np.int64))
def setup_inputs_ties(rng):
    c = rng.integers(-200, 201, (2, 8, 8, 5)); lo = np.minimum(c[0], c[1]); hi = np.maximum(c[0], c[1])
    tm = np.broadcast_to(np.concatenate([lo, -hi], axis=1), (N, 8, 16, 5))
    R = np.take_along_axis(tm, rng.integers(0, 5, (N, 8, 1, M)), 3)
    R = R + rng.integers(-1, 2, R.shape) * (rng.random(R.shape) < 0.02)
    k = rng.integers(0, 5, (N, 8, 1, L))
    x = np.where(rng.random((N, 8, 8, L)) < 0.5, np.take_along_axis(np.broadcast_to(lo, (N, 8, 8, 5)), k, 3), np.take_along_axis(np.broadcast_to(hi, (N, 8, 8, 5)), k, 3))
    x = x + rng.integers(-1, 2, x.shape)
    return pack(R, grow(rng, rng.choice(np.array([0.3, 0.6, 0.85, 1.0]), (N, 8, 1, BASE))), x, starts(rng))
def setup_inputs_ends(rng):
    F = np.array([1, 2, M - 2, M - 1]); B = np.array([3, 6, M - 5, M - 10]); B3 = (B[:, None] + np.arange(3)).reshape(-1)
    kind = rng.choice(np.array([0, 0, 1, 1, 2, 2, 3, 4, 4]), (N, 8, M)); u = rng.integers(15 - C, 18 - C, (N, 8, M))
    off = rng.random((N, 8, M)) < 0.25; off[:, :, F] = False; u[:, :, F] = 16 - C
    kind[:, :, B3] = 0; off[:, :, B3] = False
    for g in range(8):
        kind[:, g, F] = 1 + (g & 1)
        if (g >> 1) & 1 == 0: off[:, g, 1:3] = True
    few = np.where((np.arange(8)[:, None] + rng.integers(0, 8, (N, 8, 1, M))) % 8 < u[:, :, None, :], 255, -255); k = kind[:, :, None, :]
    any_ = np.where(rng.random((N, 8, 16, M)) < 0.6, -255, 255)
    low = np.where(k == 0, -255, np.where(k == 2, few, np.where(k == 4, any_[:, :, :8], 255)))
    neg = np.where(k == 0, -255, np.where(k == 1, few, np.where(k == 4, any_[:, :, 8:], 255)))
    R = np.concatenate([low, neg], axis=2)
    at = np.where(kind == 2, 8, 0) + rng.integers(0, 8, (N, 8, M))
    off[:, :, B3] = False
    R = np.where((np.arange(16)[:, None] == at[:, :, None, :]) & off[:, :, None, :], R - np.sign(R), R)
    w = rng.choice(np.array([0, 0, 0, 1, 1, 1, 2, 3]), (N, 8, 1, L)); w[..., 0] = 1; w[..., 1] = 0; w[..., L - 2] = 1; w[..., L - 1] = 0
    r = np.where(rng.random((N, 8, 8, L)) < 0.5, -255, 255); one = np.where(np.arange(8)[:, None] == rng.integers(0, 8, (N, 8, 1, L)), -255, 255)
    x = np.where(w == 0, 255, np.where(w == 1, -255, np.where(w == 2, r, one)))
    tag = tags(rng); e1 = rng.choice(F, tag.shape); e2 = rng.choice(np.array([1, 2, BASE - 2, BASE - 1]), tag.shape); h = rng.random(tag.shape) < 0.5
    name = np.where(tag == 0, np.where(h, e1, rng.integers(1, M, tag.shape)), np.where(h, e2, rng.integers(1, BASE, tag.shape)))
    p = rng.random(tag.shape); e = np.where(p < 0.42, 0, np.where(p < 0.66, 2 * M + BASE - 1, name + M * tag))
    for c in (1, BASE - 1):
        for i, n in ((0, M - 1), (1, M - 2), (2, M + BASE - 2), (13, M + 2), (14, 2), (15, 1)): e[:, :, i, c] = n
    few_nodes = np.array([3, 4, BASE - 4, BASE - 3])
    for j in range(4):
        e[:, :, :, few_nodes[j]] = 0
        for i, n in ((0, B[j] + 2), (7, B[j] + 1), (15, B[j])): e[:, :, i, few_nodes[j]] = n
    p = rng.random((N, 8, T, L)); v = np.where(p < 0.33, 1, np.where(p < 0.66, BASE - 1, rng.integers(1, BASE, p.shape)))
    v[..., 0] = 1; v[..., 1] = BASE - 1; v[..., L - 2] = 1; v[..., L - 1] = BASE - 1
    v[..., L - 10:L - 2] = np.tile(few_nodes, 2)
    return pack(R, e, x, v)
def pairs(rng, mode, P):
    if mode in (0, 1):
        a = np.full(LA, P[0]); b = np.full(LA, P[1])
        if mode == 1: j = int(rng.choice(np.array([0, LA - 1, rng.integers(0, LA)]))); a[j] = P[2]; b[j] = P[3]
        return a, b
    a = P[:LA].copy(); b = P[LA:].copy()
    if mode == 3: b[:] = P[LA]
    if mode == 4: b = P[1:LA + 1].copy()
    if mode == 5: a[LA - 1] = a[0]; b[LA - 1] = b[0]
    return a, b
def staged(rng, mode, tight, fill):
    R = boxes(rng); e = grow(rng, fill); x = rng.integers(-255, 256, (N, 8, 8, L)); v = starts(rng); P0 = BASE - 2 * T * LA
    for g in range(8):
        if mode[0, g] < 0: continue
        x[:, g] = rng.integers(-100, 101, (N, 8, L))
        for t in range(T):
            R[:, g, :, P0 + 2 * t * LA:P0 + 2 * (t + 1) * LA] = 40 * t - 255; R[:, g, :, M - (t + 1) * LA:M - t * LA] = 40 * t - 255
        R[:, g, :, Q:Q + 16] = 255; R[:, g, :8, Q + 8:Q + 16] = -255
        for q in range(N):
            for t in range(T):
                P = P0 + 2 * t * LA + rng.permutation(2 * LA); a, b = pairs(rng, int(mode[q, g]), P); sh = (16, LA); pad = Q + rng.integers(0, 16, sh)
                vals = np.zeros(sh, np.int64); nf = rng.choice(np.array([0, 1, 2, 5, 13]), LA) if tight and t % 2 == 0 else np.full(LA, 13)
                vals[0] = M + b
                if t % 2 == 0:
                    vals[2] = np.where(rng.random(LA) < 0.5, M + P0 + 2 * (t + 1) * LA - 1, 0); ty = rng.integers(0, 6, (1, LA))
                    if mode[q, g] == 2: vals[2, 0] = 0; nf[0] = 13; ty[0, 0] = 2
                    row = np.where(ty == 5, rng.integers(0, 5, sh), ty)
                    bf = np.where(row == 0, 0, np.where(row == 1, rng.integers(1, BASE, sh) + M * rng.integers(1, 3, sh), np.where(row == 2, M + P[rng.integers(0, 2 * LA, sh)],
                         np.where(row == 3, Q + rng.integers(0, 8, sh), Q + 8 + rng.integers(0, 8, sh)))))
                else:
                    c = M - 1 - np.arange(LA) - t * LA; vals[1] = c; vals[2] = np.where(rng.random(LA) < 0.5, c, 0)
                    room = rng.choice(np.array([0, 1, 2, 16]) if tight else np.array([1, 2, 9, 16]), (1, LA))
                    bf = np.where(np.argsort(rng.random(sh), axis=0) < room, 0, pad)
                vals[3:] = np.where(np.arange(3, 16)[:, None] < 16 - nf, pad[3:], 0)
                if t % 2 == 1: vals[3:5] = np.where(rng.random(LA) < 0.3, c, 0)
                ac = np.take_along_axis(vals, np.argsort(rng.random(sh), axis=0), 0)
                ev = e[q, g]; ev[:, b] = bf; ev[:, a] = ac
                v[(q - t) % N, g, t, :LA] = a
    return pack(R, e, x, v)
def setup_inputs_crowd(rng):
    mode = rng.integers(0, 6, (N, 8)); mode[0] = rng.permutation(np.array([0, 0, 1, 1, 2, 3, 4, 5])); mode[1] = 2; mode[1, rng.integers(0, 8)] = 5; mode[N - 1] = 2
    return staged(rng, mode, False, 0.6)
def setup_inputs_corners(rng):
    mode = rng.integers(0, 6, (N, 8)); mode[0] = rng.permutation(np.array([0, 1, 2, 2, 3, 4, 4, 5])); mode[:, rng.permutation(8)[:2]] = -1
    return staged(rng, mode, True, rng.choice(np.array([0.0, 0.06, 0.5, 0.94, 0.94, 1.0]), (N, 8, 1, BASE)))
def check_inputs(d):
    bad = []
    for k, lo, hi in (("rg", -255, 255), ("z", -255, 255), ("nd", 0, 2 * M + BASE - 1), ("vs", 1, BASE - 1)):
        a = np.asarray(d[k]).astype(np.float64)
        if not np.all((a >= lo) & (a <= hi)): bad.append("range of " + k)
        elif np.any(a != np.floor(a)): bad.append("whole numbers of " + k)
    a = np.asarray(d["nd"]).astype(np.int64); n = a & (M - 1)
    if np.any((a >= M) & ((n < 1) | (n >= BASE))): bad.append("names of nd")
    a = np.asarray(d["z"]).astype(np.float32).reshape(-1, 2, 8, L)
    if np.any(a[:, 0] != -a[:, 1]): bad.append("halves of z")
    return bad
def take(a, i):
    return np.take_along_axis(a, i[:, :, None, :], 3)
def pick(a, i):
    return np.take_along_axis(a, i.reshape(N, 8, -1), 2).reshape(i.shape)
def reference(rg, nd, z, vs):
    R = rg.astype(np.float32).astype(np.int16).reshape(N, 8, 16, M); X = z.astype(np.float32).astype(np.int16).reshape(N, 8, 16, L)
    W = np.stack([gentries(a) for a in vs]).astype(np.int64).reshape(N, 8, T, L)
    D = np.zeros((N, 8, 16, Q), np.int64); D[..., :BASE] = nd.reshape(N, 8, 16, BASE)
    G = np.zeros((N, 8, 3, L), np.int64); A = np.zeros(N, np.int64); LOW = -2 ** 40
    for t in range(T):
        home = (np.arange(N) - t) % N
        x = X[home]; g = G[home]; need = (C - (A[home] & 1)).reshape(N, 1, 1, 1); S = np.add.reduce(R, axis=2, dtype=np.int64)
        n = np.stack([np.add.reduce(x >= take(R, g[:, :, k]), axis=2, dtype=np.int64) for k in range(3)], axis=2)
        keep = (g > 0) & (n >= need); g = np.where(keep, g, 0); gs = np.where(keep, pick(S, g), -2 ** 20)
        h = np.zeros_like(g); v = W[home][:, :, t]
        for s in (2, 1, 0):
            e = take(D, v); nm = e & (M - 1); tg = e >> MB
            n = np.add.reduce(x[:, :, :, None, :] >= take(R, nm.reshape(N, 8, 16 * L)).reshape(N, 8, 16, 16, L), axis=2, dtype=np.int64)
            ok = (e > 0) & (n >= need); score = pick(S, nm)
            for k in range(s + 1):
                best = np.max(np.where(ok & (tg == k), score * M + (M - 1 - nm), LOW), axis=2)
                new = (best > LOW) & ((best >> MB) > gs[:, :, k])
                g[:, :, k] = np.where(new, M - 1 - (best & (M - 1)), g[:, :, k]); gs[:, :, k] = np.where(new, best >> MB, gs[:, :, k]); h[:, :, k] = np.where(new, v, h[:, :, k])
            if s > 0: v = np.where(g[:, :, s] > 0, g[:, :, s], v)
        even = t % 2 == 0
        a = h[:, :, 1 if even else 0, :LA]; b = g[:, :, 1, :LA] if even else v[:, :, :LA]
        ea = take(D, a); eb = take(D, b)
        ask = (a > 0) & (a != b) & np.any((ea if even else eb) == 0, axis=2)
        a1 = a[:, :, :, None]; b1 = b[:, :, :, None]; a2 = a[:, :, None, :]; b2 = b[:, :, None, :]
        meet = ((a1 == a2) | (a1 == b2) | (b1 == a2) | (b1 == b2)) & ask[:, :, None, :] & np.tri(LA, LA, -1, dtype=bool)
        act = ask & ~np.any(meet, axis=3); A[home] = np.add.reduce(act, axis=(1, 2), dtype=np.int64)
        q, p, l = np.nonzero(act); al = a[q, p, l]; bl = b[q, p, l]
        if even:
            nb = eb & (M - 1); full = eb > 0
            go = full & (pick(R[:, :, t], nb) >= x[:, :, t, None, :LA]); stay = full & ~go & (pick(R[:, :, 8 + t], nb) >= x[:, :, 8 + t, None, :LA])
            strad = full & ~go & ~stay; number = np.add.accumulate(strad, axis=2, dtype=np.int64)
            free = ea == 0; place = np.add.accumulate(free, axis=2, dtype=np.int64) - free
            put = strad & (number < np.add.reduce(free, axis=2, dtype=np.int64)[:, :, None, :])
            new = BASE + LA * (t >> 1) + np.arange(LA)
            ya = np.where(free & (place == 0), M + new, ea)
            for j in range(16):
                ya = np.where(free & put[:, :, j:j + 1] & (place == number[:, :, j:j + 1]), eb[:, :, j:j + 1], ya)
            yb = np.where(go | put, 0, eb); yw = np.where(go, eb, 0)
            D[q, p, :, new[l]] = yw[q, p, :, l]
            cut = R[q, p, :, bl]; half = cut.copy(); half[:, t] = x[q, p, t, l]; cut[:, 8 + t] = x[q, p, 8 + t, l]
            R[q, p, :, new[l]] = half; R[q, p, :, bl] = cut
        else:
            e0 = g[:, :, 0, None, :LA]; free = eb == 0; place = np.add.accumulate(free, axis=2, dtype=np.int64) - free
            ya = np.where(ea == e0, 0, ea); yb = np.where(free & (place == 0), e0, eb)
        D[q, p, :, al] = ya[q, p, :, l]; D[q, p, :, bl] = yb[q, p, :, l]
        G[home] = g
    return {"yn": D.reshape(N, 128, Q).astype(np.float32), "yr": R[..., :Q].reshape(N, 128, Q).astype(np.float32).astype(BF), "yg": g.reshape(N, 8, 3 * L).astype(np.float32)}

@@ -1,0 +1,639 @@
+from concourse.bass import DstId, RemoteDMATransfer
+from concourse.mybir import AluOpType as AL, ActivationFunctionType as AF
+
+M, Q, BASE, L, LA = 4096, 2048, 1920, 256, 64
+PATHS = "FFCA FFCA FFCA FFCA FFCA FFCA FFCA FFCA FFCA FFCA FFCA FFCA FFCA FFCA FFCA FFCA FFCA FFCA".split()
+SPLIT = 1
+MODEL = dict(cy=1.0e-3, g=1.56, sc=3.8, pe=0.5, lat=0.1, bw=180e3)
+TUNE = dict(slack=0.05, seed=934, noise=0.1, smallV=12.0, i=-28.5, smallA=-4.0, w20=6.0, w10=-2.5, s0=-1.0, w00=1.0, w21=-1.0, w11=1.5, cnt=-2, w01=2,
+            s1=-1.0, s2=1, fb=100, moves=20, step=1)
+B = float(2 ** 26)
+B2 = 16384.0
+THINIT = 4096.0 * 5000 - 2048
+R1, R2, RO, DUM = 4096, 8192, 10752, 6144
+WIN = DUM + 8 * LA
+F, H, BF, U, I = "float32", "float16", "bfloat16", "uint16", "int32"
+SB = {
+    "RW": (RO + WIN, BF), "D32": (WIN, F), "DI": (BASE, I), "VSI": (48, I), "VSF": (48, F),
+    "XB0": (M + L, BF), "XB1": (M + L, BF), "XB2": (M + L, BF),
+    "VU": (96, U), "VL": (48, F), "VU1": (32, U), "VL1": (16, F), "VU2": (32, U), "VL2": (16, F),
+    "SA0": (8, F), "SA1": (8, F), "RA1": (8, F), "RA2": (8, F),
+    "NM": (240, F), "ZZ": (240, F), "GS": (280, F), "TH": (48, F), "VT": (40, F), "NZ": (40, F), "UU": (40, F),
+    "S1R": (768, BF), "S1C": (768, BF), "KEEP": (48, F), "S1T": (48, F), "S1U": (48, F), "YG": (768, F),
+    "ONE": (128, BF), "ONE32": (128, F), "ID": (128, BF), "NID": (128, BF), "ID32": (128, F), "IDB": (128, BF), "ID64N": (128, BF),
+    "BOF": (128, BF), "NBOF": (128, BF), "BO": (8, BF), "BO32": (8, F), "BO16": (8, H), "SC3": (24, BF), "SC3H": (24, H),
+    "TRI": (128, BF), "TRE": (128, BF), "T1": (128, BF), "T1B": (128, BF), "T2": (128, BF), "RBN": (2048, BF), "WD": (144, F),
+    "WT": (576, BF), "WC": (32, F), "DG": (1024, BF), "SEL": (1024, BF), "NSEL": (1024, BF), "TRM": (512, BF), "VB": (768, F), "BCH": (256, H),
+    "PB": (136, BF), "P16": (136, H), "WP": (272, BF), "KC": (272, BF), "RST": (408, F), "MK": (512, F), "II": (128, I), "IJ": (128, I),
+    "LI": (96, I), "LS": (96, U), "DUMC": (16, F), "NC": (128, F), "SCL": (4, F), "CB": (4, F), "BIG3": (4, BF),
+    "BC": (384, F), "OAB": (8, U), "EAB": (128, F), "EB16": (64, U), "FR": (64, BF), "E0": (64, F), "N12": (16, BF), "UMIN": (8, F),
+    "VTH": (128, H), "PLF": (64, BF), "CMM": (1024, BF), "W3": (24, F), "BC2": (256, H), "ACB": (128, BF), "YK": (64, F), "OSC": (8, U), "ACE": (64, BF), "ASUM": (1, F),
+    "AI": (1, I), "AJ": (1, I), "CM2": (1024, BF), "STR": (64, BF), "GO": (64, BF), "N8": (64, BF), "WW": (64, F), "Y2": (1024, F),
+    "YI": (64, I), "YJ": (64, I), "YAB": (128, F), "TA": (64, F), "TB": (64, F), "TC": (64, F), "TD": (64, F), "TE": (64, F),
+    "CUT": (64, BF), "CUT2": (64, BF), "RN": (64, BF),
+}
+for _h in "01":
+    SB.update({"E16" + _h: (128, U), "FK" + _h: (384, H), "MM" + _h: (256, BF), "RB" + _h: (2048, BF), "DF" + _h: (2048, H), "CM" + _h: (2048, BF),
+               "PP" + _h: (136, BF), "SC" + _h: (408, F), "MI" + _h: (24, I), "MJ" + _h: (24, I), "O2" + _h: (40, F), "BV" + _h: (128, H),
+               "OV" + _h: (8, U), "BG" + _h: (384, F), "BH" + _h: (256, H)})
+    for _t in range(2):
+        SB.update({"SG%d" % _t + _h: (24, F), "SO%d" % _t + _h: (48, U), "RG%d" % (_t + 1) + _h: (24, F), "RO%d" % (_t + 1) + _h: (48, U)})
+DYN = ("C0", "C1")
+PS = ["K0", "K1", "C0", "C1", "P0", "P1", "Y0", "Y1"]
+POOL, FILL = {}, {}
+for _k, (_n, _d) in SB.items():
+    if _n <= 512 and _k[:2] not in ("VU", "VL", "SG", "SO", "SA", "RG", "RO", "RA", "VS"):
+        POOL[_k] = ("pool_" + _d, FILL.get(_d, 0)); FILL[_d] = FILL.get(_d, 0) + (_n + 31) // 32 * 32
+SCRATCH = {k: ("sbuf", [128, n], d) for k, (n, d) in SB.items() if k not in POOL}
+SCRATCH.update({"pool_" + d: ("sbuf", [128, n], d) for d, n in FILL.items()})
+SCRATCH.update({k: ("psum", [128, 512], F) for k in PS})
+SEMAPHORES = ["qV", "qA", "qP", "qG"] + ["d%d" % i for i in range(16)] + ["r%d" % i for i in range(16)] + ["l%d" % i for i in range(9)]
+QSEM = {"V": "qV", "A": "qA", "P": "qP", "G": "qG"}
+PLAN = {}
+
+
+def v(n, c0=0, c1=None, st=1, p0=0, p1=128):
+    if c1 is None:
+        c1 = SB[n][0] if n in SB else 512
+    return (n, p0, p1, c0, c1, st)
+
+
+def vn(n, c0, cnt, st, p0=0, p1=128):
+    return (n, p0, p1, c0, c0 + (cnt - 1) * st + 1, st)
+
+
+def ind(w, o):
+    return ("ind", w, o)
+
+
+def ap(T, x):
+    if not isinstance(x, tuple):
+        return x
+    if x[0] == "ind":
+        return ap(T, x[1]).indirect(ap(T, x[2]))
+    n, o = POOL.get(x[0], (x[0], 0))
+    if x[5] == 1:
+        return T[n][x[1]:x[2], o + x[3]:o + x[4]]
+    return T[n][x[1]:x[2], o + x[3]:o + x[4]:x[5]]
+
+
+def cols(x):
+    if x[0] == "ind":
+        return 16 * cols(x[2])
+    return (x[4] - x[3] + x[5] - 1) // x[5]
+
+
+def wide(x):
+    x = x[1] if x[0] == "ind" else x
+    return 4 if x[0] not in SB or SB[x[0]][1] in (F, I) else 2
+
+
+def build():
+    ops = []
+    nd, nr, nl, last, ph = [0], [0], [0], [], ["i"]
+
+    def add(eng, fn, rd, wr, cost, **kw):
+        r2, w2 = [], []
+        for x in rd:
+            if isinstance(x, tuple):
+                r2 += [x[1], x[2]] if x[0] == "ind" else [x]
+        for x in wr:
+            if x[0] == "ind":
+                w2.append(x[1]); r2.append(x[2])
+            else:
+                w2.append(x)
+        o = dict(eng=eng, no=len(ops), fn=fn, rd=r2, wr=w2, cost=cost, kind="c", after=[], ph=ph[0])
+        o.update(kw)
+        ops.append(o)
+        return len(ops) - 1
+
+    def vcost(out, ins, two=False):
+        n = cols(out)
+        if out[0] == "ind":
+            return (0.05, 0, 0, n, 0)
+        if ins[0][0] == "ind":
+            return (0.05, 0, n, 0, 0)
+        f = 0.5 if all(wide(x) == 2 for x in [out] + ins) else 1.0
+        if two and all(x[0] in SB for x in ins):
+            f = 2.0
+        return (0.0, max(64, n * f), 0, 0, 0)
+
+    def cp(out, a):
+        add("V", lambda g, T, c: g.vector.tensor_copy(ap(T, out), ap(T, a)), [a], [out], vcost(out, [a]))
+
+    def tt(out, a, b, op):
+        add("V", lambda g, T, c: g.vector.tensor_tensor(ap(T, out), ap(T, a), ap(T, b), op), [a, b], [out], vcost(out, [a, b], True))
+
+    def ts(out, a, s1, op0, s2=None, op1=None):
+        if s2 is None:
+            fn = lambda g, T, c: g.vector.tensor_scalar(ap(T, out), ap(T, a), ap(T, s1), None, op0)
+        else:
+            fn = lambda g, T, c: g.vector.tensor_scalar(ap(T, out), ap(T, a), ap(T, s1), ap(T, s2), op0, op1)
+        add("V", fn, [a, s1, s2], [out], vcost(out, [a]))
+
+    def scan(out, d0, d1, op0, op1):
+        add("V", lambda g, T, c: g.vector.tensor_tensor_scan(ap(T, out), ap(T, d0), ap(T, d1), 0.0, op0, op1), [d0, d1], [out], vcost(out, [d0, d1]))
+
+    def ms(out, val):
+        add("V", lambda g, T, c: g.vector.memset(ap(T, out), val), [], [out], vcost(out, [out]))
+
+    def act(out, a, func=None, bias=None, scale=None, acc=None):
+        def fn(g, T, c):
+            kw = {}
+            if bias is not None: kw["bias"] = ap(T, bias)
+            if scale is not None: kw["scale"] = ap(T, scale)
+            if acc is not None: kw["accum_out"] = ap(T, acc)
+            return g.scalar.activation(ap(T, out), ap(T, a), AF.Copy if func is None else func, **kw)
+        n = cols(out)
+        add("A", fn, [a, bias, scale], [out] + ([acc] if acc else []), (0.065, 0, n, 0, 0) if a[0] == "ind" else (0.03, max(64, n), 0, 0, 0))
+
+    def scale(out, a, f):
+        act(out, a, AF.Identity, scale=f)
+
+    def mm(out, l, r, start=True, stop=True):
+        n = max(min(64, cols(l)), cols(r)) * (4 if wide(l) == 4 else 1)
+        add("P", lambda g, T, c: g.tensor.matmul(ap(T, out), ap(T, l), ap(T, r), start, stop), [l, r], [out], (0.005, 0, 0, 0, n))
+
+    def group(lst):
+        if lst[0][0][0] in DYN:
+            def fn(g, T, c):
+                return [g.tensor.matmul(ap(T, o), ap(T, l), ap(T, r), j == 0, j == len(lst) - 1) for j, (o, l, r) in enumerate(lst)][-1]
+            n = sum(max(min(64, cols(l)), cols(r)) * (4 if wide(l) == 4 else 1) for o, l, r in lst)
+            add("P", fn, [x for o, l, r in lst for x in (l, r)], [o for o, l, r in lst], (0.005 * len(lst), 0, 0, 0, n))
+            return
+        for j, (o, l, r) in enumerate(lst):
+            mm(o, l, r, j == 0, j == len(lst) - 1)
+
+    def iota(out, pat, base, cm):
+        fl = SB[out[0]][1] != I
+        add("G", lambda g, T, c: g.iota(ap(T, out), pat, base, cm, allow_small_or_imprecise_dtypes=True) if fl else g.iota(ap(T, out), pat, base, cm),
+            [], [out], (0.13, 2 * cols(out), 0, 0, 0))
+
+    def sel(out, a, pat, op, base, cm, fill=0.0):
+        add("G", lambda g, T, c: g.affine_select(ap(T, out), ap(T, a), pat, op, fill, base, cm), [a], [out], (0.17, 2 * cols(out), 0, 0, 0))
+
+    def dma(q, out, a, rd, wr, nbytes):
+        s = "d%d" % nd[0]; nd[0] += 1
+        i = add(q, lambda g, T, c: (g.sync if q == "S" else g.scalar).dma_start(out(T), a(T)), rd, wr, (0.06, 0, 0, 0, 0), kind="d", sem=s, cnt=16,
+                nbytes=nbytes, after=last[-1:] if q == "S" else [])
+        if q == "S": last.append(i)
+
+    def send(items, lat, bulk=False, after=None, e0=0):
+        ls = "l%d" % nl[0]; nl[0] += 1
+        rs = ["r%d" % (nr[0] + j) for j in range(len(items))]; nr[0] += len(items)
+
+        def fn(g, T, c):
+            topo = c["topo"]; tr = []
+            for j, (s, d, k) in enumerate(items):
+                dst = c["ahead"](k); rid, pid, _ = topo.addr(dst)
+                mask = topo.mask(c["core"], dst) if bulk else 1 << topo.engines(c["core"], dst)[e0 + 2 * j]
+                if len(items) == 1:
+                    return g.remote_dma(ap(T, d), ap(T, s), T.sem[rs[0]], T.sem[ls], pid, rid, mask)
+                tr.append(RemoteDMATransfer(dst_ids=[DstId(rid=rid, pnc=pid)], dma_engine_mask=mask, remote_sem=T.sem[rs[j]], src=ap(T, s), dst=ap(T, d)))
+            return g.remote_dma_fused(tr, local_sem=T.sem[ls])
+        i = add("G", fn, [s for s, d, k in items], [], (1.0, 0, 0, 0, 0), kind="s", sem=ls, one=items[0][2] if bulk else None, cnt=len(items), after=after or [])
+        for j, (s, d, k) in enumerate(items):
+            add("R", None, [], [d], (lat, 0, 0, 0, 0), kind="r", sem=rs[j], one=k if bulk else None, cnt=1, src=i)
+        return i
+
+    X0 = "XB0"
+    dma("S", lambda T: T.VSI[:, :], lambda T: T.vs[:, :], [], [v("VSI")], 25000)
+    dma("S", lambda T: T.XB0[:, M:M + L], lambda T: T.z[:, :], [], [v(X0, M, M + L)], 66000)
+    dma("S", lambda T: T.RW[:, 0:Q], lambda T: T.rg[:, 0:Q], [], [v("RW", 0, Q)], 524288)
+    for a, b in ((0, 960), (960, BASE)):
+        dma("S", lambda T, a=a, b=b: T.DI[:, a:b], lambda T, a=a, b=b: T.nd[:, a:b], [], [v("DI", a, b)], 491520)
+    dma("S", lambda T: T.RW[:, Q:M], lambda T: T.rg[:, Q:M], [], [v("RW", Q, M)], 524288)
+
+    ms(v("ONE"), 1.0); ms(v("ONE32"), 1.0)
+    iota(v("II"), [[0, 8], [-1, 16]], 128, 1)
+    iota(v("LI", 0, 24), [[1, 24]], 0, 0); iota(v("LI", 24, 48), [[5, 24]], 4, 0)
+    iota(v("LI", 48, 64), [[-80, 2], [5, 8]], 124, 0); iota(v("LI", 64, 80), [[-124, 2], [5, 8]], 124, 0); iota(v("LI", 80, 96), [[5, 16]], 4, 0)
+    cp(v("LS"), v("LI"))
+    BL1, BL5 = (lambda n: v("LS", 0, n)), (lambda k0, k1: v("LS", 24 + 8 * k0, 24 + 8 * k1))
+    ts(v("IJ"), v("II"), 15, AL.bitwise_and)
+    ts(v("MK", 0, 128), v("IJ"), 0.0, AL.is_equal)
+    act(v("MK", 128, 256), v("MK", 0, 128)); act(v("MK", 256, 384), v("MK", 0, 128)); act(v("MK", 384, 512), v("ONE"))
+    sel(v("BOF"), v("ONE"), [[-16, 8], [0, 16]], AL.is_ge, 0, 1); sel(v("BOF"), v("BOF"), [[16, 8], [0, 16]], AL.is_ge, 15, -1)
+    sel(v("ID"), v("ONE"), [[-1, 128]], AL.is_equal, 0, 1)
+    ms(v("PB"), 1.0); sel(v("PB"), v("PB"), [[-16, 8], [-1, 17]], AL.is_equal, 1, 1); ms(vn("PB", 0, 8, 17), 0.0)
+    bo = vn("BOF", 0, 8, 16)
+    act(v("BO"), bo); act(v("BO32"), bo); cp(v("BO16"), bo)
+    for j in range(3):
+        scale(v("SC3", 8 * j, 8 * j + 8), bo, -4096.0)
+    cp(v("SC3H"), v("SC3"))
+    scale(v("NID"), v("ID"), -1.0); act(v("ID32"), v("ID")); scale(v("IDB"), v("ID"), B2); scale(v("ID64N"), v("ID"), -64.0)
+    cp(v("P16"), v("PB")); scale(v("WP", 0, 136), v("PB"), B); scale(v("WP", 136, 272), v("PB"), -B)
+    ms(v("KC", p1=32), B); ms(vn("KC", 0, 16, 17, 0, 32), 0.0)
+    ms(v("RST"), 0.0); ms(vn("RST", 0, 24, 17), float(2 ** 30))
+    for h in range(2):
+        ms(vn("C%d" % h, 0, 8, 17), 64.0)
+    ms(v("SCL"), -B); ms(v("CB"), 11 * B)
+    for c in range(max(p.count("F") for p in PATHS)):
+        ms(v("SCL", c + 1, 4, 1, 32 * c, 32 * c + 32), -B / 2); ms(v("CB", c + 1, 4, 1, 32 * c, 32 * c + 32), 3 * B)
+    ms(v("NM"), 0.0); ms(v("ZZ"), 1.0); ms(vn("ZZ", 0, 48, 5), 0.0); ms(v("TH"), THINIT); ms(v("VT"), 0.0); ms(v("GS"), 0.0); ms(v("W3"), 0.0)
+    ms(v("RW", R1 + Q, R2), 0.0); ms(v("D32", BASE, Q), 0.0)
+    for n in ("SA0", "SA1"): ms(v(n), 0.0)
+    for n in ("SO00", "SO01", "SO10", "SO11", "VU"): ms(v(n), 0)
+    for t in range(3):
+        cp(v("VU", 32 * t, 32 * t + 16), v("VSI", 16 * t, 16 * t + 16))
+    cp(v("VSF"), v("VSI"))
+    for a in range(16):
+        scale(vn("VB", a, 48, 16), v("VSF"), v("MK", a, a + 1))
+    for j in range(6):
+        mm(v("Y0", 8 * j, 8 * j + 8), v("VB", 128 * j, 128 * j + 128), v("BO32"))
+    act(v("VL"), v("Y0", 0, 48))
+    for i in range(16):
+        (cp if i % 4 else act)(vn(X0, i, L, 16), v(X0, M, M + L))
+    for a, b in ((0, 960), (960, BASE)):
+        cp(v("D32", a, b), v("DI", a, b))
+    cp(v("RW", R1, R1 + Q), v("RW", 0, Q)); act(v("RW", R2, R2 + Q), v("RW", 0, Q)); ms(v("RW", 0, 1), 512.0)
+    send([(v("VU", 32, 64), v("VU1"), 1), (v("VL", 16, 32), v("VL1"), 1), (v("VU", 64, 96), v("VU2"), 2), (v("VL", 32, 48), v("VL2"), 2)], 4.0)
+    sel(v("TRI"), v("BOF"), [[1, 128]], AL.is_ge, 0, -1); sel(v("TRE"), v("BOF"), [[1, 128]], AL.is_gt, 0, -1)
+    sel(v("T1"), v("TRI"), [[-1, 128]], AL.not_equal, 0, 1, -31.0); sel(v("T2"), v("TRE"), [[-1, 128]], AL.not_equal, 0, 1, -64.0)
+    for n, val in (("SEL", 1), ("NSEL", -1)):
+        iota(v(n, p1=8), [[0, 1024]], val, 0); sel(v(n, p1=8), v(n, p1=8), [[-1, 8], [0, 128]], AL.is_equal, 0, 1)
+    iota(v("TRM"), [[0, 512]], 2 ** 23, 0)
+    for p in (0, 64):
+        sel(v("TRM", p0=p, p1=p + 64), v("TRM", p0=p, p1=p + 64), [[0, 8], [-1, 64]], AL.is_ge, 0, 1)
+    iota(v("RBN"), [[0, 2048]], -int(B2), 0); sel(v("RBN"), v("RBN"), [[-1, 16], [-16, 8], [0, 16]], AL.is_equal, 0, 1)
+    iota(v("DUMC"), [[256, 2], [0, 8]], DUM, 4); iota(v("NC"), [[1, 128]], M + BASE, 0)
+    scale(v("BIG3"), v("ONE", 0, 4), B2); scale(v("NBOF"), v("BOF"), -1.0); scale(v("T1B"), v("T1"), B2)
+    iota(v("WD"), [[0, 144]], 0, 0); act(vn("WD", 15, 8, 16), bo); iota(v("WT"), [[0, 576]], 0, 0)
+    scale(v("WC", 0, 16), v("MK", 0, 16), B2); act(v("WC", 16, 32), v("MK", 0, 16), AF.Identity, bias=1.0, scale=-1.0)
+    for e, t in enumerate((0, 2)):
+        for j, row in enumerate((t, 8 + t)):
+            o = 512 * e + 256 * j
+            scale(vn("WT", 144 * (2 * e + j) + 15, 8, 16), bo, v("WC", row, row + 1))
+            scale(v("DG", o, o + 128), v("ID"), v("MK", row, row + 1)); scale(v("DG", o + 128, o + 256), v("ID"), v("WC", 16 + row, 17 + row))
+    bulk1 = send([(v(X0), v("XB1"), 1)], 14.0, True)
+    ops[bulk1]["rd"] += [v("RW", Q, M), v("DI")]
+    RWIN, DWIN = v("RW", 0, R2 + Q), v("D32", 0, Q)
+
+    def keepv(src, h, j):
+        act(vn("NM", 120 * h + 40 * (2 - j), 8, 5), src)
+        if h == 0:
+            act(vn("VT", 2 + j, 8, 5), src)
+
+    def step1(t, h):
+        Y = "Y%d" % h; o = 384 * h; x = v("XB%d" % t, M + 128 * h, M + 128 * h + 128); k24 = lambda n: v(n, 24 * h, 24 * h + 24)
+        act(v("S1R", o, o + 384), ind(v("RW", 0, M), v("RO%d%d" % (t, h), 0, 24)))
+        group([(v(Y, 0, 384), v("ID"), v("S1R", o, o + 384))] + [(v(Y, 128 * k, 128 * k + 128), v("NID"), x) for k in range(3)])
+        act(v("S1C", o, o + 384), v(Y, 0, 384), AF.Sign, bias=0.5, scale=-1.0)
+        for k in range(3):
+            mm(v(Y, 416 + 8 * k, 424 + 8 * k), v("S1R", o + 128 * k, o + 128 * k + 128), v("SC3", 0, 8))
+        for k in range(3):
+            mm(v(Y, 384 + 8 * k, 392 + 8 * k), v("S1C", o + 128 * k, o + 128 * k + 128), v("BO"))
+        ts(k24("S1T"), v(Y, 384, 408), v("RA%d" % t, 0, 1), AL.is_lt, B, AL.mult)
+        ts(k24("KEEP"), v(Y, 384, 408), v("RA%d" % t, 0, 1), AL.is_ge)
+        tt(k24("S1U"), v(Y, 416, 440), k24("S1T"), AL.add)
+        ts(k24("TH"), k24("S1U"), -2048.0, AL.add, THINIT, AL.min)
+        tt(vn("NM", 120 * h + 1, 24, 5), k24("KEEP"), v("RG%d%d" % (t, h)), AL.mult)
+        act(vn("ZZ", 120 * h + 1, 24, 5), k24("KEEP"), AF.Identity, bias=1.0, scale=-1.0)
+
+    def walk(t, s, h):
+        ph[0] = "w%d%d" % (t, h); n = str(h); xb = "XB%d" % t; nk = s + 1; K, C, P = "K" + n, "C" + n, "P" + n
+        off = v("VU" if t == 0 else "VU%d" % t, 8 * h, 8 * h + 8) if s == 2 else v("OV" + n)
+        e16 = v("E16" + n); path = PATHS[6 * t + 2 * (2 - s) + h]
+        cp(e16, ind(DWIN, off))
+        for c in range(4):
+            w = ind(RWIN, v("E16" + n, 32 * c, 32 * c + 32)); a, b = 512 * c, 512 * c + 512
+            x = v(xb, 2048 * h + a, 2048 * h + b); cm, rb = v("CM" + n, a, b), v("RB" + n, a, b); p = path[c]
+            if p in "AC":
+                for j in range(SPLIT):
+                    q = 512 // SPLIT; a2 = a + j * q
+                    tt(v(("DF" if p == "A" else "CM") + n, a2, a2 + q), ind(RWIN, v("E16" + n, a2 // 16, (a2 + q) // 16)),
+                       v(xb, 2048 * h + a2, 2048 * h + a2 + q), AL.subtract if p == "A" else AL.is_le)
+            if p == "A":
+                ts(cm, v("DF" + n, a, b), 0.0, AL.is_le)
+                continue
+            act(rb, w)
+            if p == "G": tt(cm, rb, x, AL.is_le)
+            if p in "FE":
+                group([(v(P), v("NID"), x), (v(P), v("ID"), rb)])
+                if p == "F": act(cm, v(P), AF.Sign, bias=0.5, scale=-1.0)
+                else: ts(cm, v(P), 0.0, AL.is_le)
+        ts(v("MM" + n, 0, 128), e16, 4096.0, AL.is_ge)
+        if s > 0: ts(v("MM" + n, 128, 256), e16, 8192.0, AL.is_ge)
+        for k in range(nk):
+            ts(v("FK" + n, 128 * k, 128 * k + 128), e16, -4096.0 * k - 2048, AL.add)
+        lst = [(v(K, 136 * k, 136 * k + 136), v("MM" + n, 0, 128), v("WP", 136 * k, 136 * k + 136)) for k in range(min(nk, 2))]
+        if s > 0:
+            lst = [(v(K, 136, 136 * nk), v("ONE", p1=1), v("KC", 0, 136 * s, p1=1))] + lst + [(v(K, 136, 136 * nk), v("MM" + n, 128, 256), v("WP", 0, 136 * s))]
+        lst += [(v(K, 136 * k, 136 * k + 136), v("FK" + n, 128 * k, 128 * k + 128), v("P16")) for k in range(nk)]
+        na = 32 * (4 - path.count("A")); nf = path.count("F")
+        if na < 128: lst += [(vn(K, 1 + i, 8 * nk, 17, na, 128), vn("DF" + n, 16 * na + i, 128 - na, 16), v("SC3H", 0, 8 * nk)) for i in range(16)]
+        if na > 0: lst += [(vn(K, 1 + i, 8 * nk, 17, 0, na), vn("RB" + n, i, na, 16), v("SC3", 0, 8 * nk)) for i in range(16)]
+        lst.append((vn(K, 0, 8 * nk, 17), v("ID32"), v("TH", 24 * h, 24 * h + 8 * nk)))
+        for j, (o, l, r) in enumerate(lst):
+            mm(o, l, r, j == 0, False)
+        for i in range(16):
+            mm(vn(C, 1 + i, 8, 17), vn("CM" + n, i, 128, 16), v("BO"))
+        act(v("PP" + n), v(C, 0, 136), AF.Relu, bias=v("CB", nf, nf + 1) if t == 0 else v("RA%d" % t, 1 + nf, 2 + nf), scale=v("SCL", nf, nf + 1))
+        for k in range(nk):
+            mm(v(K, 136 * k, 136 * k + 136), v("ID"), v("PP" + n), False, k == s)
+        scan(v("SC" + n, 0, 136 * nk), v("RST", 0, 136 * nk), v(K, 0, 136 * nk), AL.add, AL.min)
+        m = vn("SC" + n, 16, 8 * nk, 17); mi, mj = v("MI" + n, 0, 8 * nk), v("MJ" + n, 0, 8 * nk); o = 120 * h + 4 - s
+        ts(mi, m, 2048.0, AL.add); ts(mj, mi, 4095, AL.bitwise_and)
+        cp(vn("NM", o, 8 * nk, 5), mj)
+        if s > 0: ts(vn("ZZ", o, 8 * nk, 5), mj, 0.0, AL.is_equal)
+        else: act(vn("ZZ", o, 8, 5), vn("NM", o, 8, 5), AF.Relu, bias=1.0, scale=-1.0)
+        if s > 0:
+            b0 = 120 * h + 40 * s
+            scan(v("O2" + n), v("ZZ", b0, b0 + 40), v("NM", b0, b0 + 40), AL.mult, AL.add)
+            tt(v("BV" + n), ind(v("O2" + n), BL5(0, 1)), v("MK", 0, 128), AL.mult)
+            mm(v(C, 144, 152), v("BV" + n), v("BO16"))
+            cp(v("OV" + n), v(C, 144, 152))
+            tt(v("TH", 24 * h, 24 * h + 8 * s), vn("SC" + n, 16, 8 * s, 17), vn("NM", o, 8 * s, 5), AL.subtract)
+            keepv(vn("O2" + n, 4, 8, 5), h, 3 - s)
+
+    def guards(t, h, k0, k1):
+        n = str(h); a, b = 40 * k0, 40 * k1; C = "C" + n
+        if k1 == 3: ms(vn("ZZ", 120 * h + 1, 24, 5), 0.0)
+        scan(v("GS", 160 * h + a, 160 * h + b), v("ZZ", 120 * h + a, 120 * h + b), v("NM", 120 * h + a, 120 * h + b), AL.mult, AL.add)
+        if t < 2:
+            act(v("SG%d%d" % (t, h), 8 * k0, 8 * k1), vn("GS", 160 * h + a + 4, 8 * (k1 - k0), 5))
+            bg = ("BG" if k0 == 0 else "BH") + n
+            tt(v(bg, 0, 128 * (k1 - k0)), ind(v("GS", 160 * h, 160 * h + 120), BL5(k0, k1)), v("MK", 0, 128 * (k1 - k0)), AL.mult)
+            for k in range(k0, k1):
+                mm(v(C, 160 + 8 * k, 168 + 8 * k), v(bg, 128 * (k - k0), 128 * (k - k0) + 128), v("BO32" if k0 == 0 else "BO16"))
+            cp(v("SO%d%d" % (t, h), 8 * k0, 8 * k1), v(C, 160 + 8 * k0, 160 + 8 * k1))
+            if k0 == 0:
+                return send([(v("SG%d%d" % (t, h)), v("RG%d%d" % (t + 1, h)), 1), (v("SO%d%d" % (t, h)), v("RO%d%d" % (t + 1, h)), 1)], 3.0, e0=h)
+        else:
+            for k in range(k0, k1):
+                c = 256 + 128 * (k - k0)
+                mm(v(C, c, c + 128, p1=8), vn("GS", 160 * h + 40 * k + 4, 8, 5), v("ID32"))
+            for k in range(k0, k1):
+                c = 256 + 128 * (k - k0)
+                act(v("YG", 256 * k + 128 * h, 256 * k + 128 * h + 128, p1=8), v(C, c, c + 128, p1=8))
+
+    def step3(t):
+        ph[0] = "s%d" % t; even = t % 2 == 0; kb = 40 if even else 0; e = t // 2; xb = "XB%d" % t
+        act(v("NZ"), v("NM", kb, kb + 40), AF.Sign)
+        tt(v("UU"), v("VT"), v("NZ"), AL.mult)
+        scan(v("GS", 120, 160), v("ZZ", kb, kb + 40), v("UU"), AL.mult, AL.add)
+        a, b = vn("GS", 124, 8, 5, 0, 64), vn("GS", 44 if even else 0, 8, 5, 0, 64)
+        i64, bo4 = v("ID32", 0, 64, p1=64), v("BO16", 0, 4, p1=64)
+        tt(v("BCH"), ind(v("GS", 0, 160), v("LS", 48, 64) if even else v("LS", 64, 80)), v("MK", 0, 256), AL.mult)
+        for w in range(2):
+            mm(v("Y0", 4 * w, 4 * w + 4), v("BCH", 128 * w, 128 * w + 128, p1=64), bo4)
+        cp(v("OAB"), v("Y0", 0, 8))
+        if not even:
+            act(v("BC", 0, 128), ind(v("GS", 0, 120), BL5(0, 1)))
+            mm(v("Y0", 64, 128), v("BC", 0, 128, p1=64), i64)
+            act(v("E0"), v("Y0", 64, 128))
+        cp(v("EAB"), ind(DWIN, v("OAB")))
+        ea, eb, fr = v("EAB", 0, 64), v("EAB", 64, 128), v("FR")
+        ts(fr, ea if even else eb, 0.0, AL.is_equal)
+        tt(v("N12", 0, 8, p1=64), a, b, AL.is_equal)
+        mm(v("Y1", 0, 8, p1=64), fr, v("BO"))
+        mm(v("Y1", 256, 320), v("T2"), fr)
+        tt(v("UMIN", p1=64), v("Y1", 0, 8, p1=64), a, AL.min)
+        act(v("PLF"), v("Y1", 256, 320), AF.Identity, bias=32.0)
+        ts(v("N12", 8, 16, p1=64), v("UMIN", p1=64), 0.0, AL.is_equal)
+        for w, x in enumerate((a, b)):
+            o = v("Y1", 128 + 64 * w, 192 + 64 * w, p1=8)
+            group([(o, x, i64)] + [(o, v("N12", 8 * j, 8 * j + 8, p1=64), v("IDB", 0, 64, p1=64)) for j in range(2)])
+        vt = v("VTH", p1=8)
+        cp(vt, v("Y1", 128, 256, p1=8))
+        if even:
+            cp(v("EB16"), eb)
+            act(v("CUT"), ind(v("RW", 0, M), v("OAB", 4, 8)))
+            for c in range(2):
+                act(v("CM2", 512 * c, 512 * c + 512), ind(RWIN, v("EB16", 32 * c, 32 * c + 32)))
+        for c in range(2):
+            Y = "Y%d" % c
+            lst = [(v(Y), vt, v("NSEL", 512 * c, 512 * c + 512, p1=8))]
+            lst += [(v(Y, 128 * j, 128 * j + 128), v("SEL", 512 * c + 128 * j, 512 * c + 128 * j + 128, p1=8), vt) for j in range(4)]
+            group(lst)
+            tt(v("CMM", 512 * c, 512 * c + 512), v(Y), v("TRM"), AL.is_equal)
+        lst = [(v("C1", 384 + 8 * r, 392 + 8 * r, p1=64), v("IDB", 0, 64, p1=64), v("N12", 8 * j, 8 * j + 8, p1=64)) for r in range(3) for j in range(2)]
+        lst += [(v("C1", 384 + 8 * w, 392 + 8 * w, p1=64), i64, x) for w, x in enumerate((a, b))]
+        lst += [(vn("C1", 384 + j // 2, 3, 8, 0, 64), v("CMM", 64 * j, 64 * j + 64), v("BIG3", 0, 3)) for j in range(16)]
+        group(lst)
+        act(v("W3", 16, 24, p1=64), v("C1", 400, 408, p1=64), AF.Relu, bias=1.0, scale=-1.0, acc=v("ASUM", p1=64))
+        tt(v("W3", 0, 16, p1=64), v("C1", 384, 400, p1=64), v("DUMC", p1=64), AL.min)
+        if t < 2:
+            sa = "SA%d" % t
+            mm(v("C1", 480, 481), v("ONE32", p1=64), v("ASUM", p1=64))
+            cp(v("AI"), v("C1", 480, 481)); ts(v("AJ"), v("AI"), 1, AL.bitwise_and)
+            ts(v(sa, 0, 1), v("AJ"), -2.0, AL.mult, 6.0, AL.add)
+            for f in sorted(set(p.count("F") for p in PATHS[6 * t + 6:6 * t + 12])):
+                ts(v(sa, 1 + f, 2 + f), v("AJ"), -B, AL.mult, v("CB", f, f + 1), AL.add)
+            send([(v(sa), v("RA%d" % (t + 1)), 1)], 3.0, e0=4)
+        tt(v("BC2", 0, 256), ind(v("W3"), BL1(16)), v("MK", 0, 256), AL.mult)
+        for w in range(2):
+            mm(v("C1", 408 + 4 * w, 412 + 4 * w), v("BC2", 128 * w, 128 * w + 128, p1=64), bo4)
+        cp(v("OSC"), v("C1", 408, 416))
+        if even:
+            act(v("ACB"), ind(v("W3", 16, 24), BL1(8)))
+            mm(v("C1", 416, 480), v("ACB", p1=64), v("ID", 0, 64, p1=64))
+            act(v("ACE"), v("C1", 416, 480))
+        ya, yb = v("YAB", 0, 64), v("YAB", 64, 128)
+        ts(v("TA"), v("PLF"), -32.0, AL.is_equal)
+        if not even:
+            tt(v("TB"), ea, v("E0"), AL.not_equal); tt(ya, ea, v("TB"), AL.mult)
+            tt(v("TC"), v("TA"), v("E0"), AL.mult); tt(yb, eb, v("TC"), AL.add)
+            return
+        x = v(xb, M, M + 64); n0 = BASE + LA * e; dg = lambda j: v("DG", 512 * e + 128 * j, 512 * e + 128 * j + 128)
+        for r, row in enumerate((t, 8 + t)):
+            o, wt = v("C0", 256 + 64 * r, 320 + 64 * r), 144 * (2 * e + r)
+            group([(o, v("RBN", 128 * row, 128 * row + 128), x)] + [(o, v("WT", wt + 15 - j, wt + 143 - j), vn("CM2", j, 64, 16)) for j in range(16)])
+        half, cut = v("C0", 384, 448), v("C0", 448, 512)
+        group([(half, dg(1), v("CUT")), (half, dg(0), x), (half, v("NID"), v("RW", n0, n0 + 64))])
+        group([(cut, dg(3), v("CUT")), (cut, dg(2), x)])
+        ts(v("GO"), v("C0", 256, 320), 0.0, AL.is_ge); ts(v("N8"), v("C0", 320, 384), 0.0, AL.is_lt)
+        tt(v("TD"), half, v("ACE"), AL.mult)
+        act(v("CUT2"), cut)
+        tt(v("STR"), v("N8"), v("GO"), AL.is_gt)
+        tt(v("RN"), v("TD"), v("RW", n0, n0 + 64), AL.add)
+        mm(v("C1", 256, 320), v("T1B"), v("STR"))
+        group([(v("C1", 320, 384), v("T1"), v("STR")), (v("C1", 320, 384), v("NBOF"), fr), (v("C1", 320, 384), v("ID64N"), v("GO"))])
+        tt(v("WW"), v("C1", 256, 320), eb, AL.add)
+        ts(v("TB"), v("C1", 320, 384), -32.0, AL.is_ge); tt(yb, eb, v("TB"), AL.mult)
+        for c in range(2):
+            Y = "Y%d" % c; lst = []
+            for j in range(8):
+                i = 8 * c + j
+                lst += [(v(Y, 64 * j, 64 * j + 64), v("RBN", 128 * i, 128 * i + 128), v("PLF")), (v(Y, 64 * j, 64 * j + 64), v("ID32"), v("WW"))]
+            group(lst)
+            ts(v("Y2", 512 * c, 512 * c + 512), v(Y), 0.0, AL.max, B2, AL.min)
+            group([(v("C0", 256 + 64 * c, 320 + 64 * c), v("WD", 15 - i, 143 - i), v("Y2", 64 * i, 64 * i + 64)) for i in range(8 * c, 8 * c + 8)])
+        tt(v("TC"), v("TA"), v("NC", 64 * e, 64 * e + 64), AL.mult); tt(v("TC"), v("TC"), ea, AL.add)
+        act(v("YK"), v("C0", 256, 320)); tt(v("YI"), v("C0", 320, 384), v("YK"), AL.add)
+        ts(v("YJ"), v("YI"), 16383, AL.bitwise_and); tt(ya, v("YJ"), v("TC"), AL.add)
+        tt(v("TE"), v("GO"), v("ACE"), AL.mult)
+
+    def commit(t):
+        even = t % 2 == 0; n0 = BASE + LA * (t // 2)
+        if even: tt(v("D32", n0, n0 + 64), v("TE"), v("EAB", 64, 128), AL.mult)
+        cp(ind(v("D32"), v("OSC")), v("YAB"))
+        if even:
+            for base in ((0, R1, R2) if t == 0 else (RO,)):
+                if base != R2: act(v("RW", base + n0, base + n0 + 64), v("RN"))
+                cp(ind(v("RW", base, base + WIN), v("OSC", 4, 8)), v("CUT2"))
+        if t == 0:
+            dma("S", lambda T: T.RW[:, RO:RO + Q], lambda T: T.RW[:, R1:R1 + Q], [v("RW", R1, R1 + Q)], [v("RW", RO, RO + Q)], 524288)
+
+    for t in range(3):
+        vl = "VL" if t == 0 else "VL%d" % t
+        for h in range(2):
+            keepv(v(vl, 8 * h, 8 * h + 8), h, 0)
+            if t > 0: step1(t, h)
+        for s in (2, 1):
+            for h in range(2):
+                walk(t, s, h)
+                if s == 1: guards(t, h, 1, 3)
+        if t % 2 == 0: step3(t)
+        for h in range(2):
+            walk(t, 0, h); i = guards(t, h, 0, 1)
+            if t % 2 == 1 and h == 0: step3(t)
+        commit(t)
+        if t == 0: send([(v(X0), v("XB2"), 2)], 14.0, True, [i])
+    dma("S", lambda T: T.yr[:, :], lambda T: T.RW[:, RO:RO + Q], [v("RW", RO, RO + Q)], [], 524288)
+    dma("S", lambda T: T.yn[:, :], lambda T: T.D32[:, 0:Q], [v("D32", 0, Q)], [], 1048576)
+    dma("S", lambda T: T.yg[:, :], lambda T: T.YG[0:8, :], [v("YG")], [], 25000)
+    return ops
+
+
+def meet(a, b):
+    if a[4] <= b[3] or b[4] <= a[3] or a[2] <= b[1] or b[2] <= a[1]:
+        return False
+    if a[5] == b[5] and a[5] > 1 and (a[3] - b[3]) % a[5] != 0:
+        return False
+    return True
+
+
+def depend(ops):
+    hard = [set() for _ in ops]; soft = [set() for _ in ops]; acc = {}; bank = {}
+    for i, o in enumerate(ops):
+        soft[i].update(o["after"])
+        for x, w in [(x, False) for x in o["rd"]] + [(x, True) for x in o["wr"]]:
+            if x[0] in DYN:
+                o["dyn"] = x[0]
+            elif x[0] in PS:
+                for e, j in bank.setdefault(x[0], {}).items():
+                    if j != i: (soft if e == o["eng"] else hard)[i].add(j)
+                bank[x[0]][o["eng"]] = i
+                if o["eng"] == "P": continue
+            lst = acc.setdefault(x[0], [])
+            for y, j, wy in lst:
+                if j != i and (w or wy) and meet(x, y):
+                    (soft if o["eng"] == "P" and ops[j]["eng"] == "P" else hard)[i].add(j)
+            if w and x[5] == 1 and x[1] == 0 and x[2] == 128:
+                lst[:] = [z for z in lst if not (x[3] <= z[0][3] and z[0][4] <= x[4])]
+            lst.append((x, i, w))
+        if o["kind"] == "r": soft[i].add(o["src"])
+    return hard, soft
+
+
+def turns(ops, hard, seq):
+    hard = [set(h) for h in hard]; bank = {}
+    for i in seq:
+        o = ops[i]
+        if "dyn" in o:
+            b = bank.setdefault(o["dyn"], {})
+            hard[i].update(j for e, j in b.items() if e != o["eng"])
+            b[o["eng"]] = i
+    return hard
+
+
+def costs(ops, m):
+    return [c[0] + m["cy"] * (c[1] + m["g"] * c[2] + m["sc"] * c[3] + m["pe"] * c[4]) for c in (o["cost"] for o in ops)]
+
+
+def order(ops, hard, soft, m, tune):
+    n = len(ops); LAT = m["lat"]; cost = costs(ops, m); rnd = tune["seed"] * 7919 + 1
+    succ = [[] for _ in ops]
+    for i in range(n):
+        for j in hard[i] | soft[i]: succ[j].append(i)
+    pr = [0.0] * n
+    for i in range(n - 1, -1, -1):
+        rnd = (rnd * 1103515245 + 12345) % 2147483648
+        d = cost[i] + (1.5 + ops[i]["nbytes"] / m["bw"] if ops[i]["kind"] == "d" else 0)
+        pr[i] = d * (1 + tune["noise"] * (rnd / 2147483648 - 0.5)) + max([pr[j] + (LAT if i in hard[j] else 0) for j in succ[i]] + [0.0])
+    pr = [p + tune.get(o["ph"], 0.0) + (tune.get("small" + o["eng"], 0.0) if c < 0.45 else 0.0) + (tune.get("cnt", 0.0) if o["wr"] and o["wr"][0][0] in ("C0", "C1") else 0.0)
+          for p, o, c in zip(pr, ops, cost)]
+    pred = [list(hard[i] | soft[i]) for i in range(n)]; sl = tune["slack"]
+
+    def sweep(pr, back):
+        nxt, prv = (pred, succ) if back else (succ, pred)
+        left = [len(p) for p in prv]; ready = {e: [] for e in "VAPGSR"}; rt = [0.0] * n; end = [0.0] * n
+        for i in range(n):
+            if left[i] == 0: ready[ops[i]["eng"]].append(i)
+        free = {e: 0.0 for e in ready}; seq = []; bus = 0.0; bank = {}
+        while len(seq) < n:
+            best = None
+            for e, lst in ready.items():
+                if not lst: continue
+                for i in lst:
+                    if "dyn" in ops[i]:
+                        rt[i] = max([rt[i]] + [f + LAT for e2, f in bank.get(ops[i]["dyn"], {}).items() if e2 != e])
+                t0 = max(free[e] if e != "R" else 0.0, min([rt[i] for i in lst]))
+                if best is None or t0 < best[0]: best = (t0, e)
+            t0, e = best
+            i = max([i for i in ready[e] if rt[i] <= t0 + sl], key=lambda i: (pr[i], -i))
+            t0 = max(t0, rt[i]); o = ops[i]; ready[e].remove(i); seq.append(i)
+            if "dyn" in o:
+                b = bank.setdefault(o["dyn"], {})
+                t0 = max([t0] + [f + LAT for e2, f in b.items() if e2 != e]); b[e] = t0 + cost[i]
+            free[e] = fin = t0 + cost[i]
+            if o["kind"] == "d":
+                bus = max(bus, t0) + o["nbytes"] / m["bw"]; fin = bus + 1.5
+            end[i] = fin
+            for j in nxt[i]:
+                hd = j in hard[i] if back else i in hard[j]
+                rt[j] = max(rt[j], fin + LAT if hd else fin if "R" in (ops[j]["eng"], e) else t0); left[j] -= 1
+                if left[j] == 0: ready[ops[j]["eng"]].append(j)
+        return seq, end
+
+    seq, end = sweep(pr, False); best = (max(end), seq, end)
+    keys = sorted(set((o["ph"], o["eng"], o["wr"][0][0] if o["wr"] else "") for o in ops)); at = {k: j for j, k in enumerate(keys)}
+    kind = [at[(o["ph"], o["eng"], o["wr"][0][0] if o["wr"] else "")] for o in ops]
+    for it in range(tune.get("fb", 0)):
+        p = sweep(best[2], True)[1]; sh = {}
+        if it > 0:
+            for _ in range(tune.get("moves", 8)):
+                rnd = (rnd * 1103515245 + 12345) % 2147483648
+                sh[(rnd >> 8) % len(keys)] = tune.get("step", 1.5) * ((rnd >> 4 & 15) - 7.5) / 7.5
+        seq, end = sweep([x + sh.get(k, 0.0) for x, k in zip(p, kind)], False)
+        if max(end) <= best[0]: best = (max(end), seq, end)
+    return best[1]
+
+
+def rank_program(g, core, T, topo):
+    rank = T.rank_of(core)
+    if rank is None:
+        return
+    if "ops" not in PLAN:
+        PLAN["ops"] = build(); PLAN["hard"], soft = depend(PLAN["ops"])
+        PLAN["seq"] = order(PLAN["ops"], PLAN["hard"], soft, MODEL, TUNE)
+        PLAN["hard"] = turns(PLAN["ops"], PLAN["hard"], PLAN["seq"])
+    ops, hard = PLAN["ops"], PLAN["hard"]; cores = T.cores; N = len(cores)
+    c = {"core": core, "topo": topo, "ahead": lambda k: cores[(rank + k) % N]}
+    qs = {"V": g.vector, "A": g.scalar, "P": g.tensor, "G": g, "S": g.sync}
+    know = {e: {} for e in qs}; count = {}; done = {}
+    for i in PLAN["seq"]:
+        o = ops[i]; e = o["eng"]
+        if o["kind"] == "r":
+            n = o["cnt"] if o["one"] is None else len(topo.engines(cores[(rank - o["one"]) % N], core))
+            count[o["sem"]] = n; done[i] = (o["sem"], n, {o["sem"]: n})
+            continue
+        kn = know[e]
+        for s, n, kj in sorted((done[j] for j in hard[i]), key=lambda d: -d[1]):
+            if kn.get(s, 0) < n:
+                qs[e].wait_ge(T.sem[s], n)
+                for s2, n2 in kj.items():
+                    if kn.get(s2, 0) < n2: kn[s2] = n2
+        if e == "G" and o["kind"] == "c" and kn.get("qG", 0) < count.get("qG", 0):
+            kn["qG"] = count["qG"]; g.wait_ge(T.sem["qG"], kn["qG"])
+        ins = o["fn"](g, T, c)
+        if o["kind"] == "c":
+            s = QSEM[e]; n = count.get(s, 0) + 1; ins.then_inc(T.sem[s], 1)
+        elif o["kind"] == "d":
+            s = o["sem"]; n = 16; ins.then_inc(T.sem[s], 16)
+        else:
+            s = o["sem"]; n = o["cnt"] if o["one"] is None else len(topo.engines(core, c["ahead"](o["one"])))
+        count[s] = n; kj = dict(kn); kj[s] = n; done[i] = (s, n, kj)
+    for s, n in count.items():
+        if know["G"].get(s, 0) < n: g.wait_ge(T.sem[s], n)

@@ -4,9 +4,9 @@ from concourse.mybir import AluOpType as AL, ActivationFunctionType as AF
 M, Q, BASE, L, LA = 4096, 2048, 1920, 256, 64
 PATHS = "FFCA FFCA FFCA FFCA FFCA FFCA FFCA FFCA FFCA FFCA FFCA FFCA FFCA FFCA FFCA FFCA FFCA FFCA".split()
 SPLIT = 1
-MODEL = dict(cy=1.0e-3, g=1.56, sc=3.8, pe=0.5, lat=0.1, bw=180e3)
-TUNE = dict(slack=0.05, seed=934, noise=0.1, smallV=12.0, i=-28.5, smallA=-4.0, w20=6.0, w10=-2.5, s0=-1.0, w00=1.0, w21=-1.0, w11=1.5, cnt=-2, w01=2,
-            s1=-1.0, s2=1, fb=100, moves=20, step=1)
+MODEL = dict(cy=1.0e-3, g=1.56, sc=3.8, pe=0.5, lat=0.15, bw=180e3)
+TUNE = dict(slack=0.05, seed=6, noise=0, smallV=4.0, i=-40.5, smallA=-4.0, w20=6.0, w10=-2.0, s0=-1.0, w00=1.5, w21=-1.0, w11=-3.5, cnt=-3.5, w01=1.5,
+            s1=-2.0, s2=5, x=30, fb=80, moves=20, step=1)
 B = float(2 ** 26)
 B2 = 16384.0
 THINIT = 4096.0 * 5000 - 2048
@@ -28,7 +28,7 @@ SB = {
     "LI": (96, I), "LS": (96, U), "DUMC": (16, F), "NC": (128, F), "SCL": (4, F), "CB": (4, F), "BIG3": (4, BF),
     "BC": (384, F), "OAB": (8, U), "EAB": (128, F), "EB16": (64, U), "FR": (64, BF), "E0": (64, F), "N12": (16, BF), "UMIN": (8, F),
     "VTH": (128, H), "PLF": (64, BF), "CMM": (1024, BF), "W3": (24, F), "BC2": (256, H), "ACB": (128, BF), "YK": (64, F), "OSC": (8, U), "ACE": (64, BF), "ASUM": (1, F),
-    "AI": (1, I), "AJ": (1, I), "CM2": (1024, BF), "STR": (64, BF), "GO": (64, BF), "N8": (64, BF), "WW": (64, F), "Y2": (1024, F),
+    "AI": (1, I), "AJ": (1, I), "CM2": (1024, BF), "STR": (64, BF), "GO": (64, BF), "N8": (64, BF), "EBH": (64, H), "EBL": (64, H), "Y2": (1024, F),
     "YI": (64, I), "YJ": (64, I), "YAB": (128, F), "TA": (64, F), "TB": (64, F), "TC": (64, F), "TD": (64, F), "TE": (64, F),
     "CUT": (64, BF), "CUT2": (64, BF), "RN": (64, BF),
 }
@@ -178,27 +178,27 @@ def build():
                 nbytes=nbytes, after=last[-1:] if q == "S" else [])
         if q == "S": last.append(i)
 
-    def send(items, lat, bulk=False, after=None, e0=0):
-        ls = "l%d" % nl[0]; nl[0] += 1
+    def send(items, lat):
+        ls = "l%d" % nl[0]; nl[0] += 1; ks = [k for s, d, k in items]
         rs = ["r%d" % (nr[0] + j) for j in range(len(items))]; nr[0] += len(items)
 
         def fn(g, T, c):
             topo = c["topo"]; tr = []
             for j, (s, d, k) in enumerate(items):
                 dst = c["ahead"](k); rid, pid, _ = topo.addr(dst)
-                mask = topo.mask(c["core"], dst) if bulk else 1 << topo.engines(c["core"], dst)[e0 + 2 * j]
+                mask = sum(1 << e for e in c["share"](0, ks)[j])
                 if len(items) == 1:
                     return g.remote_dma(ap(T, d), ap(T, s), T.sem[rs[0]], T.sem[ls], pid, rid, mask)
                 tr.append(RemoteDMATransfer(dst_ids=[DstId(rid=rid, pnc=pid)], dma_engine_mask=mask, remote_sem=T.sem[rs[j]], src=ap(T, s), dst=ap(T, d)))
             return g.remote_dma_fused(tr, local_sem=T.sem[ls])
-        i = add("G", fn, [s for s, d, k in items], [], (1.0, 0, 0, 0, 0), kind="s", sem=ls, one=items[0][2] if bulk else None, cnt=len(items), after=after or [])
+        i = add("G", fn, [s for s, d, k in items], [], (1.0, 0, 0, 0, 0), kind="s", sem=ls, ks=ks)
         for j, (s, d, k) in enumerate(items):
-            add("R", None, [], [d], (lat, 0, 0, 0, 0), kind="r", sem=rs[j], one=k if bulk else None, cnt=1, src=i)
+            add("R", None, [], [d], (lat, 0, 0, 0, 0), kind="r", sem=rs[j], ks=ks, k=k, src=i)
         return i
 
     X0 = "XB0"
-    dma("S", lambda T: T.VSI[:, :], lambda T: T.vs[:, :], [], [v("VSI")], 25000)
-    dma("S", lambda T: T.XB0[:, M:M + L], lambda T: T.z[:, :], [], [v(X0, M, M + L)], 66000)
+    dma("A", lambda T: T.VSI[:, :], lambda T: T.vs[:, :], [], [v("VSI")], 25000)
+    dma("A", lambda T: T.XB0[:, M:M + L], lambda T: T.z[:, :], [], [v(X0, M, M + L)], 66000)
     dma("S", lambda T: T.RW[:, 0:Q], lambda T: T.rg[:, 0:Q], [], [v("RW", 0, Q)], 524288)
     for a, b in ((0, 960), (960, BASE)):
         dma("S", lambda T, a=a, b=b: T.DI[:, a:b], lambda T, a=a, b=b: T.nd[:, a:b], [], [v("DI", a, b)], 491520)
@@ -247,15 +247,17 @@ def build():
     for a, b in ((0, 960), (960, BASE)):
         cp(v("D32", a, b), v("DI", a, b))
     cp(v("RW", R1, R1 + Q), v("RW", 0, Q)); act(v("RW", R2, R2 + Q), v("RW", 0, Q)); ms(v("RW", 0, 1), 512.0)
-    send([(v("VU", 32, 64), v("VU1"), 1), (v("VL", 16, 32), v("VL1"), 1), (v("VU", 64, 96), v("VU2"), 2), (v("VL", 32, 48), v("VL2"), 2)], 4.0)
+    ph[0] = "x"
+    send([(v(X0, M, M + L), v("XB%d" % k, M, M + L), k) for k in (1, 2)], 6.0)
+    send([(v("VU", 32, 64), v("VU1"), 1), (v("VL", 16, 32), v("VL1"), 1), (v("VU", 64, 96), v("VU2"), 2), (v("VL", 32, 48), v("VL2"), 2)], 6.0)
+    ph[0] = "i"
     sel(v("TRI"), v("BOF"), [[1, 128]], AL.is_ge, 0, -1); sel(v("TRE"), v("BOF"), [[1, 128]], AL.is_gt, 0, -1)
     sel(v("T1"), v("TRI"), [[-1, 128]], AL.not_equal, 0, 1, -31.0); sel(v("T2"), v("TRE"), [[-1, 128]], AL.not_equal, 0, 1, -64.0)
-    for n, val in (("SEL", 1), ("NSEL", -1)):
-        iota(v(n, p1=8), [[0, 1024]], val, 0); sel(v(n, p1=8), v(n, p1=8), [[-1, 8], [0, 128]], AL.is_equal, 0, 1)
-    iota(v("TRM"), [[0, 512]], 2 ** 23, 0)
+    ms(v("SEL", p1=32), 1.0); sel(v("SEL", p1=8), v("SEL", p1=8), [[-1, 8], [0, 128]], AL.is_equal, 0, 1); scale(v("NSEL", p1=8), v("SEL", p1=8), -1.0)
+    ms(v("TRM"), 0.5)
     for p in (0, 64):
         sel(v("TRM", p0=p, p1=p + 64), v("TRM", p0=p, p1=p + 64), [[0, 8], [-1, 64]], AL.is_ge, 0, 1)
-    iota(v("RBN"), [[0, 2048]], -int(B2), 0); sel(v("RBN"), v("RBN"), [[-1, 16], [-16, 8], [0, 16]], AL.is_equal, 0, 1)
+    ms(v("RBN"), -B2); sel(v("RBN"), v("RBN"), [[-1, 16], [-16, 8], [0, 16]], AL.is_equal, 0, 1)
     iota(v("DUMC"), [[256, 2], [0, 8]], DUM, 4); iota(v("NC"), [[1, 128]], M + BASE, 0)
     scale(v("BIG3"), v("ONE", 0, 4), B2); scale(v("NBOF"), v("BOF"), -1.0); scale(v("T1B"), v("T1"), B2)
     iota(v("WD"), [[0, 144]], 0, 0); act(vn("WD", 15, 8, 16), bo); iota(v("WT"), [[0, 576]], 0, 0)
@@ -265,8 +267,13 @@ def build():
             o = 512 * e + 256 * j
             scale(vn("WT", 144 * (2 * e + j) + 15, 8, 16), bo, v("WC", row, row + 1))
             scale(v("DG", o, o + 128), v("ID"), v("MK", row, row + 1)); scale(v("DG", o + 128, o + 256), v("ID"), v("WC", 16 + row, 17 + row))
-    bulk1 = send([(v(X0), v("XB1"), 1)], 14.0, True)
-    ops[bulk1]["rd"] += [v("RW", Q, M), v("DI")]
+
+    def repeat(k, after):
+        ph[0] = "x"
+        for i in range(16):
+            sel(vn("XB%d" % k, i, L, 16), v("XB%d" % k, M, M + L), [[0, L]], AL.is_gt, 1, 0)
+            ops[-1]["after"] = after
+    repeat(1, [])
     RWIN, DWIN = v("RW", 0, R2 + Q), v("D32", 0, Q)
 
     def keepv(src, h, j):
@@ -358,7 +365,7 @@ def build():
                 mm(v(C, 160 + 8 * k, 168 + 8 * k), v(bg, 128 * (k - k0), 128 * (k - k0) + 128), v("BO32" if k0 == 0 else "BO16"))
             cp(v("SO%d%d" % (t, h), 8 * k0, 8 * k1), v(C, 160 + 8 * k0, 160 + 8 * k1))
             if k0 == 0:
-                return send([(v("SG%d%d" % (t, h)), v("RG%d%d" % (t + 1, h)), 1), (v("SO%d%d" % (t, h)), v("RO%d%d" % (t + 1, h)), 1)], 3.0, e0=h)
+                return send([(v("SG%d%d" % (t, h)), v("RG%d%d" % (t + 1, h)), 1), (v("SO%d%d" % (t, h)), v("RO%d%d" % (t + 1, h)), 1)], 3.5)
         else:
             for k in range(k0, k1):
                 c = 256 + 128 * (k - k0)
@@ -420,7 +427,7 @@ def build():
             ts(v(sa, 0, 1), v("AJ"), -2.0, AL.mult, 6.0, AL.add)
             for f in sorted(set(p.count("F") for p in PATHS[6 * t + 6:6 * t + 12])):
                 ts(v(sa, 1 + f, 2 + f), v("AJ"), -B, AL.mult, v("CB", f, f + 1), AL.add)
-            send([(v(sa), v("RA%d" % (t + 1)), 1)], 3.0, e0=4)
+            send([(v(sa), v("RA%d" % (t + 1)), 1)], 3.5)
         tt(v("BC2", 0, 256), ind(v("W3"), BL1(16)), v("MK", 0, 256), AL.mult)
         for w in range(2):
             mm(v("C1", 408 + 4 * w, 412 + 4 * w), v("BC2", 128 * w, 128 * w + 128, p1=64), bo4)
@@ -447,16 +454,16 @@ def build():
         act(v("CUT2"), cut)
         tt(v("STR"), v("N8"), v("GO"), AL.is_gt)
         tt(v("RN"), v("TD"), v("RW", n0, n0 + 64), AL.add)
-        mm(v("C1", 256, 320), v("T1B"), v("STR"))
+        cp(v("EBH"), eb); tt(v("EBL"), eb, v("EBH"), AL.subtract)
         group([(v("C1", 320, 384), v("T1"), v("STR")), (v("C1", 320, 384), v("NBOF"), fr), (v("C1", 320, 384), v("ID64N"), v("GO"))])
-        tt(v("WW"), v("C1", 256, 320), eb, AL.add)
         ts(v("TB"), v("C1", 320, 384), -32.0, AL.is_ge); tt(yb, eb, v("TB"), AL.mult)
         for c in range(2):
             Y = "Y%d" % c; lst = []
             for j in range(8):
                 i = 8 * c + j
-                lst += [(v(Y, 64 * j, 64 * j + 64), v("RBN", 128 * i, 128 * i + 128), v("PLF")), (v(Y, 64 * j, 64 * j + 64), v("ID32"), v("WW"))]
-            group(lst)
+                o = v(Y, 64 * j, 64 * j + 64)
+                lst += [(o, v("RBN", 128 * i, 128 * i + 128), v("PLF")), (o, v("ID"), v("EBH")), (o, v("ID"), v("EBL"))]
+            group(lst + [(v(Y, 64 * j, 64 * j + 64), v("T1B"), v("STR")) for j in range(8)])
             ts(v("Y2", 512 * c, 512 * c + 512), v(Y), 0.0, AL.max, B2, AL.min)
             group([(v("C0", 256 + 64 * c, 320 + 64 * c), v("WD", 15 - i, 143 - i), v("Y2", 64 * i, 64 * i + 64)) for i in range(8 * c, 8 * c + 8)])
         tt(v("TC"), v("TA"), v("NC", 64 * e, 64 * e + 64), AL.mult); tt(v("TC"), v("TC"), ea, AL.add)
@@ -473,7 +480,7 @@ def build():
                 if base != R2: act(v("RW", base + n0, base + n0 + 64), v("RN"))
                 cp(ind(v("RW", base, base + WIN), v("OSC", 4, 8)), v("CUT2"))
         if t == 0:
-            dma("S", lambda T: T.RW[:, RO:RO + Q], lambda T: T.RW[:, R1:R1 + Q], [v("RW", R1, R1 + Q)], [v("RW", RO, RO + Q)], 524288)
+            dma("S", lambda T: T.RW[:, RO:RO + Q], lambda T: T.RW[:, R1:R1 + Q], [v("RW", R1, R1 + Q), v("RO11")], [v("RW", RO, RO + Q)], 524288)
 
     for t in range(3):
         vl = "VL" if t == 0 else "VL%d" % t
@@ -489,7 +496,7 @@ def build():
             walk(t, 0, h); i = guards(t, h, 0, 1)
             if t % 2 == 1 and h == 0: step3(t)
         commit(t)
-        if t == 0: send([(v(X0), v("XB2"), 2)], 14.0, True, [i])
+        if t == 0: repeat(2, [j for j, o in enumerate(ops) if o["kind"] == "s"])
     dma("S", lambda T: T.yr[:, :], lambda T: T.RW[:, RO:RO + Q], [v("RW", RO, RO + Q)], [], 524288)
     dma("S", lambda T: T.yn[:, :], lambda T: T.D32[:, 0:Q], [v("D32", 0, Q)], [], 1048576)
     dma("S", lambda T: T.yg[:, :], lambda T: T.YG[0:8, :], [v("YG")], [], 25000)
@@ -610,13 +617,18 @@ def rank_program(g, core, T, topo):
         PLAN["seq"] = order(PLAN["ops"], PLAN["hard"], soft, MODEL, TUNE)
         PLAN["hard"] = turns(PLAN["ops"], PLAN["hard"], PLAN["seq"])
     ops, hard = PLAN["ops"], PLAN["hard"]; cores = T.cores; N = len(cores)
-    c = {"core": core, "topo": topo, "ahead": lambda k: cores[(rank + k) % N]}
+
+    def share(back, ks):
+        src = (rank - back) % N; sets = [topo.engines(cores[src], cores[(src + k) % N]) for k in ks]
+        es = [e for e in sets[0] if all(e in s for s in sets)]; n = len(es) // len(ks)
+        return [es[j * n:(j + 1) * n] for j in range(len(ks))]
+    c = {"core": core, "topo": topo, "ahead": lambda k: cores[(rank + k) % N], "share": share}
     qs = {"V": g.vector, "A": g.scalar, "P": g.tensor, "G": g, "S": g.sync}
     know = {e: {} for e in qs}; count = {}; done = {}
     for i in PLAN["seq"]:
         o = ops[i]; e = o["eng"]
         if o["kind"] == "r":
-            n = o["cnt"] if o["one"] is None else len(topo.engines(cores[(rank - o["one"]) % N], core))
+            n = len(share(o["k"], o["ks"])[0])
             count[o["sem"]] = n; done[i] = (o["sem"], n, {o["sem"]: n})
             continue
         kn = know[e]
@@ -633,7 +645,7 @@ def rank_program(g, core, T, topo):
         elif o["kind"] == "d":
             s = o["sem"]; n = 16; ins.then_inc(T.sem[s], 16)
         else:
-            s = o["sem"]; n = o["cnt"] if o["one"] is None else len(topo.engines(core, c["ahead"](o["one"])))
+            s = o["sem"]; n = sum(len(x) for x in share(0, o["ks"]))
         count[s] = n; kj = dict(kn); kj[s] = n; done[i] = (s, n, kj)
     for s, n in count.items():
         if know["G"].get(s, 0) < n: g.wait_ge(T.sem[s], n)

@@ -5,8 +5,8 @@ M, Q, BASE, L, LA = 4096, 2048, 1920, 256, 64
 PATHS = "FFCA FFCA FFCA FFCA FFCA FFCA FFCA FFCA FFCA FFCA FFCA FFCA FFCA FFCA FFCA FFCA FFCA FFCA".split()
 SPLIT = 1
 MODEL = dict(cy=1.0e-3, g=1.56, sc=3.8, pe=0.5, lat=0.15, bw=180e3)
-TUNE = dict(slack=0.05, seed=6, noise=0, smallV=4.0, i=-40.5, smallA=-4.0, w20=6.0, w10=-2.0, s0=-1.0, w00=1.5, w21=-1.0, w11=-3.5, cnt=-3.5, w01=1.5,
-            s1=-2.0, s2=5, x=30, fb=80, moves=20, step=1)
+TUNE = dict(slack=0.05, seed=23, noise=0, smallV=4.0, i=-40.5, smallA=-4.0, w20=6.0, w10=-2.0, s0=-1.0, w00=1.5, w21=-1.0, w11=-3.5, cnt=-3.5, w01=1.5,
+            s1=-2.0, s2=5, x=30, fb=50, moves=10, step=2)
 B = float(2 ** 26)
 B2 = 16384.0
 THINIT = 4096.0 * 5000 - 2048
@@ -25,7 +25,7 @@ SB = {
     "TRI": (128, BF), "TRE": (128, BF), "T1": (128, BF), "T1B": (128, BF), "T2": (128, BF), "RBN": (2048, BF), "WD": (144, F),
     "WT": (576, BF), "WC": (32, F), "DG": (1024, BF), "SEL": (1024, BF), "NSEL": (1024, BF), "TRM": (512, BF), "VB": (768, F), "BCH": (256, H),
     "PB": (136, BF), "P16": (136, H), "WP": (272, BF), "KC": (272, BF), "RST": (408, F), "MK": (512, F), "II": (128, I), "IJ": (128, I),
-    "LI": (96, I), "LS": (96, U), "DUMC": (16, F), "NC": (128, F), "SCL": (4, F), "CB": (4, F), "BIG3": (4, BF),
+    "LI": (112, I), "LS": (112, U), "DUMC": (16, F), "NC": (128, F), "SCL": (4, F), "CB": (4, F), "BIG3": (4, BF),
     "BC": (384, F), "OAB": (8, U), "EAB": (128, F), "EB16": (64, U), "FR": (64, BF), "E0": (64, F), "N12": (16, BF), "UMIN": (8, F),
     "VTH": (128, H), "PLF": (64, BF), "CMM": (1024, BF), "W3": (24, F), "BC2": (256, H), "ACB": (128, BF), "YK": (64, F), "OSC": (8, U), "ACE": (64, BF), "ASUM": (1, F),
     "AI": (1, I), "AJ": (1, I), "CM2": (1024, BF), "STR": (64, BF), "GO": (64, BF), "N8": (64, BF), "EBH": (64, H), "EBL": (64, H), "Y2": (1024, F),
@@ -34,7 +34,7 @@ SB = {
 }
 for _h in "01":
     SB.update({"E16" + _h: (128, U), "FK" + _h: (384, H), "MM" + _h: (256, BF), "RB" + _h: (2048, BF), "DF" + _h: (2048, H), "CM" + _h: (2048, BF),
-               "PP" + _h: (136, BF), "SC" + _h: (408, F), "MI" + _h: (24, I), "MJ" + _h: (24, I), "O2" + _h: (40, F), "BV" + _h: (128, H),
+               "PP" + _h: (136, BF), "SC" + _h: (408, F), "MI" + _h: (24, I), "MJ" + _h: (32, I), "O1" + _h: (40, F), "O2" + _h: (40, F), "BV" + _h: (256, H),
                "OV" + _h: (8, U), "BG" + _h: (384, F), "BH" + _h: (256, H)})
     for _t in range(2):
         SB.update({"SG%d" % _t + _h: (24, F), "SO%d" % _t + _h: (48, U), "RG%d" % (_t + 1) + _h: (24, F), "RO%d" % (_t + 1) + _h: (48, U)})
@@ -207,7 +207,8 @@ def build():
     ms(v("ONE"), 1.0); ms(v("ONE32"), 1.0)
     iota(v("II"), [[0, 8], [-1, 16]], 128, 1)
     iota(v("LI", 0, 24), [[1, 24]], 0, 0); iota(v("LI", 24, 48), [[5, 24]], 4, 0)
-    iota(v("LI", 48, 64), [[-80, 2], [5, 8]], 124, 0); iota(v("LI", 64, 80), [[-124, 2], [5, 8]], 124, 0); iota(v("LI", 80, 96), [[5, 16]], 4, 0)
+    iota(v("LI", 48, 64), [[-80, 2], [5, 8]], 124, 0); iota(v("LI", 64, 80), [[-124, 2], [5, 8]], 124, 0); iota(v("LI", 80, 96), [[16, 2], [1, 8]], 8, 0)
+    iota(v("LI", 96, 112), [[1, 16]], 16, 0); ms(v("MJ0"), 0); ms(v("MJ1"), 0)
     cp(v("LS"), v("LI"))
     BL1, BL5 = (lambda n: v("LS", 0, n)), (lambda k0, k1: v("LS", 24 + 8 * k0, 24 + 8 * k1))
     ts(v("IJ"), v("II"), 15, AL.bitwise_and)
@@ -230,7 +231,7 @@ def build():
     ms(v("SCL"), -B); ms(v("CB"), 11 * B)
     for c in range(max(p.count("F") for p in PATHS)):
         ms(v("SCL", c + 1, 4, 1, 32 * c, 32 * c + 32), -B / 2); ms(v("CB", c + 1, 4, 1, 32 * c, 32 * c + 32), 3 * B)
-    ms(v("NM"), 0.0); ms(v("ZZ"), 1.0); ms(vn("ZZ", 0, 48, 5), 0.0); ms(v("TH"), THINIT); ms(v("VT"), 0.0); ms(v("GS"), 0.0); ms(v("W3"), 0.0)
+    ms(v("NM"), 0.0); ms(v("ZZ"), 1.0); ms(vn("ZZ", 0, 48, 5), 0.0); ms(v("TH"), THINIT); ms(v("UU"), 0.0); ms(v("GS"), 0.0); ms(v("W3"), 0.0)
     ms(v("RW", R1 + Q, R2), 0.0); ms(v("D32", BASE, Q), 0.0)
     for n in ("SA0", "SA1"): ms(v(n), 0.0)
     for n in ("SO00", "SO01", "SO10", "SO11", "VU"): ms(v(n), 0)
@@ -338,18 +339,24 @@ def build():
         act(v("PP" + n), v(C, 0, 136), AF.Relu, bias=v("CB", nf, nf + 1) if t == 0 else v("RA%d" % t, 1 + nf, 2 + nf), scale=v("SCL", nf, nf + 1))
         for k in range(nk):
             mm(v(K, 136 * k, 136 * k + 136), v("ID"), v("PP" + n), False, k == s)
+        b0 = 120 * h + 40 * s
+        if s > 0: scan(v("O1" + n), v("ZZ", b0, b0 + 40), v("NM", b0, b0 + 40), AL.mult, AL.add)
         scan(v("SC" + n, 0, 136 * nk), v("RST", 0, 136 * nk), v(K, 0, 136 * nk), AL.add, AL.min)
         m = vn("SC" + n, 16, 8 * nk, 17); mi, mj = v("MI" + n, 0, 8 * nk), v("MJ" + n, 0, 8 * nk); o = 120 * h + 4 - s
         ts(mi, m, 2048.0, AL.add); ts(mj, mi, 4095, AL.bitwise_and)
-        cp(vn("NM", o, 8 * nk, 5), mj)
-        if s > 0: ts(vn("ZZ", o, 8 * nk, 5), mj, 0.0, AL.is_equal)
-        else: act(vn("ZZ", o, 8, 5), vn("NM", o, 8, 5), AF.Relu, bias=1.0, scale=-1.0)
+        tt(vn("ZZ", o, 8 * nk, 5), m, v("TH", 24 * h, 24 * h + 8 * nk), AL.is_equal)
+        kh = 1 - t % 2
+        if h == 0 and s >= kh:
+            tt(vn("NZ", 4 - s, 8, 5), vn("SC0", 136 * kh + 16, 8, 17), v("TH", 8 * kh, 8 * kh + 8), AL.not_equal)
+            tt(vn("UU", 4 - s, 8, 5), vn("NZ", 4 - s, 8, 5), vn("VT", 4 - s, 8, 5), AL.mult)
         if s > 0:
-            b0 = 120 * h + 40 * s
-            scan(v("O2" + n), v("ZZ", b0, b0 + 40), v("NM", b0, b0 + 40), AL.mult, AL.add)
-            tt(v("BV" + n), ind(v("O2" + n), BL5(0, 1)), v("MK", 0, 128), AL.mult)
-            mm(v(C, 144, 152), v("BV" + n), v("BO16"))
+            tt(v("MJ" + n, 24, 32), vn("ZZ", b0 + 4 - s, 8, 5), vn("O1" + n, 3 - s, 8, 5), AL.mult)
+            tt(v("BV" + n), ind(v("MJ" + n), v("LS", 64 + 16 * s, 80 + 16 * s)), v("MK", 0, 256), AL.mult)
+            group([(v(C, 144, 152), v("BV" + n, 128 * j, 128 * j + 128), v("BO16")) for j in range(2)])
             cp(v("OV" + n), v(C, 144, 152))
+        cp(vn("NM", o, 8 * nk, 5), mj)
+        if s > 0:
+            scan(v("O2" + n), v("ZZ", b0, b0 + 40), v("NM", b0, b0 + 40), AL.mult, AL.add)
             tt(v("TH", 24 * h, 24 * h + 8 * s), vn("SC" + n, 16, 8 * s, 17), vn("NM", o, 8 * s, 5), AL.subtract)
             keepv(vn("O2" + n, 4, 8, 5), h, 3 - s)
 
@@ -376,8 +383,7 @@ def build():
 
     def step3(t):
         ph[0] = "s%d" % t; even = t % 2 == 0; kb = 40 if even else 0; e = t // 2; xb = "XB%d" % t
-        act(v("NZ"), v("NM", kb, kb + 40), AF.Sign)
-        tt(v("UU"), v("VT"), v("NZ"), AL.mult)
+        if t == 2: ms(vn("UU", 4, 8, 5), 0.0)
         scan(v("GS", 120, 160), v("ZZ", kb, kb + 40), v("UU"), AL.mult, AL.add)
         a, b = vn("GS", 124, 8, 5, 0, 64), vn("GS", 44 if even else 0, 8, 5, 0, 64)
         i64, bo4 = v("ID32", 0, 64, p1=64), v("BO16", 0, 4, p1=64)
@@ -392,12 +398,11 @@ def build():
         cp(v("EAB"), ind(DWIN, v("OAB")))
         ea, eb, fr = v("EAB", 0, 64), v("EAB", 64, 128), v("FR")
         ts(fr, ea if even else eb, 0.0, AL.is_equal)
-        tt(v("N12", 0, 8, p1=64), a, b, AL.is_equal)
+        tt(v("UMIN", p1=64), a, b, AL.not_equal); tt(v("UMIN", p1=64), v("UMIN", p1=64), a, AL.min); ts(v("N12", 0, 8, p1=64), v("UMIN", p1=64), 0.0, AL.is_equal)
         mm(v("Y1", 0, 8, p1=64), fr, v("BO"))
-        mm(v("Y1", 256, 320), v("T2"), fr)
-        tt(v("UMIN", p1=64), v("Y1", 0, 8, p1=64), a, AL.min)
-        act(v("PLF"), v("Y1", 256, 320), AF.Identity, bias=32.0)
-        ts(v("N12", 8, 16, p1=64), v("UMIN", p1=64), 0.0, AL.is_equal)
+        mm(v("C0", 192, 256), v("T2"), fr)
+        act(v("PLF"), v("C0", 192, 256), AF.Identity, bias=32.0)
+        ts(v("N12", 8, 16, p1=64), v("Y1", 0, 8, p1=64), 0.0, AL.is_equal)
         for w, x in enumerate((a, b)):
             o = v("Y1", 128 + 64 * w, 192 + 64 * w, p1=8)
             group([(o, x, i64)] + [(o, v("N12", 8 * j, 8 * j + 8, p1=64), v("IDB", 0, 64, p1=64)) for j in range(2)])

@@ -2,52 +2,58 @@ from concourse.bass import DstId, RemoteDMATransfer
 from concourse.mybir import AluOpType as AL, ActivationFunctionType as AF
 
 M, Q, BASE, L, LA = 4096, 2048, 1920, 256, 64
-PATHS = "FFCA FFCA FFCA FFCA FFCA FFCA FFCA FFCA FFCA FFCA FFCA FFCA FFCA FFCA FFCA FFCA FFCA FFCA".split()
-SPLIT = 1
+NA = [[(64, 32), (64, 32), (64, 32)]] * 3
+FAST = (1, 0)
 MODEL = dict(cy=1.0e-3, g=1.56, sc=3.8, pe=0.5, lat=0.15, bw=180e3)
-TUNE = dict(slack=0.05, seed=23, noise=0, smallV=4.0, i=-40.5, smallA=-4.0, w20=6.0, w10=-2.0, s0=-1.0, w00=1.5, w21=-1.0, w11=-3.5, cnt=-3.5, w01=1.5,
-            s1=-2.0, s2=5, x=30, fb=50, moves=10, step=2)
+TUNE = dict(slack=0.05, seed=23, noise=0, fb=40, moves=10, step=2)
 B = float(2 ** 26)
 B2 = 16384.0
-THINIT = 4096.0 * 5000 - 2048
-R1, R2, RO, DUM = 4096, 8192, 10752, 6144
-WIN = DUM + 8 * LA
+NEG = -float(2 ** 30)
+SENT, SENT2 = 4096.0 * 4081, 4096.0 * 4082
+R1, R2, WW, DUM = 4096, 8192, 10240, 6144
+WIN = DUM + 12 * LA
+RO = R1 + WIN
+XW = 128 + max(n[1] for t in NA for n in t)
+C0 = min(min(n) for t in NA for n in t) // 32
+SEG = {(2, 0): 0, (2, 1): 144, (2, 2): 288, (1, 1): 432, (1, 0): 576, (0, 0): 720}
 F, H, BF, U, I = "float32", "float16", "bfloat16", "uint16", "int32"
 SB = {
-    "RW": (RO + WIN, BF), "D32": (WIN, F), "DI": (BASE, I), "VSI": (48, I), "VSF": (48, F),
-    "XB0": (M + L, BF), "XB1": (M + L, BF), "XB2": (M + L, BF),
+    "W0": (WW, BF), "W1": (RO + WIN, BF), "DI": (BASE, I), "DD": (2 * Q + WIN, F), "VSI": (48, I), "VSF": (48, F),
+    "XZ0": (L, BF), "XZ1": (L, BF), "XZ2": (L, BF), "XB0": (16 * XW, BF), "XB1": (16 * XW, BF), "XB2": (16 * XW, BF), "NXT": (768, BF),
     "VU": (96, U), "VL": (48, F), "VU1": (32, U), "VL1": (16, F), "VU2": (32, U), "VL2": (16, F),
-    "SA0": (8, F), "SA1": (8, F), "RA1": (8, F), "RA2": (8, F),
-    "NM": (240, F), "ZZ": (240, F), "GS": (280, F), "TH": (48, F), "VT": (40, F), "NZ": (40, F), "UU": (40, F),
-    "S1R": (768, BF), "S1C": (768, BF), "KEEP": (48, F), "S1T": (48, F), "S1U": (48, F), "YG": (768, F),
-    "ONE": (128, BF), "ONE32": (128, F), "ID": (128, BF), "NID": (128, BF), "ID32": (128, F), "IDB": (128, BF), "ID64N": (128, BF),
-    "BOF": (128, BF), "NBOF": (128, BF), "BO": (8, BF), "BO32": (8, F), "BO16": (8, H), "SC3": (24, BF), "SC3H": (24, H),
-    "TRI": (128, BF), "TRE": (128, BF), "T1": (128, BF), "T1B": (128, BF), "T2": (128, BF), "RBN": (2048, BF), "WD": (144, F),
-    "WT": (576, BF), "WC": (32, F), "DG": (1024, BF), "SEL": (1024, BF), "NSEL": (1024, BF), "TRM": (512, BF), "VB": (768, F), "BCH": (256, H),
-    "PB": (136, BF), "P16": (136, H), "WP": (272, BF), "KC": (272, BF), "RST": (408, F), "MK": (512, F), "II": (128, I), "IJ": (128, I),
-    "LI": (112, I), "LS": (112, U), "DUMC": (16, F), "NC": (128, F), "SCL": (4, F), "CB": (4, F), "BIG3": (4, BF),
-    "BC": (384, F), "OAB": (8, U), "EAB": (128, F), "EB16": (64, U), "FR": (64, BF), "E0": (64, F), "N12": (16, BF), "UMIN": (8, F),
-    "VTH": (128, H), "PLF": (64, BF), "CMM": (1024, BF), "W3": (24, F), "BC2": (256, H), "ACB": (128, BF), "YK": (64, F), "OSC": (8, U), "ACE": (64, BF), "ASUM": (1, F),
-    "AI": (1, I), "AJ": (1, I), "CM2": (1024, BF), "STR": (64, BF), "GO": (64, BF), "N8": (64, BF), "EBH": (64, H), "EBL": (64, H), "Y2": (1024, F),
-    "YI": (64, I), "YJ": (64, I), "YAB": (128, F), "TA": (64, F), "TB": (64, F), "TC": (64, F), "TD": (64, F), "TE": (64, F),
-    "CUT": (64, BF), "CUT2": (64, BF), "RN": (64, BF),
+    "SA0": (8, F), "SA1": (8, F), "RA1": (8, F), "RA2": (8, F), "YG": (768, F), "RZ": (1, BF), "NM": (192, I),
+    "ONE": (128, BF), "ONE32": (128, F), "ID": (128, BF), "NID": (128, BF), "ID32": (128, F), "ID64N": (128, BF), "I2N": (128, BF),
+    "BOF": (128, BF), "NBOF": (128, BF), "BO": (8, BF), "BO32": (8, F), "BO16": (8, H), "SC3H": (24, H), "EXP": (512 * (4 - C0), BF),
+    "TRI": (128, BF), "TRE": (128, BF), "T1": (128, BF), "T1B": (128, BF), "T2": (128, BF), "RBP": (2048, BF), "WD": (432, F),
+    "WT": (576, BF), "WC": (32, F), "DG": (1024, BF), "SEL": (1024, BF), "NSEL": (1024, BF), "TRM": (512, BF), "VB": (768, F),
+    "PB": (144, BF), "P16": (144, H), "WP": (432, BF), "KC": (576, BF), "CR": (160, BF), "LAN": (640, BF), "MK": (128, F), "II": (128, I), "IJ": (128, I),
+    "LI": (64, I), "LJ": (16, I), "LK": (16, I), "LS": (64, U), "DUMC": (24, F), "NC": (128, F), "NL": (16, F), "NB": (2, F), "CB2": (24, BF),
+    "CMP": (32, F), "MC": (96, BF), "GSEL": (240, BF),
+    "XX": (24, F), "FL": (8, I), "A2": (8, F), "DV": (8, F), "NW": (8, F), "TQ": (8, F), "BA": (96, H), "OA": (8, U), "EA": (64, F), "EB": (64, F),
+    "FR": (64, BF), "N01": (16, BF), "NZ0": (8, BF), "ASK": (32, BF), "VTH": (128, H), "PLF": (64, BF), "CMM": (1024, BF), "W3": (24, F), "OSC": (12, U),
+    "JK": (8, F), "ASUM": (1, F), "AI": (1, I), "STR": (64, BF), "GO": (64, BF), "N8": (64, BF), "NU": (64, F), "Y2": (1024, F), "YI": (64, I),
+    "YAB": (192, I), "TA": (64, F), "TB": (64, F), "TC": (64, F), "CUT": (64, BF), "CH": (128, BF), "BC": (128, F), "E0": (64, F),
+    "ZP": (32, F), "NZ": (32, F), "VV": (32, F), "UU": (32, F), "GP": (32, F), "AP": (32, F),
 }
 for _h in "01":
-    SB.update({"E16" + _h: (128, U), "FK" + _h: (384, H), "MM" + _h: (256, BF), "RB" + _h: (2048, BF), "DF" + _h: (2048, H), "CM" + _h: (2048, BF),
-               "PP" + _h: (136, BF), "SC" + _h: (408, F), "MI" + _h: (24, I), "MJ" + _h: (32, I), "O1" + _h: (40, F), "O2" + _h: (40, F), "BV" + _h: (256, H),
-               "OV" + _h: (8, U), "BG" + _h: (384, F), "BH" + _h: (256, H)})
+    SB.update({"E16" + _h: (128, U), "FK" + _h: (384, H), "MM" + _h: (256, BF), "RD" + _h: (2048, H), "CM" + _h: (2048, BF), "PP" + _h: (160, BF),
+               "SC" + _h: (864, I), "D1" + _h: (864, F), "MJ" + _h: (16, I), "A1" + _h: (8, I), "B1" + _h: (8, F), "GE" + _h: (8, F), "ZZ" + _h: (32, F),
+               "BV" + _h: (128, H), "BG" + _h: (128, F), "LT" + _h: (16, F), "S1R" + _h: (384, BF), "S1C" + _h: (384, BF)})
+    for _t in range(3):
+        SB.update({"OV%d" % _t + _h: (32, U), "SG%d" % _t + _h: (16, F), "GS%d" % _t + _h: (32, F)})
     for _t in range(2):
-        SB.update({"SG%d" % _t + _h: (24, F), "SO%d" % _t + _h: (48, U), "RG%d" % (_t + 1) + _h: (24, F), "RO%d" % (_t + 1) + _h: (48, U)})
-DYN = ("C0", "C1")
-PS = ["K0", "K1", "C0", "C1", "P0", "P1", "Y0", "Y1"]
+        SB.update({"SO%d" % _t + _h: (64, U), "RG%d" % (_t + 1) + _h: (16, F), "RO%d" % (_t + 1) + _h: (32, U),
+                   "RS%d" % (_t + 1) + _h: (32, F), "RP%d" % (_t + 1) + _h: (64, U)})
+DYN = ("A0",)
+PS = ["K0", "K1", "A0", "B0", "A1", "B1", "Y0", "Y1"]
 POOL, FILL = {}, {}
 for _k, (_n, _d) in SB.items():
-    if _n <= 512 and _k[:2] not in ("VU", "VL", "SG", "SO", "SA", "RG", "RO", "RA", "VS"):
+    if _n <= 640 and _k[:2] not in ("VU", "VL", "SG", "SO", "SA", "RG", "RO", "RA", "VS", "OV", "GS", "RS", "RP", "XZ") or _k == "GSEL":
         POOL[_k] = ("pool_" + _d, FILL.get(_d, 0)); FILL[_d] = FILL.get(_d, 0) + (_n + 31) // 32 * 32
 SCRATCH = {k: ("sbuf", [128, n], d) for k, (n, d) in SB.items() if k not in POOL}
 SCRATCH.update({"pool_" + d: ("sbuf", [128, n], d) for d, n in FILL.items()})
 SCRATCH.update({k: ("psum", [128, 512], F) for k in PS})
-SEMAPHORES = ["qV", "qA", "qP", "qG"] + ["d%d" % i for i in range(16)] + ["r%d" % i for i in range(16)] + ["l%d" % i for i in range(9)]
+SEMAPHORES = ["qV", "qA", "qP", "qG"] + ["d%d" % i for i in range(16)] + ["r%d" % i for i in range(24)] + ["l%d" % i for i in range(12)]
 QSEM = {"V": "qV", "A": "qA", "P": "qP", "G": "qG"}
 PLAN = {}
 
@@ -60,6 +66,10 @@ def v(n, c0=0, c1=None, st=1, p0=0, p1=128):
 
 def vn(n, c0, cnt, st, p0=0, p1=128):
     return (n, p0, p1, c0, c0 + (cnt - 1) * st + 1, st)
+
+
+def lo(x):
+    return (x[0], 0, LA) + x[3:]
 
 
 def ind(w, o):
@@ -172,13 +182,20 @@ def build():
     def sel(out, a, pat, op, base, cm, fill=0.0):
         add("G", lambda g, T, c: g.affine_select(ap(T, out), ap(T, a), pat, op, fill, base, cm), [a], [out], (0.17, 2 * cols(out), 0, 0, 0))
 
-    def dma(q, out, a, rd, wr, nbytes):
+    def keep(out, a):
+        sel(out, a, [[0, cols(out)]], AL.is_gt, 1, 0)
+
+    def dma(q, out, a, rd, wr, nbytes, chain=False, wait=()):
         s = "d%d" % nd[0]; nd[0] += 1
         i = add(q, lambda g, T, c: (g.sync if q == "S" else g.scalar).dma_start(out(T), a(T)), rd, wr, (0.06, 0, 0, 0, 0), kind="d", sem=s, cnt=16,
-                nbytes=nbytes, after=last[-1:] if q == "S" else [])
-        if q == "S": last.append(i)
+                nbytes=nbytes, after=last[-1:] if chain else [], wait=list(wait))
+        if chain: last.append(i)
+        return i
 
-    def send(items, lat):
+    def copy(out, a, wait=()):
+        return dma("S", lambda T: ap(T, out), lambda T: ap(T, a), [a], [out], 128 * cols(a) * wide(a), wait=wait)
+
+    def send(items, lat, wait=()):
         ls = "l%d" % nl[0]; nl[0] += 1; ks = [k for s, d, k in items]
         rs = ["r%d" % (nr[0] + j) for j in range(len(items))]; nr[0] += len(items)
 
@@ -191,50 +208,56 @@ def build():
                     return g.remote_dma(ap(T, d), ap(T, s), T.sem[rs[0]], T.sem[ls], pid, rid, mask)
                 tr.append(RemoteDMATransfer(dst_ids=[DstId(rid=rid, pnc=pid)], dma_engine_mask=mask, remote_sem=T.sem[rs[j]], src=ap(T, s), dst=ap(T, d)))
             return g.remote_dma_fused(tr, local_sem=T.sem[ls])
-        i = add("G", fn, [s for s, d, k in items], [], (1.0, 0, 0, 0, 0), kind="s", sem=ls, ks=ks)
+        i = add("G", fn, [s for s, d, k in items], [], (1.0, 0, 0, 0, 0), kind="s", sem=ls, ks=ks, wait=list(wait))
         for j, (s, d, k) in enumerate(items):
             add("R", None, [], [d], (lat, 0, 0, 0, 0), kind="r", sem=rs[j], ks=ks, k=k, src=i)
         return i
 
-    X0 = "XB0"
     dma("A", lambda T: T.VSI[:, :], lambda T: T.vs[:, :], [], [v("VSI")], 25000)
-    dma("A", lambda T: T.XB0[:, M:M + L], lambda T: T.z[:, :], [], [v(X0, M, M + L)], 66000)
-    dma("S", lambda T: T.RW[:, 0:Q], lambda T: T.rg[:, 0:Q], [], [v("RW", 0, Q)], 524288)
-    for a, b in ((0, 960), (960, BASE)):
-        dma("S", lambda T, a=a, b=b: T.DI[:, a:b], lambda T, a=a, b=b: T.nd[:, a:b], [], [v("DI", a, b)], 491520)
-    dma("S", lambda T: T.RW[:, Q:M], lambda T: T.rg[:, Q:M], [], [v("RW", Q, M)], 524288)
+    dma("A", lambda T: T.XZ0[:, :], lambda T: T.z[:, :], [], [v("XZ0")], 66000)
+    dma("S", lambda T: T.W0[:, 0:Q], lambda T: T.rg[:, 0:Q], [], [v("W0", 0, Q)], 524288, True)
+    dma("S", lambda T: T.DI[:, :], lambda T: T.nd[:, :], [], [v("DI")], 983040, True)
+    loaded = dma("S", lambda T: T.W0[:, Q:M], lambda T: T.rg[:, Q:M], [], [v("W0", Q, M)], 524288, True)
 
     ms(v("ONE"), 1.0); ms(v("ONE32"), 1.0)
     iota(v("II"), [[0, 8], [-1, 16]], 128, 1)
-    iota(v("LI", 0, 24), [[1, 24]], 0, 0); iota(v("LI", 24, 48), [[5, 24]], 4, 0)
-    iota(v("LI", 48, 64), [[-80, 2], [5, 8]], 124, 0); iota(v("LI", 64, 80), [[-124, 2], [5, 8]], 124, 0); iota(v("LI", 80, 96), [[16, 2], [1, 8]], 8, 0)
-    iota(v("LI", 96, 112), [[1, 16]], 16, 0); ms(v("MJ0"), 0); ms(v("MJ1"), 0)
+    iota(v("LI", 0, 24), [[1, 24]], 0, 0); iota(v("LI", 24, 32), [[4, 8]], 3, 0)
+    iota(v("LJ", 0, 8), [[8, 2], [0, 4]], 0, 0); iota(v("LJ", 8, 16), [[8, 4], [0, 2]], 0, 0); iota(v("LK"), [[0, 16]], 0, 1)
+    ts(v("LI", 48, 64), v("LK"), 7, AL.bitwise_and); tt(v("LI", 32, 48), v("LI", 48, 64), v("LJ"), AL.add)
     cp(v("LS"), v("LI"))
-    BL1, BL5 = (lambda n: v("LS", 0, n)), (lambda k0, k1: v("LS", 24 + 8 * k0, 24 + 8 * k1))
     ts(v("IJ"), v("II"), 15, AL.bitwise_and)
-    ts(v("MK", 0, 128), v("IJ"), 0.0, AL.is_equal)
-    act(v("MK", 128, 256), v("MK", 0, 128)); act(v("MK", 256, 384), v("MK", 0, 128)); act(v("MK", 384, 512), v("ONE"))
+    ts(v("MK"), v("IJ"), 0.0, AL.is_equal)
     sel(v("BOF"), v("ONE"), [[-16, 8], [0, 16]], AL.is_ge, 0, 1); sel(v("BOF"), v("BOF"), [[16, 8], [0, 16]], AL.is_ge, 15, -1)
     sel(v("ID"), v("ONE"), [[-1, 128]], AL.is_equal, 0, 1)
-    ms(v("PB"), 1.0); sel(v("PB"), v("PB"), [[-16, 8], [-1, 17]], AL.is_equal, 1, 1); ms(vn("PB", 0, 8, 17), 0.0)
+    ms(v("PB"), 1.0); sel(v("PB"), v("PB"), [[-16, 8], [-1, 18]], AL.is_equal, 2, 1); ms(vn("PB", 0, 8, 18), 0.0); ms(vn("PB", 1, 8, 18), 0.0)
     bo = vn("BOF", 0, 8, 16)
-    act(v("BO"), bo); act(v("BO32"), bo); cp(v("BO16"), bo)
+    act(v("BO"), bo); act(v("BO32"), bo); act(v("BO16"), bo)
     for j in range(3):
-        scale(v("SC3", 8 * j, 8 * j + 8), bo, -4096.0)
-    cp(v("SC3H"), v("SC3"))
-    scale(v("NID"), v("ID"), -1.0); act(v("ID32"), v("ID")); scale(v("IDB"), v("ID"), B2); scale(v("ID64N"), v("ID"), -64.0)
-    cp(v("P16"), v("PB")); scale(v("WP", 0, 136), v("PB"), B); scale(v("WP", 136, 272), v("PB"), -B)
-    ms(v("KC", p1=32), B); ms(vn("KC", 0, 16, 17, 0, 32), 0.0)
-    ms(v("RST"), 0.0); ms(vn("RST", 0, 24, 17), float(2 ** 30))
-    for h in range(2):
-        ms(vn("C%d" % h, 0, 8, 17), 64.0)
-    ms(v("SCL"), -B); ms(v("CB"), 11 * B)
-    for c in range(max(p.count("F") for p in PATHS)):
-        ms(v("SCL", c + 1, 4, 1, 32 * c, 32 * c + 32), -B / 2); ms(v("CB", c + 1, 4, 1, 32 * c, 32 * c + 32), 3 * B)
-    ms(v("NM"), 0.0); ms(v("ZZ"), 1.0); ms(vn("ZZ", 0, 48, 5), 0.0); ms(v("TH"), THINIT); ms(v("UU"), 0.0); ms(v("GS"), 0.0); ms(v("W3"), 0.0)
-    ms(v("RW", R1 + Q, R2), 0.0); ms(v("D32", BASE, Q), 0.0)
+        scale(v("SC3H", 8 * j, 8 * j + 8), bo, -4096.0)
+    scale(v("NID"), v("ID"), -1.0); act(v("ID32"), v("ID"))
+    act(v("P16"), v("PB")); scale(v("WP", 0, 144), v("PB"), B); scale(v("WP", 144, 288), v("PB"), -B); scale(v("WP", 288, 432), v("PB"), B)
+    ms(v("GSEL"), 0.0); act(v("GSEL", 112, 128), v("MK", 0, 16))
+    gsel = lambda g, p1: v("GSEL", 112 - 16 * g, 240 - 16 * g, p1=p1)
+    ms(v("KC", 0, 288, p1=32), 0.0); ms(v("KC", 288, 576, p1=32), B / 32); ms(vn("KC", 145, 8, 18, 0, 32), B / 32); ms(vn("KC", 433, 8, 18, 0, 32), 0.0)
+    ms(vn("KC", 0, 32, 18, 0, 32), NEG / 32)
+    ms(v("KC", p0=32, p1=64), 64.0); ms(vn("KC", 0, 32, 18, 32, 64), 0.0); ms(vn("KC", 1, 32, 18, 32, 64), 0.0)
+    kc = lambda cand, guard: v("KC", 144 * ((2 * cand) + (cand ^ guard)), 144 * ((2 * cand) + (cand ^ guard)) + 144, p1=64)
+    ms(v("CR", p1=32), 1.0); ms(v("CR", p0=32, p1=64), -6.0 / 32); ms(v("CR", 144, 160, p1=32), 0.0)
+    for j in range(2):
+        ms(vn("CR", j, 8, 18, 0, 32), 0.0); ms(vn("CR", j, 8, 18, 32, 64), 2.0)
+    nas = sorted(set(n for t in NA for s in t for n in s))
+    for j, n in enumerate(nas):
+        ms(v("LAN", 128 * j, 128 * j + 128, p0=32, p1=64), 1.0)
+        if n > 0: ms(v("LAN", 128 * j, 128 * j + n, p1=32), -0.5)
+        if n < 128: ms(v("LAN", 128 * j + n, 128 * j + 128, p1=32), 0.0)
+    for h in "01":
+        ms(v("D1" + h), NEG); ms(vn("D1" + h, 0, 8, 18), SENT); ms(vn("D1" + h, 144, 8, 18), SENT2)
+    ms(v("NM"), 0); ms(v("CMP"), 0.0); ms(vn("CMP", 0, 8, 4), -1.0)
+    ms(v("W0", R1 + Q, R2), 0.0); ms(v("DD", BASE, Q), 0.0)
     for n in ("SA0", "SA1"): ms(v(n), 0.0)
-    for n in ("SO00", "SO01", "SO10", "SO11", "VU"): ms(v(n), 0)
+    for n in ("SO00", "SO01", "SO10", "SO11", "OV00", "OV01", "OV10", "OV11", "VU"): ms(v(n), 0)
+    for j in range(16):
+        (cp if j % 2 else act)(vn("EXP", j, 128 - 32 * C0, 16), v("ID", 32 * C0, 128))
     for t in range(3):
         cp(v("VU", 32 * t, 32 * t + 16), v("VSI", 16 * t, 16 * t + 16))
     cp(v("VSF"), v("VSI"))
@@ -244,267 +267,262 @@ def build():
         mm(v("Y0", 8 * j, 8 * j + 8), v("VB", 128 * j, 128 * j + 128), v("BO32"))
     act(v("VL"), v("Y0", 0, 48))
     for i in range(16):
-        (cp if i % 4 else act)(vn(X0, i, L, 16), v(X0, M, M + L))
-    for a, b in ((0, 960), (960, BASE)):
-        cp(v("D32", a, b), v("DI", a, b))
-    cp(v("RW", R1, R1 + Q), v("RW", 0, Q)); act(v("RW", R2, R2 + Q), v("RW", 0, Q)); ms(v("RW", 0, 1), 512.0)
+        cp(vn("XB0", i, XW, 16), v("XZ0", 0, XW))
+    act(v("RZ"), v("W0", 0, 1)); ms(v("W0", 0, 1), 512.0); cp(v("W0", R1, R1 + Q), v("W0", 0, Q)); act(v("W0", R2, R2 + Q), v("W0", 0, Q))
     ph[0] = "x"
-    send([(v(X0, M, M + L), v("XB%d" % k, M, M + L), k) for k in (1, 2)], 6.0)
-    send([(v("VU", 32, 64), v("VU1"), 1), (v("VL", 16, 32), v("VL1"), 1), (v("VU", 64, 96), v("VU2"), 2), (v("VL", 32, 48), v("VL2"), 2)], 6.0)
-    ph[0] = "i"
+    s1 = send([(v("XZ0"), v("XZ%d" % k), k) for k in (1, 2)], 4.0, [loaded])
+    s2 = send([(v("VU", 32, 64), v("VU1"), 1), (v("VL", 16, 32), v("VL1"), 1), (v("VU", 64, 96), v("VU2"), 2), (v("VL", 32, 48), v("VL2"), 2)], 4.0, [loaded])
+    copy(v("W1", 0, WW), v("W0"), [s1, s2])
+    for a, b in ((0, 960), (960, BASE)):
+        keep(v("DD", a, b), v("DI", a, b))
+    ph[0] = "j"
     sel(v("TRI"), v("BOF"), [[1, 128]], AL.is_ge, 0, -1); sel(v("TRE"), v("BOF"), [[1, 128]], AL.is_gt, 0, -1)
     sel(v("T1"), v("TRI"), [[-1, 128]], AL.not_equal, 0, 1, -31.0); sel(v("T2"), v("TRE"), [[-1, 128]], AL.not_equal, 0, 1, -64.0)
     ms(v("SEL", p1=32), 1.0); sel(v("SEL", p1=8), v("SEL", p1=8), [[-1, 8], [0, 128]], AL.is_equal, 0, 1); scale(v("NSEL", p1=8), v("SEL", p1=8), -1.0)
     ms(v("TRM"), 0.5)
     for p in (0, 64):
         sel(v("TRM", p0=p, p1=p + 64), v("TRM", p0=p, p1=p + 64), [[0, 8], [-1, 64]], AL.is_ge, 0, 1)
-    ms(v("RBN"), -B2); sel(v("RBN"), v("RBN"), [[-1, 16], [-16, 8], [0, 16]], AL.is_equal, 0, 1)
-    iota(v("DUMC"), [[256, 2], [0, 8]], DUM, 4); iota(v("NC"), [[1, 128]], M + BASE, 0)
-    scale(v("BIG3"), v("ONE", 0, 4), B2); scale(v("NBOF"), v("BOF"), -1.0); scale(v("T1B"), v("T1"), B2)
-    iota(v("WD"), [[0, 144]], 0, 0); act(vn("WD", 15, 8, 16), bo); iota(v("WT"), [[0, 576]], 0, 0)
+    iota(v("DUMC"), [[256, 3], [0, 8]], DUM, 4); iota(v("NC"), [[1, 128]], M + BASE, 0); iota(v("NL"), [[64, 2], [0, 8]], BASE, 1)
+    ts(v("NB"), vn("NL", 0, 2, 8), 1.0, AL.add, B, AL.mult)
+    scale(v("NBOF"), v("BOF"), -1.0); scale(v("T1B"), v("T1"), B2); scale(v("ID64N"), v("ID"), -64.0)
+    for j in range(2):
+        act(lo(v("I2N", 64 * j, 64 * j + 64)), lo(v("ID64N", 0, 64)))
+    for j in range(3):
+        act(v("MC", 32 * j, 32 * j + 32), vn("BOF", 0, 32, 2))
+    ms(v("CB2", p1=32), B2); ms(v("XX"), 0.0); ms(v("W3"), 0.0); ms(v("VV"), 0.0)
+    iota(v("WD"), [[0, 432]], 0, 0); iota(v("WT"), [[0, 576]], 0, 0)
+    act(vn("WD", 15, 8, 16), bo); scale(vn("WD", 16, 8, 16), bo, -1.0); act(vn("WD", 144 + 15, 8, 16), bo); scale(vn("WD", 288 + 16, 8, 16), bo, -1.0)
     scale(v("WC", 0, 16), v("MK", 0, 16), B2); act(v("WC", 16, 32), v("MK", 0, 16), AF.Identity, bias=1.0, scale=-1.0)
+    for i in range(16):
+        scale(v("RBP", 128 * i, 128 * i + 128), v("BOF"), v("WC", i, i + 1))
     for e, t in enumerate((0, 2)):
         for j, row in enumerate((t, 8 + t)):
             o = 512 * e + 256 * j
-            scale(vn("WT", 144 * (2 * e + j) + 15, 8, 16), bo, v("WC", row, row + 1))
+            scale(vn("WT", 144 * (2 * e + j) + 15, 8, 16), bo, v("MK", row, row + 1))
             scale(v("DG", o, o + 128), v("ID"), v("MK", row, row + 1)); scale(v("DG", o + 128, o + 256), v("ID"), v("WC", 16 + row, 17 + row))
 
     def repeat(k, after):
         ph[0] = "x"
         for i in range(16):
-            sel(vn("XB%d" % k, i, L, 16), v("XB%d" % k, M, M + L), [[0, L]], AL.is_gt, 1, 0)
+            keep(vn("XB%d" % k, i, XW, 16), v("XZ%d" % k, 0, XW))
             ops[-1]["after"] = after
     repeat(1, [])
-    RWIN, DWIN = v("RW", 0, R2 + Q), v("D32", 0, Q)
+    rec = lambda t, a=0, b=WW: v("W1" if t else "W0", a, b)
+    node = lambda t: v("DD", Q * (t - 1), Q * t) if t else v("DI")
+    vl = lambda t, h: v("VL%d" % t if t else "VL", 8 * h, 8 * h + 8)
+    ends = lambda n, s, k, cnt=8: vn("SC" + n, SEG[s, k] + 17, cnt, 18)
+    slot = lambda n, s, k: vn("D1" + n, SEG[s, k], 8, 18)
+    nm = lambda t, h, j=None: v("NM", 64 * t + 32 * h, 64 * t + 32 * h + 32) if j is None else vn("NM", 64 * t + 32 * h + j, 8, 4)
 
-    def keepv(src, h, j):
-        act(vn("NM", 120 * h + 40 * (2 - j), 8, 5), src)
-        if h == 0:
-            act(vn("VT", 2 + j, 8, 5), src)
+    def spread(out, bv, src, lst, mask, n, p1):
+        tt(bv, ind(src, lst), mask, AL.mult)
+        group([(out, gsel(g, p1), vn(bv[0], g, n, 8, 0, p1)) for g in range(8)])
 
-    def step1(t, h):
-        Y = "Y%d" % h; o = 384 * h; x = v("XB%d" % t, M + 128 * h, M + 128 * h + 128); k24 = lambda n: v(n, 24 * h, 24 * h + 24)
-        act(v("S1R", o, o + 384), ind(v("RW", 0, M), v("RO%d%d" % (t, h), 0, 24)))
-        group([(v(Y, 0, 384), v("ID"), v("S1R", o, o + 384))] + [(v(Y, 128 * k, 128 * k + 128), v("NID"), x) for k in range(3)])
-        act(v("S1C", o, o + 384), v(Y, 0, 384), AF.Sign, bias=0.5, scale=-1.0)
-        for k in range(3):
-            mm(v(Y, 416 + 8 * k, 424 + 8 * k), v("S1R", o + 128 * k, o + 128 * k + 128), v("SC3", 0, 8))
-        for k in range(3):
-            mm(v(Y, 384 + 8 * k, 392 + 8 * k), v("S1C", o + 128 * k, o + 128 * k + 128), v("BO"))
-        ts(k24("S1T"), v(Y, 384, 408), v("RA%d" % t, 0, 1), AL.is_lt, B, AL.mult)
-        ts(k24("KEEP"), v(Y, 384, 408), v("RA%d" % t, 0, 1), AL.is_ge)
-        tt(k24("S1U"), v(Y, 416, 440), k24("S1T"), AL.add)
-        ts(k24("TH"), k24("S1U"), -2048.0, AL.add, THINIT, AL.min)
-        tt(vn("NM", 120 * h + 1, 24, 5), k24("KEEP"), v("RG%d%d" % (t, h)), AL.mult)
-        act(vn("ZZ", 120 * h + 1, 24, 5), k24("KEEP"), AF.Identity, bias=1.0, scale=-1.0)
+    def start(t, h):
+        ph[0] = "w%d%d" % (t, h); n = str(h); o = 256 * t + 128 * h
+        mm(v("A" + n, 0, 128), v("XZ%d" % t, 128 * h, 128 * h + 128), v("NID")); act(v("NXT", o, o + 128), v("A" + n, 0, 128))
+        ts(slot(n, 2, 2), vl(t, h), SENT, AL.add)
+
+    def step1(t, h, a, b, off):
+        n = str(h); P = "A" + n; x = v("XZ%d" % t, 128 * h, 128 * h + 128)
+        act(v("S1R" + n, a, b), ind(rec(t, 0, M), off))
+        group([(v(P, 0, b - a), v("ID"), v("S1R" + n, a, b))] + [(v(P, c, c + 128), v("NID"), x) for c in range(0, b - a, 128)])
+        act(v("S1C" + n, a, b), v(P, 0, b - a), AF.Sign, bias=0.5, scale=-1.0)
 
     def walk(t, s, h):
-        ph[0] = "w%d%d" % (t, h); n = str(h); xb = "XB%d" % t; nk = s + 1; K, C, P = "K" + n, "C" + n, "P" + n
-        off = v("VU" if t == 0 else "VU%d" % t, 8 * h, 8 * h + 8) if s == 2 else v("OV" + n)
-        e16 = v("E16" + n); path = PATHS[6 * t + 2 * (2 - s) + h]
-        cp(e16, ind(DWIN, off))
-        for c in range(4):
-            w = ind(RWIN, v("E16" + n, 32 * c, 32 * c + 32)); a, b = 512 * c, 512 * c + 512
-            x = v(xb, 2048 * h + a, 2048 * h + b); cm, rb = v("CM" + n, a, b), v("RB" + n, a, b); p = path[c]
-            if p in "AC":
-                for j in range(SPLIT):
-                    q = 512 // SPLIT; a2 = a + j * q
-                    tt(v(("DF" if p == "A" else "CM") + n, a2, a2 + q), ind(RWIN, v("E16" + n, a2 // 16, (a2 + q) // 16)),
-                       v(xb, 2048 * h + a2, 2048 * h + a2 + q), AL.subtract if p == "A" else AL.is_le)
-            if p == "A":
-                ts(cm, v("DF" + n, a, b), 0.0, AL.is_le)
-                continue
-            act(rb, w)
-            if p == "G": tt(cm, rb, x, AL.is_le)
-            if p in "FE":
-                group([(v(P), v("NID"), x), (v(P), v("ID"), rb)])
-                if p == "F": act(cm, v(P), AF.Sign, bias=0.5, scale=-1.0)
-                else: ts(cm, v(P), 0.0, AL.is_le)
-        ts(v("MM" + n, 0, 128), e16, 4096.0, AL.is_ge)
-        if s > 0: ts(v("MM" + n, 128, 256), e16, 8192.0, AL.is_ge)
-        for k in range(nk):
-            ts(v("FK" + n, 128 * k, 128 * k + 128), e16, -4096.0 * k - 2048, AL.add)
-        lst = [(v(K, 136 * k, 136 * k + 136), v("MM" + n, 0, 128), v("WP", 136 * k, 136 * k + 136)) for k in range(min(nk, 2))]
-        if s > 0:
-            lst = [(v(K, 136, 136 * nk), v("ONE", p1=1), v("KC", 0, 136 * s, p1=1))] + lst + [(v(K, 136, 136 * nk), v("MM" + n, 128, 256), v("WP", 0, 136 * s))]
-        lst += [(v(K, 136 * k, 136 * k + 136), v("FK" + n, 128 * k, 128 * k + 128), v("P16")) for k in range(nk)]
-        na = 32 * (4 - path.count("A")); nf = path.count("F")
-        if na < 128: lst += [(vn(K, 1 + i, 8 * nk, 17, na, 128), vn("DF" + n, 16 * na + i, 128 - na, 16), v("SC3H", 0, 8 * nk)) for i in range(16)]
-        if na > 0: lst += [(vn(K, 1 + i, 8 * nk, 17, 0, na), vn("RB" + n, i, na, 16), v("SC3", 0, 8 * nk)) for i in range(16)]
-        lst.append((vn(K, 0, 8 * nk, 17), v("ID32"), v("TH", 24 * h, 24 * h + 8 * nk)))
+        ph[0] = "w%d%d" % (t, h); n = str(h); K = "K" + n; nk = s + 1; na = NA[t][2 - s][h]; RD, CM = "RD" + n, "CM" + n
+        ov = "OV%d%d" % (t, h); e16 = v("E16" + n); tags = {2: (0, 1, 2), 1: (1, 0), 0: (0,)}[s]
+        off = v("VU%d" % t if t else "VU", 8 * h, 8 * h + 8) if s == 2 else v(ov, 8 - 8 * s, 16 - 8 * s)
+        if t > 0 and s == 2: step1(t, h, 0, 256, v("RO%d%d" % (t, h), 0, 16))
+        if t > 0 and s == 1: step1(t, h, 256, 384, v("RP%d%d" % (t, h), 0, 8))
+        cap = s == 1 or (s == 0 and h == 1)
+        if cap: ts(e16, ind(node(t), off), 4096.0 * nk, AL.min)
+        else: cp(e16, ind(node(t), off))
+        if na:
+            tt(v(RD, 0, 16 * na), ind(rec(t), v("E16" + n, 0, na)), v("XB%d" % t, 2048 * h, 2048 * h + 16 * na), AL.subtract)
+            ts(v(CM, 0, 16 * na), v(RD, 0, 16 * na), 0.0, AL.is_le, 2.0, AL.mult)
+        banks = ["B0"] if (h, s) == (0, 0) else ["A" + n, "B" + n]
+        for j, c in enumerate(range(na // 32, 4)):
+            P = banks[j % len(banks)]; a, b = 512 * c, 512 * c + 512
+            act(v(RD, a, b), ind(rec(t), v("E16" + n, 32 * c, 32 * c + 32)))
+            group([(v(P), v("NXT", 256 * t + 128 * h, 256 * t + 128 * h + 128), v("EXP", a - 512 * C0, b - 512 * C0)), (v(P), v("ID"), v(RD, a, b))])
+            act(v(CM, a, b), v(P), AF.Sign, bias=0.5, scale=-1.0)
+        masks = [0, 1] if s == 2 else [] if cap and s == 0 else [0]
+        for j in masks:
+            ts(v("MM" + n, 128 * j, 128 * j + 128), e16, 4096.0 * (j + 1), AL.is_ge)
+        for k in tags:
+            ts(v("FK" + n, 128 * k, 128 * k + 128), e16, -4096.0 * k - (2048 if k == 0 else 0), AL.add)
+        gd = [] if t == 0 else {2: [(2, 0), (1, 1)], 1: [(0, 2)], 0: []}[s]
+        run = lambda k: v(K, 144 * tags.index(k), 144 * tags.index(k) + 144)
+        gcol = lambda k: vn(K, 144 * tags.index(k) + 1, 8, 18)
+        lst = [(run(k), v("ONE", p1=64), kc(int(k > 0), int(k not in [x for x, j in gd]))) for k in tags]
+        if s == 2: lst += [(v(K, 144 * j, 144 * j + 288), v("MM" + n, 128 * j, 128 * j + 128), v("WP", 0, 288)) for j in masks]
+        elif masks: lst += [(v(K, 0, 144 * nk), v("MM" + n, 0, 128), v("WP", 144 * s, 144 * s + 144 * nk))]
+        lst += [(run(k), v("FK" + n, 128 * k, 128 * k + 128), v("P16")) for k in tags]
+        for k, j in gd:
+            lst.append((gcol(k), v("S1R" + n, 128 * j, 128 * j + 128), v("SC3H", 0, 8)))
+            if k: lst.append((gcol(k), v("ID32"), v("RG%d%d" % (t, h), 8 * j, 8 * j + 8)))
+        lst += [(vn(K, 2 + i, 8 * nk, 18), vn(RD, i, 128, 16), v("SC3H", 0, 8 * nk)) for i in range(16)]
         for j, (o, l, r) in enumerate(lst):
             mm(o, l, r, j == 0, False)
-        for i in range(16):
-            mm(vn(C, 1 + i, 8, 17), vn("CM" + n, i, 128, 16), v("BO"))
-        act(v("PP" + n), v(C, 0, 136), AF.Relu, bias=v("CB", nf, nf + 1) if t == 0 else v("RA%d" % t, 1 + nf, 2 + nf), scale=v("SCL", nf, nf + 1))
-        for k in range(nk):
-            mm(v(K, 136 * k, 136 * k + 136), v("ID"), v("PP" + n), False, k == s)
-        b0 = 120 * h + 40 * s
-        if s > 0: scan(v("O1" + n), v("ZZ", b0, b0 + 40), v("NM", b0, b0 + 40), AL.mult, AL.add)
-        scan(v("SC" + n, 0, 136 * nk), v("RST", 0, 136 * nk), v(K, 0, 136 * nk), AL.add, AL.min)
-        m = vn("SC" + n, 16, 8 * nk, 17); mi, mj = v("MI" + n, 0, 8 * nk), v("MJ" + n, 0, 8 * nk); o = 120 * h + 4 - s
-        ts(mi, m, 2048.0, AL.add); ts(mj, mi, 4095, AL.bitwise_and)
-        tt(vn("ZZ", o, 8 * nk, 5), m, v("TH", 24 * h, 24 * h + 8 * nk), AL.is_equal)
-        kh = 1 - t % 2
-        if h == 0 and s >= kh:
-            tt(vn("NZ", 4 - s, 8, 5), vn("SC0", 136 * kh + 16, 8, 17), v("TH", 8 * kh, 8 * kh + 8), AL.not_equal)
-            tt(vn("UU", 4 - s, 8, 5), vn("NZ", 4 - s, 8, 5), vn("VT", 4 - s, 8, 5), AL.mult)
+        C = "B" + n; w = 144 + 8 * len(gd); la = 128 * nas.index(na)
+        group([(v(C, 0, w), v("LAN", la, la + 128, p1=64), v("CR", 0, w, p1=64))]
+              + [(v(C, 144 + 8 * i, 152 + 8 * i), v("S1C" + n, 128 * j, 128 * j + 128), v("BO")) for i, (k, j) in enumerate(gd)]
+              + [(vn(C, 2 + i, 8, 18), vn(CM, i, 128, 16), v("BO")) for i in range(16)])
+        act(v("PP" + n, 0, w), v(C, 0, w), AF.Relu, bias=v("RA%d" % t, 0, 1) if t else None, scale=-B / 2)
+        lst = [(gcol(k), v("ID"), v("PP" + n, 144 + 8 * i, 152 + 8 * i)) for i, (k, j) in enumerate(gd)] + [(run(k), v("ID"), v("PP" + n, 0, 144)) for k in tags]
+        for j, (o, l, r) in enumerate(lst):
+            mm(o, l, r, False, j == len(lst) - 1)
+        o = SEG[s, tags[0]]
+        scan(v("SC" + n, o, o + 144 * nk), v(K, 0, 144 * nk), v("D1" + n, o, o + 144 * nk), AL.min, AL.max)
+        mj = v("MJ" + n, 16 - 8 * s, 24 - 8 * s)
         if s > 0:
-            tt(v("MJ" + n, 24, 32), vn("ZZ", b0 + 4 - s, 8, 5), vn("O1" + n, 3 - s, 8, 5), AL.mult)
-            tt(v("BV" + n), ind(v("MJ" + n), v("LS", 64 + 16 * s, 80 + 16 * s)), v("MK", 0, 256), AL.mult)
-            group([(v(C, 144, 152), v("BV" + n, 128 * j, 128 * j + 128), v("BO16")) for j in range(2)])
-            cp(v("OV" + n), v(C, 144, 152))
-        cp(vn("NM", o, 8 * nk, 5), mj)
-        if s > 0:
-            scan(v("O2" + n), v("ZZ", b0, b0 + 40), v("NM", b0, b0 + 40), AL.mult, AL.add)
-            tt(v("TH", 24 * h, 24 * h + 8 * s), vn("SC" + n, 16, 8 * s, 17), vn("NM", o, 8 * s, 5), AL.subtract)
-            keepv(vn("O2" + n, 4, 8, 5), h, 3 - s)
+            ts(mj, ends(n, s, s), 2047, AL.bitwise_and)
+            if FAST[h]:
+                tt(v("BV" + n), ind(mj, v("LS", 0, 8)), v("MK"), AL.mult)
+                mm(v(K, 440, 448), v("BV" + n), v("BO16"))
+            else:
+                spread(v(K, 440, 448), v("BV" + n, 0, 64), mj, v("LS", 32, 36), vn("BOF", 0, 64, 2), 8, 128)
+            cp(v(ov, 16 - 8 * s, 24 - 8 * s), v(K, 440, 448))
+        if s == 2:
+            ts(v("A1" + n), ends(n, 2, 1), -2049, AL.bitwise_and); ts(v("B1" + n), mj, SENT, AL.add)
+            tt(slot(n, 1, 1), v("A1" + n), v("B1" + n), AL.min)
+        if (t, s, h) == (1, 0, 0):
+            tt(v("NZ0"), ends(n, 0, 0), slot(n, 0, 0), AL.is_lt)
+        name = nm(t, h, {2: 0, 1: 2, 0: 3}[s])
+        ts(name, ends(n, s, 0), 4095, AL.bitwise_and)
+        if s > 0: tt(slot(n, s - 1, 0), ends(n, s, 0), name, AL.subtract)
+        if s == 1 and t > 0:
+            tt(v("GE" + n), slot(n, 1, 0), gcol(0), AL.is_ge); tt(nm(t, h, 1), v("GE" + n), vn("RS%d%d" % (t, h), 3, 8, 4), AL.mult)
 
-    def guards(t, h, k0, k1):
-        n = str(h); a, b = 40 * k0, 40 * k1; C = "C" + n
-        if k1 == 3: ms(vn("ZZ", 120 * h + 1, 24, 5), 0.0)
-        scan(v("GS", 160 * h + a, 160 * h + b), v("ZZ", 120 * h + a, 120 * h + b), v("NM", 120 * h + a, 120 * h + b), AL.mult, AL.add)
+    def yg(k, h, src, P, c):
+        mm(v(P, c, c + 128, p1=8), src, v("ID32")); act(v("YG", 256 * k + 128 * h, 256 * k + 128 * h + 128, p1=8), v(P, c, c + 128, p1=8))
+
+    def guards21(t, h):
+        n = str(h); sg = "SG%d%d" % (t, h)
         if t < 2:
-            act(v("SG%d%d" % (t, h), 8 * k0, 8 * k1), vn("GS", 160 * h + a + 4, 8 * (k1 - k0), 5))
-            bg = ("BG" if k0 == 0 else "BH") + n
-            tt(v(bg, 0, 128 * (k1 - k0)), ind(v("GS", 160 * h, 160 * h + 120), BL5(k0, k1)), v("MK", 0, 128 * (k1 - k0)), AL.mult)
-            for k in range(k0, k1):
-                mm(v(C, 160 + 8 * k, 168 + 8 * k), v(bg, 128 * (k - k0), 128 * (k - k0) + 128), v("BO32" if k0 == 0 else "BO16"))
-            cp(v("SO%d%d" % (t, h), 8 * k0, 8 * k1), v(C, 160 + 8 * k0, 160 + 8 * k1))
-            if k0 == 0:
-                return send([(v("SG%d%d" % (t, h)), v("RG%d%d" % (t + 1, h)), 1), (v("SO%d%d" % (t, h)), v("RO%d%d" % (t + 1, h)), 1)], 3.5)
-        else:
-            for k in range(k0, k1):
-                c = 256 + 128 * (k - k0)
-                mm(v(C, c, c + 128, p1=8), vn("GS", 160 * h + 40 * k + 4, 8, 5), v("ID32"))
-            for k in range(k0, k1):
-                c = 256 + 128 * (k - k0)
-                act(v("YG", 256 * k + 128 * h, 256 * k + 128 * h + 128, p1=8), v(C, c, c + 128, p1=8))
+            ts(v("LT" + n), ends(n, 2, 2, 16), SENT, AL.is_ge, B, AL.mult); tt(v(sg), v("LT" + n), v("MJ" + n), AL.add)
+            return send([(v(sg), v("RG%d%d" % (t + 1, h)), 1), (v("OV%d%d" % (t, h)), v("RO%d%d" % (t + 1, h)), 1)], 3.5)
+        ts(v("LT" + n), ends(n, 2, 2, 16), SENT, AL.is_lt); tt(v(sg), v("LT" + n), v("MJ" + n), AL.mult)
+        for j in range(2):
+            yg(2 - j, h, v(sg, 8 * j, 8 * j + 8), "A" + n, 128 * j)
 
-    def step3(t):
-        ph[0] = "s%d" % t; even = t % 2 == 0; kb = 40 if even else 0; e = t // 2; xb = "XB%d" % t
-        if t == 2: ms(vn("UU", 4, 8, 5), 0.0)
-        scan(v("GS", 120, 160), v("ZZ", kb, kb + 40), v("UU"), AL.mult, AL.add)
-        a, b = vn("GS", 124, 8, 5, 0, 64), vn("GS", 44 if even else 0, 8, 5, 0, 64)
-        i64, bo4 = v("ID32", 0, 64, p1=64), v("BO16", 0, 4, p1=64)
-        tt(v("BCH"), ind(v("GS", 0, 160), v("LS", 48, 64) if even else v("LS", 64, 80)), v("MK", 0, 256), AL.mult)
-        for w in range(2):
-            mm(v("Y0", 4 * w, 4 * w + 4), v("BCH", 128 * w, 128 * w + 128, p1=64), bo4)
-        cp(v("OAB"), v("Y0", 0, 8))
-        if not even:
-            act(v("BC", 0, 128), ind(v("GS", 0, 120), BL5(0, 1)))
-            mm(v("Y0", 64, 128), v("BC", 0, 128, p1=64), i64)
-            act(v("E0"), v("Y0", 64, 128))
-        cp(v("EAB"), ind(DWIN, v("OAB")))
-        ea, eb, fr = v("EAB", 0, 64), v("EAB", 64, 128), v("FR")
-        ts(fr, ea if even else eb, 0.0, AL.is_equal)
-        tt(v("UMIN", p1=64), a, b, AL.not_equal); tt(v("UMIN", p1=64), v("UMIN", p1=64), a, AL.min); ts(v("N12", 0, 8, p1=64), v("UMIN", p1=64), 0.0, AL.is_equal)
-        mm(v("Y1", 0, 8, p1=64), fr, v("BO"))
-        mm(v("C0", 192, 256), v("T2"), fr)
-        act(v("PLF"), v("C0", 192, 256), AF.Identity, bias=32.0)
-        ts(v("N12", 8, 16, p1=64), v("Y1", 0, 8, p1=64), 0.0, AL.is_equal)
-        for w, x in enumerate((a, b)):
-            o = v("Y1", 128 + 64 * w, 192 + 64 * w, p1=8)
-            group([(o, x, i64)] + [(o, v("N12", 8 * j, 8 * j + 8, p1=64), v("IDB", 0, 64, p1=64)) for j in range(2)])
-        vt = v("VTH", p1=8)
-        cp(vt, v("Y1", 128, 256, p1=8))
+    def guard0(t, h):
+        n = str(h); gs = "GS%d%d" % (t, h); K = "K" + n
+        tt(v("ZZ" + n), nm(t, h), v("CMP"), AL.is_equal); scan(v(gs), v("ZZ" + n), nm(t, h), AL.mult, AL.add)
+        if t == 2:
+            return yg(0, h, vn(gs, 3, 8, 4), K, 256)
+        tt(v("BG" + n), ind(v(gs), v("LS", 24, 32)), v("MK"), AL.mult)
+        mm(v(K, 448, 456), v("BG" + n), v("BO32")); cp(v("SO%d%d" % (t, h), 0, 8), v(K, 448, 456))
+        return send([(v(gs), v("RS%d%d" % (t + 1, h)), 1), (v("SO%d%d" % (t, h)), v("RP%d%d" % (t + 1, h)), 1)], 3.5)
+
+    i64 = lo(v("ID32", 0, 64)); xb, xa = v("XX", 0, 8), v("XX", 8, 16); P = "A0"
+    ya, yb, yw = v("YAB", 0, 64), v("YAB", 64, 128), v("YAB", 128, 192); fr = v("FR")
+
+    def source(t):
+        ph[0] = "s%d" % t; even = t % 2 == 0
+        cp(xb, v("MJ0", 8, 16))
         if even:
-            cp(v("EB16"), eb)
-            act(v("CUT"), ind(v("RW", 0, M), v("OAB", 4, 8)))
-            for c in range(2):
-                act(v("CM2", 512 * c, 512 * c + 512), ind(RWIN, v("EB16", 32 * c, 32 * c + 32)))
+            ts(v("FL"), ends("0", 2, 1), 2048, AL.bitwise_and); tt(v("A2"), v("FL"), vl(t, 0), AL.min); tt(v("DV"), v("MJ0", 0, 8), v("A2"), AL.subtract)
+            tt(v("NW"), ends("0", 1, 1), slot("0", 1, 1), AL.is_lt); tt(v("TQ"), v("NW"), v("DV"), AL.mult); tt(xa, v("TQ"), v("A2"), AL.add)
+        else:
+            tt(v("ZP"), nm(t, 0), v("CMP"), AL.is_equal); scan(v("GP"), v("ZP"), nm(t, 0), AL.mult, AL.add)
+            act(vn("VV", 0, 8, 4), vl(t, 0)); cp(vn("VV", 2, 8, 4), v("MJ0", 0, 8))
+            ts(v("NZ"), nm(t, 0), 0.0, AL.is_gt); tt(v("UU"), v("NZ"), v("VV"), AL.mult); scan(v("AP"), v("ZP"), v("UU"), AL.mult, AL.add)
+            act(xa, vn("AP", 3, 8, 4))
+            act(v("BC"), ind(v("GP"), v("LS", 24, 32))); mm(v(P, 384, 448), lo(v("BC")), i64); act(v("E0"), v(P, 384, 448))
+        spread(v(P, 0, 4), v("BA", 0, 32), xa, v("LS", 32, 34), v("MC", 0, 32), 4, LA)
+        cp(v("OA", 0, 4), v(P, 0, 4)); cp(v("EA"), ind(node(t), v("OA", 0, 4)))
+        tt(v("N01"), v("XX", 0, 16), v("XX", 8, 24), AL.is_equal)
+        for w, x in enumerate((xb, xa)):
+            mm(v(P, 192 + 64 * w, 256 + 64 * w, p1=8), lo(x), i64)
+        vt = v("VTH", p1=8)
+        act(vt, v(P, 192, 320, p1=8))
         for c in range(2):
             Y = "Y%d" % c
-            lst = [(v(Y), vt, v("NSEL", 512 * c, 512 * c + 512, p1=8))]
-            lst += [(v(Y, 128 * j, 128 * j + 128), v("SEL", 512 * c + 128 * j, 512 * c + 128 * j + 128, p1=8), vt) for j in range(4)]
-            group(lst)
+            group([(v(Y), vt, v("NSEL", 512 * c, 512 * c + 512, p1=8))]
+                  + [(v(Y, 128 * j, 128 * j + 128), v("SEL", 512 * c + 128 * j, 512 * c + 128 * j + 128, p1=8), vt) for j in range(4)])
             tt(v("CMM", 512 * c, 512 * c + 512), v(Y), v("TRM"), AL.is_equal)
-        lst = [(v("C1", 384 + 8 * r, 392 + 8 * r, p1=64), v("IDB", 0, 64, p1=64), v("N12", 8 * j, 8 * j + 8, p1=64)) for r in range(3) for j in range(2)]
-        lst += [(v("C1", 384 + 8 * w, 392 + 8 * w, p1=64), i64, x) for w, x in enumerate((a, b))]
-        lst += [(vn("C1", 384 + j // 2, 3, 8, 0, 64), v("CMM", 64 * j, 64 * j + 64), v("BIG3", 0, 3)) for j in range(16)]
+
+    def step3(t):
+        ph[0] = "s%d" % t; even = t % 2 == 0; e = t // 2; ea, eb = v("EA"), v("EB"); nr3 = 3 if even else 2
+        cp(eb, v("E160", 0, 64)); ts(fr, ea if even else eb, 0.0, AL.is_equal)
+        mm(v(P, 64, 128), v("T2"), fr)
+        if even: mm(v(P, 128, 192), v("TRI"), fr)
+        ts(v("TA"), v(P, 64, 128), -64.0, AL.is_equal)
+        if even: act(v("PLF"), v(P, 128, 192), AF.Identity, bias=-33.0)
+        bars = [v("N01", 0, 8), v("N01", 8, 16)] + ([] if even else [v("NZ0")])
+        lst = [(vn(P, 8 + r, 8, 4), lo(v("I2N")), lo(x)) for j, x in enumerate(bars) for r in range(3 if j else 4)]
+        group(lst[:4] + [(v(P, 8, 40, p0=p, p1=p + 64), fr, vn("BOF", 0, 32, 4)) for p in (0, 64)] + lst[4:])
+        ts(v("ASK"), v(P, 8, 40), 0.0, AL.is_gt, B2, AL.mult)
+        lst = [(lo(v("Y0", 0, 24)), v("ONE", 0, 64, p1=1), v("CB2", p1=1)), (lo(v("Y0", 0, 8)), i64, lo(xa)), (lo(v("Y0", 8, 16)), i64, lo(xb))]
+        if even: lst += [(lo(v("Y0", 16, 24)), i64, lo(v("NL", 8 * e, 8 * e + 8)))]
+        lst += [(lo(v("Y0", 8 * r, 8 * r + 8)), lo(v("NID", 0, 64)), lo(vn("ASK", 0, 8, 4))) for r in range(3)]
+        lst += [(lo(vn("Y0", j // 2, 3, 8)), v("CMM", 64 * j, 64 * j + 64), v("ASK", 4 * (j // 2), 4 * (j // 2) + 3)) for j in range(16)]
         group(lst)
-        act(v("W3", 16, 24, p1=64), v("C1", 400, 408, p1=64), AF.Relu, bias=1.0, scale=-1.0, acc=v("ASUM", p1=64))
-        tt(v("W3", 0, 16, p1=64), v("C1", 384, 400, p1=64), v("DUMC", p1=64), AL.min)
+        tt(lo(v("W3")), lo(v("Y0", 0, 24)), lo(v("DUMC")), AL.min)
         if t < 2:
-            sa = "SA%d" % t
-            mm(v("C1", 480, 481), v("ONE32", p1=64), v("ASUM", p1=64))
-            cp(v("AI"), v("C1", 480, 481)); ts(v("AJ"), v("AI"), 1, AL.bitwise_and)
-            ts(v(sa, 0, 1), v("AJ"), -2.0, AL.mult, 6.0, AL.add)
-            for f in sorted(set(p.count("F") for p in PATHS[6 * t + 6:6 * t + 12])):
-                ts(v(sa, 1 + f, 2 + f), v("AJ"), -B, AL.mult, v("CB", f, f + 1), AL.add)
-            send([(v(sa), v("RA%d" % (t + 1)), 1)], 3.5)
-        tt(v("BC2", 0, 256), ind(v("W3"), BL1(16)), v("MK", 0, 256), AL.mult)
-        for w in range(2):
-            mm(v("C1", 408 + 4 * w, 412 + 4 * w), v("BC2", 128 * w, 128 * w + 128, p1=64), bo4)
-        cp(v("OSC"), v("C1", 408, 416))
-        if even:
-            act(v("ACB"), ind(v("W3", 16, 24), BL1(8)))
-            mm(v("C1", 416, 480), v("ACB", p1=64), v("ID", 0, 64, p1=64))
-            act(v("ACE"), v("C1", 416, 480))
-        ya, yb = v("YAB", 0, 64), v("YAB", 64, 128)
-        ts(v("TA"), v("PLF"), -32.0, AL.is_equal)
+            act(lo(v("JK")), lo(v("Y0", 16, 24)), AF.Relu, bias=lo(v("NB", e, e + 1)) if even else B, scale=-B, acc=lo(v("ASUM")))
+            mm(v(P, 352, 353), lo(v("ONE32")), lo(v("ASUM")))
+            ts(v("AI"), v(P, 352, 353), 0.5 / B, AL.mult, -0.25, AL.add); ts(v("SA%d" % t, 0, 1), v("AI"), 2 * B, AL.mult, v(P, 352, 353), AL.subtract)
+            send([(v("SA%d" % t), v("RA%d" % (t + 1)), 1)], 3.5)
+        spread(v(P, 356, 356 + 4 * nr3), v("BA", 0, 32 * nr3), v("W3"), v("LS", 40, 40 + 2 * nr3), v("MC", 0, 32 * nr3), 4 * nr3, LA)
+        cp(v("OSC", 0, 4 * nr3), v(P, 356, 356 + 4 * nr3))
         if not even:
             tt(v("TB"), ea, v("E0"), AL.not_equal); tt(ya, ea, v("TB"), AL.mult)
             tt(v("TC"), v("TA"), v("E0"), AL.mult); tt(yb, eb, v("TC"), AL.add)
             return
-        x = v(xb, M, M + 64); n0 = BASE + LA * e; dg = lambda j: v("DG", 512 * e + 128 * j, 512 * e + 128 * j + 128)
-        for r, row in enumerate((t, 8 + t)):
-            o, wt = v("C0", 256 + 64 * r, 320 + 64 * r), 144 * (2 * e + r)
-            group([(o, v("RBN", 128 * row, 128 * row + 128), x)] + [(o, v("WT", wt + 15 - j, wt + 143 - j), vn("CM2", j, 64, 16)) for j in range(16)])
-        half, cut = v("C0", 384, 448), v("C0", 448, 512)
-        group([(half, dg(1), v("CUT")), (half, dg(0), x), (half, v("NID"), v("RW", n0, n0 + 64))])
-        group([(cut, dg(3), v("CUT")), (cut, dg(2), x)])
-        ts(v("GO"), v("C0", 256, 320), 0.0, AL.is_ge); ts(v("N8"), v("C0", 320, 384), 0.0, AL.is_lt)
-        tt(v("TD"), half, v("ACE"), AL.mult)
-        act(v("CUT2"), cut)
+        x = v("XZ%d" % t, 0, 64); dg = lambda j: v("DG", 512 * e + 128 * j, 512 * e + 128 * j + 128)
+        act(v("CUT"), ind(rec(t, 0, M), v("OV%d0" % t, 8, 12)))
+        group([(v(P, 64, 128), dg(3), v("CUT")), (v(P, 64, 128), dg(2), x)]); group([(v(P, 128, 192), dg(1), v("CUT")), (v(P, 128, 192), dg(0), x)])
+        act(v("CH"), v(P, 64, 192))
+        for r in range(2):
+            wt = 144 * (2 * e + r)
+            group([(v(P, 384 + 64 * r, 448 + 64 * r), v("WT", wt + 15 - j, wt + 143 - j), vn("RD0", j, 64, 16)) for j in range(16)])
+        ts(v("GO"), v(P, 384, 448), 0.0, AL.is_ge); ts(v("N8"), v(P, 448, 512), 0.0, AL.is_lt)
         tt(v("STR"), v("N8"), v("GO"), AL.is_gt)
-        tt(v("RN"), v("TD"), v("RW", n0, n0 + 64), AL.add)
-        cp(v("EBH"), eb); tt(v("EBL"), eb, v("EBH"), AL.subtract)
-        group([(v("C1", 320, 384), v("T1"), v("STR")), (v("C1", 320, 384), v("NBOF"), fr), (v("C1", 320, 384), v("ID64N"), v("GO"))])
-        ts(v("TB"), v("C1", 320, 384), -32.0, AL.is_ge); tt(yb, eb, v("TB"), AL.mult)
+        mm(v(P, 256, 320), v("T1B"), v("STR"))
+        group([(v(P, 192, 256), v("T1"), v("STR")), (v(P, 192, 256), v("NBOF"), fr), (v(P, 192, 256), v("ID64N"), v("GO"))])
+        tt(v("NU"), v(P, 256, 320), eb, AL.subtract)
+        ts(v("TB"), v(P, 192, 256), -32.0, AL.is_ge); tt(yb, eb, v("TB"), AL.mult); tt(yw, eb, v("GO"), AL.mult)
+        tt(v("TC"), v("TA"), v("NC", 64 * e, 64 * e + 64), AL.mult)
         for c in range(2):
-            Y = "Y%d" % c; lst = []
+            Y = "Y%d" % (1 - c)
             for j in range(8):
-                i = 8 * c + j
-                o = v(Y, 64 * j, 64 * j + 64)
-                lst += [(o, v("RBN", 128 * i, 128 * i + 128), v("PLF")), (o, v("ID"), v("EBH")), (o, v("ID"), v("EBL"))]
-            group(lst + [(v(Y, 64 * j, 64 * j + 64), v("T1B"), v("STR")) for j in range(8)])
-            ts(v("Y2", 512 * c, 512 * c + 512), v(Y), 0.0, AL.max, B2, AL.min)
-            group([(v("C0", 256 + 64 * c, 320 + 64 * c), v("WD", 15 - i, 143 - i), v("Y2", 64 * i, 64 * i + 64)) for i in range(8 * c, 8 * c + 8)])
-        tt(v("TC"), v("TA"), v("NC", 64 * e, 64 * e + 64), AL.mult); tt(v("TC"), v("TC"), ea, AL.add)
-        act(v("YK"), v("C0", 256, 320)); tt(v("YI"), v("C0", 320, 384), v("YK"), AL.add)
-        ts(v("YJ"), v("YI"), 16383, AL.bitwise_and); tt(ya, v("YJ"), v("TC"), AL.add)
-        tt(v("TE"), v("GO"), v("ACE"), AL.mult)
+                mm(v(Y, 64 * j, 64 * j + 64), v("RBP", 128 * (8 * c + j), 128 * (8 * c + j) + 128), v("PLF"))
+            for j in range(8):
+                tt(v("Y2", 512 * c + 64 * j, 512 * c + 64 * j + 64), v(Y, 64 * j, 64 * j + 64), v("NU"), AL.max)
+        wd = lambda i: 288 if i == 0 else 144 if i == 15 else 0
+        group([(v("B0", 0, 64), v("ID32"), ea)] + [(v("B0", 0, 64), v("WD", wd(i) + 15 - i, wd(i) + 143 - i), v("Y2", 64 * i, 64 * i + 64)) for i in range(16)])
+        tt(v("YI"), v("B0", 0, 64), v("TC"), AL.add); ts(ya, v("YI"), 16383, AL.bitwise_and)
 
     def commit(t):
-        even = t % 2 == 0; n0 = BASE + LA * (t // 2)
-        if even: tt(v("D32", n0, n0 + 64), v("TE"), v("EAB", 64, 128), AL.mult)
-        cp(ind(v("D32"), v("OSC")), v("YAB"))
+        ph[0] = "s%d" % t; even = t % 2 == 0; n = 12 if even else 8
+        cp(ind(v("DD", Q * t, Q * t + WIN), v("OSC", 0, n)), v("YAB", 0, 16 * n))
         if even:
             for base in ((0, R1, R2) if t == 0 else (RO,)):
-                if base != R2: act(v("RW", base + n0, base + n0 + 64), v("RN"))
-                cp(ind(v("RW", base, base + WIN), v("OSC", 4, 8)), v("CUT2"))
-        if t == 0:
-            dma("S", lambda T: T.RW[:, RO:RO + Q], lambda T: T.RW[:, R1:R1 + Q], [v("RW", R1, R1 + Q), v("RO11")], [v("RW", RO, RO + Q)], 524288)
+                n = 4 if base == R2 else 8
+                cp(ind(v("W1", base, base + WIN), v("OSC", 4, 4 + n)), v("CH", 0, 16 * n))
+        ph[0] = "c"
+        if t < 2: copy(v("DD", Q * t + Q, Q * t + 2 * Q), v("DD", Q * t, Q * t + Q))
+        if t == 0: copy(v("W1", RO, RO + Q), v("W1", 0, Q)); act(v("W1", RO, RO + 1), v("RZ"))
 
     for t in range(3):
-        vl = "VL" if t == 0 else "VL%d" % t
         for h in range(2):
-            keepv(v(vl, 8 * h, 8 * h + 8), h, 0)
-            if t > 0: step1(t, h)
+            start(t, h)
         for s in (2, 1):
             for h in range(2):
                 walk(t, s, h)
-                if s == 1: guards(t, h, 1, 3)
-        if t % 2 == 0: step3(t)
-        for h in range(2):
-            walk(t, 0, h); i = guards(t, h, 0, 1)
-            if t % 2 == 1 and h == 0: step3(t)
+                if s == 1: guards21(t, h)
+        source(t)
+        walk(t, 0, 0); step3(t); ph[0] = "w%d0" % t; guard0(t, 0)
+        walk(t, 0, 1); guard0(t, 1)
         commit(t)
-        if t == 0: repeat(2, [j for j, o in enumerate(ops) if o["kind"] == "s"])
-    dma("S", lambda T: T.yr[:, :], lambda T: T.RW[:, RO:RO + Q], [v("RW", RO, RO + Q)], [], 524288)
-    dma("S", lambda T: T.yn[:, :], lambda T: T.D32[:, 0:Q], [v("D32", 0, Q)], [], 1048576)
-    dma("S", lambda T: T.yg[:, :], lambda T: T.YG[0:8, :], [v("YG")], [], 25000)
+        if t == 0: repeat(2, [])
+    ph[0] = "o"
+    dma("S", lambda T: T.yr[:, :], lambda T: T.W1[:, RO:RO + Q], [v("W1", RO, RO + Q)], [], 524288)
+    dma("S", lambda T: T.yn[:, :], lambda T: T.DD[:, 2 * Q:3 * Q], [v("DD", 2 * Q, 3 * Q)], [], 1048576)
+    dma("S", lambda T: T.yg[:, :], lambda T: T.YG[0:8, :], [v("YG", p1=8)], [], 25000)
     return ops
 
 
@@ -519,7 +537,7 @@ def meet(a, b):
 def depend(ops):
     hard = [set() for _ in ops]; soft = [set() for _ in ops]; acc = {}; bank = {}
     for i, o in enumerate(ops):
-        soft[i].update(o["after"])
+        soft[i].update(o["after"]); hard[i].update(o.get("wait", []))
         for x, w in [(x, False) for x in o["rd"]] + [(x, True) for x in o["wr"]]:
             if x[0] in DYN:
                 o["dyn"] = x[0]
@@ -561,11 +579,9 @@ def order(ops, hard, soft, m, tune):
         for j in hard[i] | soft[i]: succ[j].append(i)
     pr = [0.0] * n
     for i in range(n - 1, -1, -1):
-        rnd = (rnd * 1103515245 + 12345) % 2147483648
         d = cost[i] + (1.5 + ops[i]["nbytes"] / m["bw"] if ops[i]["kind"] == "d" else 0)
-        pr[i] = d * (1 + tune["noise"] * (rnd / 2147483648 - 0.5)) + max([pr[j] + (LAT if i in hard[j] else 0) for j in succ[i]] + [0.0])
-    pr = [p + tune.get(o["ph"], 0.0) + (tune.get("small" + o["eng"], 0.0) if c < 0.45 else 0.0) + (tune.get("cnt", 0.0) if o["wr"] and o["wr"][0][0] in ("C0", "C1") else 0.0)
-          for p, o, c in zip(pr, ops, cost)]
+        pr[i] = d + max([pr[j] + (LAT if i in hard[j] else 0) for j in succ[i]] + [0.0])
+    pr = [p + tune.get(o["ph"], 0.0) for p, o in zip(pr, ops)]
     pred = [list(hard[i] | soft[i]) for i in range(n)]; sl = tune["slack"]
 
     def sweep(pr, back):

@@ -1,11 +1,13 @@
+import math
 from concourse.bass import DstId, RemoteDMATransfer
 from concourse.mybir import AluOpType as AL, ActivationFunctionType as AF
 
 M, Q, BASE, L, LA = 4096, 2048, 1920, 256, 64
-NA = [[(64, 32), (64, 32), (64, 32)]] * 3
-FAST = (1, 0)
+NA = [[(64, 56), (64, 56), (64, 64)]] * 3
+CUT = (96, 64)
+FAST = (1, 1)
 MODEL = dict(cy=1.0e-3, g=1.56, sc=3.8, pe=0.5, lat=0.15, bw=180e3)
-TUNE = dict(slack=0.05, seed=23, noise=0, fb=40, moves=10, step=2)
+TUNE = dict(slack=0.05, seed=23, fb=30, moves=4, step=3, polish=90000, heat=0.2)
 B = float(2 ** 26)
 B2 = 16384.0
 NEG = -float(2 ** 30)
@@ -14,7 +16,8 @@ R1, R2, WW, DUM = 4096, 8192, 10240, 6144
 WIN = DUM + 12 * LA
 RO = R1 + WIN
 XW = 128 + max(n[1] for t in NA for n in t)
-C0 = min(min(n) for t in NA for n in t) // 32
+NAS = sorted(set(n for t in NA for s in t for n in s))
+L0 = NAS[0]
 SEG = {(2, 0): 0, (2, 1): 144, (2, 2): 288, (1, 1): 432, (1, 0): 576, (0, 0): 720}
 F, H, BF, U, I = "float32", "float16", "bfloat16", "uint16", "int32"
 SB = {
@@ -23,13 +26,13 @@ SB = {
     "VU": (96, U), "VL": (48, F), "VU1": (32, U), "VL1": (16, F), "VU2": (32, U), "VL2": (16, F),
     "SA0": (8, F), "SA1": (8, F), "RA1": (8, F), "RA2": (8, F), "YG": (768, F), "RZ": (1, BF), "NM": (192, I),
     "ONE": (128, BF), "ONE32": (128, F), "ID": (128, BF), "NID": (128, BF), "ID32": (128, F), "ID64N": (128, BF), "I2N": (128, BF),
-    "BOF": (128, BF), "NBOF": (128, BF), "BO": (8, BF), "BO32": (8, F), "BO16": (8, H), "SC3H": (24, H), "EXP": (512 * (4 - C0), BF),
+    "BOF": (128, BF), "NBOF": (128, BF), "BO": (8, BF), "BO32": (8, F), "BO16": (8, H), "SC3H": (24, H), "EXP": (16 * (128 - L0), BF),
     "TRI": (128, BF), "TRE": (128, BF), "T1": (128, BF), "T1B": (128, BF), "T2": (128, BF), "RBP": (2048, BF), "WD": (432, F),
-    "WT": (576, BF), "WC": (32, F), "DG": (1024, BF), "SEL": (1024, BF), "NSEL": (1024, BF), "TRM": (512, BF), "VB": (768, F),
-    "PB": (144, BF), "P16": (144, H), "WP": (432, BF), "KC": (576, BF), "CR": (160, BF), "LAN": (640, BF), "MK": (128, F), "II": (128, I), "IJ": (128, I),
+    "WT": (288, BF), "WE": (2, F), "WX": (256, BF), "NLH": (16, H), "XA": (8, F), "TR": (64, F), "WC": (32, F), "DG": (1024, BF), "SEL": (1024, BF), "NSEL": (1024, BF), "TRM": (512, BF), "VB": (768, F),
+    "PB": (144, BF), "P16": (144, H), "WP": (432, BF), "KC": (576, BF), "CR": (160, BF), "LAN": (128 * len(NAS), BF), "MK": (128, F), "II": (128, I), "IJ": (128, I),
     "LI": (64, I), "LJ": (16, I), "LK": (16, I), "LS": (64, U), "DUMC": (24, F), "NC": (128, F), "NL": (16, F), "NB": (2, F), "CB2": (24, BF),
     "CMP": (32, F), "MC": (96, BF), "GSEL": (240, BF),
-    "XX": (24, F), "FL": (8, I), "A2": (8, F), "DV": (8, F), "NW": (8, F), "TQ": (8, F), "BA": (96, H), "OA": (8, U), "EA": (64, F), "EB": (64, F),
+    "XX": (24, H), "FL": (8, I), "A2": (8, F), "DV": (8, F), "NW": (8, F), "TQ": (8, F), "BA": (96, H), "OA": (8, U), "EA": (64, F), "EB": (64, F),
     "FR": (64, BF), "N01": (16, BF), "NZ0": (8, BF), "ASK": (32, BF), "VTH": (128, H), "PLF": (64, BF), "CMM": (1024, BF), "W3": (24, F), "OSC": (12, U),
     "JK": (8, F), "ASUM": (1, F), "AI": (1, I), "STR": (64, BF), "GO": (64, BF), "N8": (64, BF), "NU": (64, F), "Y2": (1024, F), "YI": (64, I),
     "YAB": (192, I), "TA": (64, F), "TB": (64, F), "TC": (64, F), "CUT": (64, BF), "CH": (128, BF), "BC": (128, F), "E0": (64, F),
@@ -40,10 +43,11 @@ for _h in "01":
                "SC" + _h: (864, I), "D1" + _h: (864, F), "MJ" + _h: (16, I), "A1" + _h: (8, I), "B1" + _h: (8, F), "GE" + _h: (8, F), "ZZ" + _h: (32, F),
                "BV" + _h: (128, H), "BG" + _h: (128, F), "LT" + _h: (16, F), "S1R" + _h: (384, BF), "S1C" + _h: (384, BF)})
     for _t in range(3):
-        SB.update({"OV%d" % _t + _h: (32, U), "SG%d" % _t + _h: (16, F), "GS%d" % _t + _h: (32, F)})
+        SB.update({"OV%d" % _t + _h: (32, U), "SG%d" % _t + _h: (16, F if _t < 2 else H), "GS%d" % _t + _h: (32, F)})
     for _t in range(2):
         SB.update({"SO%d" % _t + _h: (64, U), "RG%d" % (_t + 1) + _h: (16, F), "RO%d" % (_t + 1) + _h: (32, U),
                    "RS%d" % (_t + 1) + _h: (32, F), "RP%d" % (_t + 1) + _h: (64, U)})
+SB.update({"E162": (128, U), "FK2": (128, H), "RD2": (2048, H), "CM2": (2048, BF), "PP2": (160, BF)})
 DYN = ("A0",)
 PS = ["K0", "K1", "A0", "B0", "A1", "B1", "Y0", "Y1"]
 POOL, FILL = {}, {}
@@ -70,6 +74,11 @@ def vn(n, c0, cnt, st, p0=0, p1=128):
 
 def lo(x):
     return (x[0], 0, LA) + x[3:]
+
+
+def cuts(a, b, most):
+    n = (b - a + most - 1) // most
+    return [(a + (b - a) * j // n // 2 * 2, a + (b - a) * (j + 1) // n // 2 * 2) for j in range(n)]
 
 
 def ind(w, o):
@@ -164,15 +173,18 @@ def build():
         n = max(min(64, cols(l)), cols(r)) * (4 if wide(l) == 4 else 1)
         add("P", lambda g, T, c: g.tensor.matmul(ap(T, out), ap(T, l), ap(T, r), start, stop), [l, r], [out], (0.005, 0, 0, 0, n))
 
-    def group(lst):
-        if lst[0][0][0] in DYN:
-            def fn(g, T, c):
-                return [g.tensor.matmul(ap(T, o), ap(T, l), ap(T, r), j == 0, j == len(lst) - 1) for j, (o, l, r) in enumerate(lst)][-1]
-            n = sum(max(min(64, cols(l)), cols(r)) * (4 if wide(l) == 4 else 1) for o, l, r in lst)
-            add("P", fn, [x for o, l, r in lst for x in (l, r)], [o for o, l, r in lst], (0.005 * len(lst), 0, 0, 0, n))
-            return
-        for j, (o, l, r) in enumerate(lst):
-            mm(o, l, r, j == 0, j == len(lst) - 1)
+    def mms(lst, start, stop, each=False):
+        def fn(g, T, c):
+            return [g.tensor.matmul(ap(T, o), ap(T, l), ap(T, r), each or start and j == 0, each or stop and j == len(lst) - 1) for j, (o, l, r) in enumerate(lst)][-1]
+        n = sum(max(min(64, cols(l)), cols(r)) * (4 if wide(l) == 4 else 1) for o, l, r in lst)
+        add("P", fn, [x for o, l, r in lst for x in (l, r)], [o for o, l, r in lst], (0.005 * len(lst), 0, 0, 0, n))
+
+    def group(*parts, start=True, stop=True):
+        parts = [p for p in parts if p]
+        if parts[0][0][0][0] in DYN:
+            parts = [[x for p in parts for x in p]]
+        for j, p in enumerate(parts):
+            mms(p, start and j == 0, stop and j == len(parts) - 1)
 
     def iota(out, pat, base, cm):
         fl = SB[out[0]][1] != I
@@ -245,19 +257,17 @@ def build():
     ms(v("CR", p1=32), 1.0); ms(v("CR", p0=32, p1=64), -6.0 / 32); ms(v("CR", 144, 160, p1=32), 0.0)
     for j in range(2):
         ms(vn("CR", j, 8, 18, 0, 32), 0.0); ms(vn("CR", j, 8, 18, 32, 64), 2.0)
-    nas = sorted(set(n for t in NA for s in t for n in s))
-    for j, n in enumerate(nas):
-        ms(v("LAN", 128 * j, 128 * j + 128, p0=32, p1=64), 1.0)
+    ms(v("LAN", p0=32, p1=64), 1.0); ms(v("LAN", p1=32), 0.0)
+    for j, n in enumerate(NAS):
         if n > 0: ms(v("LAN", 128 * j, 128 * j + n, p1=32), -0.5)
-        if n < 128: ms(v("LAN", 128 * j + n, 128 * j + 128, p1=32), 0.0)
     for h in "01":
-        ms(v("D1" + h), NEG); ms(vn("D1" + h, 0, 8, 18), SENT); ms(vn("D1" + h, 144, 8, 18), SENT2)
+        iota(v("D1" + h), [[0, 864]], 1 - 2 ** 24, 0); ms(vn("D1" + h, 0, 8, 18), SENT); ms(vn("D1" + h, 144, 8, 18), SENT2)
     ms(v("NM"), 0); ms(v("CMP"), 0.0); ms(vn("CMP", 0, 8, 4), -1.0)
     ms(v("W0", R1 + Q, R2), 0.0); ms(v("DD", BASE, Q), 0.0)
     for n in ("SA0", "SA1"): ms(v(n), 0.0)
     for n in ("SO00", "SO01", "SO10", "SO11", "OV00", "OV01", "OV10", "OV11", "VU"): ms(v(n), 0)
     for j in range(16):
-        (cp if j % 2 else act)(vn("EXP", j, 128 - 32 * C0, 16), v("ID", 32 * C0, 128))
+        (cp if j % 2 else act)(vn("EXP", j, 128 - L0, 16), v("ID", L0, 128))
     for t in range(3):
         cp(v("VU", 32 * t, 32 * t + 16), v("VSI", 16 * t, 16 * t + 16))
     cp(v("VSF"), v("VSI"))
@@ -290,15 +300,18 @@ def build():
     for j in range(3):
         act(v("MC", 32 * j, 32 * j + 32), vn("BOF", 0, 32, 2))
     ms(v("CB2", p1=32), B2); ms(v("XX"), 0.0); ms(v("W3"), 0.0); ms(v("VV"), 0.0)
-    iota(v("WD"), [[0, 432]], 0, 0); iota(v("WT"), [[0, 576]], 0, 0)
+    iota(v("WD"), [[0, 432]], 0, 0); iota(v("WT"), [[0, 288]], 0, 0)
     act(vn("WD", 15, 8, 16), bo); scale(vn("WD", 16, 8, 16), bo, -1.0); act(vn("WD", 144 + 15, 8, 16), bo); scale(vn("WD", 288 + 16, 8, 16), bo, -1.0)
     scale(v("WC", 0, 16), v("MK", 0, 16), B2); act(v("WC", 16, 32), v("MK", 0, 16), AF.Identity, bias=1.0, scale=-1.0)
     for i in range(16):
         scale(v("RBP", 128 * i, 128 * i + 128), v("BOF"), v("WC", i, i + 1))
+    act(v("NLH"), v("NL"))
     for e, t in enumerate((0, 2)):
+        act(v("WE", e, e + 1), v("MK", t, t + 1), AF.Identity, bias=v("MK", 8 + t, 9 + t), scale=1024.0)
+        scale(vn("WT", 144 * e + 15, 8, 16), bo, v("WE", e, e + 1))
+        if NA[t][2][0] < LA: scale(v("WX", 128 * e, 128 * e + 128), v("NBOF"), v("WE", e, e + 1))
         for j, row in enumerate((t, 8 + t)):
             o = 512 * e + 256 * j
-            scale(vn("WT", 144 * (2 * e + j) + 15, 8, 16), bo, v("MK", row, row + 1))
             scale(v("DG", o, o + 128), v("ID"), v("MK", row, row + 1)); scale(v("DG", o + 128, o + 256), v("ID"), v("WC", 16 + row, 17 + row))
 
     def repeat(k, after):
@@ -314,6 +327,8 @@ def build():
     slot = lambda n, s, k: vn("D1" + n, SEG[s, k], 8, 18)
     nm = lambda t, h, j=None: v("NM", 64 * t + 32 * h, 64 * t + 32 * h + 32) if j is None else vn("NM", 64 * t + 32 * h + j, 8, 4)
 
+    aside = lambda t, s, h: (s, h) == (0, 1) and t < 2
+
     def spread(out, bv, src, lst, mask, n, p1):
         tt(bv, ind(src, lst), mask, AL.mult)
         group([(out, gsel(g, p1), vn(bv[0], g, n, 8, 0, p1)) for g in range(8)])
@@ -323,80 +338,80 @@ def build():
         mm(v("A" + n, 0, 128), v("XZ%d" % t, 128 * h, 128 * h + 128), v("NID")); act(v("NXT", o, o + 128), v("A" + n, 0, 128))
         ts(slot(n, 2, 2), vl(t, h), SENT, AL.add)
 
-    def step1(t, h, a, b, off):
-        n = str(h); P = "A" + n; x = v("XZ%d" % t, 128 * h, 128 * h + 128)
+    def step1(t, h, a, b, off, P):
+        n = str(h); x = v("XZ%d" % t, 128 * h, 128 * h + 128)
         act(v("S1R" + n, a, b), ind(rec(t, 0, M), off))
         group([(v(P, 0, b - a), v("ID"), v("S1R" + n, a, b))] + [(v(P, c, c + 128), v("NID"), x) for c in range(0, b - a, 128)])
         act(v("S1C" + n, a, b), v(P, 0, b - a), AF.Sign, bias=0.5, scale=-1.0)
 
     def walk(t, s, h):
-        ph[0] = "w%d%d" % (t, h); n = str(h); K = "K" + n; nk = s + 1; na = NA[t][2 - s][h]; RD, CM = "RD" + n, "CM" + n
-        ov = "OV%d%d" % (t, h); e16 = v("E16" + n); tags = {2: (0, 1, 2), 1: (1, 0), 0: (0,)}[s]
+        ph[0] = "w%d%d" % (t, h); n = str(h); nk = s + 1; na = NA[t][2 - s][h]
+        u, K, C, banks = ("2", "Y0", "Y1", ["Y1"]) if aside(t, s, h) else (n, "K" + n, "B" + n, ["B0"] if (h, s) == (0, 0) else ["A" + n, "B" + n])
+        RD, CM = "RD" + u, "CM" + u
+        ov = "OV%d%d" % (t, h); e16 = v("E16" + u); tags = {2: (0, 1, 2), 1: (1, 0), 0: (0,)}[s]
         off = v("VU%d" % t if t else "VU", 8 * h, 8 * h + 8) if s == 2 else v(ov, 8 - 8 * s, 16 - 8 * s)
-        if t > 0 and s == 2: step1(t, h, 0, 256, v("RO%d%d" % (t, h), 0, 16))
-        if t > 0 and s == 1: step1(t, h, 256, 384, v("RP%d%d" % (t, h), 0, 8))
+        if t > 0 and s == 2: step1(t, h, 0, 256, v("RO%d%d" % (t, h), 0, 16), "A" + n)
+        if t > 0 and s == 1 - h: step1(t, h, 256, 384, v("RP%d%d" % (t, h), 0, 8), banks[0])
         cap = s == 1 or (s == 0 and h == 1)
         if cap: ts(e16, ind(node(t), off), 4096.0 * nk, AL.min)
         else: cp(e16, ind(node(t), off))
-        if na:
-            tt(v(RD, 0, 16 * na), ind(rec(t), v("E16" + n, 0, na)), v("XB%d" % t, 2048 * h, 2048 * h + 16 * na), AL.subtract)
-            ts(v(CM, 0, 16 * na), v(RD, 0, 16 * na), 0.0, AL.is_le, 2.0, AL.mult)
-        banks = ["B0"] if (h, s) == (0, 0) else ["A" + n, "B" + n]
-        for j, c in enumerate(range(na // 32, 4)):
-            P = banks[j % len(banks)]; a, b = 512 * c, 512 * c + 512
-            act(v(RD, a, b), ind(rec(t), v("E16" + n, 32 * c, 32 * c + 32)))
-            group([(v(P), v("NXT", 256 * t + 128 * h, 256 * t + 128 * h + 128), v("EXP", a - 512 * C0, b - 512 * C0)), (v(P), v("ID"), v(RD, a, b))])
-            act(v(CM, a, b), v(P), AF.Sign, bias=0.5, scale=-1.0)
+        for l0, l1 in cuts(0, min(na, LA), CUT[h]) + cuts(LA, na, CUT[h]) if (h, s) == (0, 0) else cuts(0, na, CUT[h]):
+            a, b = 16 * l0, 16 * l1
+            tt(v(RD, a, b), ind(rec(t), v("E16" + u, l0, l1)), v("XB%d" % t, 2048 * h + a, 2048 * h + b), AL.subtract)
+            ts(v(CM, a, b), v(RD, a, b), 0.0, AL.is_le, 2.0, AL.mult)
+        for j, (l0, l1) in enumerate(cuts(na, 128, 32)):
+            P = v(banks[j % len(banks)], 0, 16 * (l1 - l0)); a, b = 16 * l0, 16 * l1
+            act(v(RD, a, b), ind(rec(t), v("E16" + u, l0, l1)))
+            group([(P, v("NXT", 256 * t + 128 * h, 256 * t + 128 * h + 128), v("EXP", a - 16 * L0, b - 16 * L0))], [(P, v("ID"), v(RD, a, b))])
+            act(v(CM, a, b), P, AF.Sign, bias=0.5, scale=-1.0)
         masks = [0, 1] if s == 2 else [] if cap and s == 0 else [0]
         for j in masks:
             ts(v("MM" + n, 128 * j, 128 * j + 128), e16, 4096.0 * (j + 1), AL.is_ge)
         for k in tags:
-            ts(v("FK" + n, 128 * k, 128 * k + 128), e16, -4096.0 * k - (2048 if k == 0 else 0), AL.add)
-        gd = [] if t == 0 else {2: [(2, 0), (1, 1)], 1: [(0, 2)], 0: []}[s]
+            ts(v("FK" + u, 128 * k, 128 * k + 128), e16, -4096.0 * k - (2048 if k == 0 else 0), AL.add)
+        gd = [] if t == 0 else [(2, 0), (1, 1)] if s == 2 else [(0, 2)] if s == 1 - h else []
         run = lambda k: v(K, 144 * tags.index(k), 144 * tags.index(k) + 144)
         gcol = lambda k: vn(K, 144 * tags.index(k) + 1, 8, 18)
-        lst = [(run(k), v("ONE", p1=64), kc(int(k > 0), int(k not in [x for x, j in gd]))) for k in tags]
-        if s == 2: lst += [(v(K, 144 * j, 144 * j + 288), v("MM" + n, 128 * j, 128 * j + 128), v("WP", 0, 288)) for j in masks]
-        elif masks: lst += [(v(K, 0, 144 * nk), v("MM" + n, 0, 128), v("WP", 144 * s, 144 * s + 144 * nk))]
-        lst += [(run(k), v("FK" + n, 128 * k, 128 * k + 128), v("P16")) for k in tags]
-        for k, j in gd:
-            lst.append((gcol(k), v("S1R" + n, 128 * j, 128 * j + 128), v("SC3H", 0, 8)))
-            if k: lst.append((gcol(k), v("ID32"), v("RG%d%d" % (t, h), 8 * j, 8 * j + 8)))
-        lst += [(vn(K, 2 + i, 8 * nk, 18), vn(RD, i, 128, 16), v("SC3H", 0, 8 * nk)) for i in range(16)]
-        for j, (o, l, r) in enumerate(lst):
-            mm(o, l, r, j == 0, False)
-        C = "B" + n; w = 144 + 8 * len(gd); la = 128 * nas.index(na)
+        p1 = [(run(k), v("ONE", p1=64), kc(int(k > 0), int(k not in [x for x, j in gd]))) for k in tags]
+        if s == 2: p2 = [(v(K, 144 * j, 144 * j + 288), v("MM" + n, 128 * j, 128 * j + 128), v("WP", 0, 288)) for j in masks]
+        else: p2 = [(v(K, 0, 144 * nk), v("MM" + n, 0, 128), v("WP", 144 * s, 144 * s + 144 * nk)) for j in masks]
+        p3 = [(run(k), v("FK" + u, 128 * k, 128 * k + 128), v("P16")) for k in tags]
+        p4 = [(vn(K, 2 + i, 8 * nk, 18), vn(RD, i, 128, 16), v("SC3H", 0, 8 * nk)) for i in range(16)]
+        p5 = [(gcol(k), v("S1R" + n, 128 * j, 128 * j + 128), v("SC3H", 0, 8)) for k, j in gd]
+        p5 += [(gcol(k), v("ID32"), v("RG%d%d" % (t, h), 8 * j, 8 * j + 8)) for k, j in gd if k]
+        group(p1, p2, p3, p4[:8], p4[8:], p5, stop=False)
+        w = 144 + 8 * len(gd); la = 128 * NAS.index(na); PP = "PP" + u
         group([(v(C, 0, w), v("LAN", la, la + 128, p1=64), v("CR", 0, w, p1=64))]
-              + [(v(C, 144 + 8 * i, 152 + 8 * i), v("S1C" + n, 128 * j, 128 * j + 128), v("BO")) for i, (k, j) in enumerate(gd)]
-              + [(vn(C, 2 + i, 8, 18), vn(CM, i, 128, 16), v("BO")) for i in range(16)])
-        act(v("PP" + n, 0, w), v(C, 0, w), AF.Relu, bias=v("RA%d" % t, 0, 1) if t else None, scale=-B / 2)
-        lst = [(gcol(k), v("ID"), v("PP" + n, 144 + 8 * i, 152 + 8 * i)) for i, (k, j) in enumerate(gd)] + [(run(k), v("ID"), v("PP" + n, 0, 144)) for k in tags]
-        for j, (o, l, r) in enumerate(lst):
-            mm(o, l, r, False, j == len(lst) - 1)
+              + [(v(C, 144 + 8 * i, 152 + 8 * i), v("S1C" + n, 128 * j, 128 * j + 128), v("BO")) for i, (k, j) in enumerate(gd)],
+              [(vn(C, 2 + i, 8, 18), vn(CM, i, 128, 16), v("BO")) for i in range(16)])
+        act(v(PP, 0, w), v(C, 0, w), AF.Relu, bias=v("RA%d" % t, 0, 1) if t else None, scale=-B / 2)
+        group([(gcol(k), v("ID"), v(PP, 144 + 8 * i, 152 + 8 * i)) for i, (k, j) in enumerate(gd)]
+              + [(run(k), v("ID"), v(PP, 0, 144)) for k in tags], start=False)
         o = SEG[s, tags[0]]
-        scan(v("SC" + n, o, o + 144 * nk), v(K, 0, 144 * nk), v("D1" + n, o, o + 144 * nk), AL.min, AL.max)
+        for a, b in ([(288, 432), (0, 288)], [(0, 144), (144, 288)], [(0, 144)])[2 - s]:
+            scan(v("SC" + n, o + a, o + b), v(K, a, b), v("D1" + n, o + a, o + b), AL.min, AL.max)
         mj = v("MJ" + n, 16 - 8 * s, 24 - 8 * s)
         if s > 0:
             ts(mj, ends(n, s, s), 2047, AL.bitwise_and)
             if FAST[h]:
                 tt(v("BV" + n), ind(mj, v("LS", 0, 8)), v("MK"), AL.mult)
-                mm(v(K, 440, 448), v("BV" + n), v("BO16"))
+                mm(v(C, 440, 448), v("BV" + n), v("BO16"))
             else:
-                spread(v(K, 440, 448), v("BV" + n, 0, 64), mj, v("LS", 32, 36), vn("BOF", 0, 64, 2), 8, 128)
-            cp(v(ov, 16 - 8 * s, 24 - 8 * s), v(K, 440, 448))
+                spread(v(C, 440, 448), v("BV" + n, 0, 64), mj, v("LS", 32, 36), vn("BOF", 0, 64, 2), 8, 128)
+            cp(v(ov, 16 - 8 * s, 24 - 8 * s), v(C, 440, 448))
         if s == 2:
             ts(v("A1" + n), ends(n, 2, 1), -2049, AL.bitwise_and); ts(v("B1" + n), mj, SENT, AL.add)
             tt(slot(n, 1, 1), v("A1" + n), v("B1" + n), AL.min)
         if (t, s, h) == (1, 0, 0):
             tt(v("NZ0"), ends(n, 0, 0), slot(n, 0, 0), AL.is_lt)
-        name = nm(t, h, {2: 0, 1: 2, 0: 3}[s])
+        name = nm(t, h, {2: 0, 1: 2 - h, 0: 3}[s])
         ts(name, ends(n, s, 0), 4095, AL.bitwise_and)
         if s > 0: tt(slot(n, s - 1, 0), ends(n, s, 0), name, AL.subtract)
-        if s == 1 and t > 0:
-            tt(v("GE" + n), slot(n, 1, 0), gcol(0), AL.is_ge); tt(nm(t, h, 1), v("GE" + n), vn("RS%d%d" % (t, h), 3, 8, 4), AL.mult)
+        if s == 1 - h and t > 0:
+            tt(v("GE" + n), slot(n, s, 0), gcol(0), AL.is_ge); tt(nm(t, h, 1 + h), v("GE" + n), vn("RS%d%d" % (t, h), 3, 8, 4), AL.mult)
 
     def yg(k, h, src, P, c):
-        mm(v(P, c, c + 128, p1=8), src, v("ID32")); act(v("YG", 256 * k + 128 * h, 256 * k + 128 * h + 128, p1=8), v(P, c, c + 128, p1=8))
+        mm(v(P, c, c + 128, p1=8), src, v("ID" if k else "ID32")); act(v("YG", 256 * k + 128 * h, 256 * k + 128 * h + 128, p1=8), v(P, c, c + 128, p1=8))
 
     def guards21(t, h):
         n = str(h); sg = "SG%d%d" % (t, h)
@@ -408,7 +423,7 @@ def build():
             yg(2 - j, h, v(sg, 8 * j, 8 * j + 8), "A" + n, 128 * j)
 
     def guard0(t, h):
-        n = str(h); gs = "GS%d%d" % (t, h); K = "K" + n
+        n = str(h); gs = "GS%d%d" % (t, h); K = "Y0" if aside(t, 0, h) else "K" + n
         tt(v("ZZ" + n), nm(t, h), v("CMP"), AL.is_equal); scan(v(gs), v("ZZ" + n), nm(t, h), AL.mult, AL.add)
         if t == 2:
             return yg(0, h, vn(gs, 3, 8, 4), K, 256)
@@ -416,7 +431,7 @@ def build():
         mm(v(K, 448, 456), v("BG" + n), v("BO32")); cp(v("SO%d%d" % (t, h), 0, 8), v(K, 448, 456))
         return send([(v(gs), v("RS%d%d" % (t + 1, h)), 1), (v("SO%d%d" % (t, h)), v("RP%d%d" % (t + 1, h)), 1)], 3.5)
 
-    i64 = lo(v("ID32", 0, 64)); xb, xa = v("XX", 0, 8), v("XX", 8, 16); P = "A0"
+    i64 = lo(v("ID", 0, 64)); xb, xa = v("XX", 0, 8), v("XX", 8, 16); P = "A0"
     ya, yb, yw = v("YAB", 0, 64), v("YAB", 64, 128), v("YAB", 128, 192); fr = v("FR")
 
     def source(t):
@@ -424,18 +439,18 @@ def build():
         cp(xb, v("MJ0", 8, 16))
         if even:
             ts(v("FL"), ends("0", 2, 1), 2048, AL.bitwise_and); tt(v("A2"), v("FL"), vl(t, 0), AL.min); tt(v("DV"), v("MJ0", 0, 8), v("A2"), AL.subtract)
-            tt(v("NW"), ends("0", 1, 1), slot("0", 1, 1), AL.is_lt); tt(v("TQ"), v("NW"), v("DV"), AL.mult); tt(xa, v("TQ"), v("A2"), AL.add)
+            tt(v("NW"), ends("0", 1, 1), slot("0", 1, 1), AL.is_lt); tt(v("TQ"), v("NW"), v("DV"), AL.mult); tt(v("XA"), v("TQ"), v("A2"), AL.add)
+            tt(xa, v("TQ"), v("A2"), AL.add)
         else:
             tt(v("ZP"), nm(t, 0), v("CMP"), AL.is_equal); scan(v("GP"), v("ZP"), nm(t, 0), AL.mult, AL.add)
             act(vn("VV", 0, 8, 4), vl(t, 0)); cp(vn("VV", 2, 8, 4), v("MJ0", 0, 8))
             ts(v("NZ"), nm(t, 0), 0.0, AL.is_gt); tt(v("UU"), v("NZ"), v("VV"), AL.mult); scan(v("AP"), v("ZP"), v("UU"), AL.mult, AL.add)
-            act(xa, vn("AP", 3, 8, 4))
-            act(v("BC"), ind(v("GP"), v("LS", 24, 32))); mm(v(P, 384, 448), lo(v("BC")), i64); act(v("E0"), v(P, 384, 448))
-        spread(v(P, 0, 4), v("BA", 0, 32), xa, v("LS", 32, 34), v("MC", 0, 32), 4, LA)
-        cp(v("OA", 0, 4), v(P, 0, 4)); cp(v("EA"), ind(node(t), v("OA", 0, 4)))
+            act(xa, vn("AP", 3, 8, 4)); act(v("XA"), vn("AP", 3, 8, 4))
+            act(v("BC"), ind(v("GP"), v("LS", 24, 32))); mm(v(P, 384, 448), lo(v("BC")), lo(v("ID32", 0, 64))); act(v("E0"), v(P, 384, 448))
+        spread(v(P, 0, 4), v("BA", 0, 32), v("XA"), v("LS", 32, 34), v("MC", 0, 32), 4, LA)
+        cp(v("OA", 0, 4), v(P, 0, 4)); (act if t else cp)(v("EA"), ind(node(t), v("OA", 0, 4)))
         tt(v("N01"), v("XX", 0, 16), v("XX", 8, 24), AL.is_equal)
-        for w, x in enumerate((xb, xa)):
-            mm(v(P, 192 + 64 * w, 256 + 64 * w, p1=8), lo(x), i64)
+        mms([(v(P, 192 + 64 * w, 256 + 64 * w, p1=8), lo(x), i64) for w, x in enumerate((xb, xa))], True, True, True)
         vt = v("VTH", p1=8)
         act(vt, v(P, 192, 320, p1=8))
         for c in range(2):
@@ -446,20 +461,19 @@ def build():
 
     def step3(t):
         ph[0] = "s%d" % t; even = t % 2 == 0; e = t // 2; ea, eb = v("EA"), v("EB"); nr3 = 3 if even else 2
-        cp(eb, v("E160", 0, 64)); ts(fr, ea if even else eb, 0.0, AL.is_equal)
-        mm(v(P, 64, 128), v("T2"), fr)
-        if even: mm(v(P, 128, 192), v("TRI"), fr)
-        ts(v("TA"), v(P, 64, 128), -64.0, AL.is_equal)
+        cp(eb, v("E160", 0, 64)); act(fr, ea if even else eb, AF.Relu, bias=1.0, scale=-1.0)
+        mms([(v(P, 64, 128), v("T2"), fr)] + ([(v(P, 128, 192), v("TRI"), fr)] if even else []), True, True, True)
+        act(v("TA"), v(P, 64, 128), AF.Relu, bias=-63.0, scale=-1.0)
         if even: act(v("PLF"), v(P, 128, 192), AF.Identity, bias=-33.0)
         bars = [v("N01", 0, 8), v("N01", 8, 16)] + ([] if even else [v("NZ0")])
         lst = [(vn(P, 8 + r, 8, 4), lo(v("I2N")), lo(x)) for j, x in enumerate(bars) for r in range(3 if j else 4)]
         group(lst[:4] + [(v(P, 8, 40, p0=p, p1=p + 64), fr, vn("BOF", 0, 32, 4)) for p in (0, 64)] + lst[4:])
         ts(v("ASK"), v(P, 8, 40), 0.0, AL.is_gt, B2, AL.mult)
         lst = [(lo(v("Y0", 0, 24)), v("ONE", 0, 64, p1=1), v("CB2", p1=1)), (lo(v("Y0", 0, 8)), i64, lo(xa)), (lo(v("Y0", 8, 16)), i64, lo(xb))]
-        if even: lst += [(lo(v("Y0", 16, 24)), i64, lo(v("NL", 8 * e, 8 * e + 8)))]
-        lst += [(lo(v("Y0", 8 * r, 8 * r + 8)), lo(v("NID", 0, 64)), lo(vn("ASK", 0, 8, 4))) for r in range(3)]
-        lst += [(lo(vn("Y0", j // 2, 3, 8)), v("CMM", 64 * j, 64 * j + 64), v("ASK", 4 * (j // 2), 4 * (j // 2) + 3)) for j in range(16)]
-        group(lst)
+        if even: lst += [(lo(v("Y0", 16, 24)), i64, lo(v("NLH", 8 * e, 8 * e + 8)))]
+        own = [(lo(v("Y0", 8 * r, 8 * r + 8)), lo(v("NID", 0, 64)), lo(vn("ASK", 0, 8, 4))) for r in range(3)]
+        met = [(lo(vn("Y0", j // 2, 3, 8)), v("CMM", 64 * j, 64 * j + 64), v("ASK", 4 * (j // 2), 4 * (j // 2) + 3)) for j in range(16)]
+        group(lst, own + met[:8], met[8:])
         tt(lo(v("W3")), lo(v("Y0", 0, 24)), lo(v("DUMC")), AL.min)
         if t < 2:
             act(lo(v("JK")), lo(v("Y0", 16, 24)), AF.Relu, bias=lo(v("NB", e, e + 1)) if even else B, scale=-B, acc=lo(v("ASUM")))
@@ -476,29 +490,31 @@ def build():
         act(v("CUT"), ind(rec(t, 0, M), v("OV%d0" % t, 8, 12)))
         group([(v(P, 64, 128), dg(3), v("CUT")), (v(P, 64, 128), dg(2), x)]); group([(v(P, 128, 192), dg(1), v("CUT")), (v(P, 128, 192), dg(0), x)])
         act(v("CH"), v(P, 64, 192))
-        for r in range(2):
-            wt = 144 * (2 * e + r)
-            group([(v(P, 384 + 64 * r, 448 + 64 * r), v("WT", wt + 15 - j, wt + 143 - j), vn("RD0", j, 64, 16)) for j in range(16)])
-        ts(v("GO"), v(P, 384, 448), 0.0, AL.is_ge); ts(v("N8"), v(P, 448, 512), 0.0, AL.is_lt)
-        tt(v("STR"), v("N8"), v("GO"), AL.is_gt)
+        d = v(P, 384, 448)
+        na = NA[t][2][0]
+        group([(d, v("WT", 144 * e + 15 - j, 144 * e + 143 - j), vn("RD0", j, 64, 16)) for j in range(15)]
+              + ([(v(P, 384 + na, 448), v("WX", 128 * e, 128 * e + 128), v("XZ%d" % t, na, LA))] if na < LA else [])
+              + [(d, v("WT", 144 * e, 144 * e + 128), vn("RD0", 15, 64, 16))])
+        ts(v("TR"), d, 1.5 * 2 ** 33, AL.add, 1.5 * 2 ** 33, AL.subtract); ts(v("GO"), d, -512.0, AL.is_ge)
+        tt(v("N8"), d, v("TR"), AL.is_lt); tt(v("STR"), v("N8"), v("GO"), AL.is_gt)
         mm(v(P, 256, 320), v("T1B"), v("STR"))
         group([(v(P, 192, 256), v("T1"), v("STR")), (v(P, 192, 256), v("NBOF"), fr), (v(P, 192, 256), v("ID64N"), v("GO"))])
         tt(v("NU"), v(P, 256, 320), eb, AL.subtract)
         ts(v("TB"), v(P, 192, 256), -32.0, AL.is_ge); tt(yb, eb, v("TB"), AL.mult); tt(yw, eb, v("GO"), AL.mult)
         tt(v("TC"), v("TA"), v("NC", 64 * e, 64 * e + 64), AL.mult)
         for c in range(2):
-            Y = "Y%d" % (1 - c)
-            for j in range(8):
-                mm(v(Y, 64 * j, 64 * j + 64), v("RBP", 128 * (8 * c + j), 128 * (8 * c + j) + 128), v("PLF"))
+            Y = "Y1"
+            mms([(v(Y, 64 * j, 64 * j + 64), v("RBP", 128 * (8 * c + j), 128 * (8 * c + j) + 128), v("PLF")) for j in range(8)], True, True, True)
             for j in range(8):
                 tt(v("Y2", 512 * c + 64 * j, 512 * c + 64 * j + 64), v(Y, 64 * j, 64 * j + 64), v("NU"), AL.max)
         wd = lambda i: 288 if i == 0 else 144 if i == 15 else 0
-        group([(v("B0", 0, 64), v("ID32"), ea)] + [(v("B0", 0, 64), v("WD", wd(i) + 15 - i, wd(i) + 143 - i), v("Y2", 64 * i, 64 * i + 64)) for i in range(16)])
-        tt(v("YI"), v("B0", 0, 64), v("TC"), AL.add); ts(ya, v("YI"), 16383, AL.bitwise_and)
+        group(*[[(v("Y0", 0, 64), v("WD", wd(i) + 15 - i, wd(i) + 143 - i), v("Y2", 64 * i, 64 * i + 64))] for i in range(16)])
+        tt(v("TC"), v("TC"), ea, AL.add); tt(v("YI"), v("Y0", 0, 64), v("TC"), AL.add); ts(ya, v("YI"), 16383, AL.bitwise_and)
 
     def commit(t):
-        ph[0] = "s%d" % t; even = t % 2 == 0; n = 12 if even else 8
-        cp(ind(v("DD", Q * t, Q * t + WIN), v("OSC", 0, n)), v("YAB", 0, 16 * n))
+        ph[0] = "s%d" % t; even = t % 2 == 0
+        for a, b in ((4, 12), (0, 4)) if even else ((0, 8),):
+            cp(ind(v("DD", Q * t, Q * t + WIN), v("OSC", a, b)), v("YAB", 16 * a, 16 * b))
         if even:
             for base in ((0, R1, R2) if t == 0 else (RO,)):
                 n = 4 if base == R2 else 8
@@ -629,13 +645,76 @@ def order(ops, hard, soft, m, tune):
     return best[1]
 
 
+def polish(ops, hard, soft, seq, m, tune):
+    n = len(ops); LAT = m["lat"]; cost = costs(ops, m); STEP = 64
+    eng = ["VAPGSR".index(o["eng"]) for o in ops]; dyn = ["dyn" in o for o in ops]
+    dm = [o["nbytes"] / m["bw"] if o["kind"] == "d" else -1.0 for o in ops]; src = [o.get("src", -1) for o in ops]
+    hp = [list(h) for h in hard]; pred = [hard[i] | soft[i] for i in range(n)]; succ = [set() for _ in ops]
+    for i in range(n):
+        for j in pred[i]: succ[j].add(i)
+
+    def run(seq, k0, end, by, marks):
+        free, lastq, bank, bl, bus, top, arg = marks[k0]; free = free[:]; lastq = lastq[:]; bank = bank[:]; bl = bl[:]; marks = marks[:k0 + 1]
+        for p in range(k0 * STEP, n, STEP):
+            for i in seq[p:p + STEP]:
+                e = eng[i]
+                if e == 5: b = src[i]; t = end[b]
+                else: t = free[e]; b = lastq[e]
+                for j in hp[i]:
+                    x = end[j] + LAT
+                    if x > t: t = x; b = j
+                if dyn[i]:
+                    for e2 in (0, 1, 2):
+                        if e2 != e and bank[e2] + LAT > t: t = bank[e2] + LAT; b = bl[e2]
+                    bank[e] = t + cost[i]; bl[e] = i
+                t += cost[i]; free[e] = t; lastq[e] = i
+                if dm[i] >= 0:
+                    bus = (bus if bus > t else t) + dm[i]; t = bus + 1.5
+                end[i] = t; by[i] = b
+                if t > top: top = t; arg = i
+            marks.append((free[:], lastq[:], bank[:], bl[:], bus, top, arg))
+        return top, arg, marks
+
+    def links(i, by):
+        out = []
+        while by[i] >= 0:
+            if by[i] not in pred[i]: out.append((by[i], i))
+            i = by[i]
+        return out
+    r = tune["seed"] * 7919 + 1; end = [0.0] * n; by = [-1] * n; its = tune["polish"]
+    cur, arg, marks = run(seq, 0, end, by, [([0.0] * 6, [-1] * 6, [-1.0] * 3, [-1] * 3, 0.0, 0.0, -1)])
+    best = (cur, seq); lk = links(arg, by)
+    for it in range(its):
+        r = (r * 1103515245 + 12345) % 2147483648
+        j, i = lk[(r >> 8) % len(lk)]; pj = seq.index(j); pi = seq.index(i, pj); mid = seq[pj:pi + 1]
+        if r >> 7 & 1:
+            mv = {i}
+            for x in reversed(mid):
+                if not mv.isdisjoint(succ[x]): mv.add(x)
+            if j in mv: continue
+            mid = [x for x in mid if x in mv] + [x for x in mid if x not in mv]
+        else:
+            mv = {j}
+            for x in mid:
+                if not mv.isdisjoint(pred[x]): mv.add(x)
+            if i in mv: continue
+            mid = [x for x in mid if x not in mv] + [x for x in mid if x in mv]
+        new = seq[:pj] + mid + seq[pi + 1:]; e2 = end[:]; b2 = by[:]
+        val, a2, m2 = run(new, pj // STEP, e2, b2, marks)
+        r = (r * 1103515245 + 12345) % 2147483648
+        if val <= cur - (tune["heat"] * (1 - it / its) + 0.01) * math.log((r + 1) / 2147483648):
+            seq, cur, end, by, marks = new, val, e2, b2, m2; lk = links(a2, by)
+            if cur < best[0]: best = (cur, seq)
+    return best[1]
+
+
 def rank_program(g, core, T, topo):
     rank = T.rank_of(core)
     if rank is None:
         return
     if "ops" not in PLAN:
         PLAN["ops"] = build(); PLAN["hard"], soft = depend(PLAN["ops"])
-        PLAN["seq"] = order(PLAN["ops"], PLAN["hard"], soft, MODEL, TUNE)
+        PLAN["seq"] = polish(PLAN["ops"], PLAN["hard"], soft, order(PLAN["ops"], PLAN["hard"], soft, MODEL, TUNE), MODEL, TUNE)
         PLAN["hard"] = turns(PLAN["ops"], PLAN["hard"], PLAN["seq"])
     ops, hard = PLAN["ops"], PLAN["hard"]; cores = T.cores; N = len(cores)
 

@@ -3,11 +3,14 @@ from concourse.bass import DstId, RemoteDMATransfer
 from concourse.mybir import AluOpType as AL, ActivationFunctionType as AF
 
 M, Q, BASE, L, LA = 4096, 2048, 1920, 256, 64
-NA = [[(64, 56), (64, 56), (64, 64)]] * 3
+NA = [[(64, 48), (64, 48), (64, 64)]] * 3
 CUT = (96, 64)
 FAST = (1, 1)
-MODEL = dict(cy=1.0e-3, g=1.56, sc=3.8, pe=0.5, lat=0.15, bw=180e3)
-TUNE = dict(slack=0.05, seed=23, fb=30, moves=4, step=3, polish=90000, heat=0.2)
+MODEL = dict(cy=0.95e-3, g=1.56, sc=3.8, pe=0.5, lat=0.17, bw=330e3, far=1.3)
+TUNE = dict(slack=0.05, seed=1, fb=30, moves=4, step=3, renew=5000, w0=30, w1=80, noise=4, look=0.7, warm=0.2, polish=15000, heat=0.1)
+PIECE, LASTD = 4096, 2
+TT2 = 1.0
+EQS = (0, 0, 0, 0, 0, 0)
 B = float(2 ** 26)
 B2 = 16384.0
 NEG = -float(2 ** 30)
@@ -15,9 +18,8 @@ SENT, SENT2 = 4096.0 * 4081, 4096.0 * 4082
 R1, R2, WW, DUM = 4096, 8192, 10240, 6144
 WIN = DUM + 12 * LA
 RO = R1 + WIN
-XW = 128 + max(n[1] for t in NA for n in t)
-NAS = sorted(set(n for t in NA for s in t for n in s))
-L0 = NAS[0]
+NV = [max(NA[t][s][h] for t in range(3) for s in range(3)) for h in range(2)]
+X0, XW = 128 - NV[0], NV[0] + NV[1]
 SEG = {(2, 0): 0, (2, 1): 144, (2, 2): 288, (1, 1): 432, (1, 0): 576, (0, 0): 720}
 F, H, BF, U, I = "float32", "float16", "bfloat16", "uint16", "int32"
 SB = {
@@ -25,11 +27,11 @@ SB = {
     "XZ0": (L, BF), "XZ1": (L, BF), "XZ2": (L, BF), "XB0": (16 * XW, BF), "XB1": (16 * XW, BF), "XB2": (16 * XW, BF), "NXT": (768, BF),
     "VU": (96, U), "VL": (48, F), "VU1": (32, U), "VL1": (16, F), "VU2": (32, U), "VL2": (16, F),
     "SA0": (8, F), "SA1": (8, F), "RA1": (8, F), "RA2": (8, F), "YG": (768, F), "RZ": (1, BF), "NM": (192, I),
-    "ONE": (128, BF), "ONE32": (128, F), "ID": (128, BF), "NID": (128, BF), "ID32": (128, F), "ID64N": (128, BF), "I2N": (128, BF),
-    "BOF": (128, BF), "NBOF": (128, BF), "BO": (8, BF), "BO32": (8, F), "BO16": (8, H), "SC3H": (24, H), "EXP": (16 * (128 - L0), BF),
+    "ONE": (128, BF), "ONE32": (128, F), "ID": (128, BF), "NID": (128, BF), "ID32": (128, F), "ID64N": (128, BF), "IDK": (128, BF), "I2N": (128, BF),
+    "BOF": (128, BF), "NBOF": (128, BF), "BO": (8, BF), "BO32": (8, F), "BO16": (8, H), "SC3H": (24, H), "EXP": (2048, BF),
     "TRI": (128, BF), "TRE": (128, BF), "T1": (128, BF), "T1B": (128, BF), "T2": (128, BF), "RBP": (2048, BF), "WD": (432, F),
-    "WT": (288, BF), "WE": (2, F), "WX": (256, BF), "NLH": (16, H), "XA": (8, F), "TR": (64, F), "WC": (32, F), "DG": (1024, BF), "SEL": (1024, BF), "NSEL": (1024, BF), "TRM": (512, BF), "VB": (768, F),
-    "PB": (144, BF), "P16": (144, H), "WP": (432, BF), "KC": (576, BF), "CR": (160, BF), "LAN": (128 * len(NAS), BF), "MK": (128, F), "II": (128, I), "IJ": (128, I),
+    "WT": (288, BF), "WE": (2, F), "WX": (256, BF), "NLH": (16, H), "XA": (8, F), "TR": (64, F), "WC": (32, F), "DG": (1024, BF), "SEL": (1024, BF), "AB": (1024, BF), "NX": (8, F), "TRM": (128, BF), "VB": (768, F),
+    "PB": (144, BF), "P16": (144, H), "WP": (432, BF), "KC": (576, BF), "CR": (160, BF), "LAN": (384, BF), "MK": (128, F), "II": (128, I), "IJ": (128, I),
     "LI": (64, I), "LJ": (16, I), "LK": (16, I), "LS": (64, U), "DUMC": (24, F), "NC": (128, F), "NL": (16, F), "NB": (2, F), "CB2": (24, BF),
     "CMP": (32, F), "MC": (96, BF), "GSEL": (240, BF),
     "XX": (24, H), "FL": (8, I), "A2": (8, F), "DV": (8, F), "NW": (8, F), "TQ": (8, F), "BA": (96, H), "OA": (8, U), "EA": (64, F), "EB": (64, F),
@@ -43,21 +45,26 @@ for _h in "01":
                "SC" + _h: (864, I), "D1" + _h: (864, F), "MJ" + _h: (16, I), "A1" + _h: (8, I), "B1" + _h: (8, F), "GE" + _h: (8, F), "ZZ" + _h: (32, F),
                "BV" + _h: (128, H), "BG" + _h: (128, F), "LT" + _h: (16, F), "S1R" + _h: (384, BF), "S1C" + _h: (384, BF)})
     for _t in range(3):
-        SB.update({"OV%d" % _t + _h: (32, U), "SG%d" % _t + _h: (16, F if _t < 2 else H), "GS%d" % _t + _h: (32, F)})
+        SB.update({"OV%d" % _t + _h: (32, U), "SG%d" % _t + _h: (32, H), "GS%d" % _t + _h: (32, F)})
     for _t in range(2):
-        SB.update({"SO%d" % _t + _h: (64, U), "RG%d" % (_t + 1) + _h: (16, F), "RO%d" % (_t + 1) + _h: (32, U),
+        SB.update({"SO%d" % _t + _h: (64, U), "RG%d" % (_t + 1) + _h: (32, H), "RO%d" % (_t + 1) + _h: (32, U),
                    "RS%d" % (_t + 1) + _h: (32, F), "RP%d" % (_t + 1) + _h: (64, U)})
-SB.update({"E162": (128, U), "FK2": (128, H), "RD2": (2048, H), "CM2": (2048, BF), "PP2": (160, BF)})
+for _h in "23":
+    SB.update({"E16" + _h: (128, U), "FK" + _h: (128, H), "MM" + _h: (128, BF), "RD" + _h: (2048, H), "CM" + _h: (2048, BF), "PP" + _h: (160, BF)})
 DYN = ("A0",)
 PS = ["K0", "K1", "A0", "B0", "A1", "B1", "Y0", "Y1"]
 POOL, FILL = {}, {}
 for _k, (_n, _d) in SB.items():
     if _n <= 640 and _k[:2] not in ("VU", "VL", "SG", "SO", "SA", "RG", "RO", "RA", "VS", "OV", "GS", "RS", "RP", "XZ") or _k == "GSEL":
         POOL[_k] = ("pool_" + _d, FILL.get(_d, 0)); FILL[_d] = FILL.get(_d, 0) + (_n + 31) // 32 * 32
-SCRATCH = {k: ("sbuf", [128, n], d) for k, (n, d) in SB.items() if k not in POOL}
-SCRATCH.update({"pool_" + d: ("sbuf", [128, n], d) for d, n in FILL.items()})
+SCRATCH = {"pool_" + d: ("sbuf", [128, n], d) for d, n in FILL.items()}
+SENTU = ["VU"] + [n + str(t) + h for n in ("OV", "SO") for t in range(2) for h in "01"]
+for _k in SENTU:
+    POOL[_k] = ("sent", FILL.get("sent", 0)); FILL["sent"] = FILL.get("sent", 0) + SB[_k][0]
+SCRATCH["sent"] = ("sbuf", [128, FILL["sent"]], U)
+SCRATCH.update({k: ("sbuf", [128, n], d) for k, (n, d) in SB.items() if k not in POOL})
 SCRATCH.update({k: ("psum", [128, 512], F) for k in PS})
-SEMAPHORES = ["qV", "qA", "qP", "qG"] + ["d%d" % i for i in range(16)] + ["r%d" % i for i in range(24)] + ["l%d" % i for i in range(12)]
+SEMAPHORES = ["qV", "qA", "qP", "qG"] + ["d%d" % i for i in range(40)] + ["r%d" % i for i in range(24)] + ["l%d" % i for i in range(12)]
 QSEM = {"V": "qV", "A": "qA", "P": "qP", "G": "qG"}
 PLAN = {}
 
@@ -134,7 +141,7 @@ def build():
             return (0.05, 0, n, 0, 0)
         f = 0.5 if all(wide(x) == 2 for x in [out] + ins) else 1.0
         if two and all(x[0] in SB for x in ins):
-            f = 2.0
+            f = TT2 if f == 0.5 else 2.0
         return (0.0, max(64, n * f), 0, 0, 0)
 
     def cp(out, a):
@@ -168,6 +175,9 @@ def build():
 
     def scale(out, a, f):
         act(out, a, AF.Identity, scale=f)
+
+    def covers(out, d):
+        act(out, d, AF.Sign, bias=0.5, scale=-1.0)
 
     def mm(out, l, r, start=True, stop=True):
         n = max(min(64, cols(l)), cols(r)) * (4 if wide(l) == 4 else 1)
@@ -204,8 +214,13 @@ def build():
         if chain: last.append(i)
         return i
 
-    def copy(out, a, wait=()):
-        return dma("S", lambda T: ap(T, out), lambda T: ap(T, a), [a], [out], 128 * cols(a) * wide(a), wait=wait)
+    def copy(out, a, wait=(), piece=PIECE):
+        n = piece // wide(a)
+        for c in range(0, cols(a), n):
+            o2, a2 = v(out[0], out[3] + c, out[3] + c + n), v(a[0], a[3] + c, a[3] + c + n)
+            wait = [dma("S", lambda T, o2=o2: ap(T, o2), lambda T, a2=a2: ap(T, a2), [a2], [o2], 128 * piece, wait=wait)]
+            ops[-1]["bulk"] = True
+        return wait
 
     def send(items, lat, wait=()):
         ls = "l%d" % nl[0]; nl[0] += 1; ks = [k for s, d, k in items]
@@ -246,7 +261,7 @@ def build():
     act(v("BO"), bo); act(v("BO32"), bo); act(v("BO16"), bo)
     for j in range(3):
         scale(v("SC3H", 8 * j, 8 * j + 8), bo, -4096.0)
-    scale(v("NID"), v("ID"), -1.0); act(v("ID32"), v("ID"))
+    scale(v("NID"), v("ID"), -1.0); act(v("ID32"), v("ID")); scale(v("IDK"), v("ID"), 4096.0)
     act(v("P16"), v("PB")); scale(v("WP", 0, 144), v("PB"), B); scale(v("WP", 144, 288), v("PB"), -B); scale(v("WP", 288, 432), v("PB"), B)
     ms(v("GSEL"), 0.0); act(v("GSEL", 112, 128), v("MK", 0, 16))
     gsel = lambda g, p1: v("GSEL", 112 - 16 * g, 240 - 16 * g, p1=p1)
@@ -257,17 +272,15 @@ def build():
     ms(v("CR", p1=32), 1.0); ms(v("CR", p0=32, p1=64), -6.0 / 32); ms(v("CR", 144, 160, p1=32), 0.0)
     for j in range(2):
         ms(vn("CR", j, 8, 18, 0, 32), 0.0); ms(vn("CR", j, 8, 18, 32, 64), 2.0)
-    ms(v("LAN", p0=32, p1=64), 1.0); ms(v("LAN", p1=32), 0.0)
-    for j, n in enumerate(NAS):
-        if n > 0: ms(v("LAN", 128 * j, 128 * j + n, p1=32), -0.5)
+    ms(v("LAN", p0=32, p1=64), 1.0); ms(v("LAN", p1=32), 0.0); ms(v("LAN", 128, 256, p1=32), -0.5)
     for h in "01":
         iota(v("D1" + h), [[0, 864]], 1 - 2 ** 24, 0); ms(vn("D1" + h, 0, 8, 18), SENT); ms(vn("D1" + h, 144, 8, 18), SENT2)
     ms(v("NM"), 0); ms(v("CMP"), 0.0); ms(vn("CMP", 0, 8, 4), -1.0)
-    ms(v("W0", R1 + Q, R2), 0.0); ms(v("DD", BASE, Q), 0.0)
+    xb0 = ("XB0", 0); ms(v("W0", R1 + Q, R2), 0.0); ms(v("DD", BASE, Q), 0.0)
     for n in ("SA0", "SA1"): ms(v(n), 0.0)
-    for n in ("SO00", "SO01", "SO10", "SO11", "OV00", "OV01", "OV10", "OV11", "VU"): ms(v(n), 0)
+    add("V", lambda g, T, c: g.vector.memset(T.sent[:, :], 0), [], [v(n) for n in SENTU], (0, FILL["sent"] / 2, 0, 0, 0))
     for j in range(16):
-        (cp if j % 2 else act)(vn("EXP", j, 128 - L0, 16), v("ID", L0, 128))
+        (cp if j % 2 else act)(vn("EXP", j, 128, 16), v("ID"))
     for t in range(3):
         cp(v("VU", 32 * t, 32 * t + 16), v("VSI", 16 * t, 16 * t + 16))
     cp(v("VSF"), v("VSI"))
@@ -277,21 +290,23 @@ def build():
         mm(v("Y0", 8 * j, 8 * j + 8), v("VB", 128 * j, 128 * j + 128), v("BO32"))
     act(v("VL"), v("Y0", 0, 48))
     for i in range(16):
-        cp(vn("XB0", i, XW, 16), v("XZ0", 0, XW))
+        cp(vn(xb0[0], xb0[1] + i, XW, 16), v("XZ0", X0, X0 + XW))
     act(v("RZ"), v("W0", 0, 1)); ms(v("W0", 0, 1), 512.0); cp(v("W0", R1, R1 + Q), v("W0", 0, Q)); act(v("W0", R2, R2 + Q), v("W0", 0, Q))
     ph[0] = "x"
     s1 = send([(v("XZ0"), v("XZ%d" % k), k) for k in (1, 2)], 4.0, [loaded])
     s2 = send([(v("VU", 32, 64), v("VU1"), 1), (v("VL", 16, 32), v("VL1"), 1), (v("VU", 64, 96), v("VU2"), 2), (v("VL", 32, 48), v("VL2"), 2)], 4.0, [loaded])
-    copy(v("W1", 0, WW), v("W0"), [s1, s2])
+    copy(v("W1", 0, R1 + Q), v("W0", 0, R1 + Q), [s1, s2], 3 * PIECE); copy(v("W1", R2, WW), v("W0", R2, WW), [s1, s2]); ms(v("W1", R1 + Q, R2), 0.0)
     for a, b in ((0, 960), (960, BASE)):
         keep(v("DD", a, b), v("DI", a, b))
     ph[0] = "j"
     sel(v("TRI"), v("BOF"), [[1, 128]], AL.is_ge, 0, -1); sel(v("TRE"), v("BOF"), [[1, 128]], AL.is_gt, 0, -1)
     sel(v("T1"), v("TRI"), [[-1, 128]], AL.not_equal, 0, 1, -31.0); sel(v("T2"), v("TRE"), [[-1, 128]], AL.not_equal, 0, 1, -64.0)
-    ms(v("SEL", p1=32), 1.0); sel(v("SEL", p1=8), v("SEL", p1=8), [[-1, 8], [0, 128]], AL.is_equal, 0, 1); scale(v("NSEL", p1=8), v("SEL", p1=8), -1.0)
-    ms(v("TRM"), 0.5)
-    for p in (0, 64):
-        sel(v("TRM", p0=p, p1=p + 64), v("TRM", p0=p, p1=p + 64), [[0, 8], [-1, 64]], AL.is_ge, 0, 1)
+    ms(v("SEL", p0=64, p1=96), 1.0); sel(v("SEL", p0=64, p1=72), v("SEL", p0=64, p1=72), [[-1, 8], [0, 128]], AL.is_equal, 0, 1)
+    ms(lo(v("TRM")), 0.5); sel(lo(v("TRM")), lo(v("TRM")), [[0, 2], [-1, 64]], AL.is_ge, 0, 1); act(lo(v("VTH")), lo(v("TRM")))
+    for j in range(2):
+        cp(lo(v("SEL", 64 * j, 64 * j + 64)), lo(v("ID", 0, 64)))
+    for j in (128, 256, 512):
+        cp(lo(v("SEL", j, 2 * j)), lo(v("SEL", 0, j)))
     iota(v("DUMC"), [[256, 3], [0, 8]], DUM, 4); iota(v("NC"), [[1, 128]], M + BASE, 0); iota(v("NL"), [[64, 2], [0, 8]], BASE, 1)
     ts(v("NB"), vn("NL", 0, 2, 8), 1.0, AL.add, B, AL.mult)
     scale(v("NBOF"), v("BOF"), -1.0); scale(v("T1B"), v("T1"), B2); scale(v("ID64N"), v("ID"), -64.0)
@@ -304,12 +319,12 @@ def build():
     act(vn("WD", 15, 8, 16), bo); scale(vn("WD", 16, 8, 16), bo, -1.0); act(vn("WD", 144 + 15, 8, 16), bo); scale(vn("WD", 288 + 16, 8, 16), bo, -1.0)
     scale(v("WC", 0, 16), v("MK", 0, 16), B2); act(v("WC", 16, 32), v("MK", 0, 16), AF.Identity, bias=1.0, scale=-1.0)
     for i in range(16):
-        scale(v("RBP", 128 * i, 128 * i + 128), v("BOF"), v("WC", i, i + 1))
+        ts(v("RBP", 128 * i, 128 * i + 128), v("BOF"), v("WC", i, i + 1), AL.mult)
     act(v("NLH"), v("NL"))
     for e, t in enumerate((0, 2)):
         act(v("WE", e, e + 1), v("MK", t, t + 1), AF.Identity, bias=v("MK", 8 + t, 9 + t), scale=1024.0)
         scale(vn("WT", 144 * e + 15, 8, 16), bo, v("WE", e, e + 1))
-        if NA[t][2][0] < LA: scale(v("WX", 128 * e, 128 * e + 128), v("NBOF"), v("WE", e, e + 1))
+        scale(v("WX", 128 * e, 128 * e + 128), v("NBOF"), v("WE", e, e + 1))
         for j, row in enumerate((t, 8 + t)):
             o = 512 * e + 256 * j
             scale(v("DG", o, o + 128), v("ID"), v("MK", row, row + 1)); scale(v("DG", o + 128, o + 256), v("ID"), v("WC", 16 + row, 17 + row))
@@ -317,7 +332,7 @@ def build():
     def repeat(k, after):
         ph[0] = "x"
         for i in range(16):
-            keep(vn("XB%d" % k, i, XW, 16), v("XZ%d" % k, 0, XW))
+            keep(vn("XB%d" % k, i, XW, 16), v("XZ%d" % k, X0, X0 + XW))
             ops[-1]["after"] = after
     repeat(1, [])
     rec = lambda t, a=0, b=WW: v("W1" if t else "W0", a, b)
@@ -327,7 +342,7 @@ def build():
     slot = lambda n, s, k: vn("D1" + n, SEG[s, k], 8, 18)
     nm = lambda t, h, j=None: v("NM", 64 * t + 32 * h, 64 * t + 32 * h + 32) if j is None else vn("NM", 64 * t + 32 * h + j, 8, 4)
 
-    aside = lambda t, s, h: (s, h) == (0, 1) and t < 2
+    aside = lambda t, s, h: s == 0 and t <= h
 
     def spread(out, bv, src, lst, mask, n, p1):
         tt(bv, ind(src, lst), mask, AL.mult)
@@ -342,11 +357,11 @@ def build():
         n = str(h); x = v("XZ%d" % t, 128 * h, 128 * h + 128)
         act(v("S1R" + n, a, b), ind(rec(t, 0, M), off))
         group([(v(P, 0, b - a), v("ID"), v("S1R" + n, a, b))] + [(v(P, c, c + 128), v("NID"), x) for c in range(0, b - a, 128)])
-        act(v("S1C" + n, a, b), v(P, 0, b - a), AF.Sign, bias=0.5, scale=-1.0)
+        covers(v("S1C" + n, a, b), v(P, 0, b - a))
 
-    def walk(t, s, h):
+    def walk(t, s, h, between=None):
         ph[0] = "w%d%d" % (t, h); n = str(h); nk = s + 1; na = NA[t][2 - s][h]
-        u, K, C, banks = ("2", "Y0", "Y1", ["Y1"]) if aside(t, s, h) else (n, "K" + n, "B" + n, ["B0"] if (h, s) == (0, 0) else ["A" + n, "B" + n])
+        u, K, C, banks = (str(3 - h), "Y0", "Y1", ["Y1"]) if aside(t, s, h) else (n, "K" + n, "B" + n, ["B0", "A0"][:3 - t] if (h, s) == (0, 0) else ["A" + n, "B" + n])
         RD, CM = "RD" + u, "CM" + u
         ov = "OV%d%d" % (t, h); e16 = v("E16" + u); tags = {2: (0, 1, 2), 1: (1, 0), 0: (0,)}[s]
         off = v("VU%d" % t if t else "VU", 8 * h, 8 * h + 8) if s == 2 else v(ov, 8 - 8 * s, 16 - 8 * s)
@@ -355,18 +370,22 @@ def build():
         cap = s == 1 or (s == 0 and h == 1)
         if cap: ts(e16, ind(node(t), off), 4096.0 * nk, AL.min)
         else: cp(e16, ind(node(t), off))
-        for l0, l1 in cuts(0, min(na, LA), CUT[h]) + cuts(LA, na, CUT[h]) if (h, s) == (0, 0) else cuts(0, na, CUT[h]):
+        xn, xo = ("XB%d" % t, 0) if t else xb0; xo += 16 * (128 * h - X0)
+        for l0, l1 in cuts(0, na, CUT[h]) if h else cuts(128 - na, 128, CUT[h]):
             a, b = 16 * l0, 16 * l1
-            tt(v(RD, a, b), ind(rec(t), v("E16" + u, l0, l1)), v("XB%d" % t, 2048 * h + a, 2048 * h + b), AL.subtract)
+            tt(v(RD, a, b), ind(rec(t), v("E16" + u, l0, l1)), v(xn, xo + a, xo + b), AL.subtract)
             ts(v(CM, a, b), v(RD, a, b), 0.0, AL.is_le, 2.0, AL.mult)
-        for j, (l0, l1) in enumerate(cuts(na, 128, 32)):
+        fs = cuts(na, 128, 32) if h else cuts(0, 128 - na, 32)
+        for l0, l1 in fs:
+            act(v(RD, 16 * l0, 16 * l1), ind(rec(t), v("E16" + u, l0, l1)))
+        if between and aside(t, s, h): between(u); ph[0] = "w%d%d" % (t, h)
+        for j, (l0, l1) in enumerate(fs):
             P = v(banks[j % len(banks)], 0, 16 * (l1 - l0)); a, b = 16 * l0, 16 * l1
-            act(v(RD, a, b), ind(rec(t), v("E16" + u, l0, l1)))
-            group([(P, v("NXT", 256 * t + 128 * h, 256 * t + 128 * h + 128), v("EXP", a - 16 * L0, b - 16 * L0))], [(P, v("ID"), v(RD, a, b))])
-            act(v(CM, a, b), P, AF.Sign, bias=0.5, scale=-1.0)
+            group([(P, v("NXT", 256 * t + 128 * h, 256 * t + 128 * h + 128), v("EXP", a, b))], [(P, v("ID"), v(RD, a, b))])
+            covers(v(CM, a, b), P)
         masks = [0, 1] if s == 2 else [] if cap and s == 0 else [0]
         for j in masks:
-            ts(v("MM" + n, 128 * j, 128 * j + 128), e16, 4096.0 * (j + 1), AL.is_ge)
+            ts(v("MM" + u, 128 * j, 128 * j + 128), e16, 4096.0 * (j + 1), AL.is_ge)
         for k in tags:
             ts(v("FK" + u, 128 * k, 128 * k + 128), e16, -4096.0 * k - (2048 if k == 0 else 0), AL.add)
         gd = [] if t == 0 else [(2, 0), (1, 1)] if s == 2 else [(0, 2)] if s == 1 - h else []
@@ -374,13 +393,13 @@ def build():
         gcol = lambda k: vn(K, 144 * tags.index(k) + 1, 8, 18)
         p1 = [(run(k), v("ONE", p1=64), kc(int(k > 0), int(k not in [x for x, j in gd]))) for k in tags]
         if s == 2: p2 = [(v(K, 144 * j, 144 * j + 288), v("MM" + n, 128 * j, 128 * j + 128), v("WP", 0, 288)) for j in masks]
-        else: p2 = [(v(K, 0, 144 * nk), v("MM" + n, 0, 128), v("WP", 144 * s, 144 * s + 144 * nk)) for j in masks]
+        else: p2 = [(v(K, 0, 144 * nk), v("MM" + u, 0, 128), v("WP", 144 * s, 144 * s + 144 * nk)) for j in masks]
         p3 = [(run(k), v("FK" + u, 128 * k, 128 * k + 128), v("P16")) for k in tags]
         p4 = [(vn(K, 2 + i, 8 * nk, 18), vn(RD, i, 128, 16), v("SC3H", 0, 8 * nk)) for i in range(16)]
         p5 = [(gcol(k), v("S1R" + n, 128 * j, 128 * j + 128), v("SC3H", 0, 8)) for k, j in gd]
-        p5 += [(gcol(k), v("ID32"), v("RG%d%d" % (t, h), 8 * j, 8 * j + 8)) for k, j in gd if k]
+        p5 += [(gcol(k), v(i), v("RG%d%d" % (t, h), o + 8 * j, o + 8 * j + 8)) for k, j in gd if k for i, o in (("ID", 0), ("IDK", 16))]
         group(p1, p2, p3, p4[:8], p4[8:], p5, stop=False)
-        w = 144 + 8 * len(gd); la = 128 * NAS.index(na); PP = "PP" + u
+        w = 144 + 8 * len(gd); la = 256 - na if h else na; PP = "PP" + u
         group([(v(C, 0, w), v("LAN", la, la + 128, p1=64), v("CR", 0, w, p1=64))]
               + [(v(C, 144 + 8 * i, 152 + 8 * i), v("S1C" + n, 128 * j, 128 * j + 128), v("BO")) for i, (k, j) in enumerate(gd)],
               [(vn(C, 2 + i, 8, 18), vn(CM, i, 128, 16), v("BO")) for i in range(16)])
@@ -416,9 +435,9 @@ def build():
     def guards21(t, h):
         n = str(h); sg = "SG%d%d" % (t, h)
         if t < 2:
-            ts(v("LT" + n), ends(n, 2, 2, 16), SENT, AL.is_ge, B, AL.mult); tt(v(sg), v("LT" + n), v("MJ" + n), AL.add)
+            cp(v(sg, 0, 16), v("MJ" + n)); ts(v(sg, 16, 32), ends(n, 2, 2, 16), SENT, AL.is_ge, 32768.0, AL.mult)
             return send([(v(sg), v("RG%d%d" % (t + 1, h)), 1), (v("OV%d%d" % (t, h)), v("RO%d%d" % (t + 1, h)), 1)], 3.5)
-        ts(v("LT" + n), ends(n, 2, 2, 16), SENT, AL.is_lt); tt(v(sg), v("LT" + n), v("MJ" + n), AL.mult)
+        ts(v("LT" + n), ends(n, 2, 2, 16), SENT, AL.is_lt); tt(v(sg, 0, 16), v("LT" + n), v("MJ" + n), AL.mult)
         for j in range(2):
             yg(2 - j, h, v(sg, 8 * j, 8 * j + 8), "A" + n, 128 * j)
 
@@ -450,18 +469,21 @@ def build():
         spread(v(P, 0, 4), v("BA", 0, 32), v("XA"), v("LS", 32, 34), v("MC", 0, 32), 4, LA)
         cp(v("OA", 0, 4), v(P, 0, 4)); (act if t else cp)(v("EA"), ind(node(t), v("OA", 0, 4)))
         tt(v("N01"), v("XX", 0, 16), v("XX", 8, 24), AL.is_equal)
-        mms([(v(P, 192 + 64 * w, 256 + 64 * w, p1=8), lo(x), i64) for w, x in enumerate((xb, xa))], True, True, True)
-        vt = v("VTH", p1=8)
-        act(vt, v(P, 192, 320, p1=8))
+        mms([(v(P, 192 + 64 * w, 256 + 64 * w, p0=64, p1=72), lo(x), i64) for w, x in enumerate((xb, xa))]
+            + [(v(P, 320, 328, p0=64 * w, p1=64 * w + 64), i64, lo(x)) for w, x in enumerate((xb, xa))], True, True, True)
+        act(v("VTH", p0=64, p1=72), v(P, 192, 320, p0=64, p1=72)); scale(v("NX"), v(P, 320, 328), -1.0)
         for c in range(2):
             Y = "Y%d" % c
-            group([(v(Y), vt, v("NSEL", 512 * c, 512 * c + 512, p1=8))]
-                  + [(v(Y, 128 * j, 128 * j + 128), v("SEL", 512 * c + 128 * j, 512 * c + 128 * j + 128, p1=8), vt) for j in range(4)])
-            tt(v("CMM", 512 * c, 512 * c + 512), v(Y), v("TRM"), AL.is_equal)
+            mms([(v(Y, 128 * j, 128 * j + 128), v("SEL", 512 * c + 128 * j, 512 * c + 128 * j + 128, p1=72), v("VTH", p1=72)) for j in range(4)], True, True, True)
+            for j in range(4):
+                o = 512 * c + 128 * j; nx = v("NX", 4 * c + j, 4 * c + j + 1)
+                if EQS[2 * t + c]: act(v("AB", o, o + 128), v(Y, 128 * j, 128 * j + 128), AF.Abs, bias=nx)
+                else: ts(v("CMM", o, o + 128), v(Y, 128 * j, 128 * j + 128), nx, AL.add, 0.0, AL.is_equal)
+            if EQS[2 * t + c]: act(v("CMM", 512 * c, 512 * c + 512), v("AB", 512 * c, 512 * c + 512), AF.Relu, bias=1.0, scale=-2.0)
 
-    def step3(t):
+    def step3(t, u):
         ph[0] = "s%d" % t; even = t % 2 == 0; e = t // 2; ea, eb = v("EA"), v("EB"); nr3 = 3 if even else 2
-        cp(eb, v("E160", 0, 64)); act(fr, ea if even else eb, AF.Relu, bias=1.0, scale=-1.0)
+        cp(eb, v("E16" + u, 0, 64)); act(fr, ea if even else eb, AF.Relu, bias=1.0, scale=-1.0)
         mms([(v(P, 64, 128), v("T2"), fr)] + ([(v(P, 128, 192), v("TRI"), fr)] if even else []), True, True, True)
         act(v("TA"), v(P, 64, 128), AF.Relu, bias=-63.0, scale=-1.0)
         if even: act(v("PLF"), v(P, 128, 192), AF.Identity, bias=-33.0)
@@ -491,10 +513,10 @@ def build():
         group([(v(P, 64, 128), dg(3), v("CUT")), (v(P, 64, 128), dg(2), x)]); group([(v(P, 128, 192), dg(1), v("CUT")), (v(P, 128, 192), dg(0), x)])
         act(v("CH"), v(P, 64, 192))
         d = v(P, 384, 448)
-        na = NA[t][2][0]
-        group([(d, v("WT", 144 * e + 15 - j, 144 * e + 143 - j), vn("RD0", j, 64, 16)) for j in range(15)]
-              + ([(v(P, 384 + na, 448), v("WX", 128 * e, 128 * e + 128), v("XZ%d" % t, na, LA))] if na < LA else [])
-              + [(d, v("WT", 144 * e, 144 * e + 128), vn("RD0", 15, 64, 16))])
+        nf = min(LA, 128 - NA[t][2][0])
+        group([(d, v("WT", 144 * e + 15 - j, 144 * e + 143 - j), vn("RD" + u, j, 64, 16)) for j in range(15)]
+              + [(v(P, 384, 384 + nf), v("WX", 128 * e, 128 * e + 128), v("XZ%d" % t, 0, nf))]
+              + [(d, v("WT", 144 * e, 144 * e + 128), vn("RD" + u, 15, 64, 16))])
         ts(v("TR"), d, 1.5 * 2 ** 33, AL.add, 1.5 * 2 ** 33, AL.subtract); ts(v("GO"), d, -512.0, AL.is_ge)
         tt(v("N8"), d, v("TR"), AL.is_lt); tt(v("STR"), v("N8"), v("GO"), AL.is_gt)
         mm(v(P, 256, 320), v("T1B"), v("STR"))
@@ -514,13 +536,14 @@ def build():
     def commit(t):
         ph[0] = "s%d" % t; even = t % 2 == 0
         for a, b in ((4, 12), (0, 4)) if even else ((0, 8),):
-            cp(ind(v("DD", Q * t, Q * t + WIN), v("OSC", a, b)), v("YAB", 16 * a, 16 * b))
+            cp(ind(v("DD", Q * min(t, LASTD), Q * min(t, LASTD) + WIN), v("OSC", a, b)), v("YAB", 16 * a, 16 * b))
         if even:
             for base in ((0, R1, R2) if t == 0 else (RO,)):
-                n = 4 if base == R2 else 8
+                n = 4 if base in (R1, R2) else 8
                 cp(ind(v("W1", base, base + WIN), v("OSC", 4, 4 + n)), v("CH", 0, 16 * n))
+            if t == 0: act(v("W1", R1 + BASE, R1 + BASE + LA), v("W1", BASE, BASE + LA))
         ph[0] = "c"
-        if t < 2: copy(v("DD", Q * t + Q, Q * t + 2 * Q), v("DD", Q * t, Q * t + Q))
+        if t < LASTD: copy(v("DD", Q * t + Q, Q * t + 2 * Q), v("DD", Q * t, Q * t + Q))
         if t == 0: copy(v("W1", RO, RO + Q), v("W1", 0, Q)); act(v("W1", RO, RO + 1), v("RZ"))
 
     for t in range(3):
@@ -531,13 +554,15 @@ def build():
                 walk(t, s, h)
                 if s == 1: guards21(t, h)
         source(t)
-        walk(t, 0, 0); step3(t); ph[0] = "w%d0" % t; guard0(t, 0)
+        walk(t, 0, 0, lambda u: step3(t, u))
+        if not aside(t, 0, 0): step3(t, "0")
+        ph[0] = "w%d0" % t; guard0(t, 0)
         walk(t, 0, 1); guard0(t, 1)
         commit(t)
         if t == 0: repeat(2, [])
     ph[0] = "o"
     dma("S", lambda T: T.yr[:, :], lambda T: T.W1[:, RO:RO + Q], [v("W1", RO, RO + Q)], [], 524288)
-    dma("S", lambda T: T.yn[:, :], lambda T: T.DD[:, 2 * Q:3 * Q], [v("DD", 2 * Q, 3 * Q)], [], 1048576)
+    dma("S", lambda T: T.yn[:, :], lambda T: T.DD[:, LASTD * Q:LASTD * Q + Q], [v("DD", LASTD * Q, LASTD * Q + Q)], [], 1048576)
     dma("S", lambda T: T.yg[:, :], lambda T: T.YG[0:8, :], [v("YG", p1=8)], [], 25000)
     return ops
 
@@ -574,9 +599,11 @@ def depend(ops):
 
 
 def turns(ops, hard, seq):
-    hard = [set(h) for h in hard]; bank = {}
+    hard = [set(h) for h in hard]; bank = {}; sent = []
     for i in seq:
         o = ops[i]
+        if o["kind"] == "s": sent = [i]
+        if "bulk" in o: hard[i].update(sent)
         if "dyn" in o:
             b = bank.setdefault(o["dyn"], {})
             hard[i].update(j for e, j in b.items() if e != o["eng"])
@@ -585,7 +612,7 @@ def turns(ops, hard, seq):
 
 
 def costs(ops, m):
-    return [c[0] + m["cy"] * (c[1] + m["g"] * c[2] + m["sc"] * c[3] + m["pe"] * c[4]) for c in (o["cost"] for o in ops)]
+    return [c[0] * (m["far"] if k in "rs" else 1) + m["cy"] * (c[1] + m["g"] * c[2] + m["sc"] * c[3] + m["pe"] * c[4]) for c, k in ((o["cost"], o["kind"]) for o in ops)]
 
 
 def order(ops, hard, soft, m, tune):
@@ -645,21 +672,131 @@ def order(ops, hard, soft, m, tune):
     return best[1]
 
 
+def renew(ops, hard, soft, seq, m, tune):
+    n = len(ops); LAT = m["lat"]; cost = costs(ops, m)
+    eng = ["VAPGSR".index(o["eng"]) for o in ops]; dyn = ["dyn" in o for o in ops]; bulk = ["bulk" in o for o in ops]; out = [o["kind"] == "s" for o in ops]
+    dm = [o["nbytes"] / m["bw"] if o["kind"] == "d" else -1.0 for o in ops]; src = [o.get("src", -1) for o in ops]
+    dur = [c + (d + 1.5 if d >= 0 else 0) for c, d in zip(cost, dm)]
+    hp = [list(h) for h in hard]; pred = [list(hard[i] | soft[i]) for i in range(n)]; succ = [[] for _ in ops]
+    for i in range(n):
+        for j in pred[i]: succ[j].append((i, LAT if j in hard[i] else 0.0))
+
+    def run(part, state, end):
+        free, bank, bus, top, sent = state; free = free[:]; bank = bank[:]
+        for i in part:
+            e = eng[i]
+            if e == 5:
+                t = end[src[i]]
+                if bus > t: t = bus
+            else:
+                t = free[e]
+                if out[i]: sent = i
+                elif bulk[i] and sent >= 0 and end[sent] + 1.0 > t: t = end[sent] + 1.0
+            for j in hp[i]:
+                x = end[j] + LAT
+                if x > t: t = x
+            if dyn[i]:
+                for e2 in (0, 1, 2):
+                    if e2 != e and bank[e2] + LAT > t: t = bank[e2] + LAT
+                bank[e] = t + cost[i]
+            t += cost[i]; free[e] = t
+            if dm[i] >= 0:
+                bus = (bus if bus > t else t) + dm[i]; t = bus + 1.5
+            end[i] = t
+            if t > top: top = t
+        return free, bank, bus, top, sent
+    zero = ([0.0] * 6, [-1.0] * 3, 0.0, 0.0, -1); STEP = 32
+
+    def settle(seq):
+        end = [0.0] * n; run(seq, zero, end)
+        s2 = sorted(range(n), key=lambda p: (end[seq[p]] - dur[seq[p]] if eng[seq[p]] != 5 else end[src[seq[p]]] - cost[src[seq[p]]], p))
+        seq = [seq[p] for p in s2]; marks = [zero]
+        for p in range(0, n, STEP): marks.append(run(seq[p:p + STEP], marks[-1], end))
+        q = [0.0] * n; nx = [0.0] * 6
+        for i in reversed(seq):
+            t = nx[eng[i]] + cost[i] if eng[i] != 5 else 0.0; u = 0.0
+            for j, w in succ[i]:
+                if q[j] + w > u: u = q[j] + w
+            u += dur[i]
+            q[i] = nx[eng[i]] = t if t > u else u
+        return seq, end, marks, q
+    r = [tune["seed"] * 7919 + 1]
+
+    def rnd():
+        r[0] = (r[0] * 1103515245 + 12345) % 2147483648
+        return (r[0] + 1) / 2147483649
+    seq, end, marks, q = settle(seq); cur = marks[-1][3]; best = (cur, seq); its = tune["renew"]
+    for it in range(its):
+        k0 = int(rnd() * (n // STEP)); p0 = k0 * STEP; p1 = min(n, p0 + int(tune["w0"] + rnd() * tune["w1"])); win = seq[p0:p1]; ins = set(win)
+        noise = tune["noise"] * rnd(); look = rnd() * tune["look"]; pr = {}
+        for i in reversed(win):
+            u = 0.0
+            for j, w in succ[i]:
+                x = (pr[j] if j in ins else q[j]) + w
+                if x > u: u = x
+            pr[i] = u + dur[i]
+        key = {i: pr[i] + noise * rnd() for i in win}
+        left = {i: sum(1 for j in pred[i] if j in ins) for i in win}
+        e2 = end[:]; state = marks[k0]; new = []; ready = {}
+
+        def when(i):
+            t = 0.0
+            for j in hp[i]:
+                if e2[j] + LAT > t: t = e2[j] + LAT
+            return t
+        for i in win:
+            if left[i] == 0: ready[i] = when(i)
+        while ready:
+            free, bank = state[0], state[1]; b = 1e9
+            for i, t in ready.items():
+                e = eng[i]
+                if free[e] > t and e != 5: t = free[e]
+                if dyn[i]:
+                    for x in (0, 1, 2):
+                        if x != e and bank[x] + LAT > t: t = bank[x] + LAT
+                if e == 5: b = -1.0; bi = i; break
+                if t < b: b = t; bi = i
+            if b >= 0:
+                e = eng[bi]; lim = b + look * cost[bi] + 0.02; k = key[bi]
+                for i, t in ready.items():
+                    if eng[i] == e and t <= lim and key[i] > k: bi = i; k = key[i]
+            del ready[bi]; new.append(bi); state = run((bi,), state, e2)
+            for j, w in succ[bi]:
+                if j in ins:
+                    left[j] -= 1
+                    if left[j] == 0: ready[j] = when(j)
+        if new == win: continue
+        val = run(seq[p1:], state, e2)[3]
+        if val <= cur - (tune["warm"] * (1 - it / its) + 0.003) * math.log(rnd()):
+            seq, end, marks, q = settle(seq[:p0] + new + seq[p1:]); cur = marks[-1][3]
+            if cur < best[0]: best = (cur, seq)
+    return best[1]
+
+
+def plan(ops, hard, soft, m, tune):
+    return polish(ops, hard, soft, renew(ops, hard, soft, order(ops, hard, soft, m, tune), m, tune), m, tune)
+
+
 def polish(ops, hard, soft, seq, m, tune):
     n = len(ops); LAT = m["lat"]; cost = costs(ops, m); STEP = 64
-    eng = ["VAPGSR".index(o["eng"]) for o in ops]; dyn = ["dyn" in o for o in ops]
+    eng = ["VAPGSR".index(o["eng"]) for o in ops]; dyn = ["dyn" in o for o in ops]; bulk = ["bulk" in o for o in ops]; out = [o["kind"] == "s" for o in ops]
     dm = [o["nbytes"] / m["bw"] if o["kind"] == "d" else -1.0 for o in ops]; src = [o.get("src", -1) for o in ops]
     hp = [list(h) for h in hard]; pred = [hard[i] | soft[i] for i in range(n)]; succ = [set() for _ in ops]
     for i in range(n):
         for j in pred[i]: succ[j].add(i)
 
     def run(seq, k0, end, by, marks):
-        free, lastq, bank, bl, bus, top, arg = marks[k0]; free = free[:]; lastq = lastq[:]; bank = bank[:]; bl = bl[:]; marks = marks[:k0 + 1]
+        free, lastq, bank, bl, bus, top, arg, sent, bb = marks[k0]; free = free[:]; lastq = lastq[:]; bank = bank[:]; bl = bl[:]; marks = marks[:k0 + 1]
         for p in range(k0 * STEP, n, STEP):
             for i in seq[p:p + STEP]:
                 e = eng[i]
-                if e == 5: b = src[i]; t = end[b]
-                else: t = free[e]; b = lastq[e]
+                if e == 5:
+                    b = src[i]; t = end[b]
+                    if bus > t: t = bus; b = bb
+                else:
+                    t = free[e]; b = lastq[e]
+                    if out[i]: sent = i
+                if bulk[i] and sent >= 0 and end[sent] + 1.0 > t: t = end[sent] + 1.0; b = sent
                 for j in hp[i]:
                     x = end[j] + LAT
                     if x > t: t = x; b = j
@@ -669,10 +806,11 @@ def polish(ops, hard, soft, seq, m, tune):
                     bank[e] = t + cost[i]; bl[e] = i
                 t += cost[i]; free[e] = t; lastq[e] = i
                 if dm[i] >= 0:
-                    bus = (bus if bus > t else t) + dm[i]; t = bus + 1.5
+                    if bus > t: t = bus; b = bb
+                    bus = t + dm[i]; t = bus + 1.5; bb = i
                 end[i] = t; by[i] = b
                 if t > top: top = t; arg = i
-            marks.append((free[:], lastq[:], bank[:], bl[:], bus, top, arg))
+            marks.append((free[:], lastq[:], bank[:], bl[:], bus, top, arg, sent, bb))
         return top, arg, marks
 
     def links(i, by):
@@ -681,8 +819,8 @@ def polish(ops, hard, soft, seq, m, tune):
             if by[i] not in pred[i]: out.append((by[i], i))
             i = by[i]
         return out
-    r = tune["seed"] * 7919 + 1; end = [0.0] * n; by = [-1] * n; its = tune["polish"]
-    cur, arg, marks = run(seq, 0, end, by, [([0.0] * 6, [-1] * 6, [-1.0] * 3, [-1] * 3, 0.0, 0.0, -1)])
+    r = 1; end = [0.0] * n; by = [-1] * n; its = tune["polish"]
+    cur, arg, marks = run(seq, 0, end, by, [([0.0] * 6, [-1] * 6, [-1.0] * 3, [-1] * 3, 0.0, 0.0, -1, -1, -1)])
     best = (cur, seq); lk = links(arg, by)
     for it in range(its):
         r = (r * 1103515245 + 12345) % 2147483648
@@ -714,7 +852,7 @@ def rank_program(g, core, T, topo):
         return
     if "ops" not in PLAN:
         PLAN["ops"] = build(); PLAN["hard"], soft = depend(PLAN["ops"])
-        PLAN["seq"] = polish(PLAN["ops"], PLAN["hard"], soft, order(PLAN["ops"], PLAN["hard"], soft, MODEL, TUNE), MODEL, TUNE)
+        PLAN["seq"] = plan(PLAN["ops"], PLAN["hard"], soft, MODEL, TUNE)
         PLAN["hard"] = turns(PLAN["ops"], PLAN["hard"], PLAN["seq"])
     ops, hard = PLAN["ops"], PLAN["hard"]; cores = T.cores; N = len(cores)
 

@@ -3,11 +3,16 @@ from concourse.bass import DstId, RemoteDMATransfer
 from concourse.mybir import AluOpType as AL, ActivationFunctionType as AF
 
 M, Q, BASE, L, LA = 4096, 2048, 1920, 256, 64
-NA = [[(64, 48), (64, 48), (64, 64)]] * 3
-CUT = (96, 64)
+LAY = [[("b32 c32 a64", "a32 c16 b80"), ("b32 c32 a64", "a32 c16 b80"), ("b32 a32 c64", "a32 c16 b80")]] * 3
+CUT = dict(a=(96, 32), b=(32, 32), c=(48, 64), g=(32, 56))
+REP, VREP = ((0, 256),), (0, 0)
+RB, FAR = 2, 3.3
+GF, AREP = (1, 0, 0), 4
 FAST = (1, 1)
-MODEL = dict(cy=0.95e-3, g=1.56, sc=3.8, pe=0.5, lat=0.17, bw=330e3, far=1.3)
-TUNE = dict(slack=0.05, seed=1, fb=30, moves=4, step=3, renew=5000, w0=30, w1=80, noise=4, look=0.7, warm=0.2, polish=15000, heat=0.1)
+MODEL = dict(cy=0.95e-3, g=1.56, sc=3.8, pe=0.5, lat=0.17, bw=330e3, dl=1.5, far=1.3)
+TUNE = dict(slack=0.05, seed=1, fb=60, moves=4, step=4, renew=0, w0=30, w1=80, noise=4, look=0.7, warm=0.06, polish=0, heat=0.03, rounds=1, hope=0.03, age=4, sweeps=260, cool=0.04, wide=20, tries=20, soft=0.3, lays=3, narrow=24,
+            also=[dict(cy=.9e-3, g=1.35, lat=.18, far=1.25), dict(cy=1.08e-3, g=1.75, lat=.13, far=1.0, sc=4.5)])
+FIRST = 1.5
 PIECE, LASTD = 4096, 2
 TT2 = 1.0
 EQS = (0, 0, 0, 0, 0, 0)
@@ -18,39 +23,37 @@ SENT, SENT2 = 4096.0 * 4081, 4096.0 * 4082
 R1, R2, WW, DUM = 4096, 8192, 10240, 6144
 WIN = DUM + 12 * LA
 RO = R1 + WIN
-NV = [max(NA[t][s][h] for t in range(3) for s in range(3)) for h in range(2)]
-X0, XW = 128 - NV[0], NV[0] + NV[1]
 SEG = {(2, 0): 0, (2, 1): 144, (2, 2): 288, (1, 1): 432, (1, 0): 576, (0, 0): 720}
 F, H, BF, U, I = "float32", "float16", "bfloat16", "uint16", "int32"
 SB = {
     "W0": (WW, BF), "W1": (RO + WIN, BF), "DI": (BASE, I), "DD": (2 * Q + WIN, F), "VSI": (48, I), "VSF": (48, F),
-    "XZ0": (L, BF), "XZ1": (L, BF), "XZ2": (L, BF), "XB0": (16 * XW, BF), "XB1": (16 * XW, BF), "XB2": (16 * XW, BF), "NXT": (768, BF),
+    "XZ0": (L, BF), "XZ1": (L, BF), "XZ2": (L, BF), "XB0": (16 * L, BF), "XB1": (16 * L, BF), "XB2": (16 * L, BF),
     "VU": (96, U), "VL": (48, F), "VU1": (32, U), "VL1": (16, F), "VU2": (32, U), "VL2": (16, F),
     "SA0": (8, F), "SA1": (8, F), "RA1": (8, F), "RA2": (8, F), "YG": (768, F), "RZ": (1, BF), "NM": (192, I),
     "ONE": (128, BF), "ONE32": (128, F), "ID": (128, BF), "NID": (128, BF), "ID32": (128, F), "ID64N": (128, BF), "IDK": (128, BF), "I2N": (128, BF),
-    "BOF": (128, BF), "NBOF": (128, BF), "BO": (8, BF), "BO32": (8, F), "BO16": (8, H), "SC3H": (24, H), "EXP": (2048, BF),
+    "BOF": (128, BF), "NBOF": (128, BF), "BO32": (8, F), "SC3H": (24, H), "SCL": (18, F),
     "TRI": (128, BF), "TRE": (128, BF), "T1": (128, BF), "T1B": (128, BF), "T2": (128, BF), "RBP": (2048, BF), "WD": (432, F),
-    "WT": (288, BF), "WE": (2, F), "WX": (256, BF), "NLH": (16, H), "XA": (8, F), "TR": (64, F), "WC": (32, F), "DG": (1024, BF), "SEL": (1024, BF), "AB": (1024, BF), "NX": (8, F), "TRM": (128, BF), "VB": (768, F),
-    "PB": (144, BF), "P16": (144, H), "WP": (432, BF), "KC": (576, BF), "CR": (160, BF), "LAN": (384, BF), "MK": (128, F), "II": (128, I), "IJ": (128, I),
-    "LI": (64, I), "LJ": (16, I), "LK": (16, I), "LS": (64, U), "DUMC": (24, F), "NC": (128, F), "NL": (16, F), "NB": (2, F), "CB2": (24, BF),
+    "WT": (288, BF), "WE": (2, F), "WX": (256, BF), "NLH": (16, H), "XA": (8, F), "TR": (64, I), "WC": (16, F), "DG": (512, BF), "SEL": (1024, BF), "AB": (1024, BF), "NX": (8, F), "TRM": (128, BF), "VB": (384, H),
+    "WP": (720, BF), "KC": (576, BF), "CR": (160, BF), "LAN": (384, BF), "MK": (128, F), "II": (128, I), "IJ": (128, I),
+    "LI": (64, I), "LJ": (16, I), "LK": (16, I), "LS": (64, U), "DUMC": (24, F), "NC": (128, BF), "NL": (16, F), "NB": (2, F), "CB2": (24, BF),
     "CMP": (32, F), "MC": (96, BF), "GSEL": (240, BF),
     "XX": (24, H), "FL": (8, I), "A2": (8, F), "DV": (8, F), "NW": (8, F), "TQ": (8, F), "BA": (96, H), "OA": (8, U), "EA": (64, F), "EB": (64, F),
     "FR": (64, BF), "N01": (16, BF), "NZ0": (8, BF), "ASK": (32, BF), "VTH": (128, H), "PLF": (64, BF), "CMM": (1024, BF), "W3": (24, F), "OSC": (12, U),
-    "JK": (8, F), "ASUM": (1, F), "AI": (1, I), "STR": (64, BF), "GO": (64, BF), "N8": (64, BF), "NU": (64, F), "Y2": (1024, F), "YI": (64, I),
-    "YAB": (192, I), "TA": (64, F), "TB": (64, F), "TC": (64, F), "CUT": (64, BF), "CH": (128, BF), "BC": (128, F), "E0": (64, F),
+    "JK": (8, F), "ASUM": (1, F), "AI": (1, I), "STR": (64, BF), "GO": (64, BF), "NU": (64, F), "Y2": (1024, F), "YI": (64, I),
+    "YAB": (192, I), "TA": (64, BF), "TB": (64, F), "TC": (64, F), "TD": (64, BF), "CUT": (64, H), "CH": (128, BF), "BC": (128, F),
     "ZP": (32, F), "NZ": (32, F), "VV": (32, F), "UU": (32, F), "GP": (32, F), "AP": (32, F),
 }
 for _h in "01":
-    SB.update({"E16" + _h: (128, U), "FK" + _h: (384, H), "MM" + _h: (256, BF), "RD" + _h: (2048, H), "CM" + _h: (2048, BF), "PP" + _h: (160, BF),
+    SB.update({"E16" + _h: (128, U), "FK" + _h: (512, H), "RD" + _h: (2048, H), "CM" + _h: (2048, BF), "PP" + _h: (160, BF),
                "SC" + _h: (864, I), "D1" + _h: (864, F), "MJ" + _h: (16, I), "A1" + _h: (8, I), "B1" + _h: (8, F), "GE" + _h: (8, F), "ZZ" + _h: (32, F),
                "BV" + _h: (128, H), "BG" + _h: (128, F), "LT" + _h: (16, F), "S1R" + _h: (384, BF), "S1C" + _h: (384, BF)})
     for _t in range(3):
-        SB.update({"OV%d" % _t + _h: (32, U), "SG%d" % _t + _h: (32, H), "GS%d" % _t + _h: (32, F)})
+        SB.update({"OV%d" % _t + _h: (48, U), "SG%d" % _t + _h: (32, H), "GS%d" % _t + _h: (32, F)})
     for _t in range(2):
-        SB.update({"SO%d" % _t + _h: (64, U), "RG%d" % (_t + 1) + _h: (32, H), "RO%d" % (_t + 1) + _h: (32, U),
-                   "RS%d" % (_t + 1) + _h: (32, F), "RP%d" % (_t + 1) + _h: (64, U)})
+        SB.update({"SO%d" % _t + _h: (16, U), "RG%d" % (_t + 1) + _h: (32, H), "RO%d" % (_t + 1) + _h: (48, U),
+                   "RS%d" % (_t + 1) + _h: (8, F), "RP%d" % (_t + 1) + _h: (16, U)})
 for _h in "23":
-    SB.update({"E16" + _h: (128, U), "FK" + _h: (128, H), "MM" + _h: (128, BF), "RD" + _h: (2048, H), "CM" + _h: (2048, BF), "PP" + _h: (160, BF)})
+    SB.update({"E16" + _h: (128, U), "FK" + _h: (256, H), "RD" + _h: (2048, H), "CM" + _h: (2048, BF), "PP" + _h: (160, BF)})
 DYN = ("A0",)
 PS = ["K0", "K1", "A0", "B0", "A1", "B1", "Y0", "Y1"]
 POOL, FILL = {}, {}
@@ -58,14 +61,14 @@ for _k, (_n, _d) in SB.items():
     if _n <= 640 and _k[:2] not in ("VU", "VL", "SG", "SO", "SA", "RG", "RO", "RA", "VS", "OV", "GS", "RS", "RP", "XZ") or _k == "GSEL":
         POOL[_k] = ("pool_" + _d, FILL.get(_d, 0)); FILL[_d] = FILL.get(_d, 0) + (_n + 31) // 32 * 32
 SCRATCH = {"pool_" + d: ("sbuf", [128, n], d) for d, n in FILL.items()}
-SENTU = ["VU"] + [n + str(t) + h for n in ("OV", "SO") for t in range(2) for h in "01"]
+SENTU = ["VU"]
 for _k in SENTU:
     POOL[_k] = ("sent", FILL.get("sent", 0)); FILL["sent"] = FILL.get("sent", 0) + SB[_k][0]
 SCRATCH["sent"] = ("sbuf", [128, FILL["sent"]], U)
 SCRATCH.update({k: ("sbuf", [128, n], d) for k, (n, d) in SB.items() if k not in POOL})
 SCRATCH.update({k: ("psum", [128, 512], F) for k in PS})
-SEMAPHORES = ["qV", "qA", "qP", "qG"] + ["d%d" % i for i in range(40)] + ["r%d" % i for i in range(24)] + ["l%d" % i for i in range(12)]
-QSEM = {"V": "qV", "A": "qA", "P": "qP", "G": "qG"}
+SEMAPHORES = ["qV", "qA", "qP"] + ["d%d" % i for i in range(40)] + ["r%d" % i for i in range(24)] + ["l%d" % i for i in range(12)] + ["g%d" % i for i in range(48)]
+QSEM = {"V": "qV", "A": "qA", "P": "qP"}
 PLAN = {}
 
 
@@ -86,6 +89,22 @@ def lo(x):
 def cuts(a, b, most):
     n = (b - a + most - 1) // most
     return [(a + (b - a) * j // n // 2 * 2, a + (b - a) * (j + 1) // n // 2 * 2) for j in range(n)]
+
+
+def lanes(t, s, h, kinds):
+    out = []; a = 0
+    for x in LAY[t][2 - s][h].split():
+        if x[0] in kinds: out += cuts(a, a + int(x[1:]), CUT[x[0]][h])
+        a += int(x[1:])
+    return out
+
+
+def joined(pieces, most):
+    out = []
+    for a, b in pieces:
+        if out and out[-1][1] == a and b - out[-1][0] <= most: out[-1][1] = b
+        else: out.append([a, b])
+    return out
 
 
 def ind(w, o):
@@ -116,7 +135,7 @@ def wide(x):
 
 def build():
     ops = []
-    nd, nr, nl, last, ph = [0], [0], [0], [], ["i"]
+    nd, nr, nl, ng, last, ph = [0], [0], [0], [0], [], ["i"]
 
     def add(eng, fn, rd, wr, cost, **kw):
         r2, w2 = [], []
@@ -129,6 +148,8 @@ def build():
             else:
                 w2.append(x)
         o = dict(eng=eng, no=len(ops), fn=fn, rd=r2, wr=w2, cost=cost, kind="c", after=[], ph=ph[0])
+        if eng == "G" and "kind" not in kw:
+            o.update(sem="g%d" % ng[0], cnt=1); ng[0] += 1
         o.update(kw)
         ops.append(o)
         return len(ops) - 1
@@ -235,7 +256,7 @@ def build():
                     return g.remote_dma(ap(T, d), ap(T, s), T.sem[rs[0]], T.sem[ls], pid, rid, mask)
                 tr.append(RemoteDMATransfer(dst_ids=[DstId(rid=rid, pnc=pid)], dma_engine_mask=mask, remote_sem=T.sem[rs[j]], src=ap(T, s), dst=ap(T, d)))
             return g.remote_dma_fused(tr, local_sem=T.sem[ls])
-        i = add("G", fn, [s for s, d, k in items], [], (1.0, 0, 0, 0, 0), kind="s", sem=ls, ks=ks, wait=list(wait))
+        i = add("G", fn, [s for s, d, k in items], [], (1.0 if nl[0] > 1 else FIRST, 0, 0, 0, 0), kind="s", sem=ls, ks=ks, wait=list(wait))
         for j, (s, d, k) in enumerate(items):
             add("R", None, [], [d], (lat, 0, 0, 0, 0), kind="r", sem=rs[j], ks=ks, k=k, src=i)
         return i
@@ -246,6 +267,7 @@ def build():
     dma("S", lambda T: T.DI[:, :], lambda T: T.nd[:, :], [], [v("DI")], 983040, True)
     loaded = dma("S", lambda T: T.W0[:, Q:M], lambda T: T.rg[:, Q:M], [], [v("W0", Q, M)], 524288, True)
 
+    NB = [[sum(b - a for a, b in lanes(t, s, h, "b")) for t in range(3) for s in range(3)] for h in range(2)]
     ms(v("ONE"), 1.0); ms(v("ONE32"), 1.0)
     iota(v("II"), [[0, 8], [-1, 16]], 128, 1)
     iota(v("LI", 0, 24), [[1, 24]], 0, 0); iota(v("LI", 24, 32), [[4, 8]], 3, 0)
@@ -256,58 +278,65 @@ def build():
     ts(v("MK"), v("IJ"), 0.0, AL.is_equal)
     sel(v("BOF"), v("ONE"), [[-16, 8], [0, 16]], AL.is_ge, 0, 1); sel(v("BOF"), v("BOF"), [[16, 8], [0, 16]], AL.is_ge, 15, -1)
     sel(v("ID"), v("ONE"), [[-1, 128]], AL.is_equal, 0, 1)
-    ms(v("PB"), 1.0); sel(v("PB"), v("PB"), [[-16, 8], [-1, 18]], AL.is_equal, 2, 1); ms(vn("PB", 0, 8, 18), 0.0); ms(vn("PB", 1, 8, 18), 0.0)
+    pb = v("WP", 288, 432)
+    ms(pb, 1.0); sel(pb, pb, [[-16, 8], [-1, 18]], AL.is_equal, 2, 1); ms(vn("WP", 288, 8, 18), 0.0); ms(vn("WP", 289, 8, 18), 0.0)
     bo = vn("BOF", 0, 8, 16)
-    act(v("BO"), bo); act(v("BO32"), bo); act(v("BO16"), bo)
+    act(v("BO32"), bo)
     for j in range(3):
         scale(v("SC3H", 8 * j, 8 * j + 8), bo, -4096.0)
     scale(v("NID"), v("ID"), -1.0); act(v("ID32"), v("ID")); scale(v("IDK"), v("ID"), 4096.0)
-    act(v("P16"), v("PB")); scale(v("WP", 0, 144), v("PB"), B); scale(v("WP", 144, 288), v("PB"), -B); scale(v("WP", 288, 432), v("PB"), B)
+    for j, f in ((0, -B), (1, B), (3, 1.0), (4, B)):
+        scale(v("WP", 144 * j, 144 * j + 144), pb, f)
     ms(v("GSEL"), 0.0); act(v("GSEL", 112, 128), v("MK", 0, 16))
     gsel = lambda g, p1: v("GSEL", 112 - 16 * g, 240 - 16 * g, p1=p1)
-    ms(v("KC", 0, 288, p1=32), 0.0); ms(v("KC", 288, 576, p1=32), B / 32); ms(vn("KC", 145, 8, 18, 0, 32), B / 32); ms(vn("KC", 433, 8, 18, 0, 32), 0.0)
+    ms(v("KC", 0, 288, p1=32), 64.0); ms(v("KC", 288, 576, p1=32), 64 * B); ms(vn("KC", 1, 8, 18, 0, 32), B / 32); ms(vn("KC", 145, 16, 18, 0, 32), 0.0)
     ms(vn("KC", 0, 32, 18, 0, 32), NEG / 32)
-    ms(v("KC", p0=32, p1=64), 64.0); ms(vn("KC", 0, 32, 18, 32, 64), 0.0); ms(vn("KC", 1, 32, 18, 32, 64), 0.0)
-    kc = lambda cand, guard: v("KC", 144 * ((2 * cand) + (cand ^ guard)), 144 * ((2 * cand) + (cand ^ guard)) + 144, p1=64)
-    ms(v("CR", p1=32), 1.0); ms(v("CR", p0=32, p1=64), -6.0 / 32); ms(v("CR", 144, 160, p1=32), 0.0)
+    kc = lambda cand, guard: v("KC", 144 * (2 + guard if cand else 1 - guard), 144 * (3 + guard if cand else 2 - guard), p1=32)
+    ms(v("CR", p1=32), 5.0 / 16); ms(v("CR", p0=32, p1=64), -6.0 / 32); ms(v("CR", 144, 160, p1=32), -1.0 / 16)
+    ms(v("SCL"), -B); sel(v("SCL", 0, 9), v("SCL", 0, 9), [[-16, 9]], AL.is_ge, 0, 1, -B / 2); sel(v("SCL", 9, 18), v("SCL", 9, 18), [[-16, 9]], AL.is_gt, 128, -1, -B / 2)
     for j in range(2):
-        ms(vn("CR", j, 8, 18, 0, 32), 0.0); ms(vn("CR", j, 8, 18, 32, 64), 2.0)
-    ms(v("LAN", p0=32, p1=64), 1.0); ms(v("LAN", p1=32), 0.0); ms(v("LAN", 128, 256, p1=32), -0.5)
-    for h in "01":
-        iota(v("D1" + h), [[0, 864]], 1 - 2 ** 24, 0); ms(vn("D1" + h, 0, 8, 18), SENT); ms(vn("D1" + h, 144, 8, 18), SENT2)
-    ms(v("NM"), 0); ms(v("CMP"), 0.0); ms(vn("CMP", 0, 8, 4), -1.0)
-    xb0 = ("XB0", 0); ms(v("W0", R1 + Q, R2), 0.0); ms(v("DD", BASE, Q), 0.0)
+        ms(vn("CR", j, 8, 18, 32, 64), 2.0)
+    l0, l1 = 128 - max(NB[0]), 256 + max(NB[1])
+    ms(v("LAN", l0, l1, p0=32, p1=64), 1.0); ms(v("LAN", l0, l1, p1=32), 0.0); ms(v("LAN", 128, 256, p1=32), -0.5)
+    move = lambda out, a: dma("S", lambda T: ap(T, out), lambda T: ap(T, a), [a], [out], (a[2] - a[1]) * cols(a) * wide(a), wait=[loaded])
+    iota(v("D11"), [[0, 864]], 1 - 2 ** 24, 0); ms(vn("D11", 0, 8, 18), SENT); ms(vn("D11", 144, 8, 18), SENT2)
+    if GF[0]: iota(v("D10"), [[0, 864]], 1 - 2 ** 24, 0); ms(vn("D10", 0, 8, 18), SENT); ms(vn("D10", 144, 8, 18), SENT2)
+    else:
+        for a, b in ((0, 432), (432, 864)): act(v("D10", a, b), v("WP", 288, 720), AF.Identity, bias=1.0 - 2 ** 24, scale=0.0)
+        ms(vn("D10", 0, 8, 18), SENT); ms(vn("D10", 144, 8, 18), SENT2)
+    ms(v("NM", 0, 96), 0); ms(v("CMP"), 0.0); ms(vn("CMP", 0, 8, 4), -1.0)
+    ms(v("DD", BASE, Q), 0.0)
     for n in ("SA0", "SA1"): ms(v(n), 0.0)
     add("V", lambda g, T, c: g.vector.memset(T.sent[:, :], 0), [], [v(n) for n in SENTU], (0, FILL["sent"] / 2, 0, 0, 0))
-    for j in range(16):
-        (cp if j % 2 else act)(vn("EXP", j, 128, 16), v("ID"))
     for t in range(3):
         cp(v("VU", 32 * t, 32 * t + 16), v("VSI", 16 * t, 16 * t + 16))
     cp(v("VSF"), v("VSI"))
-    for a in range(16):
-        scale(vn("VB", a, 48, 16), v("VSF"), v("MK", a, a + 1))
+    for a in range(8):
+        scale(vn("VB", a, 48, 8), v("VSF"), v("BO32", a, a + 1))
     for j in range(6):
-        mm(v("Y0", 8 * j, 8 * j + 8), v("VB", 128 * j, 128 * j + 128), v("BO32"))
+        group([(v("Y0", 8 * j, 8 * j + 8), gsel(b, 128), v("VB", 64 * j + 8 * b, 64 * j + 8 * b + 8)) for b in range(8)])
     act(v("VL"), v("Y0", 0, 48))
     for i in range(16):
-        cp(vn(xb0[0], xb0[1] + i, XW, 16), v("XZ0", X0, X0 + XW))
+        (act if i < AREP else cp)(vn("XB0", i, L, 16), v("XZ0"))
     act(v("RZ"), v("W0", 0, 1)); ms(v("W0", 0, 1), 512.0); cp(v("W0", R1, R1 + Q), v("W0", 0, Q)); act(v("W0", R2, R2 + Q), v("W0", 0, Q))
     ph[0] = "x"
     s1 = send([(v("XZ0"), v("XZ%d" % k), k) for k in (1, 2)], 4.0, [loaded])
     s2 = send([(v("VU", 32, 64), v("VU1"), 1), (v("VL", 16, 32), v("VL1"), 1), (v("VU", 64, 96), v("VU2"), 2), (v("VL", 32, 48), v("VL2"), 2)], 4.0, [loaded])
-    copy(v("W1", 0, R1 + Q), v("W0", 0, R1 + Q), [s1, s2], 3 * PIECE); copy(v("W1", R2, WW), v("W0", R2, WW), [s1, s2]); ms(v("W1", R1 + Q, R2), 0.0)
+    copy(v("W1", 0, R1 + Q), v("W0", 0, R1 + Q), [s1, s2], 3 * PIECE); copy(v("W1", R2, WW), v("W0", R2, WW), [s1, s2])
     for a, b in ((0, 960), (960, BASE)):
         keep(v("DD", a, b), v("DI", a, b))
     ph[0] = "j"
     sel(v("TRI"), v("BOF"), [[1, 128]], AL.is_ge, 0, -1); sel(v("TRE"), v("BOF"), [[1, 128]], AL.is_gt, 0, -1)
     sel(v("T1"), v("TRI"), [[-1, 128]], AL.not_equal, 0, 1, -31.0); sel(v("T2"), v("TRE"), [[-1, 128]], AL.not_equal, 0, 1, -64.0)
-    ms(v("SEL", p0=64, p1=96), 1.0); sel(v("SEL", p0=64, p1=72), v("SEL", p0=64, p1=72), [[-1, 8], [0, 128]], AL.is_equal, 0, 1)
+    ms(v("SEL", 0, 128, p0=64, p1=96), 0.0); ms(v("SEL", 0, 128, p0=64, p1=65), 1.0)
     ms(lo(v("TRM")), 0.5); sel(lo(v("TRM")), lo(v("TRM")), [[0, 2], [-1, 64]], AL.is_ge, 0, 1); act(lo(v("VTH")), lo(v("TRM")))
     for j in range(2):
         cp(lo(v("SEL", 64 * j, 64 * j + 64)), lo(v("ID", 0, 64)))
-    for j in (128, 256, 512):
-        cp(lo(v("SEL", j, 2 * j)), lo(v("SEL", 0, j)))
-    iota(v("DUMC"), [[256, 3], [0, 8]], DUM, 4); iota(v("NC"), [[1, 128]], M + BASE, 0); iota(v("NL"), [[64, 2], [0, 8]], BASE, 1)
+    for j in (1, 2, 4):
+        move(lo(v("SEL", 128 * j, 256 * j)), lo(v("SEL", 0, 128 * j)))
+        move(v("SEL", 128 * j, 256 * j, p0=64 + j, p1=72), v("SEL", 0, 128 * j, p0=64, p1=72 - j))
+        move(v("SEL", 128 * j, 256 * j, p0=64, p1=64 + j), v("SEL", 0, 128 * j, p0=72 - j, p1=72))
+    iota(v("DUMC"), [[256, 3], [0, 8]], DUM, 4); iota(v("NC"), [[1, 128]], 0, 0); iota(v("NL"), [[64, 2], [0, 8]], BASE, 1)
     ts(v("NB"), vn("NL", 0, 2, 8), 1.0, AL.add, B, AL.mult)
     scale(v("NBOF"), v("BOF"), -1.0); scale(v("T1B"), v("T1"), B2); scale(v("ID64N"), v("ID"), -64.0)
     for j in range(2):
@@ -315,26 +344,33 @@ def build():
     for j in range(3):
         act(v("MC", 32 * j, 32 * j + 32), vn("BOF", 0, 32, 2))
     ms(v("CB2", p1=32), B2); ms(v("XX"), 0.0); ms(v("W3"), 0.0); ms(v("VV"), 0.0)
-    iota(v("WD"), [[0, 432]], 0, 0); iota(v("WT"), [[0, 288]], 0, 0)
+    for n, f in (("WD", GF[1]), ("WT", GF[2])):
+        if f: iota(v(n), [[0, SB[n][0]]], 0, 0)
+        else: scale(v(n), v("WP", 0, SB[n][0]), 0.0)
     act(vn("WD", 15, 8, 16), bo); scale(vn("WD", 16, 8, 16), bo, -1.0); act(vn("WD", 144 + 15, 8, 16), bo); scale(vn("WD", 288 + 16, 8, 16), bo, -1.0)
-    scale(v("WC", 0, 16), v("MK", 0, 16), B2); act(v("WC", 16, 32), v("MK", 0, 16), AF.Identity, bias=1.0, scale=-1.0)
-    for i in range(16):
-        ts(v("RBP", 128 * i, 128 * i + 128), v("BOF"), v("WC", i, i + 1), AL.mult)
+    act(v("WC"), v("MK", 0, 16), AF.Identity, bias=1.0, scale=-1.0)
+    for i in range(RB):
+        ts(v("RBP", 128 * i, 128 * i + 128), v("BOF"), v("MK", i, i + 1), AL.mult, B2, AL.mult)
+    for j in (1, 2, 4, 8)[RB // 2:]:
+        move(v("RBP", 128 * j, 256 * j, p0=j), v("RBP", 0, 128 * j, p1=128 - j)); move(v("RBP", 128 * j, 256 * j, p1=j), v("RBP", 0, 128 * j, p0=128 - j))
     act(v("NLH"), v("NL"))
     for e, t in enumerate((0, 2)):
-        act(v("WE", e, e + 1), v("MK", t, t + 1), AF.Identity, bias=v("MK", 8 + t, 9 + t), scale=1024.0)
+        act(v("WE", e, e + 1), v("MK", 8 + t, 9 + t), AF.Identity, bias=v("MK", t, t + 1), scale=1.0 / 1024)
         scale(vn("WT", 144 * e + 15, 8, 16), bo, v("WE", e, e + 1))
         scale(v("WX", 128 * e, 128 * e + 128), v("NBOF"), v("WE", e, e + 1))
         for j, row in enumerate((t, 8 + t)):
-            o = 512 * e + 256 * j
-            scale(v("DG", o, o + 128), v("ID"), v("MK", row, row + 1)); scale(v("DG", o + 128, o + 256), v("ID"), v("WC", 16 + row, 17 + row))
+            scale(v("DG", 256 * e + 128 * j, 256 * e + 128 * j + 128), v("ID"), v("WC", row, row + 1))
 
-    def repeat(k, after):
+    def repeat(k):
         ph[0] = "x"
-        for i in range(16):
-            keep(vn("XB%d" % k, i, XW, 16), v("XZ%d" % k, X0, X0 + XW))
-            ops[-1]["after"] = after
-    repeat(1, [])
+        for a, b in REP:
+            for i in range(16):
+                if i < VREP[k - 1]:
+                    cp(vn("XB%d" % k, 16 * a + i, b - a, 16), v("XZ%d" % k, a, b)); continue
+                keep(vn("XB%d" % k, 16 * a + i, b - a, 16), v("XZ%d" % k, a, b))
+                ops[-1]["cnt"] = 16 - VREP[k - 1]; ng[0] -= 1
+            ng[0] += 1
+    repeat(1)
     rec = lambda t, a=0, b=WW: v("W1" if t else "W0", a, b)
     node = lambda t: v("DD", Q * (t - 1), Q * t) if t else v("DI")
     vl = lambda t, h: v("VL%d" % t if t else "VL", 8 * h, 8 * h + 8)
@@ -349,8 +385,7 @@ def build():
         group([(out, gsel(g, p1), vn(bv[0], g, n, 8, 0, p1)) for g in range(8)])
 
     def start(t, h):
-        ph[0] = "w%d%d" % (t, h); n = str(h); o = 256 * t + 128 * h
-        mm(v("A" + n, 0, 128), v("XZ%d" % t, 128 * h, 128 * h + 128), v("NID")); act(v("NXT", o, o + 128), v("A" + n, 0, 128))
+        ph[0] = "w%d%d" % (t, h); n = str(h)
         ts(slot(n, 2, 2), vl(t, h), SENT, AL.add)
 
     def step1(t, h, a, b, off, P):
@@ -360,7 +395,7 @@ def build():
         covers(v("S1C" + n, a, b), v(P, 0, b - a))
 
     def walk(t, s, h, between=None):
-        ph[0] = "w%d%d" % (t, h); n = str(h); nk = s + 1; na = NA[t][2 - s][h]
+        ph[0] = "w%d%d" % (t, h); n = str(h); nk = s + 1; nb = sum(l1 - l0 for l0, l1 in lanes(t, s, h, "b"))
         u, K, C, banks = (str(3 - h), "Y0", "Y1", ["Y1"]) if aside(t, s, h) else (n, "K" + n, "B" + n, ["B0", "A0"][:3 - t] if (h, s) == (0, 0) else ["A" + n, "B" + n])
         RD, CM = "RD" + u, "CM" + u
         ov = "OV%d%d" % (t, h); e16 = v("E16" + u); tags = {2: (0, 1, 2), 1: (1, 0), 0: (0,)}[s]
@@ -370,40 +405,38 @@ def build():
         cap = s == 1 or (s == 0 and h == 1)
         if cap: ts(e16, ind(node(t), off), 4096.0 * nk, AL.min)
         else: cp(e16, ind(node(t), off))
-        xn, xo = ("XB%d" % t, 0) if t else xb0; xo += 16 * (128 * h - X0)
-        for l0, l1 in cuts(0, na, CUT[h]) if h else cuts(128 - na, 128, CUT[h]):
-            a, b = 16 * l0, 16 * l1
-            tt(v(RD, a, b), ind(rec(t), v("E16" + u, l0, l1)), v(xn, xo + a, xo + b), AL.subtract)
-            ts(v(CM, a, b), v(RD, a, b), 0.0, AL.is_le, 2.0, AL.mult)
-        fs = cuts(na, 128, 32) if h else cuts(0, 128 - na, 32)
-        for l0, l1 in fs:
+        x16 = lambda l0, l1: v("XB%d" % t, 16 * (128 * h + l0), 16 * (128 * h + l1))
+        for l0, l1 in lanes(t, s, h, "a"):
+            tt(v(RD, 16 * l0, 16 * l1), ind(rec(t), v("E16" + u, l0, l1)), x16(l0, l1), AL.subtract)
+            ts(v(CM, 16 * l0, 16 * l1), v(RD, 16 * l0, 16 * l1), 0.0, AL.is_le)
+        for l0, l1 in joined(lanes(t, s, h, "bc"), CUT["g"][h]):
             act(v(RD, 16 * l0, 16 * l1), ind(rec(t), v("E16" + u, l0, l1)))
+        for l0, l1 in lanes(t, s, h, "c"):
+            tt(v(CM, 16 * l0, 16 * l1), v(RD, 16 * l0, 16 * l1), x16(l0, l1), AL.is_le)
         if between and aside(t, s, h): between(u); ph[0] = "w%d%d" % (t, h)
-        for j, (l0, l1) in enumerate(fs):
+        for j, (l0, l1) in enumerate(lanes(t, s, h, "b")):
             P = v(banks[j % len(banks)], 0, 16 * (l1 - l0)); a, b = 16 * l0, 16 * l1
-            group([(P, v("NXT", 256 * t + 128 * h, 256 * t + 128 * h + 128), v("EXP", a, b))], [(P, v("ID"), v(RD, a, b))])
+            group([(P, v("NID"), x16(l0, l1))], [(P, v("ID"), v(RD, a, b))])
             covers(v(CM, a, b), P)
-        masks = [0, 1] if s == 2 else [] if cap and s == 0 else [0]
-        for j in masks:
-            ts(v("MM" + u, 128 * j, 128 * j + 128), e16, 4096.0 * (j + 1), AL.is_ge)
-        for k in tags:
-            ts(v("FK" + u, 128 * k, 128 * k + 128), e16, -4096.0 * k - (2048 if k == 0 else 0), AL.add)
+        fk = lambda j: v("FK" + u, 128 * j, 128 * j + 128); wp = lambda j, k: v("WP", 144 * j, 144 * (j + k))
+        for j in range(4 if s == 2 else 1 if cap and s == 0 else 2):
+            ts(fk(j), e16, (-2048.0, -4096.0, -8192.0, -8192.0)[j], AL.add, 2048.0 * (j == 0), AL.max if j in (1, 2) else AL.min)
         gd = [] if t == 0 else [(2, 0), (1, 1)] if s == 2 else [(0, 2)] if s == 1 - h else []
         run = lambda k: v(K, 144 * tags.index(k), 144 * tags.index(k) + 144)
         gcol = lambda k: vn(K, 144 * tags.index(k) + 1, 8, 18)
-        p1 = [(run(k), v("ONE", p1=64), kc(int(k > 0), int(k not in [x for x, j in gd]))) for k in tags]
-        if s == 2: p2 = [(v(K, 144 * j, 144 * j + 288), v("MM" + n, 128 * j, 128 * j + 128), v("WP", 0, 288)) for j in masks]
-        else: p2 = [(v(K, 0, 144 * nk), v("MM" + u, 0, 128), v("WP", 144 * s, 144 * s + 144 * nk)) for j in masks]
-        p3 = [(run(k), v("FK" + u, 128 * k, 128 * k + 128), v("P16")) for k in tags]
+        p1 = [(run(k), v("ONE", p1=32), kc(int(k == 1), int(k not in [x for x, j in gd]))) for k in tags]
+        p2 = [(run(1), fk(0), wp(0, 1)), (v(K, 0, 288), fk(0), wp(2, 2))] if s else [(run(0), fk(0), wp(2, 1))]
+        p3 = ([] if cap else [(run(0), fk(1), wp(1, 1))], [(v(K, 0, 288), fk(1), wp(3, 2))],
+              [(v(K, 0, 288), fk(1), wp(1, 2)), (v(K, 144, 432), fk(2), wp(1, 2)), (v(K, 288, 432), fk(3), wp(0, 1))])[s]
         p4 = [(vn(K, 2 + i, 8 * nk, 18), vn(RD, i, 128, 16), v("SC3H", 0, 8 * nk)) for i in range(16)]
         p5 = [(gcol(k), v("S1R" + n, 128 * j, 128 * j + 128), v("SC3H", 0, 8)) for k, j in gd]
         p5 += [(gcol(k), v(i), v("RG%d%d" % (t, h), o + 8 * j, o + 8 * j + 8)) for k, j in gd if k for i, o in (("ID", 0), ("IDK", 16))]
         group(p1, p2, p3, p4[:8], p4[8:], p5, stop=False)
-        w = 144 + 8 * len(gd); la = 256 - na if h else na; PP = "PP" + u
+        w = 144 + 8 * len(gd); la = 128 + nb if h else 128 - nb; PP = "PP" + u; sc = 9 * h + nb // 16
         group([(v(C, 0, w), v("LAN", la, la + 128, p1=64), v("CR", 0, w, p1=64))]
-              + [(v(C, 144 + 8 * i, 152 + 8 * i), v("S1C" + n, 128 * j, 128 * j + 128), v("BO")) for i, (k, j) in enumerate(gd)],
-              [(vn(C, 2 + i, 8, 18), vn(CM, i, 128, 16), v("BO")) for i in range(16)])
-        act(v(PP, 0, w), v(C, 0, w), AF.Relu, bias=v("RA%d" % t, 0, 1) if t else None, scale=-B / 2)
+              + [(v(C, 144 + 8 * i, 152 + 8 * i), v("S1C" + n, 128 * j, 128 * j + 128), bo) for i, (k, j) in enumerate(gd)],
+              [(vn(C, 2 + i, 8, 18), vn(CM, i, 128, 16), bo) for i in range(16)])
+        act(v(PP, 0, w), v(C, 0, w), AF.Relu, bias=v("RA%d" % t, 0, 1) if t else None, scale=v("SCL", sc, sc + 1))
         group([(gcol(k), v("ID"), v(PP, 144 + 8 * i, 152 + 8 * i)) for i, (k, j) in enumerate(gd)]
               + [(run(k), v("ID"), v(PP, 0, 144)) for k in tags], start=False)
         o = SEG[s, tags[0]]
@@ -414,7 +447,7 @@ def build():
             ts(mj, ends(n, s, s), 2047, AL.bitwise_and)
             if FAST[h]:
                 tt(v("BV" + n), ind(mj, v("LS", 0, 8)), v("MK"), AL.mult)
-                mm(v(C, 440, 448), v("BV" + n), v("BO16"))
+                mm(v(C, 440, 448), v("BV" + n), bo)
             else:
                 spread(v(C, 440, 448), v("BV" + n, 0, 64), mj, v("LS", 32, 36), vn("BOF", 0, 64, 2), 8, 128)
             cp(v(ov, 16 - 8 * s, 24 - 8 * s), v(C, 440, 448))
@@ -427,7 +460,7 @@ def build():
         ts(name, ends(n, s, 0), 4095, AL.bitwise_and)
         if s > 0: tt(slot(n, s - 1, 0), ends(n, s, 0), name, AL.subtract)
         if s == 1 - h and t > 0:
-            tt(v("GE" + n), slot(n, s, 0), gcol(0), AL.is_ge); tt(nm(t, h, 1 + h), v("GE" + n), vn("RS%d%d" % (t, h), 3, 8, 4), AL.mult)
+            tt(v("GE" + n), slot(n, s, 0), gcol(0), AL.is_ge); tt(nm(t, h, 1 + h), v("GE" + n), v("RS%d%d" % (t, h)), AL.mult)
 
     def yg(k, h, src, P, c):
         mm(v(P, c, c + 128, p1=8), src, v("ID" if k else "ID32")); act(v("YG", 256 * k + 128 * h, 256 * k + 128 * h + 128, p1=8), v(P, c, c + 128, p1=8))
@@ -435,8 +468,11 @@ def build():
     def guards21(t, h):
         n = str(h); sg = "SG%d%d" % (t, h)
         if t < 2:
-            cp(v(sg, 0, 16), v("MJ" + n)); ts(v(sg, 16, 32), ends(n, 2, 2, 16), SENT, AL.is_ge, 32768.0, AL.mult)
-            return send([(v(sg), v("RG%d%d" % (t + 1, h)), 1), (v("OV%d%d" % (t, h)), v("RO%d%d" % (t + 1, h)), 1)], 3.5)
+            ov, ro = "OV%d%d" % (t, h), "RO%d%d" % (t + 1, h)
+            cp(v(ov, 16, 32), v("MJ" + n)); ts(v(ov, 32, 48), ends(n, 2, 2, 16), SENT, AL.is_ge, 32768.0, AL.mult)
+            send([(v(ov), v(ro), 1)], FAR)
+            ph[0] = "w%d%d" % (t + 1, h)
+            return cp(v("RG%d%d" % (t + 1, h)), v(ro, 16, 48))
         ts(v("LT" + n), ends(n, 2, 2, 16), SENT, AL.is_lt); tt(v(sg, 0, 16), v("LT" + n), v("MJ" + n), AL.mult)
         for j in range(2):
             yg(2 - j, h, v(sg, 8 * j, 8 * j + 8), "A" + n, 128 * j)
@@ -447,8 +483,11 @@ def build():
         if t == 2:
             return yg(0, h, vn(gs, 3, 8, 4), K, 256)
         tt(v("BG" + n), ind(v(gs), v("LS", 24, 32)), v("MK"), AL.mult)
-        mm(v(K, 448, 456), v("BG" + n), v("BO32")); cp(v("SO%d%d" % (t, h), 0, 8), v(K, 448, 456))
-        return send([(v(gs), v("RS%d%d" % (t + 1, h)), 1), (v("SO%d%d" % (t, h)), v("RP%d%d" % (t + 1, h)), 1)], 3.5)
+        so, rp = "SO%d%d" % (t, h), "RP%d%d" % (t + 1, h)
+        mm(v(K, 448, 456), v("BG" + n), v("BO32")); cp(v(so, 0, 8), v(K, 448, 456)); cp(v(so, 8, 16), vn(gs, 3, 8, 4))
+        send([(v(so), v(rp), 1)], FAR)
+        ph[0] = "w%d%d" % (t + 1, h)
+        cp(v("RS%d%d" % (t + 1, h)), v(rp, 8, 16))
 
     i64 = lo(v("ID", 0, 64)); xb, xa = v("XX", 0, 8), v("XX", 8, 16); P = "A0"
     ya, yb, yw = v("YAB", 0, 64), v("YAB", 64, 128), v("YAB", 128, 192); fr = v("FR")
@@ -465,7 +504,7 @@ def build():
             act(vn("VV", 0, 8, 4), vl(t, 0)); cp(vn("VV", 2, 8, 4), v("MJ0", 0, 8))
             ts(v("NZ"), nm(t, 0), 0.0, AL.is_gt); tt(v("UU"), v("NZ"), v("VV"), AL.mult); scan(v("AP"), v("ZP"), v("UU"), AL.mult, AL.add)
             act(xa, vn("AP", 3, 8, 4)); act(v("XA"), vn("AP", 3, 8, 4))
-            act(v("BC"), ind(v("GP"), v("LS", 24, 32))); mm(v(P, 384, 448), lo(v("BC")), lo(v("ID32", 0, 64))); act(v("E0"), v(P, 384, 448))
+            act(v("BC"), ind(v("GP"), v("LS", 24, 32))); mm(v(P, 384, 448), lo(v("BC")), lo(v("ID32", 0, 64)))
         spread(v(P, 0, 4), v("BA", 0, 32), v("XA"), v("LS", 32, 34), v("MC", 0, 32), 4, LA)
         cp(v("OA", 0, 4), v(P, 0, 4)); (act if t else cp)(v("EA"), ind(node(t), v("OA", 0, 4)))
         tt(v("N01"), v("XX", 0, 16), v("XX", 8, 24), AL.is_equal)
@@ -485,7 +524,7 @@ def build():
         ph[0] = "s%d" % t; even = t % 2 == 0; e = t // 2; ea, eb = v("EA"), v("EB"); nr3 = 3 if even else 2
         cp(eb, v("E16" + u, 0, 64)); act(fr, ea if even else eb, AF.Relu, bias=1.0, scale=-1.0)
         mms([(v(P, 64, 128), v("T2"), fr)] + ([(v(P, 128, 192), v("TRI"), fr)] if even else []), True, True, True)
-        act(v("TA"), v(P, 64, 128), AF.Relu, bias=-63.0, scale=-1.0)
+        act(v("TA"), v(P, 64, 128), AF.Relu, bias=-63.0 * (M + BASE), scale=-1.0 * (M + BASE))
         if even: act(v("PLF"), v(P, 128, 192), AF.Identity, bias=-33.0)
         bars = [v("N01", 0, 8), v("N01", 8, 16)] + ([] if even else [v("NZ0")])
         lst = [(vn(P, 8 + r, 8, 4), lo(v("I2N")), lo(x)) for j, x in enumerate(bars) for r in range(3 if j else 4)]
@@ -501,37 +540,36 @@ def build():
             act(lo(v("JK")), lo(v("Y0", 16, 24)), AF.Relu, bias=lo(v("NB", e, e + 1)) if even else B, scale=-B, acc=lo(v("ASUM")))
             mm(v(P, 352, 353), lo(v("ONE32")), lo(v("ASUM")))
             ts(v("AI"), v(P, 352, 353), 0.5 / B, AL.mult, -0.25, AL.add); ts(v("SA%d" % t, 0, 1), v("AI"), 2 * B, AL.mult, v(P, 352, 353), AL.subtract)
-            send([(v("SA%d" % t), v("RA%d" % (t + 1)), 1)], 3.5)
+            send([(v("SA%d" % t), v("RA%d" % (t + 1)), 1)], FAR)
         spread(v(P, 356, 356 + 4 * nr3), v("BA", 0, 32 * nr3), v("W3"), v("LS", 40, 40 + 2 * nr3), v("MC", 0, 32 * nr3), 4 * nr3, LA)
         cp(v("OSC", 0, 4 * nr3), v(P, 356, 356 + 4 * nr3))
         if not even:
-            tt(v("TB"), ea, v("E0"), AL.not_equal); tt(ya, ea, v("TB"), AL.mult)
-            tt(v("TC"), v("TA"), v("E0"), AL.mult); tt(yb, eb, v("TC"), AL.add)
+            tt(v("TB"), ea, v(P, 384, 448), AL.not_equal); tt(ya, ea, v("TB"), AL.mult)
+            tt(v("TC"), v("TA"), v(P, 384, 448), AL.min); tt(yb, eb, v("TC"), AL.add)
             return
-        x = v("XZ%d" % t, 0, 64); dg = lambda j: v("DG", 512 * e + 128 * j, 512 * e + 128 * j + 128)
-        act(v("CUT"), ind(rec(t, 0, M), v("OV%d0" % t, 8, 12)))
-        group([(v(P, 64, 128), dg(3), v("CUT")), (v(P, 64, 128), dg(2), x)]); group([(v(P, 128, 192), dg(1), v("CUT")), (v(P, 128, 192), dg(0), x)])
+        x = v("XZ%d" % t, 0, 64); dg = lambda j: v("DG", 256 * e + 128 * j, 256 * e + 128 * j + 128)
+        tt(v("CUT"), ind(rec(t, 0, M), v("OV%d0" % t, 8, 12)), x, AL.subtract)
+        group([(v(P, 64, 128), dg(1), v("CUT")), (v(P, 64, 128), v("ID"), x)]); group([(v(P, 128, 192), dg(0), v("CUT")), (v(P, 128, 192), v("ID"), x)])
         act(v("CH"), v(P, 64, 192))
-        d = v(P, 384, 448)
-        nf = min(LA, 128 - NA[t][2][0])
+        d = v(P, 384, 448); raw = [(a, min(b, LA)) for a, b in joined(lanes(t, 0, 0, "bc"), 128) if a < LA]
         group([(d, v("WT", 144 * e + 15 - j, 144 * e + 143 - j), vn("RD" + u, j, 64, 16)) for j in range(15)]
-              + [(v(P, 384, 384 + nf), v("WX", 128 * e, 128 * e + 128), v("XZ%d" % t, 0, nf))]
+              + [(v(P, 384 + a, 384 + b), v("WX", 128 * e, 128 * e + 128), v("XZ%d" % t, a, b)) for a, b in raw]
               + [(d, v("WT", 144 * e, 144 * e + 128), vn("RD" + u, 15, 64, 16))])
-        ts(v("TR"), d, 1.5 * 2 ** 33, AL.add, 1.5 * 2 ** 33, AL.subtract); ts(v("GO"), d, -512.0, AL.is_ge)
-        tt(v("N8"), d, v("TR"), AL.is_lt); tt(v("STR"), v("N8"), v("GO"), AL.is_gt)
+        ts(v("TR"), d, -1.0, AL.min); ts(v("GO"), d, -0.5, AL.is_ge); tt(v("STR"), d, v("TR"), AL.is_lt)
         mm(v(P, 256, 320), v("T1B"), v("STR"))
         group([(v(P, 192, 256), v("T1"), v("STR")), (v(P, 192, 256), v("NBOF"), fr), (v(P, 192, 256), v("ID64N"), v("GO"))])
         tt(v("NU"), v(P, 256, 320), eb, AL.subtract)
         ts(v("TB"), v(P, 192, 256), -32.0, AL.is_ge); tt(yb, eb, v("TB"), AL.mult); tt(yw, eb, v("GO"), AL.mult)
-        tt(v("TC"), v("TA"), v("NC", 64 * e, 64 * e + 64), AL.mult)
+        tt(v("TD"), v("TA"), v("NC", 64 * e, 64 * e + 64), AL.min)
         for c in range(2):
             Y = "Y1"
             mms([(v(Y, 64 * j, 64 * j + 64), v("RBP", 128 * (8 * c + j), 128 * (8 * c + j) + 128), v("PLF")) for j in range(8)], True, True, True)
             for j in range(8):
                 tt(v("Y2", 512 * c + 64 * j, 512 * c + 64 * j + 64), v(Y, 64 * j, 64 * j + 64), v("NU"), AL.max)
         wd = lambda i: 288 if i == 0 else 144 if i == 15 else 0
-        group(*[[(v("Y0", 0, 64), v("WD", wd(i) + 15 - i, wd(i) + 143 - i), v("Y2", 64 * i, 64 * i + 64))] for i in range(16)])
-        tt(v("TC"), v("TC"), ea, AL.add); tt(v("YI"), v("Y0", 0, 64), v("TC"), AL.add); ts(ya, v("YI"), 16383, AL.bitwise_and)
+        group([(v("Y0", 0, 64), v("ID32"), ea), (v("Y0", 0, 64), v("ID"), v("TA")), (v("Y0", 0, 64), v("ID"), v("TD"))],
+              *[[(v("Y0", 0, 64), v("WD", wd(i) + 15 - i, wd(i) + 143 - i), v("Y2", 64 * i, 64 * i + 64))] for i in range(16)])
+        cp(v("YI"), v("Y0", 0, 64)); ts(ya, v("YI"), 16383, AL.bitwise_and)
 
     def commit(t):
         ph[0] = "s%d" % t; even = t % 2 == 0
@@ -559,7 +597,7 @@ def build():
         ph[0] = "w%d0" % t; guard0(t, 0)
         walk(t, 0, 1); guard0(t, 1)
         commit(t)
-        if t == 0: repeat(2, [])
+        if t == 0: repeat(2)
     ph[0] = "o"
     dma("S", lambda T: T.yr[:, :], lambda T: T.W1[:, RO:RO + Q], [v("W1", RO, RO + Q)], [], 524288)
     dma("S", lambda T: T.yn[:, :], lambda T: T.DD[:, LASTD * Q:LASTD * Q + Q], [v("DD", LASTD * Q, LASTD * Q + Q)], [], 1048576)
@@ -612,7 +650,7 @@ def turns(ops, hard, seq):
 
 
 def costs(ops, m):
-    return [c[0] * (m["far"] if k in "rs" else 1) + m["cy"] * (c[1] + m["g"] * c[2] + m["sc"] * c[3] + m["pe"] * c[4]) for c, k in ((o["cost"], o["kind"]) for o in ops)]
+    return [c[0] * (m["far"] if k in "rs" else m["cy"] / 0.9e-3) + m["cy"] * (c[1] + m["g"] * c[2] + m["sc"] * c[3] + m["pe"] * c[4]) for c, k in ((o["cost"], o["kind"]) for o in ops)]
 
 
 def order(ops, hard, soft, m, tune):
@@ -773,8 +811,222 @@ def renew(ops, hard, soft, seq, m, tune):
     return best[1]
 
 
+def refine(ops, hard, soft, seq, ms, tune):
+    n = len(ops); STEP = 32; nm = len(ms); cost = [costs(ops, m) for m in ms]
+    eng = ["VAPGSR".index(o["eng"]) for o in ops]; dyn = ["dyn" in o for o in ops]; bulk = ["bulk" in o for o in ops]; out = [o["kind"] == "s" for o in ops]
+    dm = [[o["nbytes"] / m["bw"] if o["kind"] == "d" else -1.0 for o in ops] for m in ms]; src = [o.get("src", -1) for o in ops]
+    dur = [[c + (d + ms[k]["dl"] if d >= 0 else 0) for c, d in zip(cost[k], dm[k])] for k in range(nm)]
+    hp = [list(h) for h in hard]; pred = [hard[i] | soft[i] for i in range(n)]; succ = [set() for _ in ops]
+    for i in range(n):
+        for j in pred[i]: succ[j].add(i)
+    hs = [[(j, i in hard[j]) for j in succ[i]] for i in range(n)]
+
+    def run(k, part, state, end, by):
+        free, lastq, bank, bl, bus, bb, top, arg, sent = state; free = free[:]; lastq = lastq[:]; bank = bank[:]; bl = bl[:]
+        LAT = ms[k]["lat"]; co = cost[k]; dk = dm[k]
+        for i in part:
+            e = eng[i]
+            if e == 5:
+                b = src[i]; t = end[b]
+                if bus > t: t = bus; b = bb
+            else:
+                t = free[e]; b = lastq[e]
+                if out[i]: sent = i
+                elif bulk[i] and sent >= 0 and end[sent] + 1.0 > t: t = end[sent] + 1.0; b = sent
+            t -= LAT
+            for j in hp[i]:
+                if end[j] > t: t = end[j]; b = j
+            if dyn[i]:
+                for e2 in (0, 1, 2):
+                    if e2 != e and bank[e2] > t: t = bank[e2]; b = bl[e2]
+                bank[e] = t + LAT + co[i]; bl[e] = i
+            t += LAT + co[i]; free[e] = t; lastq[e] = i
+            if dk[i] >= 0:
+                if bus > t: t = bus; b = bb
+                bus = t + dk[i]; t = bus + ms[k]["dl"]; bb = i
+            end[i] = t; by[i] = b
+            if t > top: top = t; arg = i
+        return free, lastq, bank, bl, bus, bb, top, arg, sent
+
+    def times(k, seq, k0, old):
+        end, by, marks = old[0][:], old[1][:], old[2][:k0 + 1]
+        for p in range(k0 * STEP, n, STEP): marks.append(run(k, seq[p:p + STEP], marks[-1], end, by))
+        return end, by, marks
+    zero = ([0.0] * n, [-1] * n, [([0.0] * 6, [-1] * 6, [-9.0] * 3, [-1] * 3, 0.0, -1, 0.0, -1, -1)])
+
+    def settle(seq, end, k=0):
+        d, c = dur[k], cost[k]
+        s2 = sorted(range(n), key=lambda p: (end[seq[p]] - d[seq[p]] if eng[seq[p]] != 5 else end[src[seq[p]]] - c[src[seq[p]]], p))
+        seq = [seq[p] for p in s2]
+        return seq, [times(k, seq, 0, zero) for k in range(nm)]
+
+    def rest(k, seq):
+        q = [0.0] * n; nx = [0.0] * 6; LAT = ms[k]["lat"]
+        for i in reversed(seq):
+            t = nx[eng[i]] + cost[k][i] if eng[i] != 5 else 0.0; u = 0.0
+            for j, h in hs[i]:
+                x = q[j] + LAT if h else q[j]
+                if x > u: u = x
+            u += dur[k][i]
+            q[i] = nx[eng[i]] = t if t > u else u
+        return q
+    r = [tune["seed"] * 7919 + 1]
+
+    def rnd():
+        r[0] = (r[0] * 1103515245 + 12345) % 2147483648
+        return (r[0] + 1) / 2147483649
+
+    def window(k, seq, st, q):
+        k0 = int(rnd() * (n // STEP)); p0 = k0 * STEP; p1 = min(n, p0 + int(tune["w0"] + rnd() * tune["w1"])); win = seq[p0:p1]
+        new = lay(k, win, st[2][k0], st[0][:], st[1][:], q)
+        return None if new == win else (p0, seq[:p0] + new + seq[p1:], p1)
+
+    def lay(k, win, state, e2, b2, q):
+        LAT = ms[k]["lat"]; ins = set(win); new = []
+        noise = tune["noise"] * rnd(); look = rnd() * tune["look"]; pr = {}
+        for i in reversed(win):
+            pr[i] = dur[k][i] + max([(pr[j] if j in ins else q[j]) + (LAT if h else 0.0) for j, h in hs[i]] + [0.0])
+        key = {i: pr[i] + noise * rnd() for i in win}; left = {i: len(pred[i] & ins) for i in win}
+        when = lambda i: max([e2[j] + LAT for j in hp[i]] + [0.0])
+        ready = {i: when(i) for i in win if left[i] == 0}
+        while ready:
+            free, bank = state[0], state[2]; b = 1e9
+            for i, t in ready.items():
+                e = eng[i]
+                if e == 5: b = -1.0; bi = i; break
+                if free[e] > t: t = free[e]
+                if dyn[i]:
+                    for x in (0, 1, 2):
+                        if x != e and bank[x] + LAT > t: t = bank[x] + LAT
+                if t < b: b = t; bi = i
+            if b >= 0:
+                e = eng[bi]; lim = b + look * cost[k][bi] + 0.02; ky = key[bi]
+                for i, t in ready.items():
+                    if eng[i] == e and t <= lim and key[i] > ky: bi = i; ky = key[i]
+            del ready[bi]; new.append(bi); state = run(k, (bi,), state, e2, b2)
+            for j in succ[bi]:
+                if j in ins:
+                    left[j] -= 1
+                    if left[j] == 0: ready[j] = when(j)
+        return new
+
+    def swap(seq, st):
+        i = st[2][-1][7]; by = st[1]; lk = []
+        while by[i] >= 0:
+            if by[i] not in pred[i]: lk.append((by[i], i))
+            i = by[i]
+        j, i = lk[int(rnd() * len(lk))]; pj = seq.index(j); pi = seq.index(i, pj); mid = seq[pj:pi + 1]
+        if rnd() < 0.5:
+            mv = {i}
+            for x in reversed(mid):
+                if not mv.isdisjoint(succ[x]): mv.add(x)
+            return None if j in mv else (pj, seq[:pj] + [x for x in mid if x in mv] + [x for x in mid if x not in mv] + seq[pi + 1:], pi + 1)
+        mv = {j}
+        for x in mid:
+            if not mv.isdisjoint(pred[x]): mv.add(x)
+        return None if i in mv else (pj, seq[:pj] + [x for x in mid if x not in mv] + [x for x in mid if x in mv] + seq[pi + 1:], pi + 1)
+    def tails(k, seq):
+        LAT = ms[k]["lat"]; co = cost[k]; dk = dm[k]; q = [0.0] * n; nx = [0.0] * 6; nb = [-99.0] * 3; qb = qs = -99.0; at = [None] * n + [(nx[:], nb[:], qb, qs)]
+        for p in range(n - 1, -1, -1):
+            i = seq[p]; e = eng[i]; u = 0.0
+            for j in far[i]:
+                if q[j] > u: u = q[j]
+            if u: u += LAT
+            if dk[i] >= 0: qb = u = dk[i] + max(ms[k]["dl"] + u, qb)
+            if out[i]:
+                u = max([u, 1.0 + qs] + [q[j] for j in land[i]]); qs = -99.0
+            if e != 5 and nx[e] > u: u = nx[e]
+            if dyn[i] and nb[e] > u: u = nb[e]
+            q[i] = nx[e] = u = u + co[i]
+            if e == 5 and u > qb: qb = u
+            if bulk[i] and u > qs: qs = u
+            if dyn[i]:
+                for x in (0, 1, 2):
+                    if x != e and u + LAT > nb[x]: nb[x] = u + LAT
+            at[p] = (nx[:], nb[:], qb, qs)
+        return q, at
+
+    def sweep(seq, heat, W, tries):
+        seq = seq[:]; tl = [tails(k, seq) for k in range(nm)]; pos = {i: p for p, i in enumerate(seq)}
+        state = [zero[2][0]] * nm; end = [[0.0] * n for k in range(nm)]; by = [[-1] * n for k in range(nm)]; over = [[] for k in range(nm)]
+        for p0 in range(0, n, W // 3):
+            p1 = min(n, p0 + W); win = seq[p0:p1]; ins = set(win); ex = []; base = []
+            for k in range(nm):
+                q = tl[k][0]; LAT = ms[k]["lat"]
+                ex.append([(i, max([q[j] + LAT for j in far[i] if pos[j] >= p1] + [q[j] for j in land[i] if pos[j] >= p1])) for i in win if last[i](pos) >= p1])
+                over[k] = [x for x in over[k] if x[0] >= p1]; base.append(max([x[1] for x in over[k]] + [0.0]))
+
+            def value(win):
+                tot = 0.0; args = []
+                for k in range(nm):
+                    en = end[k]; s = run(k, win, state[k], en, by[k]); nx, nb, qb, qs = tl[k][1][p1]
+                    c = [(en[i] + x, i) for i, x in ex[k]] + [(s[0][e] + nx[e], s[1][e]) for e in range(5)] + [(s[2][e] + nb[e], s[3][e]) for e in range(3)]
+                    c += [(s[4] + qb, s[5]), (s[6], s[7]), (en[s[8]] + 1.0 + qs, s[8])]
+                    m, a = max(c); args.append(a); t = max(m, base[k])
+                    tot += w[k] * (t + tune["soft"] * math.log(math.exp((base[k] - t) / tune["soft"]) + sum([math.exp((x - t) / tune["soft"]) for x, i in c if x > t - 2.0])))
+                return tot, args
+            cur, args = value(win); lk = None
+            for it in range(tries):
+                if lk is None:
+                    lk = []
+                    for k in range(nm):
+                        i = args[k]
+                        while i in ins and by[k][i] in ins:
+                            if by[k][i] not in pred[i]: lk.append((by[k][i], i))
+                            i = by[k][i]
+                if not lk: break
+                j, i = lk[int(rnd() * len(lk))]; pj = win.index(j); pi = win.index(i); mid = win[pj:pi + 1]
+                if it < tune["lays"]:
+                    k = int(rnd() * nm); new = lay(k, win, state[k], end[k], by[k][:], tl[k][0])
+                    if new == win: continue
+                elif rnd() < 0.5:
+                    mv = {i}
+                    for x in reversed(mid):
+                        if not mv.isdisjoint(succ[x]): mv.add(x)
+                    if j in mv: continue
+                    new = win[:pj] + [x for x in mid if x in mv] + [x for x in mid if x not in mv] + win[pi + 1:]
+                else:
+                    mv = {j}
+                    for x in mid:
+                        if not mv.isdisjoint(pred[x]): mv.add(x)
+                    if i in mv: continue
+                    new = win[:pj] + [x for x in mid if x not in mv] + [x for x in mid if x in mv] + win[pi + 1:]
+                val, a2 = value(new)
+                if val <= cur - heat * math.log(rnd()): win, cur, args, lk = new, val, a2, None
+            seq[p0:p1] = win
+            for k in range(nm):
+                part = win[:W // 3]; state[k] = run(k, part, state[k], end[k], by[k]); q = tl[k][0]; lim = q[seq[0]] - 4.0
+                over[k] += [x for i in part for x in [(pos[j], end[k][i] + ms[k]["lat"] + q[j]) for j in far[i]] + [(pos[j], end[k][i] + q[j]) for j in land[i]] if x[1] > lim]
+        return seq
+    far = [[j for j, h in x if h] for x in hs]; land = [[j for j in succ[i] if src[j] == i] for i in range(n)]
+    last = [(lambda pos, js=far[i] + land[i]: max([pos[j] for j in js] + [-1])) for i in range(n)]
+    seq, st = settle(seq, times(0, seq, 0, zero)[0]); top = lambda s: s[2][-1][6]
+    w = [90.0 / nm / top(s) for s in st]; cur = sum(a * top(s) for a, s in zip(w, st)); best = (cur, seq); q = {}
+    for move, its, heat in ((0, tune["renew"], tune["warm"]), (1, tune["polish"], tune["heat"])) * tune["rounds"]:
+        seq = best[1]; seq, st = settle(seq, times(0, seq, 0, zero)[0]); cur = best[0]; q = {}
+        for it in range(its):
+            k = it % nm
+            if move == 0 and it % tune["age"] == 0:
+                seq, st = settle(seq, st[k][0], k); cur = sum(a * top(s) for a, s in zip(w, st)); q = [rest(a, seq) for a in range(nm)]
+            new = swap(seq, st[k]) if move else window(k, seq, st[k], q[k])
+            if not new: continue
+            lim = cur - (heat * (1 - it / its) + 0.003) * math.log(rnd()); s2 = st[:]; val = cur
+            for a in range(nm):
+                k2 = (k + a) % nm; s2[k2] = times(k2, new[1], new[0] // STEP, st[k2]); val += w[k2] * (top(s2[k2]) - top(st[k2]))
+                if val > lim + tune["hope"] * (nm - 1 - a): break
+            if val <= lim:
+                seq, st, cur = new[1], s2, val
+                if cur < best[0]: best = (cur, seq)
+    seq = best[1]
+    for it in range(tune["sweeps"]):
+        seq = sweep(seq, tune["cool"] * (1 - it / tune["sweeps"]) + 0.002, tune["narrow"] + 3 * int(rnd() * tune["wide"]), tune["tries"])
+        seq, st = settle(seq, times(it % nm, seq, 0, zero)[0], it % nm); cur = sum(a * top(s) for a, s in zip(w, st))
+        if cur < best[0]: best = (cur, seq)
+    return best[1]
+
+
 def plan(ops, hard, soft, m, tune):
-    return polish(ops, hard, soft, renew(ops, hard, soft, order(ops, hard, soft, m, tune), m, tune), m, tune)
+    return refine(ops, hard, soft, order(ops, hard, soft, m, tune), [dict(m, **x) for x in tune["also"]], tune)
 
 
 def polish(ops, hard, soft, seq, m, tune):
@@ -875,10 +1127,10 @@ def rank_program(g, core, T, topo):
                 qs[e].wait_ge(T.sem[s], n)
                 for s2, n2 in kj.items():
                     if kn.get(s2, 0) < n2: kn[s2] = n2
-        if e == "G" and o["kind"] == "c" and kn.get("qG", 0) < count.get("qG", 0):
-            kn["qG"] = count["qG"]; g.wait_ge(T.sem["qG"], kn["qG"])
         ins = o["fn"](g, T, c)
-        if o["kind"] == "c":
+        if e == "G" and o["kind"] == "c":
+            s, n = o["sem"], o["cnt"]; ins.then_inc(T.sem[s], 1)
+        elif o["kind"] == "c":
             s = QSEM[e]; n = count.get(s, 0) + 1; ins.then_inc(T.sem[s], 1)
         elif o["kind"] == "d":
             s = o["sem"]; n = 16; ins.then_inc(T.sem[s], 16)

import math
from concourse.bass import DstId, RemoteDMATransfer
from concourse.mybir import AluOpType as AL, ActivationFunctionType as AF

M, Q, BASE, L, LA = 4096, 2048, 1920, 256, 64
LAY = [[("b32 c32 a64", "a32 c16 b80"), ("b32 c32 a64", "a32 c16 b80"), ("b32 a32 c64", "a32 c16 b80")]] * 3
CUT = dict(a=(96, 32), b=(32, 32), c=(48, 64), g=(32, 56))
REP, VREP = ((0, 256),), (0, 0)
RB, FAR = 2, 3.3
GF, AREP = (1, 0, 0), 4
FAST = (1, 1)
MODEL = dict(cy=0.95e-3, g=1.56, sc=3.8, pe=0.5, lat=0.17, bw=330e3, dl=1.5, far=1.3)
TUNE = dict(slack=0.05, seed=1, fb=60, moves=4, step=4, renew=0, w0=30, w1=80, noise=4, look=0.7, warm=0.06, polish=0, heat=0.03, rounds=1, hope=0.03, age=4, sweeps=260, cool=0.04, wide=20, tries=20, soft=0.3, lays=3, narrow=24,
            also=[dict(cy=.9e-3, g=1.35, lat=.18, far=1.25), dict(cy=1.08e-3, g=1.75, lat=.13, far=1.0, sc=4.5)])
FIRST = 1.5
PIECE, LASTD = 4096, 2
TT2 = 1.0
EQS = (0, 0, 0, 0, 0, 0)
B = float(2 ** 26)
B2 = 16384.0
NEG = -float(2 ** 30)
SENT, SENT2 = 4096.0 * 4081, 4096.0 * 4082
R1, R2, WW, DUM = 4096, 8192, 10240, 6144
WIN = DUM + 12 * LA
RO = R1 + WIN
SEG = {(2, 0): 0, (2, 1): 144, (2, 2): 288, (1, 1): 432, (1, 0): 576, (0, 0): 720}
F, H, BF, U, I = "float32", "float16", "bfloat16", "uint16", "int32"
SB = {
    "W0": (WW, BF), "W1": (RO + WIN, BF), "DI": (BASE, I), "DD": (2 * Q + WIN, F), "VSI": (48, I), "VSF": (48, F),
    "XZ0": (L, BF), "XZ1": (L, BF), "XZ2": (L, BF), "XB0": (16 * L, BF), "XB1": (16 * L, BF), "XB2": (16 * L, BF),
    "VU": (96, U), "VL": (48, F), "VU1": (32, U), "VL1": (16, F), "VU2": (32, U), "VL2": (16, F),
    "SA0": (8, F), "SA1": (8, F), "RA1": (8, F), "RA2": (8, F), "YG": (768, F), "RZ": (1, BF), "NM": (192, I),
    "ONE": (128, BF), "ONE32": (128, F), "ID": (128, BF), "NID": (128, BF), "ID32": (128, F), "ID64N": (128, BF), "IDK": (128, BF), "I2N": (128, BF),
    "BOF": (128, BF), "NBOF": (128, BF), "BO32": (8, F), "SC3H": (24, H), "SCL": (18, F),
    "TRI": (128, BF), "TRE": (128, BF), "T1": (128, BF), "T1B": (128, BF), "T2": (128, BF), "RBP": (2048, BF), "WD": (432, F),
    "WT": (288, BF), "WE": (2, F), "WX": (256, BF), "NLH": (16, H), "XA": (8, F), "TR": (64, I), "WC": (16, F), "DG": (512, BF), "SEL": (1024, BF), "AB": (1024, BF), "NX": (8, F), "TRM": (128, BF), "VB": (384, H),
    "WP": (720, BF), "KC": (576, BF), "CR": (160, BF), "LAN": (384, BF), "MK": (128, F), "II": (128, I), "IJ": (128, I),
    "LI": (64, I), "LJ": (16, I), "LK": (16, I), "LS": (64, U), "DUMC": (24, F), "NC": (128, BF), "NL": (16, F), "NB": (2, F), "CB2": (24, BF),
    "CMP": (32, F), "MC": (96, BF), "GSEL": (240, BF),
    "XX": (24, H), "FL": (8, I), "A2": (8, F), "DV": (8, F), "NW": (8, F), "TQ": (8, F), "BA": (96, H), "OA": (8, U), "EA": (64, F), "EB": (64, F),
    "FR": (64, BF), "N01": (16, BF), "NZ0": (8, BF), "ASK": (32, BF), "VTH": (128, H), "PLF": (64, BF), "CMM": (1024, BF), "W3": (24, F), "OSC": (12, U),
    "JK": (8, F), "ASUM": (1, F), "AI": (1, I), "STR": (64, BF), "GO": (64, BF), "NU": (64, F), "Y2": (1024, F), "YI": (64, I),
    "YAB": (192, I), "TA": (64, BF), "TB": (64, F), "TC": (64, F), "TD": (64, BF), "CUT": (64, H), "CH": (128, BF), "BC": (128, F),
    "ZP": (32, F), "NZ": (32, F), "VV": (32, F), "UU": (32, F), "GP": (32, F), "AP": (32, F),
}
for _h in "01":
    SB.update({"E16" + _h: (128, U), "FK" + _h: (512, H), "RD" + _h: (2048, H), "CM" + _h: (2048, BF), "PP" + _h: (160, BF),
               "SC" + _h: (864, I), "D1" + _h: (864, F), "MJ" + _h: (16, I), "A1" + _h: (8, I), "B1" + _h: (8, F), "GE" + _h: (8, F), "ZZ" + _h: (32, F),
               "BV" + _h: (128, H), "BG" + _h: (128, F), "LT" + _h: (16, F), "S1R" + _h: (384, BF), "S1C" + _h: (384, BF)})
    for _t in range(3):
        SB.update({"OV%d" % _t + _h: (48, U), "SG%d" % _t + _h: (32, H), "GS%d" % _t + _h: (32, F)})
    for _t in range(2):
        SB.update({"SO%d" % _t + _h: (16, U), "RG%d" % (_t + 1) + _h: (32, H), "RO%d" % (_t + 1) + _h: (48, U),
                   "RS%d" % (_t + 1) + _h: (8, F), "RP%d" % (_t + 1) + _h: (16, U)})
for _h in "23":
    SB.update({"E16" + _h: (128, U), "FK" + _h: (256, H), "RD" + _h: (2048, H), "CM" + _h: (2048, BF), "PP" + _h: (160, BF)})
DYN = ("A0",)
PS = ["K0", "K1", "A0", "B0", "A1", "B1", "Y0", "Y1"]
POOL, FILL = {}, {}
for _k, (_n, _d) in SB.items():
    if _n <= 640 and _k[:2] not in ("VU", "VL", "SG", "SO", "SA", "RG", "RO", "RA", "VS", "OV", "GS", "RS", "RP", "XZ") or _k == "GSEL":
        POOL[_k] = ("pool_" + _d, FILL.get(_d, 0)); FILL[_d] = FILL.get(_d, 0) + (_n + 31) // 32 * 32
SCRATCH = {"pool_" + d: ("sbuf", [128, n], d) for d, n in FILL.items()}
SENTU = ["VU"]
for _k in SENTU:
    POOL[_k] = ("sent", FILL.get("sent", 0)); FILL["sent"] = FILL.get("sent", 0) + SB[_k][0]
SCRATCH["sent"] = ("sbuf", [128, FILL["sent"]], U)
SCRATCH.update({k: ("sbuf", [128, n], d) for k, (n, d) in SB.items() if k not in POOL})
SCRATCH.update({k: ("psum", [128, 512], F) for k in PS})
SEMAPHORES = ["qV", "qA", "qP"] + ["d%d" % i for i in range(40)] + ["r%d" % i for i in range(24)] + ["l%d" % i for i in range(12)] + ["g%d" % i for i in range(48)]
QSEM = {"V": "qV", "A": "qA", "P": "qP"}
PLAN = {}


def v(n, c0=0, c1=None, st=1, p0=0, p1=128):
    if c1 is None:
        c1 = SB[n][0] if n in SB else 512
    return (n, p0, p1, c0, c1, st)


def vn(n, c0, cnt, st, p0=0, p1=128):
    return (n, p0, p1, c0, c0 + (cnt - 1) * st + 1, st)


def lo(x):
    return (x[0], 0, LA) + x[3:]


def cuts(a, b, most):
    n = (b - a + most - 1) // most
    return [(a + (b - a) * j // n // 2 * 2, a + (b - a) * (j + 1) // n // 2 * 2) for j in range(n)]


def lanes(t, s, h, kinds):
    out = []; a = 0
    for x in LAY[t][2 - s][h].split():
        if x[0] in kinds: out += cuts(a, a + int(x[1:]), CUT[x[0]][h])
        a += int(x[1:])
    return out


def joined(pieces, most):
    out = []
    for a, b in pieces:
        if out and out[-1][1] == a and b - out[-1][0] <= most: out[-1][1] = b
        else: out.append([a, b])
    return out


def ind(w, o):
    return ("ind", w, o)


def ap(T, x):
    if not isinstance(x, tuple):
        return x
    if x[0] == "ind":
        return ap(T, x[1]).indirect(ap(T, x[2]))
    n, o = POOL.get(x[0], (x[0], 0))
    if x[5] == 1:
        return T[n][x[1]:x[2], o + x[3]:o + x[4]]
    return T[n][x[1]:x[2], o + x[3]:o + x[4]:x[5]]


def cols(x):
    if x[0] == "ind":
        return 16 * cols(x[2])
    return (x[4] - x[3] + x[5] - 1) // x[5]


def wide(x):
    x = x[1] if x[0] == "ind" else x
    return 4 if x[0] not in SB or SB[x[0]][1] in (F, I) else 2


def build():
    ops = []
    nd, nr, nl, ng, last, ph = [0], [0], [0], [0], [], ["i"]

    def add(eng, fn, rd, wr, cost, **kw):
        r2, w2 = [], []
        for x in rd:
            if isinstance(x, tuple):
                r2 += [x[1], x[2]] if x[0] == "ind" else [x]
        for x in wr:
            if x[0] == "ind":
                w2.append(x[1]); r2.append(x[2])
            else:
                w2.append(x)
        o = dict(eng=eng, no=len(ops), fn=fn, rd=r2, wr=w2, cost=cost, kind="c", after=[], ph=ph[0])
        if eng == "G" and "kind" not in kw:
            o.update(sem="g%d" % ng[0], cnt=1); ng[0] += 1
        o.update(kw)
        ops.append(o)
        return len(ops) - 1

    def vcost(out, ins, two=False):
        n = cols(out)
        if out[0] == "ind":
            return (0.05, 0, 0, n, 0)
        if ins[0][0] == "ind":
            return (0.05, 0, n, 0, 0)
        f = 0.5 if all(wide(x) == 2 for x in [out] + ins) else 1.0
        if two and all(x[0] in SB for x in ins):
            f = TT2 if f == 0.5 else 2.0
        return (0.0, max(64, n * f), 0, 0, 0)

    def cp(out, a):
        add("V", lambda g, T, c: g.vector.tensor_copy(ap(T, out), ap(T, a)), [a], [out], vcost(out, [a]))

    def tt(out, a, b, op):
        add("V", lambda g, T, c: g.vector.tensor_tensor(ap(T, out), ap(T, a), ap(T, b), op), [a, b], [out], vcost(out, [a, b], True))

    def ts(out, a, s1, op0, s2=None, op1=None):
        if s2 is None:
            fn = lambda g, T, c: g.vector.tensor_scalar(ap(T, out), ap(T, a), ap(T, s1), None, op0)
        else:
            fn = lambda g, T, c: g.vector.tensor_scalar(ap(T, out), ap(T, a), ap(T, s1), ap(T, s2), op0, op1)
        add("V", fn, [a, s1, s2], [out], vcost(out, [a]))

    def scan(out, d0, d1, op0, op1):
        add("V", lambda g, T, c: g.vector.tensor_tensor_scan(ap(T, out), ap(T, d0), ap(T, d1), 0.0, op0, op1), [d0, d1], [out], vcost(out, [d0, d1]))

    def ms(out, val):
        add("V", lambda g, T, c: g.vector.memset(ap(T, out), val), [], [out], vcost(out, [out]))

    def act(out, a, func=None, bias=None, scale=None, acc=None):
        def fn(g, T, c):
            kw = {}
            if bias is not None: kw["bias"] = ap(T, bias)
            if scale is not None: kw["scale"] = ap(T, scale)
            if acc is not None: kw["accum_out"] = ap(T, acc)
            return g.scalar.activation(ap(T, out), ap(T, a), AF.Copy if func is None else func, **kw)
        n = cols(out)
        add("A", fn, [a, bias, scale], [out] + ([acc] if acc else []), (0.065, 0, n, 0, 0) if a[0] == "ind" else (0.03, max(64, n), 0, 0, 0))

    def scale(out, a, f):
        act(out, a, AF.Identity, scale=f)

    def covers(out, d):
        act(out, d, AF.Sign, bias=0.5, scale=-1.0)

    def mm(out, l, r, start=True, stop=True):
        n = max(min(64, cols(l)), cols(r)) * (4 if wide(l) == 4 else 1)
        add("P", lambda g, T, c: g.tensor.matmul(ap(T, out), ap(T, l), ap(T, r), start, stop), [l, r], [out], (0.005, 0, 0, 0, n))

    def mms(lst, start, stop, each=False):
        def fn(g, T, c):
            return [g.tensor.matmul(ap(T, o), ap(T, l), ap(T, r), each or start and j == 0, each or stop and j == len(lst) - 1) for j, (o, l, r) in enumerate(lst)][-1]
        n = sum(max(min(64, cols(l)), cols(r)) * (4 if wide(l) == 4 else 1) for o, l, r in lst)
        add("P", fn, [x for o, l, r in lst for x in (l, r)], [o for o, l, r in lst], (0.005 * len(lst), 0, 0, 0, n))

    def group(*parts, start=True, stop=True):
        parts = [p for p in parts if p]
        if parts[0][0][0][0] in DYN:
            parts = [[x for p in parts for x in p]]
        for j, p in enumerate(parts):
            mms(p, start and j == 0, stop and j == len(parts) - 1)

    def iota(out, pat, base, cm):
        fl = SB[out[0]][1] != I
        add("G", lambda g, T, c: g.iota(ap(T, out), pat, base, cm, allow_small_or_imprecise_dtypes=True) if fl else g.iota(ap(T, out), pat, base, cm),
            [], [out], (0.13, 2 * cols(out), 0, 0, 0))

    def sel(out, a, pat, op, base, cm, fill=0.0):
        add("G", lambda g, T, c: g.affine_select(ap(T, out), ap(T, a), pat, op, fill, base, cm), [a], [out], (0.17, 2 * cols(out), 0, 0, 0))

    def keep(out, a):
        sel(out, a, [[0, cols(out)]], AL.is_gt, 1, 0)

    def dma(q, out, a, rd, wr, nbytes, chain=False, wait=()):
        s = "d%d" % nd[0]; nd[0] += 1
        i = add(q, lambda g, T, c: (g.sync if q == "S" else g.scalar).dma_start(out(T), a(T)), rd, wr, (0.06, 0, 0, 0, 0), kind="d", sem=s, cnt=16,
                nbytes=nbytes, after=last[-1:] if chain else [], wait=list(wait))
        if chain: last.append(i)
        return i

    def copy(out, a, wait=(), piece=PIECE):
        n = piece // wide(a)
        for c in range(0, cols(a), n):
            o2, a2 = v(out[0], out[3] + c, out[3] + c + n), v(a[0], a[3] + c, a[3] + c + n)
            wait = [dma("S", lambda T, o2=o2: ap(T, o2), lambda T, a2=a2: ap(T, a2), [a2], [o2], 128 * piece, wait=wait)]
            ops[-1]["bulk"] = True
        return wait

    def send(items, lat, wait=()):
        ls = "l%d" % nl[0]; nl[0] += 1; ks = [k for s, d, k in items]
        rs = ["r%d" % (nr[0] + j) for j in range(len(items))]; nr[0] += len(items)

        def fn(g, T, c):
            topo = c["topo"]; tr = []
            for j, (s, d, k) in enumerate(items):
                dst = c["ahead"](k); rid, pid, _ = topo.addr(dst)
                mask = sum(1 << e for e in c["share"](0, ks)[j])
                if len(items) == 1:
                    return g.remote_dma(ap(T, d), ap(T, s), T.sem[rs[0]], T.sem[ls], pid, rid, mask)
                tr.append(RemoteDMATransfer(dst_ids=[DstId(rid=rid, pnc=pid)], dma_engine_mask=mask, remote_sem=T.sem[rs[j]], src=ap(T, s), dst=ap(T, d)))
            return g.remote_dma_fused(tr, local_sem=T.sem[ls])
        i = add("G", fn, [s for s, d, k in items], [], (1.0 if nl[0] > 1 else FIRST, 0, 0, 0, 0), kind="s", sem=ls, ks=ks, wait=list(wait))
        for j, (s, d, k) in enumerate(items):
            add("R", None, [], [d], (lat, 0, 0, 0, 0), kind="r", sem=rs[j], ks=ks, k=k, src=i)
        return i

    dma("A", lambda T: T.VSI[:, :], lambda T: T.vs[:, :], [], [v("VSI")], 25000)
    dma("A", lambda T: T.XZ0[:, :], lambda T: T.z[:, :], [], [v("XZ0")], 66000)
    dma("S", lambda T: T.W0[:, 0:Q], lambda T: T.rg[:, 0:Q], [], [v("W0", 0, Q)], 524288, True)
    dma("S", lambda T: T.DI[:, :], lambda T: T.nd[:, :], [], [v("DI")], 983040, True)
    loaded = dma("S", lambda T: T.W0[:, Q:M], lambda T: T.rg[:, Q:M], [], [v("W0", Q, M)], 524288, True)

    NB = [[sum(b - a for a, b in lanes(t, s, h, "b")) for t in range(3) for s in range(3)] for h in range(2)]
    ms(v("ONE"), 1.0); ms(v("ONE32"), 1.0)
    iota(v("II"), [[0, 8], [-1, 16]], 128, 1)
    iota(v("LI", 0, 24), [[1, 24]], 0, 0); iota(v("LI", 24, 32), [[4, 8]], 3, 0)
    iota(v("LJ", 0, 8), [[8, 2], [0, 4]], 0, 0); iota(v("LJ", 8, 16), [[8, 4], [0, 2]], 0, 0); iota(v("LK"), [[0, 16]], 0, 1)
    ts(v("LI", 48, 64), v("LK"), 7, AL.bitwise_and); tt(v("LI", 32, 48), v("LI", 48, 64), v("LJ"), AL.add)
    cp(v("LS"), v("LI"))
    ts(v("IJ"), v("II"), 15, AL.bitwise_and)
    ts(v("MK"), v("IJ"), 0.0, AL.is_equal)
    sel(v("BOF"), v("ONE"), [[-16, 8], [0, 16]], AL.is_ge, 0, 1); sel(v("BOF"), v("BOF"), [[16, 8], [0, 16]], AL.is_ge, 15, -1)
    sel(v("ID"), v("ONE"), [[-1, 128]], AL.is_equal, 0, 1)
    pb = v("WP", 288, 432)
    ms(pb, 1.0); sel(pb, pb, [[-16, 8], [-1, 18]], AL.is_equal, 2, 1); ms(vn("WP", 288, 8, 18), 0.0); ms(vn("WP", 289, 8, 18), 0.0)
    bo = vn("BOF", 0, 8, 16)
    act(v("BO32"), bo)
    for j in range(3):
        scale(v("SC3H", 8 * j, 8 * j + 8), bo, -4096.0)
    scale(v("NID"), v("ID"), -1.0); act(v("ID32"), v("ID")); scale(v("IDK"), v("ID"), 4096.0)
    for j, f in ((0, -B), (1, B), (3, 1.0), (4, B)):
        scale(v("WP", 144 * j, 144 * j + 144), pb, f)
    ms(v("GSEL"), 0.0); act(v("GSEL", 112, 128), v("MK", 0, 16))
    gsel = lambda g, p1: v("GSEL", 112 - 16 * g, 240 - 16 * g, p1=p1)
    ms(v("KC", 0, 288, p1=32), 64.0); ms(v("KC", 288, 576, p1=32), 64 * B); ms(vn("KC", 1, 8, 18, 0, 32), B / 32); ms(vn("KC", 145, 16, 18, 0, 32), 0.0)
    ms(vn("KC", 0, 32, 18, 0, 32), NEG / 32)
    kc = lambda cand, guard: v("KC", 144 * (2 + guard if cand else 1 - guard), 144 * (3 + guard if cand else 2 - guard), p1=32)
    ms(v("CR", p1=32), 5.0 / 16); ms(v("CR", p0=32, p1=64), -6.0 / 32); ms(v("CR", 144, 160, p1=32), -1.0 / 16)
    ms(v("SCL"), -B); sel(v("SCL", 0, 9), v("SCL", 0, 9), [[-16, 9]], AL.is_ge, 0, 1, -B / 2); sel(v("SCL", 9, 18), v("SCL", 9, 18), [[-16, 9]], AL.is_gt, 128, -1, -B / 2)
    for j in range(2):
        ms(vn("CR", j, 8, 18, 32, 64), 2.0)
    l0, l1 = 128 - max(NB[0]), 256 + max(NB[1])
    ms(v("LAN", l0, l1, p0=32, p1=64), 1.0); ms(v("LAN", l0, l1, p1=32), 0.0); ms(v("LAN", 128, 256, p1=32), -0.5)
    move = lambda out, a: dma("S", lambda T: ap(T, out), lambda T: ap(T, a), [a], [out], (a[2] - a[1]) * cols(a) * wide(a), wait=[loaded])
    iota(v("D11"), [[0, 864]], 1 - 2 ** 24, 0); ms(vn("D11", 0, 8, 18), SENT); ms(vn("D11", 144, 8, 18), SENT2)
    if GF[0]: iota(v("D10"), [[0, 864]], 1 - 2 ** 24, 0); ms(vn("D10", 0, 8, 18), SENT); ms(vn("D10", 144, 8, 18), SENT2)
    else:
        for a, b in ((0, 432), (432, 864)): act(v("D10", a, b), v("WP", 288, 720), AF.Identity, bias=1.0 - 2 ** 24, scale=0.0)
        ms(vn("D10", 0, 8, 18), SENT); ms(vn("D10", 144, 8, 18), SENT2)
    ms(v("NM", 0, 96), 0); ms(v("CMP"), 0.0); ms(vn("CMP", 0, 8, 4), -1.0)
    ms(v("DD", BASE, Q), 0.0)
    for n in ("SA0", "SA1"): ms(v(n), 0.0)
    add("V", lambda g, T, c: g.vector.memset(T.sent[:, :], 0), [], [v(n) for n in SENTU], (0, FILL["sent"] / 2, 0, 0, 0))
    for t in range(3):
        cp(v("VU", 32 * t, 32 * t + 16), v("VSI", 16 * t, 16 * t + 16))
    cp(v("VSF"), v("VSI"))
    for a in range(8):
        scale(vn("VB", a, 48, 8), v("VSF"), v("BO32", a, a + 1))
    for j in range(6):
        group([(v("Y0", 8 * j, 8 * j + 8), gsel(b, 128), v("VB", 64 * j + 8 * b, 64 * j + 8 * b + 8)) for b in range(8)])
    act(v("VL"), v("Y0", 0, 48))
    for i in range(16):
        (act if i < AREP else cp)(vn("XB0", i, L, 16), v("XZ0"))
    act(v("RZ"), v("W0", 0, 1)); ms(v("W0", 0, 1), 512.0); cp(v("W0", R1, R1 + Q), v("W0", 0, Q)); act(v("W0", R2, R2 + Q), v("W0", 0, Q))
    ph[0] = "x"
    s1 = send([(v("XZ0"), v("XZ%d" % k), k) for k in (1, 2)], 4.0, [loaded])
    s2 = send([(v("VU", 32, 64), v("VU1"), 1), (v("VL", 16, 32), v("VL1"), 1), (v("VU", 64, 96), v("VU2"), 2), (v("VL", 32, 48), v("VL2"), 2)], 4.0, [loaded])
    copy(v("W1", 0, R1 + Q), v("W0", 0, R1 + Q), [s1, s2], 3 * PIECE); copy(v("W1", R2, WW), v("W0", R2, WW), [s1, s2])
    for a, b in ((0, 960), (960, BASE)):
        keep(v("DD", a, b), v("DI", a, b))
    ph[0] = "j"
    sel(v("TRI"), v("BOF"), [[1, 128]], AL.is_ge, 0, -1); sel(v("TRE"), v("BOF"), [[1, 128]], AL.is_gt, 0, -1)
    sel(v("T1"), v("TRI"), [[-1, 128]], AL.not_equal, 0, 1, -31.0); sel(v("T2"), v("TRE"), [[-1, 128]], AL.not_equal, 0, 1, -64.0)
    ms(v("SEL", 0, 128, p0=64, p1=96), 0.0); ms(v("SEL", 0, 128, p0=64, p1=65), 1.0)
    ms(lo(v("TRM")), 0.5); sel(lo(v("TRM")), lo(v("TRM")), [[0, 2], [-1, 64]], AL.is_ge, 0, 1); act(lo(v("VTH")), lo(v("TRM")))
    for j in range(2):
        cp(lo(v("SEL", 64 * j, 64 * j + 64)), lo(v("ID", 0, 64)))
    for j in (1, 2, 4):
        move(lo(v("SEL", 128 * j, 256 * j)), lo(v("SEL", 0, 128 * j)))
        move(v("SEL", 128 * j, 256 * j, p0=64 + j, p1=72), v("SEL", 0, 128 * j, p0=64, p1=72 - j))
        move(v("SEL", 128 * j, 256 * j, p0=64, p1=64 + j), v("SEL", 0, 128 * j, p0=72 - j, p1=72))
    iota(v("DUMC"), [[256, 3], [0, 8]], DUM, 4); iota(v("NC"), [[1, 128]], 0, 0); iota(v("NL"), [[64, 2], [0, 8]], BASE, 1)
    ts(v("NB"), vn("NL", 0, 2, 8), 1.0, AL.add, B, AL.mult)
    scale(v("NBOF"), v("BOF"), -1.0); scale(v("T1B"), v("T1"), B2); scale(v("ID64N"), v("ID"), -64.0)
    for j in range(2):
        act(lo(v("I2N", 64 * j, 64 * j + 64)), lo(v("ID64N", 0, 64)))
    for j in range(3):
        act(v("MC", 32 * j, 32 * j + 32), vn("BOF", 0, 32, 2))
    ms(v("CB2", p1=32), B2); ms(v("XX"), 0.0); ms(v("W3"), 0.0); ms(v("VV"), 0.0)
    for n, f in (("WD", GF[1]), ("WT", GF[2])):
        if f: iota(v(n), [[0, SB[n][0]]], 0, 0)
        else: scale(v(n), v("WP", 0, SB[n][0]), 0.0)
    act(vn("WD", 15, 8, 16), bo); scale(vn("WD", 16, 8, 16), bo, -1.0); act(vn("WD", 144 + 15, 8, 16), bo); scale(vn("WD", 288 + 16, 8, 16), bo, -1.0)
    act(v("WC"), v("MK", 0, 16), AF.Identity, bias=1.0, scale=-1.0)
    for i in range(RB):
        ts(v("RBP", 128 * i, 128 * i + 128), v("BOF"), v("MK", i, i + 1), AL.mult, B2, AL.mult)
    for j in (1, 2, 4, 8)[RB // 2:]:
        move(v("RBP", 128 * j, 256 * j, p0=j), v("RBP", 0, 128 * j, p1=128 - j)); move(v("RBP", 128 * j, 256 * j, p1=j), v("RBP", 0, 128 * j, p0=128 - j))
    act(v("NLH"), v("NL"))
    for e, t in enumerate((0, 2)):
        act(v("WE", e, e + 1), v("MK", 8 + t, 9 + t), AF.Identity, bias=v("MK", t, t + 1), scale=1.0 / 1024)
        scale(vn("WT", 144 * e + 15, 8, 16), bo, v("WE", e, e + 1))
        scale(v("WX", 128 * e, 128 * e + 128), v("NBOF"), v("WE", e, e + 1))
        for j, row in enumerate((t, 8 + t)):
            scale(v("DG", 256 * e + 128 * j, 256 * e + 128 * j + 128), v("ID"), v("WC", row, row + 1))

    def repeat(k):
        ph[0] = "x"
        for a, b in REP:
            for i in range(16):
                if i < VREP[k - 1]:
                    cp(vn("XB%d" % k, 16 * a + i, b - a, 16), v("XZ%d" % k, a, b)); continue
                keep(vn("XB%d" % k, 16 * a + i, b - a, 16), v("XZ%d" % k, a, b))
                ops[-1]["cnt"] = 16 - VREP[k - 1]; ng[0] -= 1
            ng[0] += 1
    repeat(1)
    rec = lambda t, a=0, b=WW: v("W1" if t else "W0", a, b)
    node = lambda t: v("DD", Q * (t - 1), Q * t) if t else v("DI")
    vl = lambda t, h: v("VL%d" % t if t else "VL", 8 * h, 8 * h + 8)
    ends = lambda n, s, k, cnt=8: vn("SC" + n, SEG[s, k] + 17, cnt, 18)
    slot = lambda n, s, k: vn("D1" + n, SEG[s, k], 8, 18)
    nm = lambda t, h, j=None: v("NM", 64 * t + 32 * h, 64 * t + 32 * h + 32) if j is None else vn("NM", 64 * t + 32 * h + j, 8, 4)

    aside = lambda t, s, h: s == 0 and t <= h

    def spread(out, bv, src, lst, mask, n, p1):
        tt(bv, ind(src, lst), mask, AL.mult)
        group([(out, gsel(g, p1), vn(bv[0], g, n, 8, 0, p1)) for g in range(8)])

    def start(t, h):
        ph[0] = "w%d%d" % (t, h); n = str(h)
        ts(slot(n, 2, 2), vl(t, h), SENT, AL.add)

    def step1(t, h, a, b, off, P):
        n = str(h); x = v("XZ%d" % t, 128 * h, 128 * h + 128)
        act(v("S1R" + n, a, b), ind(rec(t, 0, M), off))
        group([(v(P, 0, b - a), v("ID"), v("S1R" + n, a, b))] + [(v(P, c, c + 128), v("NID"), x) for c in range(0, b - a, 128)])
        covers(v("S1C" + n, a, b), v(P, 0, b - a))

    def walk(t, s, h, between=None):
        ph[0] = "w%d%d" % (t, h); n = str(h); nk = s + 1; nb = sum(l1 - l0 for l0, l1 in lanes(t, s, h, "b"))
        u, K, C, banks = (str(3 - h), "Y0", "Y1", ["Y1"]) if aside(t, s, h) else (n, "K" + n, "B" + n, ["B0", "A0"][:3 - t] if (h, s) == (0, 0) else ["A" + n, "B" + n])
        RD, CM = "RD" + u, "CM" + u
        ov = "OV%d%d" % (t, h); e16 = v("E16" + u); tags = {2: (0, 1, 2), 1: (1, 0), 0: (0,)}[s]
        off = v("VU%d" % t if t else "VU", 8 * h, 8 * h + 8) if s == 2 else v(ov, 8 - 8 * s, 16 - 8 * s)
        if t > 0 and s == 2: step1(t, h, 0, 256, v("RO%d%d" % (t, h), 0, 16), "A" + n)
        if t > 0 and s == 1 - h: step1(t, h, 256, 384, v("RP%d%d" % (t, h), 0, 8), banks[0])
        cap = s == 1 or (s == 0 and h == 1)
        if cap: ts(e16, ind(node(t), off), 4096.0 * nk, AL.min)
        else: cp(e16, ind(node(t), off))
        x16 = lambda l0, l1: v("XB%d" % t, 16 * (128 * h + l0), 16 * (128 * h + l1))
        for l0, l1 in lanes(t, s, h, "a"):
            tt(v(RD, 16 * l0, 16 * l1), ind(rec(t), v("E16" + u, l0, l1)), x16(l0, l1), AL.subtract)
            ts(v(CM, 16 * l0, 16 * l1), v(RD, 16 * l0, 16 * l1), 0.0, AL.is_le)
        for l0, l1 in joined(lanes(t, s, h, "bc"), CUT["g"][h]):
            act(v(RD, 16 * l0, 16 * l1), ind(rec(t), v("E16" + u, l0, l1)))
        for l0, l1 in lanes(t, s, h, "c"):
            tt(v(CM, 16 * l0, 16 * l1), v(RD, 16 * l0, 16 * l1), x16(l0, l1), AL.is_le)
        if between and aside(t, s, h): between(u); ph[0] = "w%d%d" % (t, h)
        for j, (l0, l1) in enumerate(lanes(t, s, h, "b")):
            P = v(banks[j % len(banks)], 0, 16 * (l1 - l0)); a, b = 16 * l0, 16 * l1
            group([(P, v("NID"), x16(l0, l1))], [(P, v("ID"), v(RD, a, b))])
            covers(v(CM, a, b), P)
        fk = lambda j: v("FK" + u, 128 * j, 128 * j + 128); wp = lambda j, k: v("WP", 144 * j, 144 * (j + k))
        for j in range(4 if s == 2 else 1 if cap and s == 0 else 2):
            ts(fk(j), e16, (-2048.0, -4096.0, -8192.0, -8192.0)[j], AL.add, 2048.0 * (j == 0), AL.max if j in (1, 2) else AL.min)
        gd = [] if t == 0 else [(2, 0), (1, 1)] if s == 2 else [(0, 2)] if s == 1 - h else []
        run = lambda k: v(K, 144 * tags.index(k), 144 * tags.index(k) + 144)
        gcol = lambda k: vn(K, 144 * tags.index(k) + 1, 8, 18)
        p1 = [(run(k), v("ONE", p1=32), kc(int(k == 1), int(k not in [x for x, j in gd]))) for k in tags]
        p2 = [(run(1), fk(0), wp(0, 1)), (v(K, 0, 288), fk(0), wp(2, 2))] if s else [(run(0), fk(0), wp(2, 1))]
        p3 = ([] if cap else [(run(0), fk(1), wp(1, 1))], [(v(K, 0, 288), fk(1), wp(3, 2))],
              [(v(K, 0, 288), fk(1), wp(1, 2)), (v(K, 144, 432), fk(2), wp(1, 2)), (v(K, 288, 432), fk(3), wp(0, 1))])[s]
        p4 = [(vn(K, 2 + i, 8 * nk, 18), vn(RD, i, 128, 16), v("SC3H", 0, 8 * nk)) for i in range(16)]
        p5 = [(gcol(k), v("S1R" + n, 128 * j, 128 * j + 128), v("SC3H", 0, 8)) for k, j in gd]
        p5 += [(gcol(k), v(i), v("RG%d%d" % (t, h), o + 8 * j, o + 8 * j + 8)) for k, j in gd if k for i, o in (("ID", 0), ("IDK", 16))]
        group(p1, p2, p3, p4[:8], p4[8:], p5, stop=False)
        w = 144 + 8 * len(gd); la = 128 + nb if h else 128 - nb; PP = "PP" + u; sc = 9 * h + nb // 16
        group([(v(C, 0, w), v("LAN", la, la + 128, p1=64), v("CR", 0, w, p1=64))]
              + [(v(C, 144 + 8 * i, 152 + 8 * i), v("S1C" + n, 128 * j, 128 * j + 128), bo) for i, (k, j) in enumerate(gd)],
              [(vn(C, 2 + i, 8, 18), vn(CM, i, 128, 16), bo) for i in range(16)])
        act(v(PP, 0, w), v(C, 0, w), AF.Relu, bias=v("RA%d" % t, 0, 1) if t else None, scale=v("SCL", sc, sc + 1))
        group([(gcol(k), v("ID"), v(PP, 144 + 8 * i, 152 + 8 * i)) for i, (k, j) in enumerate(gd)]
              + [(run(k), v("ID"), v(PP, 0, 144)) for k in tags], start=False)
        o = SEG[s, tags[0]]
        for a, b in ([(288, 432), (0, 288)], [(0, 144), (144, 288)], [(0, 144)])[2 - s]:
            scan(v("SC" + n, o + a, o + b), v(K, a, b), v("D1" + n, o + a, o + b), AL.min, AL.max)
        mj = v("MJ" + n, 16 - 8 * s, 24 - 8 * s)
        if s > 0:
            ts(mj, ends(n, s, s), 2047, AL.bitwise_and)
            if FAST[h]:
                tt(v("BV" + n), ind(mj, v("LS", 0, 8)), v("MK"), AL.mult)
                mm(v(C, 440, 448), v("BV" + n), bo)
            else:
                spread(v(C, 440, 448), v("BV" + n, 0, 64), mj, v("LS", 32, 36), vn("BOF", 0, 64, 2), 8, 128)
            cp(v(ov, 16 - 8 * s, 24 - 8 * s), v(C, 440, 448))
        if s == 2:
            ts(v("A1" + n), ends(n, 2, 1), -2049, AL.bitwise_and); ts(v("B1" + n), mj, SENT, AL.add)
            tt(slot(n, 1, 1), v("A1" + n), v("B1" + n), AL.min)
        if (t, s, h) == (1, 0, 0):
            tt(v("NZ0"), ends(n, 0, 0), slot(n, 0, 0), AL.is_lt)
        name = nm(t, h, {2: 0, 1: 2 - h, 0: 3}[s])
        ts(name, ends(n, s, 0), 4095, AL.bitwise_and)
        if s > 0: tt(slot(n, s - 1, 0), ends(n, s, 0), name, AL.subtract)
        if s == 1 - h and t > 0:
            tt(v("GE" + n), slot(n, s, 0), gcol(0), AL.is_ge); tt(nm(t, h, 1 + h), v("GE" + n), v("RS%d%d" % (t, h)), AL.mult)

    def yg(k, h, src, P, c):
        mm(v(P, c, c + 128, p1=8), src, v("ID" if k else "ID32")); act(v("YG", 256 * k + 128 * h, 256 * k + 128 * h + 128, p1=8), v(P, c, c + 128, p1=8))

    def guards21(t, h):
        n = str(h); sg = "SG%d%d" % (t, h)
        if t < 2:
            ov, ro = "OV%d%d" % (t, h), "RO%d%d" % (t + 1, h)
            cp(v(ov, 16, 32), v("MJ" + n)); ts(v(ov, 32, 48), ends(n, 2, 2, 16), SENT, AL.is_ge, 32768.0, AL.mult)
            send([(v(ov), v(ro), 1)], FAR)
            ph[0] = "w%d%d" % (t + 1, h)
            return cp(v("RG%d%d" % (t + 1, h)), v(ro, 16, 48))
        ts(v("LT" + n), ends(n, 2, 2, 16), SENT, AL.is_lt); tt(v(sg, 0, 16), v("LT" + n), v("MJ" + n), AL.mult)
        for j in range(2):
            yg(2 - j, h, v(sg, 8 * j, 8 * j + 8), "A" + n, 128 * j)

    def guard0(t, h):
        n = str(h); gs = "GS%d%d" % (t, h); K = "Y0" if aside(t, 0, h) else "K" + n
        tt(v("ZZ" + n), nm(t, h), v("CMP"), AL.is_equal); scan(v(gs), v("ZZ" + n), nm(t, h), AL.mult, AL.add)
        if t == 2:
            return yg(0, h, vn(gs, 3, 8, 4), K, 256)
        tt(v("BG" + n), ind(v(gs), v("LS", 24, 32)), v("MK"), AL.mult)
        so, rp = "SO%d%d" % (t, h), "RP%d%d" % (t + 1, h)
        mm(v(K, 448, 456), v("BG" + n), v("BO32")); cp(v(so, 0, 8), v(K, 448, 456)); cp(v(so, 8, 16), vn(gs, 3, 8, 4))
        send([(v(so), v(rp), 1)], FAR)
        ph[0] = "w%d%d" % (t + 1, h)
        cp(v("RS%d%d" % (t + 1, h)), v(rp, 8, 16))

    i64 = lo(v("ID", 0, 64)); xb, xa = v("XX", 0, 8), v("XX", 8, 16); P = "A0"
    ya, yb, yw = v("YAB", 0, 64), v("YAB", 64, 128), v("YAB", 128, 192); fr = v("FR")

    def source(t):
        ph[0] = "s%d" % t; even = t % 2 == 0
        cp(xb, v("MJ0", 8, 16))
        if even:
            ts(v("FL"), ends("0", 2, 1), 2048, AL.bitwise_and); tt(v("A2"), v("FL"), vl(t, 0), AL.min); tt(v("DV"), v("MJ0", 0, 8), v("A2"), AL.subtract)
            tt(v("NW"), ends("0", 1, 1), slot("0", 1, 1), AL.is_lt); tt(v("TQ"), v("NW"), v("DV"), AL.mult); tt(v("XA"), v("TQ"), v("A2"), AL.add)
            tt(xa, v("TQ"), v("A2"), AL.add)
        else:
            tt(v("ZP"), nm(t, 0), v("CMP"), AL.is_equal); scan(v("GP"), v("ZP"), nm(t, 0), AL.mult, AL.add)
            act(vn("VV", 0, 8, 4), vl(t, 0)); cp(vn("VV", 2, 8, 4), v("MJ0", 0, 8))
            ts(v("NZ"), nm(t, 0), 0.0, AL.is_gt); tt(v("UU"), v("NZ"), v("VV"), AL.mult); scan(v("AP"), v("ZP"), v("UU"), AL.mult, AL.add)
            act(xa, vn("AP", 3, 8, 4)); act(v("XA"), vn("AP", 3, 8, 4))
            act(v("BC"), ind(v("GP"), v("LS", 24, 32))); mm(v(P, 384, 448), lo(v("BC")), lo(v("ID32", 0, 64)))
        spread(v(P, 0, 4), v("BA", 0, 32), v("XA"), v("LS", 32, 34), v("MC", 0, 32), 4, LA)
        cp(v("OA", 0, 4), v(P, 0, 4)); (act if t else cp)(v("EA"), ind(node(t), v("OA", 0, 4)))
        tt(v("N01"), v("XX", 0, 16), v("XX", 8, 24), AL.is_equal)
        mms([(v(P, 192 + 64 * w, 256 + 64 * w, p0=64, p1=72), lo(x), i64) for w, x in enumerate((xb, xa))]
            + [(v(P, 320, 328, p0=64 * w, p1=64 * w + 64), i64, lo(x)) for w, x in enumerate((xb, xa))], True, True, True)
        act(v("VTH", p0=64, p1=72), v(P, 192, 320, p0=64, p1=72)); scale(v("NX"), v(P, 320, 328), -1.0)
        for c in range(2):
            Y = "Y%d" % c
            mms([(v(Y, 128 * j, 128 * j + 128), v("SEL", 512 * c + 128 * j, 512 * c + 128 * j + 128, p1=72), v("VTH", p1=72)) for j in range(4)], True, True, True)
            for j in range(4):
                o = 512 * c + 128 * j; nx = v("NX", 4 * c + j, 4 * c + j + 1)
                if EQS[2 * t + c]: act(v("AB", o, o + 128), v(Y, 128 * j, 128 * j + 128), AF.Abs, bias=nx)
                else: ts(v("CMM", o, o + 128), v(Y, 128 * j, 128 * j + 128), nx, AL.add, 0.0, AL.is_equal)
            if EQS[2 * t + c]: act(v("CMM", 512 * c, 512 * c + 512), v("AB", 512 * c, 512 * c + 512), AF.Relu, bias=1.0, scale=-2.0)

    def step3(t, u):
        ph[0] = "s%d" % t; even = t % 2 == 0; e = t // 2; ea, eb = v("EA"), v("EB"); nr3 = 3 if even else 2
        cp(eb, v("E16" + u, 0, 64)); act(fr, ea if even else eb, AF.Relu, bias=1.0, scale=-1.0)
        mms([(v(P, 64, 128), v("T2"), fr)] + ([(v(P, 128, 192), v("TRI"), fr)] if even else []), True, True, True)
        act(v("TA"), v(P, 64, 128), AF.Relu, bias=-63.0 * (M + BASE), scale=-1.0 * (M + BASE))
        if even: act(v("PLF"), v(P, 128, 192), AF.Identity, bias=-33.0)
        bars = [v("N01", 0, 8), v("N01", 8, 16)] + ([] if even else [v("NZ0")])
        lst = [(vn(P, 8 + r, 8, 4), lo(v("I2N")), lo(x)) for j, x in enumerate(bars) for r in range(3 if j else 4)]
        group(lst[:4] + [(v(P, 8, 40, p0=p, p1=p + 64), fr, vn("BOF", 0, 32, 4)) for p in (0, 64)] + lst[4:])
        ts(v("ASK"), v(P, 8, 40), 0.0, AL.is_gt, B2, AL.mult)
        lst = [(lo(v("Y0", 0, 24)), v("ONE", 0, 64, p1=1), v("CB2", p1=1)), (lo(v("Y0", 0, 8)), i64, lo(xa)), (lo(v("Y0", 8, 16)), i64, lo(xb))]
        if even: lst += [(lo(v("Y0", 16, 24)), i64, lo(v("NLH", 8 * e, 8 * e + 8)))]
        own = [(lo(v("Y0", 8 * r, 8 * r + 8)), lo(v("NID", 0, 64)), lo(vn("ASK", 0, 8, 4))) for r in range(3)]
        met = [(lo(vn("Y0", j // 2, 3, 8)), v("CMM", 64 * j, 64 * j + 64), v("ASK", 4 * (j // 2), 4 * (j // 2) + 3)) for j in range(16)]
        group(lst, own + met[:8], met[8:])
        tt(lo(v("W3")), lo(v("Y0", 0, 24)), lo(v("DUMC")), AL.min)
        if t < 2:
            act(lo(v("JK")), lo(v("Y0", 16, 24)), AF.Relu, bias=lo(v("NB", e, e + 1)) if even else B, scale=-B, acc=lo(v("ASUM")))
            mm(v(P, 352, 353), lo(v("ONE32")), lo(v("ASUM")))
            ts(v("AI"), v(P, 352, 353), 0.5 / B, AL.mult, -0.25, AL.add); ts(v("SA%d" % t, 0, 1), v("AI"), 2 * B, AL.mult, v(P, 352, 353), AL.subtract)
            send([(v("SA%d" % t), v("RA%d" % (t + 1)), 1)], FAR)
        spread(v(P, 356, 356 + 4 * nr3), v("BA", 0, 32 * nr3), v("W3"), v("LS", 40, 40 + 2 * nr3), v("MC", 0, 32 * nr3), 4 * nr3, LA)
        cp(v("OSC", 0, 4 * nr3), v(P, 356, 356 + 4 * nr3))
        if not even:
            tt(v("TB"), ea, v(P, 384, 448), AL.not_equal); tt(ya, ea, v("TB"), AL.mult)
            tt(v("TC"), v("TA"), v(P, 384, 448), AL.min); tt(yb, eb, v("TC"), AL.add)
            return
        x = v("XZ%d" % t, 0, 64); dg = lambda j: v("DG", 256 * e + 128 * j, 256 * e + 128 * j + 128)
        tt(v("CUT"), ind(rec(t, 0, M), v("OV%d0" % t, 8, 12)), x, AL.subtract)
        group([(v(P, 64, 128), dg(1), v("CUT")), (v(P, 64, 128), v("ID"), x)]); group([(v(P, 128, 192), dg(0), v("CUT")), (v(P, 128, 192), v("ID"), x)])
        act(v("CH"), v(P, 64, 192))
        d = v(P, 384, 448); raw = [(a, min(b, LA)) for a, b in joined(lanes(t, 0, 0, "bc"), 128) if a < LA]
        group([(d, v("WT", 144 * e + 15 - j, 144 * e + 143 - j), vn("RD" + u, j, 64, 16)) for j in range(15)]
              + [(v(P, 384 + a, 384 + b), v("WX", 128 * e, 128 * e + 128), v("XZ%d" % t, a, b)) for a, b in raw]
              + [(d, v("WT", 144 * e, 144 * e + 128), vn("RD" + u, 15, 64, 16))])
        ts(v("TR"), d, -1.0, AL.min); ts(v("GO"), d, -0.5, AL.is_ge); tt(v("STR"), d, v("TR"), AL.is_lt)
        mm(v(P, 256, 320), v("T1B"), v("STR"))
        group([(v(P, 192, 256), v("T1"), v("STR")), (v(P, 192, 256), v("NBOF"), fr), (v(P, 192, 256), v("ID64N"), v("GO"))])
        tt(v("NU"), v(P, 256, 320), eb, AL.subtract)
        ts(v("TB"), v(P, 192, 256), -32.0, AL.is_ge); tt(yb, eb, v("TB"), AL.mult); tt(yw, eb, v("GO"), AL.mult)
        tt(v("TD"), v("TA"), v("NC", 64 * e, 64 * e + 64), AL.min)
        for c in range(2):
            Y = "Y1"
            mms([(v(Y, 64 * j, 64 * j + 64), v("RBP", 128 * (8 * c + j), 128 * (8 * c + j) + 128), v("PLF")) for j in range(8)], True, True, True)
            for j in range(8):
                tt(v("Y2", 512 * c + 64 * j, 512 * c + 64 * j + 64), v(Y, 64 * j, 64 * j + 64), v("NU"), AL.max)
        wd = lambda i: 288 if i == 0 else 144 if i == 15 else 0
        group([(v("Y0", 0, 64), v("ID32"), ea), (v("Y0", 0, 64), v("ID"), v("TA")), (v("Y0", 0, 64), v("ID"), v("TD"))],
              *[[(v("Y0", 0, 64), v("WD", wd(i) + 15 - i, wd(i) + 143 - i), v("Y2", 64 * i, 64 * i + 64))] for i in range(16)])
        cp(v("YI"), v("Y0", 0, 64)); ts(ya, v("YI"), 16383, AL.bitwise_and)

    def commit(t):
        ph[0] = "s%d" % t; even = t % 2 == 0
        for a, b in ((4, 12), (0, 4)) if even else ((0, 8),):
            cp(ind(v("DD", Q * min(t, LASTD), Q * min(t, LASTD) + WIN), v("OSC", a, b)), v("YAB", 16 * a, 16 * b))
        if even:
            for base in ((0, R1, R2) if t == 0 else (RO,)):
                n = 4 if base in (R1, R2) else 8
                cp(ind(v("W1", base, base + WIN), v("OSC", 4, 4 + n)), v("CH", 0, 16 * n))
            if t == 0: act(v("W1", R1 + BASE, R1 + BASE + LA), v("W1", BASE, BASE + LA))
        ph[0] = "c"
        if t < LASTD: copy(v("DD", Q * t + Q, Q * t + 2 * Q), v("DD", Q * t, Q * t + Q))
        if t == 0: copy(v("W1", RO, RO + Q), v("W1", 0, Q)); act(v("W1", RO, RO + 1), v("RZ"))

    for t in range(3):
        for h in range(2):
            start(t, h)
        for s in (2, 1):
            for h in range(2):
                walk(t, s, h)
                if s == 1: guards21(t, h)
        source(t)
        walk(t, 0, 0, lambda u: step3(t, u))
        if not aside(t, 0, 0): step3(t, "0")
        ph[0] = "w%d0" % t; guard0(t, 0)
        walk(t, 0, 1); guard0(t, 1)
        commit(t)
        if t == 0: repeat(2)
    ph[0] = "o"
    dma("S", lambda T: T.yr[:, :], lambda T: T.W1[:, RO:RO + Q], [v("W1", RO, RO + Q)], [], 524288)
    dma("S", lambda T: T.yn[:, :], lambda T: T.DD[:, LASTD * Q:LASTD * Q + Q], [v("DD", LASTD * Q, LASTD * Q + Q)], [], 1048576)
    dma("S", lambda T: T.yg[:, :], lambda T: T.YG[0:8, :], [v("YG", p1=8)], [], 25000)
    return ops


def meet(a, b):
    if a[4] <= b[3] or b[4] <= a[3] or a[2] <= b[1] or b[2] <= a[1]:
        return False
    if a[5] == b[5] and a[5] > 1 and (a[3] - b[3]) % a[5] != 0:
        return False
    return True


def depend(ops):
    hard = [set() for _ in ops]; soft = [set() for _ in ops]; acc = {}; bank = {}
    for i, o in enumerate(ops):
        soft[i].update(o["after"]); hard[i].update(o.get("wait", []))
        for x, w in [(x, False) for x in o["rd"]] + [(x, True) for x in o["wr"]]:
            if x[0] in DYN:
                o["dyn"] = x[0]
            elif x[0] in PS:
                for e, j in bank.setdefault(x[0], {}).items():
                    if j != i: (soft if e == o["eng"] else hard)[i].add(j)
                bank[x[0]][o["eng"]] = i
                if o["eng"] == "P": continue
            lst = acc.setdefault(x[0], [])
            for y, j, wy in lst:
                if j != i and (w or wy) and meet(x, y):
                    (soft if o["eng"] == "P" and ops[j]["eng"] == "P" else hard)[i].add(j)
            if w and x[5] == 1 and x[1] == 0 and x[2] == 128:
                lst[:] = [z for z in lst if not (x[3] <= z[0][3] and z[0][4] <= x[4])]
            lst.append((x, i, w))
        if o["kind"] == "r": soft[i].add(o["src"])
    return hard, soft


def turns(ops, hard, seq):
    hard = [set(h) for h in hard]; bank = {}; sent = []
    for i in seq:
        o = ops[i]
        if o["kind"] == "s": sent = [i]
        if "bulk" in o: hard[i].update(sent)
        if "dyn" in o:
            b = bank.setdefault(o["dyn"], {})
            hard[i].update(j for e, j in b.items() if e != o["eng"])
            b[o["eng"]] = i
    return hard


def costs(ops, m):
    return [c[0] * (m["far"] if k in "rs" else m["cy"] / 0.9e-3) + m["cy"] * (c[1] + m["g"] * c[2] + m["sc"] * c[3] + m["pe"] * c[4]) for c, k in ((o["cost"], o["kind"]) for o in ops)]


def order(ops, hard, soft, m, tune):
    n = len(ops); LAT = m["lat"]; cost = costs(ops, m); rnd = tune["seed"] * 7919 + 1
    succ = [[] for _ in ops]
    for i in range(n):
        for j in hard[i] | soft[i]: succ[j].append(i)
    pr = [0.0] * n
    for i in range(n - 1, -1, -1):
        d = cost[i] + (1.5 + ops[i]["nbytes"] / m["bw"] if ops[i]["kind"] == "d" else 0)
        pr[i] = d + max([pr[j] + (LAT if i in hard[j] else 0) for j in succ[i]] + [0.0])
    pr = [p + tune.get(o["ph"], 0.0) for p, o in zip(pr, ops)]
    pred = [list(hard[i] | soft[i]) for i in range(n)]; sl = tune["slack"]

    def sweep(pr, back):
        nxt, prv = (pred, succ) if back else (succ, pred)
        left = [len(p) for p in prv]; ready = {e: [] for e in "VAPGSR"}; rt = [0.0] * n; end = [0.0] * n
        for i in range(n):
            if left[i] == 0: ready[ops[i]["eng"]].append(i)
        free = {e: 0.0 for e in ready}; seq = []; bus = 0.0; bank = {}
        while len(seq) < n:
            best = None
            for e, lst in ready.items():
                if not lst: continue
                for i in lst:
                    if "dyn" in ops[i]:
                        rt[i] = max([rt[i]] + [f + LAT for e2, f in bank.get(ops[i]["dyn"], {}).items() if e2 != e])
                t0 = max(free[e] if e != "R" else 0.0, min([rt[i] for i in lst]))
                if best is None or t0 < best[0]: best = (t0, e)
            t0, e = best
            i = max([i for i in ready[e] if rt[i] <= t0 + sl], key=lambda i: (pr[i], -i))
            t0 = max(t0, rt[i]); o = ops[i]; ready[e].remove(i); seq.append(i)
            if "dyn" in o:
                b = bank.setdefault(o["dyn"], {})
                t0 = max([t0] + [f + LAT for e2, f in b.items() if e2 != e]); b[e] = t0 + cost[i]
            free[e] = fin = t0 + cost[i]
            if o["kind"] == "d":
                bus = max(bus, t0) + o["nbytes"] / m["bw"]; fin = bus + 1.5
            end[i] = fin
            for j in nxt[i]:
                hd = j in hard[i] if back else i in hard[j]
                rt[j] = max(rt[j], fin + LAT if hd else fin if "R" in (ops[j]["eng"], e) else t0); left[j] -= 1
                if left[j] == 0: ready[ops[j]["eng"]].append(j)
        return seq, end

    seq, end = sweep(pr, False); best = (max(end), seq, end)
    keys = sorted(set((o["ph"], o["eng"], o["wr"][0][0] if o["wr"] else "") for o in ops)); at = {k: j for j, k in enumerate(keys)}
    kind = [at[(o["ph"], o["eng"], o["wr"][0][0] if o["wr"] else "")] for o in ops]
    for it in range(tune.get("fb", 0)):
        p = sweep(best[2], True)[1]; sh = {}
        if it > 0:
            for _ in range(tune.get("moves", 8)):
                rnd = (rnd * 1103515245 + 12345) % 2147483648
                sh[(rnd >> 8) % len(keys)] = tune.get("step", 1.5) * ((rnd >> 4 & 15) - 7.5) / 7.5
        seq, end = sweep([x + sh.get(k, 0.0) for x, k in zip(p, kind)], False)
        if max(end) <= best[0]: best = (max(end), seq, end)
    return best[1]


def renew(ops, hard, soft, seq, m, tune):
    n = len(ops); LAT = m["lat"]; cost = costs(ops, m)
    eng = ["VAPGSR".index(o["eng"]) for o in ops]; dyn = ["dyn" in o for o in ops]; bulk = ["bulk" in o for o in ops]; out = [o["kind"] == "s" for o in ops]
    dm = [o["nbytes"] / m["bw"] if o["kind"] == "d" else -1.0 for o in ops]; src = [o.get("src", -1) for o in ops]
    dur = [c + (d + 1.5 if d >= 0 else 0) for c, d in zip(cost, dm)]
    hp = [list(h) for h in hard]; pred = [list(hard[i] | soft[i]) for i in range(n)]; succ = [[] for _ in ops]
    for i in range(n):
        for j in pred[i]: succ[j].append((i, LAT if j in hard[i] else 0.0))

    def run(part, state, end):
        free, bank, bus, top, sent = state; free = free[:]; bank = bank[:]
        for i in part:
            e = eng[i]
            if e == 5:
                t = end[src[i]]
                if bus > t: t = bus
            else:
                t = free[e]
                if out[i]: sent = i
                elif bulk[i] and sent >= 0 and end[sent] + 1.0 > t: t = end[sent] + 1.0
            for j in hp[i]:
                x = end[j] + LAT
                if x > t: t = x
            if dyn[i]:
                for e2 in (0, 1, 2):
                    if e2 != e and bank[e2] + LAT > t: t = bank[e2] + LAT
                bank[e] = t + cost[i]
            t += cost[i]; free[e] = t
            if dm[i] >= 0:
                bus = (bus if bus > t else t) + dm[i]; t = bus + 1.5
            end[i] = t
            if t > top: top = t
        return free, bank, bus, top, sent
    zero = ([0.0] * 6, [-1.0] * 3, 0.0, 0.0, -1); STEP = 32

    def settle(seq):
        end = [0.0] * n; run(seq, zero, end)
        s2 = sorted(range(n), key=lambda p: (end[seq[p]] - dur[seq[p]] if eng[seq[p]] != 5 else end[src[seq[p]]] - cost[src[seq[p]]], p))
        seq = [seq[p] for p in s2]; marks = [zero]
        for p in range(0, n, STEP): marks.append(run(seq[p:p + STEP], marks[-1], end))
        q = [0.0] * n; nx = [0.0] * 6
        for i in reversed(seq):
            t = nx[eng[i]] + cost[i] if eng[i] != 5 else 0.0; u = 0.0
            for j, w in succ[i]:
                if q[j] + w > u: u = q[j] + w
            u += dur[i]
            q[i] = nx[eng[i]] = t if t > u else u
        return seq, end, marks, q
    r = [tune["seed"] * 7919 + 1]

    def rnd():
        r[0] = (r[0] * 1103515245 + 12345) % 2147483648
        return (r[0] + 1) / 2147483649
    seq, end, marks, q = settle(seq); cur = marks[-1][3]; best = (cur, seq); its = tune["renew"]
    for it in range(its):
        k0 = int(rnd() * (n // STEP)); p0 = k0 * STEP; p1 = min(n, p0 + int(tune["w0"] + rnd() * tune["w1"])); win = seq[p0:p1]; ins = set(win)
        noise = tune["noise"] * rnd(); look = rnd() * tune["look"]; pr = {}
        for i in reversed(win):
            u = 0.0
            for j, w in succ[i]:
                x = (pr[j] if j in ins else q[j]) + w
                if x > u: u = x
            pr[i] = u + dur[i]
        key = {i: pr[i] + noise * rnd() for i in win}
        left = {i: sum(1 for j in pred[i] if j in ins) for i in win}
        e2 = end[:]; state = marks[k0]; new = []; ready = {}

        def when(i):
            t = 0.0
            for j in hp[i]:
                if e2[j] + LAT > t: t = e2[j] + LAT
            return t
        for i in win:
            if left[i] == 0: ready[i] = when(i)
        while ready:
            free, bank = state[0], state[1]; b = 1e9
            for i, t in ready.items():
                e = eng[i]
                if free[e] > t and e != 5: t = free[e]
                if dyn[i]:
                    for x in (0, 1, 2):
                        if x != e and bank[x] + LAT > t: t = bank[x] + LAT
                if e == 5: b = -1.0; bi = i; break
                if t < b: b = t; bi = i
            if b >= 0:
                e = eng[bi]; lim = b + look * cost[bi] + 0.02; k = key[bi]
                for i, t in ready.items():
                    if eng[i] == e and t <= lim and key[i] > k: bi = i; k = key[i]
            del ready[bi]; new.append(bi); state = run((bi,), state, e2)
            for j, w in succ[bi]:
                if j in ins:
                    left[j] -= 1
                    if left[j] == 0: ready[j] = when(j)
        if new == win: continue
        val = run(seq[p1:], state, e2)[3]
        if val <= cur - (tune["warm"] * (1 - it / its) + 0.003) * math.log(rnd()):
            seq, end, marks, q = settle(seq[:p0] + new + seq[p1:]); cur = marks[-1][3]
            if cur < best[0]: best = (cur, seq)
    return best[1]


def refine(ops, hard, soft, seq, ms, tune):
    n = len(ops); STEP = 32; nm = len(ms); cost = [costs(ops, m) for m in ms]
    eng = ["VAPGSR".index(o["eng"]) for o in ops]; dyn = ["dyn" in o for o in ops]; bulk = ["bulk" in o for o in ops]; out = [o["kind"] == "s" for o in ops]
    dm = [[o["nbytes"] / m["bw"] if o["kind"] == "d" else -1.0 for o in ops] for m in ms]; src = [o.get("src", -1) for o in ops]
    dur = [[c + (d + ms[k]["dl"] if d >= 0 else 0) for c, d in zip(cost[k], dm[k])] for k in range(nm)]
    hp = [list(h) for h in hard]; pred = [hard[i] | soft[i] for i in range(n)]; succ = [set() for _ in ops]
    for i in range(n):
        for j in pred[i]: succ[j].add(i)
    hs = [[(j, i in hard[j]) for j in succ[i]] for i in range(n)]

    def run(k, part, state, end, by):
        free, lastq, bank, bl, bus, bb, top, arg, sent = state; free = free[:]; lastq = lastq[:]; bank = bank[:]; bl = bl[:]
        LAT = ms[k]["lat"]; co = cost[k]; dk = dm[k]
        for i in part:
            e = eng[i]
            if e == 5:
                b = src[i]; t = end[b]
                if bus > t: t = bus; b = bb
            else:
                t = free[e]; b = lastq[e]
                if out[i]: sent = i
                elif bulk[i] and sent >= 0 and end[sent] + 1.0 > t: t = end[sent] + 1.0; b = sent
            t -= LAT
            for j in hp[i]:
                if end[j] > t: t = end[j]; b = j
            if dyn[i]:
                for e2 in (0, 1, 2):
                    if e2 != e and bank[e2] > t: t = bank[e2]; b = bl[e2]
                bank[e] = t + LAT + co[i]; bl[e] = i
            t += LAT + co[i]; free[e] = t; lastq[e] = i
            if dk[i] >= 0:
                if bus > t: t = bus; b = bb
                bus = t + dk[i]; t = bus + ms[k]["dl"]; bb = i
            end[i] = t; by[i] = b
            if t > top: top = t; arg = i
        return free, lastq, bank, bl, bus, bb, top, arg, sent

    def times(k, seq, k0, old):
        end, by, marks = old[0][:], old[1][:], old[2][:k0 + 1]
        for p in range(k0 * STEP, n, STEP): marks.append(run(k, seq[p:p + STEP], marks[-1], end, by))
        return end, by, marks
    zero = ([0.0] * n, [-1] * n, [([0.0] * 6, [-1] * 6, [-9.0] * 3, [-1] * 3, 0.0, -1, 0.0, -1, -1)])

    def settle(seq, end, k=0):
        d, c = dur[k], cost[k]
        s2 = sorted(range(n), key=lambda p: (end[seq[p]] - d[seq[p]] if eng[seq[p]] != 5 else end[src[seq[p]]] - c[src[seq[p]]], p))
        seq = [seq[p] for p in s2]
        return seq, [times(k, seq, 0, zero) for k in range(nm)]

    def rest(k, seq):
        q = [0.0] * n; nx = [0.0] * 6; LAT = ms[k]["lat"]
        for i in reversed(seq):
            t = nx[eng[i]] + cost[k][i] if eng[i] != 5 else 0.0; u = 0.0
            for j, h in hs[i]:
                x = q[j] + LAT if h else q[j]
                if x > u: u = x
            u += dur[k][i]
            q[i] = nx[eng[i]] = t if t > u else u
        return q
    r = [tune["seed"] * 7919 + 1]

    def rnd():
        r[0] = (r[0] * 1103515245 + 12345) % 2147483648
        return (r[0] + 1) / 2147483649

    def window(k, seq, st, q):
        k0 = int(rnd() * (n // STEP)); p0 = k0 * STEP; p1 = min(n, p0 + int(tune["w0"] + rnd() * tune["w1"])); win = seq[p0:p1]
        new = lay(k, win, st[2][k0], st[0][:], st[1][:], q)
        return None if new == win else (p0, seq[:p0] + new + seq[p1:], p1)

    def lay(k, win, state, e2, b2, q):
        LAT = ms[k]["lat"]; ins = set(win); new = []
        noise = tune["noise"] * rnd(); look = rnd() * tune["look"]; pr = {}
        for i in reversed(win):
            pr[i] = dur[k][i] + max([(pr[j] if j in ins else q[j]) + (LAT if h else 0.0) for j, h in hs[i]] + [0.0])
        key = {i: pr[i] + noise * rnd() for i in win}; left = {i: len(pred[i] & ins) for i in win}
        when = lambda i: max([e2[j] + LAT for j in hp[i]] + [0.0])
        ready = {i: when(i) for i in win if left[i] == 0}
        while ready:
            free, bank = state[0], state[2]; b = 1e9
            for i, t in ready.items():
                e = eng[i]
                if e == 5: b = -1.0; bi = i; break
                if free[e] > t: t = free[e]
                if dyn[i]:
                    for x in (0, 1, 2):
                        if x != e and bank[x] + LAT > t: t = bank[x] + LAT
                if t < b: b = t; bi = i
            if b >= 0:
                e = eng[bi]; lim = b + look * cost[k][bi] + 0.02; ky = key[bi]
                for i, t in ready.items():
                    if eng[i] == e and t <= lim and key[i] > ky: bi = i; ky = key[i]
            del ready[bi]; new.append(bi); state = run(k, (bi,), state, e2, b2)
            for j in succ[bi]:
                if j in ins:
                    left[j] -= 1
                    if left[j] == 0: ready[j] = when(j)
        return new

    def swap(seq, st):
        i = st[2][-1][7]; by = st[1]; lk = []
        while by[i] >= 0:
            if by[i] not in pred[i]: lk.append((by[i], i))
            i = by[i]
        j, i = lk[int(rnd() * len(lk))]; pj = seq.index(j); pi = seq.index(i, pj); mid = seq[pj:pi + 1]
        if rnd() < 0.5:
            mv = {i}
            for x in reversed(mid):
                if not mv.isdisjoint(succ[x]): mv.add(x)
            return None if j in mv else (pj, seq[:pj] + [x for x in mid if x in mv] + [x for x in mid if x not in mv] + seq[pi + 1:], pi + 1)
        mv = {j}
        for x in mid:
            if not mv.isdisjoint(pred[x]): mv.add(x)
        return None if i in mv else (pj, seq[:pj] + [x for x in mid if x not in mv] + [x for x in mid if x in mv] + seq[pi + 1:], pi + 1)
    def tails(k, seq):
        LAT = ms[k]["lat"]; co = cost[k]; dk = dm[k]; q = [0.0] * n; nx = [0.0] * 6; nb = [-99.0] * 3; qb = qs = -99.0; at = [None] * n + [(nx[:], nb[:], qb, qs)]
        for p in range(n - 1, -1, -1):
            i = seq[p]; e = eng[i]; u = 0.0
            for j in far[i]:
                if q[j] > u: u = q[j]
            if u: u += LAT
            if dk[i] >= 0: qb = u = dk[i] + max(ms[k]["dl"] + u, qb)
            if out[i]:
                u = max([u, 1.0 + qs] + [q[j] for j in land[i]]); qs = -99.0
            if e != 5 and nx[e] > u: u = nx[e]
            if dyn[i] and nb[e] > u: u = nb[e]
            q[i] = nx[e] = u = u + co[i]
            if e == 5 and u > qb: qb = u
            if bulk[i] and u > qs: qs = u
            if dyn[i]:
                for x in (0, 1, 2):
                    if x != e and u + LAT > nb[x]: nb[x] = u + LAT
            at[p] = (nx[:], nb[:], qb, qs)
        return q, at

    def sweep(seq, heat, W, tries):
        seq = seq[:]; tl = [tails(k, seq) for k in range(nm)]; pos = {i: p for p, i in enumerate(seq)}
        state = [zero[2][0]] * nm; end = [[0.0] * n for k in range(nm)]; by = [[-1] * n for k in range(nm)]; over = [[] for k in range(nm)]
        for p0 in range(0, n, W // 3):
            p1 = min(n, p0 + W); win = seq[p0:p1]; ins = set(win); ex = []; base = []
            for k in range(nm):
                q = tl[k][0]; LAT = ms[k]["lat"]
                ex.append([(i, max([q[j] + LAT for j in far[i] if pos[j] >= p1] + [q[j] for j in land[i] if pos[j] >= p1])) for i in win if last[i](pos) >= p1])
                over[k] = [x for x in over[k] if x[0] >= p1]; base.append(max([x[1] for x in over[k]] + [0.0]))

            def value(win):
                tot = 0.0; args = []
                for k in range(nm):
                    en = end[k]; s = run(k, win, state[k], en, by[k]); nx, nb, qb, qs = tl[k][1][p1]
                    c = [(en[i] + x, i) for i, x in ex[k]] + [(s[0][e] + nx[e], s[1][e]) for e in range(5)] + [(s[2][e] + nb[e], s[3][e]) for e in range(3)]
                    c += [(s[4] + qb, s[5]), (s[6], s[7]), (en[s[8]] + 1.0 + qs, s[8])]
                    m, a = max(c); args.append(a); t = max(m, base[k])
                    tot += w[k] * (t + tune["soft"] * math.log(math.exp((base[k] - t) / tune["soft"]) + sum([math.exp((x - t) / tune["soft"]) for x, i in c if x > t - 2.0])))
                return tot, args
            cur, args = value(win); lk = None
            for it in range(tries):
                if lk is None:
                    lk = []
                    for k in range(nm):
                        i = args[k]
                        while i in ins and by[k][i] in ins:
                            if by[k][i] not in pred[i]: lk.append((by[k][i], i))
                            i = by[k][i]
                if not lk: break
                j, i = lk[int(rnd() * len(lk))]; pj = win.index(j); pi = win.index(i); mid = win[pj:pi + 1]
                if it < tune["lays"]:
                    k = int(rnd() * nm); new = lay(k, win, state[k], end[k], by[k][:], tl[k][0])
                    if new == win: continue
                elif rnd() < 0.5:
                    mv = {i}
                    for x in reversed(mid):
                        if not mv.isdisjoint(succ[x]): mv.add(x)
                    if j in mv: continue
                    new = win[:pj] + [x for x in mid if x in mv] + [x for x in mid if x not in mv] + win[pi + 1:]
                else:
                    mv = {j}
                    for x in mid:
                        if not mv.isdisjoint(pred[x]): mv.add(x)
                    if i in mv: continue
                    new = win[:pj] + [x for x in mid if x not in mv] + [x for x in mid if x in mv] + win[pi + 1:]
                val, a2 = value(new)
                if val <= cur - heat * math.log(rnd()): win, cur, args, lk = new, val, a2, None
            seq[p0:p1] = win
            for k in range(nm):
                part = win[:W // 3]; state[k] = run(k, part, state[k], end[k], by[k]); q = tl[k][0]; lim = q[seq[0]] - 4.0
                over[k] += [x for i in part for x in [(pos[j], end[k][i] + ms[k]["lat"] + q[j]) for j in far[i]] + [(pos[j], end[k][i] + q[j]) for j in land[i]] if x[1] > lim]
        return seq
    far = [[j for j, h in x if h] for x in hs]; land = [[j for j in succ[i] if src[j] == i] for i in range(n)]
    last = [(lambda pos, js=far[i] + land[i]: max([pos[j] for j in js] + [-1])) for i in range(n)]
    seq, st = settle(seq, times(0, seq, 0, zero)[0]); top = lambda s: s[2][-1][6]
    w = [90.0 / nm / top(s) for s in st]; cur = sum(a * top(s) for a, s in zip(w, st)); best = (cur, seq); q = {}
    for move, its, heat in ((0, tune["renew"], tune["warm"]), (1, tune["polish"], tune["heat"])) * tune["rounds"]:
        seq = best[1]; seq, st = settle(seq, times(0, seq, 0, zero)[0]); cur = best[0]; q = {}
        for it in range(its):
            k = it % nm
            if move == 0 and it % tune["age"] == 0:
                seq, st = settle(seq, st[k][0], k); cur = sum(a * top(s) for a, s in zip(w, st)); q = [rest(a, seq) for a in range(nm)]
            new = swap(seq, st[k]) if move else window(k, seq, st[k], q[k])
            if not new: continue
            lim = cur - (heat * (1 - it / its) + 0.003) * math.log(rnd()); s2 = st[:]; val = cur
            for a in range(nm):
                k2 = (k + a) % nm; s2[k2] = times(k2, new[1], new[0] // STEP, st[k2]); val += w[k2] * (top(s2[k2]) - top(st[k2]))
                if val > lim + tune["hope"] * (nm - 1 - a): break
            if val <= lim:
                seq, st, cur = new[1], s2, val
                if cur < best[0]: best = (cur, seq)
    seq = best[1]
    for it in range(tune["sweeps"]):
        seq = sweep(seq, tune["cool"] * (1 - it / tune["sweeps"]) + 0.002, tune["narrow"] + 3 * int(rnd() * tune["wide"]), tune["tries"])
        seq, st = settle(seq, times(it % nm, seq, 0, zero)[0], it % nm); cur = sum(a * top(s) for a, s in zip(w, st))
        if cur < best[0]: best = (cur, seq)
    return best[1]


def plan(ops, hard, soft, m, tune):
    return refine(ops, hard, soft, order(ops, hard, soft, m, tune), [dict(m, **x) for x in tune["also"]], tune)


def polish(ops, hard, soft, seq, m, tune):
    n = len(ops); LAT = m["lat"]; cost = costs(ops, m); STEP = 64
    eng = ["VAPGSR".index(o["eng"]) for o in ops]; dyn = ["dyn" in o for o in ops]; bulk = ["bulk" in o for o in ops]; out = [o["kind"] == "s" for o in ops]
    dm = [o["nbytes"] / m["bw"] if o["kind"] == "d" else -1.0 for o in ops]; src = [o.get("src", -1) for o in ops]
    hp = [list(h) for h in hard]; pred = [hard[i] | soft[i] for i in range(n)]; succ = [set() for _ in ops]
    for i in range(n):
        for j in pred[i]: succ[j].add(i)

    def run(seq, k0, end, by, marks):
        free, lastq, bank, bl, bus, top, arg, sent, bb = marks[k0]; free = free[:]; lastq = lastq[:]; bank = bank[:]; bl = bl[:]; marks = marks[:k0 + 1]
        for p in range(k0 * STEP, n, STEP):
            for i in seq[p:p + STEP]:
                e = eng[i]
                if e == 5:
                    b = src[i]; t = end[b]
                    if bus > t: t = bus; b = bb
                else:
                    t = free[e]; b = lastq[e]
                    if out[i]: sent = i
                if bulk[i] and sent >= 0 and end[sent] + 1.0 > t: t = end[sent] + 1.0; b = sent
                for j in hp[i]:
                    x = end[j] + LAT
                    if x > t: t = x; b = j
                if dyn[i]:
                    for e2 in (0, 1, 2):
                        if e2 != e and bank[e2] + LAT > t: t = bank[e2] + LAT; b = bl[e2]
                    bank[e] = t + cost[i]; bl[e] = i
                t += cost[i]; free[e] = t; lastq[e] = i
                if dm[i] >= 0:
                    if bus > t: t = bus; b = bb
                    bus = t + dm[i]; t = bus + 1.5; bb = i
                end[i] = t; by[i] = b
                if t > top: top = t; arg = i
            marks.append((free[:], lastq[:], bank[:], bl[:], bus, top, arg, sent, bb))
        return top, arg, marks

    def links(i, by):
        out = []
        while by[i] >= 0:
            if by[i] not in pred[i]: out.append((by[i], i))
            i = by[i]
        return out
    r = 1; end = [0.0] * n; by = [-1] * n; its = tune["polish"]
    cur, arg, marks = run(seq, 0, end, by, [([0.0] * 6, [-1] * 6, [-1.0] * 3, [-1] * 3, 0.0, 0.0, -1, -1, -1)])
    best = (cur, seq); lk = links(arg, by)
    for it in range(its):
        r = (r * 1103515245 + 12345) % 2147483648
        j, i = lk[(r >> 8) % len(lk)]; pj = seq.index(j); pi = seq.index(i, pj); mid = seq[pj:pi + 1]
        if r >> 7 & 1:
            mv = {i}
            for x in reversed(mid):
                if not mv.isdisjoint(succ[x]): mv.add(x)
            if j in mv: continue
            mid = [x for x in mid if x in mv] + [x for x in mid if x not in mv]
        else:
            mv = {j}
            for x in mid:
                if not mv.isdisjoint(pred[x]): mv.add(x)
            if i in mv: continue
            mid = [x for x in mid if x not in mv] + [x for x in mid if x in mv]
        new = seq[:pj] + mid + seq[pi + 1:]; e2 = end[:]; b2 = by[:]
        val, a2, m2 = run(new, pj // STEP, e2, b2, marks)
        r = (r * 1103515245 + 12345) % 2147483648
        if val <= cur - (tune["heat"] * (1 - it / its) + 0.01) * math.log((r + 1) / 2147483648):
            seq, cur, end, by, marks = new, val, e2, b2, m2; lk = links(a2, by)
            if cur < best[0]: best = (cur, seq)
    return best[1]


def rank_program(g, core, T, topo):
    rank = T.rank_of(core)
    if rank is None:
        return
    if "ops" not in PLAN:
        PLAN["ops"] = build(); PLAN["hard"], soft = depend(PLAN["ops"])
        PLAN["seq"] = plan(PLAN["ops"], PLAN["hard"], soft, MODEL, TUNE)
        PLAN["hard"] = turns(PLAN["ops"], PLAN["hard"], PLAN["seq"])
    ops, hard = PLAN["ops"], PLAN["hard"]; cores = T.cores; N = len(cores)

    def share(back, ks):
        src = (rank - back) % N; sets = [topo.engines(cores[src], cores[(src + k) % N]) for k in ks]
        es = [e for e in sets[0] if all(e in s for s in sets)]; n = len(es) // len(ks)
        return [es[j * n:(j + 1) * n] for j in range(len(ks))]
    c = {"core": core, "topo": topo, "ahead": lambda k: cores[(rank + k) % N], "share": share}
    qs = {"V": g.vector, "A": g.scalar, "P": g.tensor, "G": g, "S": g.sync}
    know = {e: {} for e in qs}; count = {}; done = {}
    for i in PLAN["seq"]:
        o = ops[i]; e = o["eng"]
        if o["kind"] == "r":
            n = len(share(o["k"], o["ks"])[0])
            count[o["sem"]] = n; done[i] = (o["sem"], n, {o["sem"]: n})
            continue
        kn = know[e]
        for s, n, kj in sorted((done[j] for j in hard[i]), key=lambda d: -d[1]):
            if kn.get(s, 0) < n:
                qs[e].wait_ge(T.sem[s], n)
                for s2, n2 in kj.items():
                    if kn.get(s2, 0) < n2: kn[s2] = n2
        ins = o["fn"](g, T, c)
        if e == "G" and o["kind"] == "c":
            s, n = o["sem"], o["cnt"]; ins.then_inc(T.sem[s], 1)
        elif o["kind"] == "c":
            s = QSEM[e]; n = count.get(s, 0) + 1; ins.then_inc(T.sem[s], 1)
        elif o["kind"] == "d":
            s = o["sem"]; n = 16; ins.then_inc(T.sem[s], 16)
        else:
            s = o["sem"]; n = sum(len(x) for x in share(0, o["ks"]))
        count[s] = n; kj = dict(kn); kj[s] = n; done[i] = (s, n, kj)
    for s, n in count.items():
        if know["G"].get(s, 0) < n: g.wait_ge(T.sem[s], n)
